import numpy as np, ml_dtypes
CORES = [1,5,17,21,33,37,49,53]
N = 8
BF = ml_dtypes.bfloat16
def gentries(a):
    return np.ascontiguousarray(a.reshape(8, 16, -1).transpose(0, 2, 1)).reshape(8, -1)
def gtable(e):
    e = np.asarray(e); return np.ascontiguousarray(e.reshape(8, -1, 16).transpose(0, 2, 1)).reshape(128, -1).astype(np.int32)
V, NL, NB, L, CAP, T = 1536, 5120, 2048, 384, 192, 5
CN, Q = 128, NL // 64
D = np.arange(16)
def nearby(rng, J, K, P):
    a = 2 * int(rng.integers(0, 8)); x = int(rng.integers(0, 16))
    P[2, a] = rng.integers(1, 8); P[2, a + 1] = rng.integers(-7, 7); P[3] = P[2]; P[3, a] -= 8; P[3, a + 1] += 1
    P[6, x] = rng.integers(-5, 8); P[7] = P[6]; P[7, x] -= 2
    P[10, x] = rng.integers(-7, 7); P[11] = P[10]; P[11, x] += 1
    for r in range(8):
        c = 64 + r; o = rng.permutation(16); d = 2 * int(rng.integers(0, 8))
        J[c, o[:8]] = 7; J[c, o[8:15]] = 6; J[c, o[15]] = 0
        K[c] = rng.integers(0, Q, 16); K[c, d] = 6; K[c, d + 1] = 10; K[c, d ^ 2] = 2
        for k in range(1, 5): J[c + 8 * k] = J[c]; K[c + 8 * k] = K[c]
        J[c + 8, o[15]] = 1
        J[c + 16, o[0]] = 6; J[c + 16, o[8]] = 7
        K[c + 24, d ^ 2] = 3
        K[c + 32, d] = 7; K[c + 32, d + 1] = 11
def classes(rng, how):
    c = np.arange(CN); fam = (c // 8 % 4)[:, None]; q = np.arange(Q)[:, None]; bits = 1 << rng.integers(0, 4, 3)
    if how == "ends":
        k = rng.integers(0, 17, CN); k[[0, 8, 16, 24]] = (16, 0, 1, 15)
        J = 7 * (np.argsort(rng.random((CN, 16)), axis=1) < k[:, None]); K = rng.integers(0, 2, (CN, 16)); K[0] = 0; K[8] = 1
        P = 7 - 14 * rng.integers(0, 2, (Q, 16)); P[1] = 7
        return J, K, P
    J = rng.integers(0, 8, (CN, 16)); K = rng.integers(0, Q, (CN, 16)); P = rng.integers(-7, 8, (Q, 16))
    mk = np.where(c // 32 == 0, 15 - bits[0], 15)
    if how == "spread":
        J = (8 * rng.random((CN, 16)) ** 3).astype(np.int64); P = np.rint(rng.integers(1, 8, (Q, 1)) * (2 * rng.random((Q, 16)) - 1)).astype(np.int64)
    if how == "alike": mk = rng.choice(np.array([0, 1, 6, 8, 9, 15]), CN)
    K = np.where(fam == 0, K // 4 * 4, np.where(fam == 1, K // 4 * 4 + 1, K))
    if how == "alike": K[c // 32 == 1] = 0
    km = np.where(rng.random(CN) < 0.5, mk, 15)
    J = np.take_along_axis(J, D[None, :] & mk[:, None], 1); K = np.take_along_axis(K, D[None, :] & km[:, None], 1)
    P = np.where(q % 4 == 0, P[:, D & (15 - bits[1])], P)
    P = np.where(q % 4 == 1, P[:, D & (15 - bits[2])] * (1 - 2 * ((D & bits[2]) > 0)), P)
    if how == "alike":
        P[0] = 0; nearby(rng, J, K, P)
    else:
        pa = np.where(mk == 15, 1, 15 - mk); J[c, 0] = 0; J[c, pa] = 0
        x = (c - np.add.reduce(J, axis=1) // 2) % 8; J[c, 0] = x; J[c, pa] = x
    return J, K, P
def swap(p, i, x):
    j = int(np.flatnonzero(p == x)[0]); p[j] = p[i]; p[i] = x
def places(rng, J, K, P, faults, ends=False):
    idx = np.argsort(rng.random((N, 8, V)), axis=-1); cp = np.argsort(rng.random((N, 8, NL)), axis=-1)
    sh = rng.integers(0, 16, (N, 8, V)); lm = rng.integers(0, 16, (N, 8, V)); ls = rng.integers(0, 2, (N, 8, V))
    if ends:
        own = rng.random((N, 8, V)) < 0.75; own[..., 0] = True; own[..., V - 1] = True
        pm = 15 * rng.integers(0, 2, (N, 8, 1)); ps = rng.integers(0, 2, (N, 8, 1)); lm = np.where(own, pm, lm); ls = np.where(own, ps, ls)
        sh[..., 0] = 15 * rng.integers(0, 2, (N, 8)); sh[..., V - 1] = 15 * rng.integers(0, 2, (N, 8))
        for q in range(N):
            for h in range(8):
                z = rng.permutation(np.array([0, 8, 16, 24]))[:2] + CN * rng.integers(0, 2, 2)
                if q == N - 1 and h == 7: z = np.array([8, 0])
                swap(idx[q, h], 0, int(z[0])); swap(idx[q, h], V - 1, int(z[1]))
                tr = int(2 * pm[q, h, 0] + ps[q, h, 0]); swap(cp[q, h], tr, 0); swap(cp[q, h], 32 + tr, NL - 1)
    cls = (idx % CN)[:, :, None, :]; fault = np.where(idx // CN % 2 == 0, 0, rng.choice(np.array(faults), (N, 8, V)))[:, :, None, :]
    e = D[:, None] ^ sh[:, :, None, :]; iv = J[cls, e]; lc = K[cls, e]
    at = rng.integers(0, 16, (N, 8, 1, V)) == D[:, None]
    lc = np.where(at & (fault == 4), (lc + rng.integers(1, Q, (N, 8, 1, V))) % Q, lc)
    m = np.where(at & (fault == 2), (lm ^ rng.integers(1, 16, (N, 8, V)))[:, :, None, :], lm[:, :, None, :])
    s = np.where(at & (fault == 3), 1 - ls[:, :, None, :], ls[:, :, None, :])
    made = lc * 32 + m * 2 + s + (at & (fault == 1)) * (NL // 2)
    kids = np.take_along_axis(cp, made.reshape(N, 8, 16 * V), 2).reshape(N, 8, 16, V)
    i = np.arange(NL // 2); z = (P[i // 32, D[:, None] ^ (i % 32 // 2)] * (1 - 2 * (i % 2))).astype(np.int8)
    near = np.where(rng.integers(0, 16, (N, 8, 1, NL // 2)) == D[:, None], np.where(z > 0, z - 1, z + 1), z).astype(np.int8)
    x = np.concatenate([np.broadcast_to(z, near.shape), near], axis=3)
    lf = np.take_along_axis(x, np.argsort(cp, axis=-1)[:, :, None, :], 3)
    return lf, iv, kids, idx, np.argsort(idx, axis=-1)
def nodes(rng, inv, odd):
    c = np.arange(N)[:, None, None] + 8 * rng.integers(0, CN // 8, (N, 8, L))
    return np.take_along_axis(inv, (2 * rng.integers(0, V // CN // 2, (N, 8, L)) + (rng.random((N, 8, L)) < odd)) * CN + c, 2)
def cold(rng, inv):
    col = np.array([7 if N < 8 else (q + 1) % 8 for q in range(N)])[:, None, None]
    code = col + 8 * rng.integers(0, CN // 8, (N, 8, 16 * NB)) + CN * rng.integers(0, V // CN, (N, 8, 16 * NB))
    return np.take_along_axis(inv, code, 2).reshape(N, 8, 16, NB)
def buckets(rng, inv, idx, v, b, want, base, reps):
    bk = base.copy()
    for t in range(T):
        for q in range(N):
            for h in range(8):
                r, g = (q - t) % N, (h - t * (t + 1) // 2) % 8
                c = idx[r, g][v[r, g]] % CN; w = want[r, g, t]
                for j in range(reps):
                    odd = np.where(w == 3, rng.integers(0, 2, L), (w == 1).astype(np.int64))
                    n = inv[q, h][(2 * rng.integers(0, V // CN // 2, L) + odd) * CN + c]
                    on = (w > 0) & ((j == 0) | (rng.random(L) < 0.4))
                    bk[q, h, 3 * t + j, b[r, g][on]] = n[on]
    return np.take_along_axis(bk, np.argsort(rng.random(bk.shape), axis=2), 2)
def wish(rng, rates, values):
    rate = rng.choice(np.array(rates), (N, 8, T, 1))
    return np.where(rng.random((N, 8, T, L)) < rate, rng.choice(np.array(values), (N, 8, T, L)), 0)
def pack(lf, iv, kids, bk, v, b):
    return {"lf": lf.reshape(N, 128, NL).astype(np.float32).astype(BF), "iv": iv.reshape(N, 128, V).astype(np.float32).astype(BF), "kd": kids.reshape(N, 128, V).astype(np.int32),
            "bk": bk.reshape(N, 128, NB).astype(np.int32), "lv": np.stack([gtable(x) for x in v]), "lb": np.stack([gtable(x) for x in b])}
def setup_inputs(rng):
    lf, iv, kids, idx, inv = places(rng, *classes(rng, "plain"), (1, 2, 3, 4))
    v = nodes(rng, inv, 0.2); b = rng.integers(0, NB, (N, 8, L))
    bk = buckets(rng, inv, idx, v, b, wish(rng, [0.25, 0.5, 0.75, 0.97], [1, 2, 2, 3]), rng.integers(0, V, (N, 8, 16, NB)), 3)
    return pack(lf, iv, kids, bk, v, b)
def setup_inputs_spread(rng):
    lf, iv, kids, idx, inv = places(rng, *classes(rng, "spread"), (1, 2, 3, 4))
    v = nodes(rng, inv, 0.2); b = (NB * rng.random((N, 8, L)) ** 2).astype(np.int64)
    bk = buckets(rng, inv, idx, v, b, wish(rng, [0.1, 0.6, 0.9, 1.0], [1, 2, 2, 3]), (V * rng.random((N, 8, 16, NB)) ** 3).astype(np.int64), 3)
    return pack(lf, iv, kids, bk, v, b)
def setup_inputs_alike(rng):
    lf, iv, kids, idx, inv = places(rng, *classes(rng, "alike"), (1, 2, 3, 4))
    v = nodes(rng, inv, 0.2); b = rng.integers(0, NB, (N, 8, L)); want = wish(rng, [0.3, 0.6, 0.9], [1, 2, 2, 3]); n4 = L // 4
    v[..., 1::4] = np.take_along_axis(inv, 64 + np.arange(N)[:, None, None] + 2 * CN * rng.integers(0, V // CN // 2, (N, 8, n4)), 2); want[..., 1::4] = 0
    bk = buckets(rng, inv, idx, v, b, want, rng.integers(0, V, (N, 8, 16, NB)), 3)
    for r in range(N):
        for g in range(8):
            when = rng.integers(0, T, n4); how = rng.integers(1, 5, n4)
            for t in range(T):
                q, h = (r + t) % N, (g + t * (t + 1) // 2) % 8; on = np.flatnonzero(when == t)
                code = 64 + r + 2 * CN * rng.integers(0, V // CN // 2, (16, len(on))); code[:15] += 8 * how[on]
                bk[q, h][:, b[r, g, 1::4][on]] = inv[q, h][code]
    return pack(lf, iv, kids, bk, v, b)
def setup_inputs_corners(rng):
    lf, iv, kids, idx, inv = places(rng, *classes(rng, "plain"), (1,))
    v = nodes(rng, inv, 0.0); b = np.argsort(rng.random((N, 8, NB)), axis=-1)[..., :L]; want = np.zeros((N, 8, T, L), np.int64)
    counts = (0, 1, CAP - 1, CAP, CAP + 1, L)
    for r in range(N):
        full = (5 * r + 2) % 8
        for g in range(8):
            e = 7 * r + g - int(g > full)
            ts = e % T
            for t in range(T):
                n = counts[int(rng.integers(0, 6))]
                if t == ts: n = counts[(e // T + 2 * ts) % 6]
                want[r, g, t, rng.permutation(L)[:n]] = 1 if t < ts else 2
            if g == full:
                c = r + 8 * rng.integers(4, CN // 8, L); v[r, g] = inv[r, g][2 * CN * rng.integers(0, V // CN // 2, L) + c]
                want[r, g] = 2; want[r, g][:T - 1, rng.permutation(L)[:r % 4]] = 0
    return pack(lf, iv, kids, buckets(rng, inv, idx, v, b, want, cold(rng, inv), 3), v, b)
def setup_inputs_crowd(rng):
    lf, iv, kids, idx, inv = places(rng, *classes(rng, "plain"), (1,))
    v = nodes(rng, inv, 0.0); b = np.argsort(rng.random((N, 8, NB)), axis=-1)[..., :L].copy(); want = np.zeros((N, 8, T, L), np.int64)
    for r in range(N):
        for g in range(8):
            if g % 4 == 3:
                i = rng.integers(0, 3, L); v[r, g] = v[r, g, :3][i]; b[r, g] = b[r, g, :3][i]; want[r, g] = rng.integers(0, 3, (T, 3))[:, i]
                continue
            x = (r + g // 2) % T; v0, v1, b0 = int(v[r, g, 0]), int(v[r, g, 1]), int(b[r, g, 0]); e = int(rng.integers(0, L))
            v[r, g] = v0; b[r, g] = b0; want[r, g, :x] = 1; want[r, g, x:] = 2
            if g % 2 == 1: v[r, g, e] = v1; b[r, g, e] = (b0 + 1) % NB; want[r, g, :, e] = 0
    return pack(lf, iv, kids, buckets(rng, inv, idx, v, b, want, cold(rng, inv), 3), v, b)
def setup_inputs_ends(rng):
    lf, iv, kids, idx, inv = places(rng, *classes(rng, "ends"), (1, 2, 3), True)
    u = rng.random((N, 8, L)); v = np.where(u < 0.35, 0, np.where(u < 0.7, V - 1, nodes(rng, inv, 0.2)))
    u = rng.random((N, 8, L)); b = np.where(u < 0.35, 0, np.where(u < 0.7, NB - 1, rng.integers(0, NB, (N, 8, L))))
    v[..., 0] = 0; b[..., 0] = 0; v[..., L - 1] = V - 1; b[..., L - 1] = NB - 1
    base = (V - 1) * np.where(rng.random((N, 8, 1, NB)) < 0.25, rng.integers(0, 2, (N, 8, 16, NB)), rng.integers(0, 2, (N, 8, 1, NB)))
    bk = buckets(rng, inv, idx, v, b, wish(rng, [0.4, 0.7], [1, 2, 2]), base, 1)
    bk[:, :, :15, 0] = V - 1; bk[:, :, 15, 0] = 0; bk[:, :, :15, NB - 1] = 0; bk[:, :, 15, NB - 1] = V - 1
    return pack(lf, iv, kids, bk, v, b)
def check_inputs(d):
    bad = []
    for k, lo, hi in (("lf", -7, 7), ("iv", 0, 7), ("kd", 0, NL - 1), ("bk", 0, V - 1), ("lv", 0, V - 1), ("lb", 0, NB - 1)):
        x = np.asarray(d[k]).astype(np.float64)
        if not (np.min(x) >= lo and np.max(x) <= hi): bad.append("range of " + k)
        if np.any(x != np.floor(x)): bad.append("whole numbers of " + k)
    return bad
def codes(x, base):
    return np.matmul(np.swapaxes(x, -1, -2), base ** (D[:, None] ^ D[None, :]))
def reference(lf, iv, kd, bk, lv, lb):
    x = lf.astype(np.float32).astype(np.int64).reshape(N, 8, 16, NL); inv = iv.astype(np.float32).astype(np.int64).reshape(N, 8, 16, V)
    kids = kd.astype(np.int64).reshape(N, 8, 16, V); slots = bk.astype(np.int64).reshape(N, 8, 16, NB)
    v = np.stack([gentries(e) for e in lv]).astype(np.int64); b = np.stack([gentries(e) for e in lb]).astype(np.int64)
    node = codes(inv, 8)
    leaf = np.stack([codes(7 + x, 15), codes(7 - x, 15)], axis=-1)
    live = np.ones((N, 8, L), bool); out = np.zeros((N, 8, 5, L), np.int64); out[:, :, 0] = -1
    for t in range(T):
        for r in range(N):
            for g in range(8):
                q, h = (r + t) % N, (g + t * (t + 1) // 2) % 8; vv = v[r, g]
                w = slots[q, h][:, b[r, g]].T
                hit = (node[q, h][w] == node[r, g][vv, 0][:, None, None]).reshape(L, 256) & live[r, g][:, None]
                lanes = np.flatnonzero(np.any(hit, axis=1))[:CAP]
                first = np.argmax(hit[lanes], axis=1); w = w[lanes, first >> 4]; M = first & 15
                A = leaf[r, g][kids[r, g][:, vv[lanes]], 0, 0]
                B = leaf[q, h][kids[q, h][D[:, None] ^ M[None, :], w[None, :]]]
                same = np.all(B == A[:, :, None, None], axis=0).reshape(len(lanes), 32)
                won = np.any(same, axis=1); s = np.argmax(same, axis=1)[won]; j = lanes[won]
                out[r, g][:, j] = np.stack([np.full(len(j), q), w[won], M[won], s >> 1, 1 - 2 * (s & 1)])
                live[r, g, j] = False
    return {"y": out.reshape(N, 40, L).astype(np.float32)}

@@ -1,0 +1,823 @@
+import numpy as np
+from concourse.bass import DstId, RemoteDMATransfer, IndirectOffsetOnAxis
+from concourse.mybir import AluOpType as ALU, ActivationFunctionType as ACT
+
+NR, NV, NL, NB, L, CAP, NT = 8, 1536, 5120, 2048, 384, 192, 5
+SH = [t * (t + 1) // 2 % 8 for t in range(NT)]
+HF = "float16"
+AOFF = 7 * 4369
+MID = 4.0 * (8 ** 8 - 1) / 7
+BIG = 4096.0
+
+KB_NAMES = ["Z", "E", "BS", "I", "I2", "LS", "FT", "WHI", "WLO", "LVH", "LVL", "PAY", "TRIU", "ONES",
+            "H", "FP", "FM", "LT0", "LT1", "RP", "RM"]
+KH_NAMES = ["CROW", "CROW2", "CONE", "I", "NI", "PW"]
+ONPE = ()
+KF_NAMES = ["I", "H"] + (["NH"] if ONPE else [])
+SCALED = [("I16", "I", 16.0), ("I256", "I", 256.0), ("I4096", "I", 4096.0), ("I22", "I", 2.0 ** 22), ("I44", "I", 2.0 ** 44), ("I66", "I", 2.0 ** 66)]
+SCALED += [("H%d_%d" % (w, i), "H", 2.0 ** (22 * w + 4 * i)) for w in range(4) for i in range(4) if w or i]
+NKB, NKH, NKF = len(KB_NAMES), len(KH_NAMES), len(KF_NAMES)
+NMAT = NKB + NKH + NKF
+
+
+def _sb(n, d):
+    return ("sbuf", [128, n], d)
+
+
+F, B, I32, U = "float32", "bfloat16", "int32", "uint16"
+SCRATCH = {
+    "LF": _sb(NL, B), "IV": _sb(NV, B), "KD": _sb(4 * NV, I32), "BK": _sb(NB, I32), "LVI": _sb(24, I32), "LBI": _sb(120, I32),
+    "PI": _sb(1, I32), "RBI": _sb(12, I32), "RB": _sb(12, F), "S1": _sb(8, F), "XB": _sb(64, F), "X": _sb(16, F),
+    "EB": _sb(64, F), "FB": _sb(64, F), "TM": _sb(128, F), "HB": _sb(96, F), "G3": _sb(24, F), "CC": _sb(16, F),
+    "KT": _sb(16 * (NMAT + 2), F), "KTC": _sb(32, F), "OA": _sb(8 * NMAT, F), "OB": _sb(8 * NMAT, F), "OU": _sb(8 * NMAT, U),
+    "OCA": _sb(8, F), "OCB": _sb(8, F), "OCU": _sb(8, U),
+    "KB": _sb(128 * (NKB + len(SCALED)), B), "KH": _sb(128 * NKH, HF), "KF": _sb(128 * NKF, F), "WC": _sb(128, B),
+    "IOT": _sb(384, F), "CJ": _sb(384, HF), "DJ": _sb(24, HF), "DJ1": _sb(24, F), "JT": _sb(24, F), "ONE": _sb(24, F),
+    "GI": _sb(8, I32), "GF": _sb(8, F), "OUTM": _sb(5 * 208, HF), "CN": _sb(128, HF), "KIX": _sb(4, I32), "KIF": _sb(4, F),
+    "RS": _sb(768, B),
+    "WI": _sb(384, F), "WP": _sb(384, F), "ZO": _sb(6, F), "ZU": _sb(6, U), "NTT": _sb(NV, B), "NTB": _sb(NV, B),
+    "LVU": _sb(24, U), "KA": _sb(384, U), "XC": _sb(16 * L, B), "XA": _sb(16 * L, B), "XT": _sb(32 * CAP, B),
+    "AU": _sb(5 * 1536, U), "AR": _sb(3 * 1536, F), "LT": _sb(5 * 384, B),
+    "LBU": _sb(120, U), "WF": _sb(768, F), "WU": _sb(768, U), "NE": _sb(768, B), "FIT": _sb(384, B), "VAL": _sb(384, HF),
+    "WX": _sb(24, U), "WL": _sb(24, F), "CL": _sb(120, F), "CLJ": _sb(120, F), "IW": _sb(384, B), "FM": _sb(384, B), "OH": _sb(384, B),
+    "P": _sb(2000, F), "KP": _sb(768, F), "MP": _sb(384, HF),
+    "LV": _sb(5 * 24, B), "CAND": _sb(24, B), "CANJ": _sb(24, HF), "CUM": _sb(24, F), "RI": _sb(24, F),
+    "RU": _sb(24, F), "POS": _sb(24, U), "POS2": _sb(24, U), "Z": _sb(1184, F), "ZT": _sb(384, F), "LLU": _sb(80, U),
+    "KL": _sb(192, U), "AF": _sb(1536, F), "AH": _sb(1536, F), "DM": _sb(1536, B), "DP": _sb(1536, B), "BD": _sb(768, B),
+    "KU": _sb(1920, U), "ALU": _sb(800, U), "ZA": _sb(768, F), "ZV": _sb(10, U), "ZW": _sb(16, F), "RESF": _sb(384, B), "ROF": _sb(1920, HF),
+    "NOK": _sb(120, F), "MG": _sb(24, B), "TF": _sb(768, B), "TO": _sb(768, B), "RES": _sb(208, B), "MSG": _sb(4 * 24, B), "RO": _sb(384, HF),
+    "OM": _sb(5 * 128, HF), "OL": _sb(4 * 128, HF), "ACC": _sb(128, F),
+    "DLB": ("dram", [240, 24], I32), "DLT": ("dram", [240, 384], B), "DAU": ("dram", [240, 1536], U),
+}
+for _i in range(8):
+    SCRATCH["B%d" % _i] = ("psum", [128, 512], F)
+DMA_SEMS = ["d%d" % _i for _i in range(24)]
+ARR_SEMS = ["a_%s%d" % (k, t) for k in ("lb", "lt", "au", "lv", "om") for t in range(1, NT)]
+SEMAPHORES = ["sV", "sS", "sP", "sG", "sent"] + DMA_SEMS + ARR_SEMS
+
+CY, PCY, GF_, LAT = 1.04e-3, 0.52e-3, 1.56, 0.15
+VBIAS = 1.0
+AHEAD = (3, 4)
+CORDER = (0, 1, 3, 2, 4)
+ROUNDS, SEED, HEAT, TURN = 3500, 2, 0.4, 0.15
+MODELS = ((0.75, 0.9, 0.1, 0.8), (1.25, 1.0, 0.25, 1.3), (1.0, 1.15, 0.2, 1.0))
+OFFS = {"N": 20, "A": 30}
+PCC, PCT, CH1, CH2 = 96, 96, 32, 96
+CHC = 96
+PLAN = {}
+
+
+def A(name, lo, hi, step=1):
+    return (name, lo, hi, step)
+
+
+def cnt(a):
+    return (a[2] - a[1] + a[3] - 1) // a[3]
+
+
+def build(g, T, topo, core, rank):
+    ops = []
+    nd = [0]
+    tag = ["K"]
+
+    def ap(a):
+        return T[a[0]][:, a[1]:a[2]:a[3]] if a[3] != 1 else T[a[0]][:, a[1]:a[2]]
+
+    def two(*aps):
+        return all(SCRATCH[a[0]][2] in (B, HF, U) for a in aps)
+
+    def add(alts, reads, writes, **kw):
+        o = {"alts": alts, "r": [a for a in reads if isinstance(a, tuple)], "w": list(writes), "tag": tag[0]}
+        o.update(kw)
+        ops.append(o)
+        return len(ops) - 1
+
+    def sc(x):
+        return ap(x) if isinstance(x, tuple) else x
+
+    def src(i, off):
+        return ap(i).indirect(ap(off)) if off else ap(i)
+
+    def cost(out, i, off, c=1.0):
+        n = cnt(out)
+        if off:
+            return 0.06 + n * GF_ * CY
+        return 0.06 + max(64, n * c * (0.5 if two(out, i) else 1.0)) * CY
+
+    def okS(*aps):
+        return all(SCRATCH[a[0]][2] in (B, F) for a in aps)
+
+    def act(out, i, func, bias=0.0, scale=1.0, off=None):
+        c = 0.075 + (cnt(out) * GF_ if off else max(64, cnt(out))) * CY
+        return ("S", lambda e: [e.activation(ap(out), src(i, off), func, bias=sc(bias), scale=sc(scale))], c)
+
+    def ts(out, i, s1, s2, op0, op1=None, s=None):
+        def f(e):
+            if op1 is None:
+                return [e.tensor_scalar(ap(out), ap(i), sc(s1), None, op0)]
+            return [e.tensor_scalar(ap(out), ap(i), sc(s1), sc(s2), op0, op1)]
+        alts = [("V", f, cost(out, i, None))]
+        if s is None and okS(out, i):
+            if op0 == ALU.mult and op1 is None:
+                s = act(out, i, ACT.Identity, 0.0, s1)
+            elif op0 == ALU.mult and op1 == ALU.add:
+                s = act(out, i, ACT.Identity, s2, s1)
+            elif op0 == ALU.add and op1 is None:
+                s = act(out, i, ACT.Identity, s1, 1.0)
+        if s:
+            alts.append(s)
+        return add(alts, [i, s1, s2], [out])
+
+    def cp(out, i, off=None):
+        alts = [("V", lambda e: [e.tensor_copy(ap(out), src(i, off))], cost(out, i, off))]
+        if okS(out, i):
+            alts.append(act(out, i, ACT.Copy, off=off))
+        return add(alts, [i, off], [out], g=off)
+
+    def tt(out, a, b, op):
+        c = 1.0 if a[0][0] == "B" and a[0][1:].isdigit() else 2.0
+        return add([("V", lambda e: [e.tensor_tensor(ap(out), ap(a), ap(b), op)], 0.06 + max(64, cnt(out) * c) * CY)], [a, b], [out])
+
+    def ms(out, v):
+        return add([("V", lambda e: [e.memset(ap(out), v)], cost(out, out, None))], [], [out])
+
+    def scan(out, d0, d1, op0, op1):
+        return add([("V", lambda e: [e.tensor_tensor_scan(ap(out), ap(d0), ap(d1), 0.0, op0, op1)], cost(out, d1, None))], [d0, d1], [out])
+
+    def turn(out, i):
+        return add([("V", lambda e: [e.transpose(ap(out), ap(i))], cost(out, i, None))], [i], [out])
+
+    def mm(out, pairs):
+        def f(e):
+            return [e.matmul(ap(out), ap(a), ap(b), k == 0, k == len(pairs) - 1) for k, (a, b) in enumerate(pairs)]
+        c = 0.04 + sum(max(64, cnt(b)) * (4 if SCRATCH[b[0]][2] == F else 1) for a, b in pairs) * PCY
+        return add([("P", f, c)], [x for p in pairs for x in p], [out])
+
+    def iota(out, pat, base=0, cm=0):
+        if SCRATCH[out[0]][2] == I32:
+            f = lambda e: [e.iota(ap(out), pat, base, cm)]
+        else:
+            f = lambda e: [e.iota(ap(out), pat, base, cm, allow_small_or_imprecise_dtypes=True)]
+        return add([("G", f, 0.15 + 2 * cnt(out) * CY)], [], [out])
+
+    def dma(q, f, reads, writes, nbytes, issue=0.1, n=1):
+        nd[0] += 1
+        return add([(q, f, issue)], reads, writes, dma=DMA_SEMS[nd[0] - 1], n=16 * n, bytes=nbytes)
+
+    def peer(d):
+        return T.cores[(rank + d) % NR]
+
+    def send(items, pick, nbytes, lat):
+        def f(e):
+            trs = []
+            for k, (s, _, d, land, sem) in enumerate(items):
+                rid, pid, _se = topo.addr(peer(d))
+                en = topo.engines(core, peer(d))
+                m = sum(1 << en[j] for j in pick(k))
+                if len(items) == 1:
+                    e.remote_dma(ap(land), s, T.sem[sem], T.sem["sent"], pid, rid, m)
+                else:
+                    trs.append(RemoteDMATransfer(dst_ids=[DstId(rid=rid, pnc=pid)], dma_engine_mask=m, remote_sem=T.sem[sem], src=s, dst=ap(land)))
+            if trs:
+                e.remote_dma_fused(trs, local_sem=T.sem["sent"])
+            return []
+        o = add([("G", f, 0.6)], [it[1] for it in items], [], send=sum(len(pick(k)) for k in range(len(items))))
+        for k, it in enumerate(items):
+            add([("X", None, lat)], [], [it[3]], arr=it[4], n=len(pick(k)), after=o, link=nbytes)
+
+    def K(name, shift=0):
+        names = KB_NAMES + [s[0] for s in SCALED]
+        c = 128 * names.index(name) - shift
+        return A("KB", c, c + 128)
+
+    def KHm(name, shift=0):
+        c = 128 * KH_NAMES.index(name) - shift
+        return A("KH", c, c + 128)
+
+    def KFm(name):
+        c = 128 * KF_NAMES.index(name)
+        return A("KF", c, c + 128)
+
+    def kt(name, lo=0, hi=16, step=1, grp="b"):
+        n = 1 + (KB_NAMES.index(name) if grp == "b" else NKB + KH_NAMES.index(name) if grp == "h" else NKB + NKH + KF_NAMES.index(name))
+        return A("KT", 16 * n + lo, 16 * n + hi, step)
+
+    def bank(i, lo, hi):
+        return A("B%d" % i, lo, hi)
+
+    dma("Y", lambda e: [e.dma_start(T.IV[:], T.iv[:])], [], [A("IV", 0, NV)], 393216)
+    dma("Y", lambda e: [e.dma_start(T.LVI[:], T.lv[:])], [], [A("LVI", 0, 24)], 12288)
+    dma("Y", lambda e: [e.dma_start(T.DLB[0:128, :], T.lb[:]), e.dma_start(T.DLB[128:240, :], T.lb[0:112, :])], [], [A("DLB", 0, 24)], 24576, n=2)
+    dma("Y", lambda e: [e.dma_start(T.KD[:, 0:NV], T.kd[:])], [], [A("KD", 0, NV)], 786432)
+    dma("Y", lambda e: [e.dma_start(T.LF[:], T.lf[:])], [], [A("LF", 0, NL)], 1310720)
+    dma("Y", lambda e: [e.dma_start(T.LBI[:, 0:24], T.lb[:])], [], [A("LBI", 0, 24)], 12288)
+    dma("Y", lambda e: [e.dma_start(T.BK[:], T.bk[:])], [], [A("BK", 0, NB)], 1048576)
+
+    def rows(name, t):
+        r0 = 16 * ((8 - SH[t]) % 8)
+        return T[name][r0:r0 + 128, :]
+
+    send([(rows("DLB", t), A("DLB", 0, 24), t, A("LBI", 24 * t, 24 * t + 24), "a_lb%d" % t) for t in range(1, NT)], lambda k: [2 * k, 2 * k + 1], 12288, 3.0)
+
+    iota(A("PI", 0, 1), [[0, 1]], 0, 1)
+    for b, pat in enumerate(([[0, 8], [1, 2]], [[0, 4], [1, 2], [0, 2]], [[0, 2], [1, 2], [0, 4]], [[1, 2], [0, 8]])):
+        iota(A("XB", 16 * b, 16 * b + 16), pat)
+    iota(A("OCA", 0, 8), [[0, 2], [2, 4]])
+    iota(A("OCB", 0, 8), [[8, 2], [0, 4]], 16)
+    iota(A("X", 0, 16), [[1, 16]])
+    iota(A("OA", 0, 8 * NMAT), [[16, NMAT], [0, 8]], 16)
+    iota(A("OB", 0, 8 * NMAT), [[0, NMAT], [1, 8]])
+    iota(A("IOT", 0, 384), [[1, 384]])
+    iota(A("JT", 0, 24), [[16, 24]], 384)
+    for c, (s, m) in enumerate(((0, 1), (1, 1), (2, 1), (3, 1), (0, 15), (4, 7), (4, 1), (0, 3), (1, 7), (0, 7), (0, 127), (2, 3))):
+        ts(A("RBI", c, c + 1), A("PI", 0, 1), s, m, ALU.logical_shift_right, ALU.bitwise_and)
+    cp(A("RB", 0, 12), A("RBI", 0, 12))
+
+    def rb(c):
+        return A("RB", c, c + 1)
+    r_, g_, g0_, r3_, rh_, r7_, p_ = rb(4), rb(5), rb(6), rb(7), rb(8), rb(9), rb(10)
+    X = A("X", 0, 16)
+    ts(A("S1", 0, 4), A("RB", 0, 4), -2.0, 1.0, ALU.mult, ALU.add)
+    ts(A("S1", 4, 8), A("RB", 0, 4), -2.0, None, ALU.mult)
+
+    def s1(c):
+        return A("S1", c, c + 1)
+
+    def xb(b, n=16):
+        return A("XB", 16 * b, 16 * b + n)
+    for b in range(4):
+        ts(A("EB", 16 * b, 16 * b + 16), xb(b), s1(b), rb(b), ALU.mult, ALU.add)
+    for b, c in enumerate((7.0, 63.0, 4095.0)):
+        ts(A("FB", 16 * b, 16 * b + 16), A("EB", 16 * b, 16 * b + 16), c, 1.0, ALU.mult, ALU.add)
+    ts(A("FB", 48, 64), A("EB", 48, 64), -1.0, 1.0, ALU.mult, ALU.add)
+    tt(A("TM", 0, 16), A("FB", 0, 16), A("FB", 16, 32), ALU.mult)
+    tt(A("TM", 16, 32), A("FB", 32, 48), A("FB", 48, 64), ALU.mult)
+    tt(A("TM", 32, 48), A("TM", 0, 16), A("TM", 16, 32), ALU.mult)
+    ms(A("KTC", 0, 16), 0.0)
+    ts(A("KTC", 16, 32), A("TM", 32, 48), 2.0 ** -24, None, ALU.mult)
+    tt(A("TM", 64, 65), g_, rb(3), ALU.subtract)
+    ts(A("OCA", 0, 8), A("OCA", 0, 8), A("TM", 64, 65), None, ALU.is_equal)
+    ts(A("OCB", 0, 8), A("OCB", 0, 8), r7_, None, ALU.add)
+    tt(A("OCB", 0, 8), A("OCB", 0, 8), A("OCA", 0, 8), ALU.mult)
+    cp(A("OCU", 0, 8), A("OCB", 0, 8))
+    cp(A("WC", 0, 128), A("KTC", 0, 32), A("OCU", 0, 8))
+    iota(A("RS", 0, 768), [[0, 768]])
+    iota(A("RS", 0, 768, 8), [[0, 96]], 2)
+    iota(A("NTT", 3, NV, 4), [[0, 384]])
+    iota(A("KT", 0, 16 * (NMAT + 2)), [[0, 16 * (NMAT + 2)]])
+    ts(kt("WHI"), A("TM", 32, 48), 2.0 ** 24, None, ALU.mult)
+    tt(A("TM", 48, 64), A("FB", 32, 48), A("EB", 48, 64), ALU.mult)
+    tt(kt("WLO"), A("TM", 0, 16), A("TM", 48, 64), ALU.mult)
+    ts(kt("I"), X, r_, None, ALU.is_equal)
+    Ik = kt("I")
+
+    def icol(c):
+        return A("KT", Ik[1] + c, Ik[1] + c + 1)
+    cp(kt("I2"), Ik)
+    cp(kt("I", grp="h"), Ik)
+    cp(kt("I", grp="f"), Ik)
+    ts(kt("NI", grp="h"), Ik, -1.0, None, ALU.mult)
+    ts(kt("CROW", 0, 1, grp="h"), icol(10), -1.0, None, ALU.mult)
+    ts(kt("CROW2", 0, 1, grp="h"), icol(10), -1.0, None, ALU.mult)
+    ts(A("G3", 16, 20), A("X", 0, 4), rb(11), None, ALU.is_equal)
+    ts(A("G3", 20, 24), A("G3", 16, 20), -1.0, None, ALU.mult)
+    cp(kt("E", 0, 2), A("G3", 16, 18))
+    iota(kt("ONES"), [[0, 16]], 1)
+    ts(kt("LS", 0, 16, 2), kt("ONES", 0, 8), A("G3", 20, 21), None, ALU.mult)
+    ts(kt("LS", 1, 16, 2), kt("ONES", 0, 8), A("G3", 21, 22), None, ALU.mult)
+    ts(kt("LVH"), kt("ONES"), A("G3", 22, 23), 2.0 ** 24, ALU.mult, ALU.mult)
+    ts(kt("LVL"), kt("ONES"), A("G3", 23, 24), None, ALU.mult)
+    ts(kt("BS"), X, rh_, None, ALU.is_equal)
+    ts(kt("LT0"), X, r_, -BIG, ALU.is_gt, ALU.mult)
+    ts(kt("LT1"), X, r_, -BIG, ALU.is_ge, ALU.mult)
+    ts(A("TM", 80, 96), Ik, BIG, None, ALU.mult)
+    tt(kt("FT"), kt("LT0"), A("TM", 80, 96), ALU.add)
+    ts(kt("TRIU"), X, r_, -1.0, ALU.is_lt, ALU.mult)
+    for b in range(4):
+        ts(A("HB", 16 * b, 16 * b + 16), xb(b), s1(4 + b), 1.0, ALU.mult, ALU.add)
+    tt(A("HB", 64, 96), A("HB", 0, 32), A("HB", 32, 64), ALU.mult)
+    tt(kt("H"), A("HB", 64, 80), A("HB", 80, 96), ALU.mult)
+    cp(kt("H", grp="f"), kt("H"))
+    if ONPE:
+        ts(kt("NH", grp="f"), kt("H"), -1.0, None, ALU.mult)
+    ts(kt("FP"), kt("H"), 0.5, 0.5, ALU.mult, ALU.add)
+    ts(kt("FM"), kt("H"), -0.5, 0.5, ALU.mult, ALU.add)
+    ts(A("TM", 96, 100), xb(0, 4), s1(2), rb(2), ALU.mult, ALU.add)
+    ts(A("TM", 100, 104), xb(1, 4), s1(3), rb(3), ALU.mult, ALU.add)
+    ts(A("TM", 104, 108), A("TM", 96, 100), 384.0, None, ALU.mult)
+    ts(A("TM", 108, 112), A("TM", 100, 104), 768.0, None, ALU.mult)
+    tt(kt("PAY", 1, 5), A("TM", 104, 108), A("TM", 108, 112), ALU.add)
+    cp(kt("PAY", 7, 8), r_)
+    ts(kt("PAY", 0, 1), r3_, 1536.0, None, ALU.mult)
+    for nm in ("RP", "RM"):
+        iota(kt(nm, 5, 11), [[0, 6]], 1)
+        cp(kt(nm, 8, 9), r_)
+    iota(kt("RM", 9, 10), [[0, 1]], -1)
+    iota(kt("PW", 0, 7, 6, grp="h"), [[0, 2]], 1)
+    iota(kt("CONE", 0, 1, grp="h"), [[0, 1]], 1)
+    allo = 8 * NMAT
+    ts(A("OA", 0, allo), A("OA", 0, allo), r_, None, ALU.add)
+    ts(A("OB", 0, allo), A("OB", 0, allo), g_, None, ALU.is_equal)
+    tt(A("OA", 0, allo), A("OA", 0, allo), A("OB", 0, allo), ALU.mult)
+    cp(A("OU", 0, allo), A("OA", 0, allo))
+    KTW = A("KT", 0, 16 * (NMAT + 2))
+    for m0 in range(0, NKB, 4):
+        m1 = min(NKB, m0 + 4)
+        cp(A("KB", 128 * m0, 128 * m1), KTW, A("OU", 8 * m0, 8 * m1))
+    cp(A("KH", 0, 128 * NKH), KTW, A("OU", 8 * NKB, 8 * (NKB + NKH)))
+    cp(A("KF", 0, 128 * NKF), KTW, A("OU", 8 * (NKB + NKH), allo))
+    for nm, base, v in SCALED:
+        if (len(ONPE) < 2 or nm not in ("I22", "I44", "I66")) and (ONPE or nm[:2] not in ("H1", "H2", "H3")):
+            ts(K(nm), K(base), v, None, ALU.mult)
+    ts(A("CC", 0, 1), icol(5), float(rank + 1), icol(6), ALU.mult, ALU.subtract)
+    ts(A("CC", 6, 7), A("CC", 0, 1), icol(8), icol(9), ALU.add, ALU.add)
+    ts(A("CC", 1, 2), A("CC", 6, 7), icol(10), None, ALU.add)
+    ts(A("CC", 2, 3), r_, 5.0, None, ALU.is_lt)
+    ts(A("CC", 15, 16), icol(0), -1.0, None, ALU.mult)
+    ts(A("CC", 7, 8), r_, 5.0, icol(0), ALU.is_lt, ALU.subtract)
+    ts(A("CJ", 0, 384), A("IOT", 0, 384), A("CC", 7, 8), A("CC", 1, 2), ALU.mult, ALU.add)
+    ts(A("CC", 3, 4), g0_, 16.0, None, ALU.mult)
+    ts(A("DJ", 0, 24), A("JT", 0, 24), r_, A("CC", 3, 4), ALU.add, ALU.add)
+    ts(A("CC", 8, 9), rh_, 32.0, A("CC", 3, 4), ALU.mult, ALU.add)
+    ts(A("CC", 9, 10), rb(0), 192.0, A("CC", 8, 9), ALU.mult, ALU.add)
+    ts(A("ZU", 0, 6), A("X", 0, 6), A("CC", 9, 10), 383.0, ALU.add, ALU.min)
+    ts(A("CC", 10, 11), g0_, s1(0), rb(0), ALU.mult, ALU.add)
+    ts(A("CC", 11, 12), A("CC", 10, 11), 384.0, A("CC", 8, 9), ALU.mult, ALU.add)
+    ts(A("CC", 12, 13), A("CC", 10, 11), g0_, -32.0, ALU.mult, ALU.mult)
+    ts(A("CC", 13, 14), icol(0), g0_, 384.0, ALU.mult, ALU.mult)
+    ts(A("CC", 14, 15), A("CC", 11, 12), A("CC", 12, 13), None, ALU.add)
+    iota(A("ZW", 0, 10), [[1, 5], [256, 2]])
+    ts(A("ZW", 0, 10, 2), A("ZW", 0, 10, 2), A("CC", 13, 14), None, ALU.add)
+    ts(A("ZV", 0, 10), A("ZW", 0, 10), A("CC", 14, 15), 767.0, ALU.add, ALU.min)
+    ts(A("DJ1", 0, 24), A("JT", 0, 24), r_, 1.0, ALU.add, ALU.add)
+    iota(A("ONE", 0, 24), [[0, 24]], 1)
+    iota(A("LV", 0, 24), [[0, 24]], 1)
+    for t in range(NT):
+        ts(A("GI", t, t + 1), A("RBI", 5, 6), float(8 - SH[t]), None, ALU.add)
+    ts(A("GI", 0, 5), A("GI", 0, 5), 7, None, ALU.bitwise_and)
+    ts(A("CC", 4, 5), r_, 76.0, None, ALU.add)
+    ts(A("GF", 0, 5), A("GI", 0, 5), 5.0, A("CC", 4, 5), ALU.mult, ALU.add)
+    ts(A("CC", 5, 6), r_, 10.0, A("CC", 2, 3), ALU.is_lt, ALU.subtract)
+    ts(A("GF", 0, 5), A("GF", 0, 5), A("CC", 5, 6), -1.0, ALU.mult, ALU.add)
+    for t in range(NT):
+        ts(A("OUTM", 208 * t, 208 * t + 208), A("IOT", 0, 208), A("GF", t, t + 1), None, ALU.is_equal)
+    ts(A("CN", 0, 128), A("IOT", 0, 128), 0.0, icol(5), ALU.mult, ALU.subtract)
+    iota(A("Z", 0, 208), [[0, 208]])
+    iota(A("RES", 192, 208), [[0, 16]])
+    ts(A("KIF", 1, 2), s1(0), p_, None, ALU.add)
+    ts(A("KIF", 2, 3), s1(1), 2.0, p_, ALU.mult, ALU.add)
+    ts(A("KIF", 3, 4), A("KIF", 2, 3), s1(0), None, ALU.add)
+    cp(A("KIX", 1, 4), A("KIF", 1, 4))
+    for m in (1, 2, 3):
+        dma("G", lambda e, m=m: [e.indirect_dma_start(T.KD[:, NV * m:NV * m + NV], None, T.kd[:], IndirectOffsetOnAxis(ap=T.KIX[:, m:m + 1], axis=0),
+                                                      bounds_check=127)],
+            [A("KIX", m, m + 1), A("BK", 0, NB)], [A("KD", NV * m, NV * m + NV)], 786432, issue=1.7)
+
+    tag[0] = "N"
+    for i in range(12):
+        bk0, bk1, c0 = (0, 2, 64 * i) if i < 6 else (1, 7, 64 * (i - 6))
+        mm(bank(bk1, c0, c0 + 64), [(A("IV", 128 * i, 128 * i + 128), A("WC", 64, 128))])
+        mm(bank(bk0, c0, c0 + 64), [(A("IV", 128 * i, 128 * i + 128), A("WC", 0, 64))])
+    def cb(n, lo=0, hi=768, step=1):
+        nm, o = {"C1": ("AF", 0), "CA": ("AF", 768), "CB": ("AH", 0), "CD": ("AH", 768), "CM1": ("KP", 0)}[n]
+        return A(nm, o + lo, o + hi, step)
+    for h, (b0, b1) in enumerate(((0, 2), (1, 7))):
+        lo, hi = 384 * h, 384 * h + 384
+        cp(cb("C1", lo, hi), bank(b1, 0, 384))
+        tt(cb("CA", lo, hi), bank(b0, 0, 384), cb("C1", lo, hi), ALU.min)
+        tt(cb("CB", lo, hi), bank(b0, 0, 384), cb("C1", lo, hi), ALU.max)
+        ts(A("WI", 2 + 192 * h, 192 + 192 * h, 4), A("B%d" % b0, 0, 384, 8), 2.0 ** 24, -MID, ALU.mult, ALU.add)
+    ts(A("WI", 3, 384, 4), cb("C1", 0, 768, 8), 2.0 ** 24, -MID, ALU.mult, ALU.add)
+    scan(cb("CM1"), A("RS", 0, 768), cb("CA"), ALU.add, ALU.min)
+    for i in range(8):
+        tt(cb("CD", i, 768, 8), cb("CA", i, 768, 8), cb("CM1", 7, 768, 8), ALU.is_gt)
+    ts(A("WI", 0, 384, 4), cb("CM1", 7, 768, 8), 2.0 ** 24, -MID, ALU.mult, ALU.add)
+    tt(cb("CD"), cb("CD"), cb("CB"), ALU.max)
+    scan(cb("CA"), A("RS", 0, 768), cb("CD"), ALU.add, ALU.min)
+    ts(A("WI", 1, 384, 4), cb("CA", 7, 768, 8), 2.0 ** 24, -MID, ALU.mult, ALU.add)
+    cp(A("NTT", 0, NV, 4), A("WI", 0, 384))
+    tt(A("WP", 0, 384), A("WI", 0, 384), A("NTT", 0, NV, 4), ALU.subtract)
+    cp(A("NTT", 1, NV, 4), A("WP", 0, 384))
+    tt(A("NTT", 2, NV, 4), A("WP", 0, 384), A("NTT", 1, NV, 4), ALU.subtract)
+    for j in range(3):
+        for i in range(4 * j, 4 * j + 4):
+            mm(bank(j, 128 * (i % 4), 128 * (i % 4) + 128), [(A("NTT", 128 * i, 128 * i + 128), K("I"))])
+        cp(A("NTB", 512 * j, 512 * j + 512), bank(j, 0, 512))
+
+    tag[0] = "A"
+    cp(A("LVU", 0, 24), A("LVI", 0, 24))
+    cp(A("KA", 0, 384), A("KD", 0, NV), A("LVU", 0, 24))
+    for c in range(0, 384, CHC):
+        cp(A("XA", 16 * c, 16 * (c + CHC)), A("LF", 0, NL), A("KA", c, c + CHC))
+    for c in range(3):
+        for w in range(4):
+            mm(bank(3 + w, 128 * c, 128 * c + 128),
+               [(K(("I", "I16", "I256", "I4096")[i]), A("XA", 2048 * c + 4 * w + i, 2048 * c + 2048, 16)) for i in range(4)])
+    for w in range(4):
+        ts(A("AU", 384 * w, 384 * w + 384), bank(3 + w, 0, 384), float(AOFF), None, ALU.add)
+        cp(A("AR", 384 * w, 384 * w + 384), bank(3 + w, 0, 384))
+    cp(A("LT", 0, 384), A("NTB", 0, NV), A("LVU", 0, 24))
+    dma("Y", lambda e: [e.dma_start(T.DLT[0:128, :], T.LT[:, 0:384]), e.dma_start(T.DLT[128:240, :], T.LT[0:112, 0:384])],
+        [A("LT", 0, 384)], [A("DLT", 0, 384)], 98304 * 2, n=2)
+    send([(rows("DLT", t), A("DLT", 0, 384), t, A("LT", 384 * t, 384 * t + 384), "a_lt%d" % t) for t in range(1, NT)], lambda k: [2 * k, 2 * k + 1], 98304, 3.0)
+    dma("Y", lambda e: [e.dma_start(T.DAU[0:128, :], T.AU[:, 0:1536]), e.dma_start(T.DAU[128:240, :], T.AU[0:112, 0:1536])],
+        [A("AU", 0, 1536)], [A("DAU", 0, 1536)], 393216 * 2, n=2)
+    for t in range(1, NT):
+        send([(rows("DAU", t), A("DAU", 0, 1536), t, A("AU", 1536 * t, 1536 * t + 1536), "a_au%d" % t)], lambda k: [0, 2, 4, 6], 393216, 3.0)
+
+    def nonzero(out, i):
+        return ts(out, i, 0.0, None, ALU.not_equal, s=act(out, i, ACT.Abs))
+
+    def iszero(out, i):
+        return ts(out, i, 0.0, None, ALU.is_equal, s=act(out, i, ACT.Relu, 1.0, -1.0))
+
+    def first(out, i):
+        return ts(out, i, 1.0 / BIG, 0.0, ALU.mult, ALU.max, s=act(out, i, ACT.Relu, 0.0, 1.0 / BIG))
+
+    def lessone(out, i):
+        return ts(out, i, A("CC", 15, 16), 0.0, ALU.add, ALU.max, s=act(out, i, ACT.Relu, A("CC", 15, 16), 1.0))
+
+    def claims(t):
+        par = t
+        lt0 = 384 * t
+        LTa = A("LT", lt0, lt0 + 384)
+        w0 = 384 * (CORDER.index(t) % 2)
+        cp(A("LBU", 24 * t, 24 * t + 24), A("LBI", 24 * t, 24 * t + 24))
+        cp(A("WF", w0, w0 + 384), A("BK", 0, NB), A("LBU", 24 * t, 24 * t + 24))
+        cp(A("WU", w0, w0 + 384), A("WF", w0, w0 + 384))
+        for c in range(0, 384, CHC):
+            cp(A("XC", 16 * c, 16 * (c + CHC)), A("NTB", 0, NV), A("WU", w0 + c, w0 + c + CHC))
+        for c in range(0, 384, PCC):
+            for h in range(2):
+                mm(bank(h, c, c + PCC), [(K("LS"), A("LT", lt0 + c, lt0 + c + PCC))] +
+                   [(K("E", 2 * k), A("XC", 16 * c + 8 * h + k, 16 * (c + PCC), 16)) for k in range(8)])
+        for h in range(2):
+            nonzero(A("NE", 384 * h, 384 * h + 384), bank(h, 0, 384))
+        b2 = bank(2, 0, 384)
+        mm(b2, [(K("BS"), A("NE", 0, 384)), (K("BS", 8), A("NE", 384, 768))])
+        iszero(A("FIT", 0, 384), b2)
+        mm(b2, [(K("FT"), A("FIT", 0, 384)), (KFm("I"), A("WF", w0, w0 + 384))])
+        ts(A("VAL", 0, 384), b2, 1.0 - BIG, 0.0, ALU.add, ALU.max)
+        bl = bank(2, 384, 408)
+        mm(bl, [(KHm("CONE", l), A("VAL", l, 384, 16)) for l in range(16)])
+        ts(A("WX", 0, 24), bl, -1.0, 0.0, ALU.add, ALU.max)
+        ts(A("CL", 24 * par, 24 * par + 24), bl, 1.0, None, ALU.min)
+        tt(A("CLJ", 24 * par, 24 * par + 24), A("CL", 24 * par, 24 * par + 24), A("DJ1", 0, 24), ALU.mult)
+        iw, win, off = A("IW", 0, 384), A("IV", 0, NV), A("WX", 0, 24)
+        add([("V", lambda e: [e.tensor_scalar(ap(iw), src(win, off), -4.0, None, ALU.add)], cost(iw, win, off)), act(iw, win, ACT.Identity, -4.0, 1.0, off)],
+            [win, off], [iw], g=off)
+        mm(b2, [(K("WHI"), A("IW", 0, 384)), (K("LVH"), LTa), (K("WLO"), A("IW", 0, 384)), (K("LVL"), LTa)])
+        ts(A("FM", 0, 384), b2, 0.0, None, ALU.is_equal)
+        mm(b2, [(K("FT"), A("FM", 0, 384))])
+        first(A("OH", 0, 384), b2)
+        mm(b2, [(KHm("I"), A("CJ", 0, 384)), (KHm("PW"), A("VAL", 0, 384)), (K("PAY"), A("OH", 0, 384))])
+        lessone(A("P", 400 * t, 400 * t + 384), b2)
+        if t in AHEAD:
+            lessone(A("P", 400 * t + 384, 400 * t + 400), bank(2, 0, 16))
+            for h in range(2):
+                turn(A("ZA", 384 * h, 384 * h + 384), A("P", 400 * t + 16 * h, 400 * t + 16 * h + 384))
+            cp(A("ALU", 160 * t, 160 * t + 160), A("ZA", 0, 768), A("ZV", 0, 10))
+            cp(A("KU", 384 * t, 384 * t + 384), A("KD", 0, 4 * NV), A("ALU", 160 * t, 160 * t + 24))
+
+    def ar0(t):
+        return 1536 * (2 if t in AHEAD else t % 2)
+
+    def unpack(t):
+        for w in range(0, 1536, 768):
+            ts(A("AR", ar0(t) + w, ar0(t) + w + 768), A("AU", 1536 * t + w, 1536 * t + w + 768), float(-AOFF), None, ALU.add)
+
+    def tests(t):
+        par = t
+        live = A("LV", 24 * t, 24 * t + 24)
+        Pt = A("P", 400 * t, 400 * t + 384)
+        l24 = lambda n: A(n, 0, 24)
+        tt(l24("CAND"), live, A("CL", 24 * par, 24 * par + 24), ALU.mult)
+        tt(l24("CANJ"), live, A("CLJ", 24 * par, 24 * par + 24), ALU.mult)
+        mm(bank(7, 24, 48), [(K("ONES"), l24("CAND"))])
+        mm(bank(7, 0, 24), [(K("TRIU"), l24("CAND")), (KHm("I"), l24("DJ")), (KHm("NI"), l24("CANJ"))])
+        scan(l24("CUM"), l24("ONE"), bank(7, 24, 48), ALU.mult, ALU.add)
+        tt(l24("RI"), bank(7, 0, 24), l24("CUM"), ALU.add)
+        rot = 16 * (8 - (SH[(t + 1) % NT] - SH[t]) % 8)
+
+        def masked(win, off, other, out=A("RO", 0, 384)):
+            add([("V", lambda e: [e.tensor_tensor(ap(out), src(win, off), ap(other), ALU.mult)], 0.06 + 384 * GF_ * CY)], [win, off, other], [out])
+
+        def hand_on(prs):
+            mm(bank(7, 0, 24), [(K("I", -rot), live)] + prs)
+            m = A("MSG", 24 * t, 24 * t + 24)
+            cp(m, bank(7, 0, 24))
+            send([(ap(m), m, 1, A("LV", 24 * t + 24, 24 * t + 48), "a_lv%d" % (t + 1))], lambda k: [1, 3, 5, 7], 6144, 2.5)
+        if t in AHEAD:
+            if t < NT - 1:
+                ts(l24("RU"), l24("RI"), A("CC", 3, 4), float(CAP), ALU.subtract, ALU.is_lt)
+                tt(l24("MG"), l24("RU"), A("NOK", 24 * t, 24 * t + 24), ALU.mult)
+                hand_on([(K("I", -rot), l24("MG"))])
+            ts(l24("POS2"), l24("RI"), A("CC", 3, 4), float(CAP), ALU.subtract, ALU.is_lt)
+            if t < NT - 1:
+                masked(X, l24("POS2"), A("ROF", 384 * t, 384 * t + 384))
+            else:
+                masked(X, l24("POS2"), Pt, A("MP", 0, 384))
+                for c in (0, 192):
+                    tt(A("RO", c, c + 192), A("RESF", c, c + 192), A("MP", c, c + 192), ALU.mult)
+        else:
+            if t:
+                unpack(t)
+            cp(l24("POS"), l24("RI"))
+            add([("V", lambda e: [e.tensor_copy(T.Z[:, 0:1184].indirect(T.POS[:, 0:24]), ap(Pt))], 0.06 + 384 * 3.8 * CY)], [Pt, l24("POS")], [A("Z", 0, 1184)])
+            ts(l24("POS2"), l24("RI"), A("CC", 3, 4), float(CAP), ALU.subtract, ALU.min)
+            for h in range(2):
+                turn(A("ZT", 192 * h, 192 * h + 192), A("Z", 16 * h, 16 * h + 192))
+            cp(A("LLU", 0, 80), A("ZT", 0, 384), A("ZU", 0, 5))
+            cp(A("KL", 0, 192), A("KD", 0, 4 * NV), A("LLU", 0, 12))
+            batch(t, 0, (3, 4, 7, 7), A("KL", 0, 192), [A("LLU", 16 + 16 * a, 28 + 16 * a) for a in range(4)], A("RES", 0, 192), CH1)
+            masked(A("RES", 0, 208), l24("POS2"), Pt)
+            if t < NT - 1:
+                hand_on([(KHm("CROW", l - rot), A("RO", l, 384, 16)) for l in range(16)])
+        prs = [(A("OUTM", 208 * t + 80 - 40 * i, 208 * t + 208 - 40 * i), A("RO", 128 * i, 128 * i + 128)) for i in range(3)]
+        if t == 0:
+            prs += [(A("OUTM", 80 - 40 * i, 208 - 40 * i), A("CN", 0, 128)) for i in range(3)]
+        mm(bank(7, 384, 512), prs)
+        om = A("OM", 128 * t, 128 * t + 128)
+        cp(om if t else A("ACC", 0, 128), bank(7, 384, 512))
+        if t:
+            land = A("OL", 128 * (t - 1), 128 * t)
+            send([(ap(om), om, -t, land, "a_om%d" % t)], lambda k: [1, 3, 5, 7] if t < NT - 1 else list(range(8)), 32768, 2.5)
+            tt(A("ACC", 0, 128), A("ACC", 0, 128), land, ALU.add)
+
+    def batch(t, x, bk, kl, alists, res, ch):
+        def S(n, lo, hi, step=1):
+            w = SCRATCH[n][1][1] // 2
+            return A(n, w * x + lo, w * x + hi, step)
+        lo, hi, al = bank(bk[3], 0, 192), bank(bk[3], 192, 384), bank(bk[3], 0, 384)
+        for a, off in enumerate(alists):
+            out, win, v = S("AF", 192 * a, 192 * a + 192), A("AR", ar0(t), ar0(t) + 1536), 2.0 ** (22 * a)
+            if x in ONPE and a:
+                add([("V", lambda e, out=out, win=win, off=off, v=v: [e.tensor_scalar(ap(out), src(win, off), v, None, ALU.mult)], cost(out, win, off)),
+                     act(out, win, ACT.Identity, 0.0, v, off)], [win, off], [out], g=off)
+            else:
+                cp(out, win, off)
+        if x in ONPE:
+            for c in range(0, 192, ch):
+                cp(S("XT", 16 * c, 16 * (c + ch)), A("LF", 0, NL), A(kl[0], kl[1] + c, kl[1] + c + ch))
+            al = bank(bk[0], 0, 384)
+            for h in range(2):
+                for y, nm in enumerate(("NH", "H")):
+                    prs = []
+                    for w in (3, 2, 1, 0):
+                        prs.append((KFm(nm), S("AF", 192 * w + 96 * h, 192 * w + 96 * h + 96)))
+                        prs += [(K("H%d_%d" % (w, i) if w or i else "H"), S("XT", 1536 * h + 4 * w + i, 1536 * h + 1536, 16)) for i in range(4)]
+                    mm(bank(bk[0], 192 * y + 96 * h, 192 * y + 96 * h + 96), prs)
+        else:
+            light(S, bk, kl, ch)
+        nonzero(S("BD", 0, 384), al)
+        al = bank(bk[3], 0, 384)
+        mm(lo, [(K("FP"), S("BD", 0, 192)), (K("FM"), S("BD", 192, 384))])
+        mm(hi, [(K("FM"), S("BD", 0, 192)), (K("FP"), S("BD", 192, 384))])
+        iszero(S("TF", 0, 384), al)
+        mm(lo, [(K("FT"), S("TF", 0, 192)), (K("LT0"), S("TF", 192, 384))])
+        mm(hi, [(K("FT"), S("TF", 192, 384)), (K("LT1"), S("TF", 0, 192))])
+        first(S("TO", 0, 384), al)
+        mm(lo, [(K("RP"), S("TO", 0, 192)), (K("RM"), S("TO", 192, 384))])
+        cp(res, lo)
+
+    def light(S, bk, kl, ch):
+        for h in range(2):
+            for w in range(4):
+                mm(bank(bk[2], 96 * w, 96 * w + 96), [(KFm("H"), S("AF", 192 * w + 96 * h, 192 * w + 96 * h + 96))])
+            cp(S("AH", 384 * h, 384 * h + 384), bank(bk[2], 0, 384))
+        for c in range(0, 192, ch):
+            cp(S("XT", 16 * c, 16 * (c + ch)), A("LF", 0, NL), A(kl[0], kl[1] + c, kl[1] + c + ch))
+        for h in range(2):
+            for w in range(4):
+                mm(bank(bk[h], 96 * w, 96 * w + 96),
+                   [(K("H0_%d" % i if i else "H"), S("XT", 1536 * h + 4 * w + i, 1536 * h + 1536, 16)) for i in range(4)])
+            tt(S("DM", 384 * h, 384 * h + 384), bank(bk[h], 0, 384), S("AH", 384 * h, 384 * h + 384), ALU.subtract)
+            tt(S("DP", 384 * h, 384 * h + 384), bank(bk[h], 0, 384), S("AH", 384 * h, 384 * h + 384), ALU.add)
+        wt = ("I", "I22", "I44", "I66")
+        for h in range(2):
+            for y, nm in enumerate(("DM", "DP")):
+                c0 = 192 * y + 96 * h
+                mm(bank(bk[3], c0, c0 + 96), [(K(wt[w]), S(nm, 384 * h + 96 * w, 384 * h + 96 * w + 96)) for w in range(4)])
+
+    def ahead(t):
+        unpack(t)
+        for hb in range(2):
+            c0 = 160 * t + 32 + 12 * hb
+            batch(t, 1, (5, 6, 6, 5), A("KU", 384 * t + 192 * hb, 384 * t + 192 * hb + 192),
+                  [A("ALU", c0 + 32 * a, c0 + 32 * a + 12) for a in range(4)], A("RESF", 192 * hb, 192 * hb + 192), CH2)
+        if t < NT - 1:
+            tt(A("ROF", 384 * t, 384 * t + 384), A("RESF", 0, 384), A("P", 400 * t, 400 * t + 384), ALU.mult)
+            mm(bank(5, 384, 408), [(KHm("CROW2", l), A("ROF", 384 * t + l, 384 * t + 384, 16)) for l in range(16)])
+            cp(A("NOK", 24 * t, 24 * t + 24), bank(5, 384, 408))
+
+    for t in CORDER:
+        tag[0] = "C%d" % t
+        claims(t)
+    for t in AHEAD:
+        tag[0] = "H%d" % t
+        ahead(t)
+    for t in range(NT):
+        tag[0] = "T%d" % t
+        tests(t)
+    dma("Y", lambda e: [e.dma_start(T.y[:, 128 * i:128 * i + 128], T.ACC[40 * i:40 * i + 40, :]) for i in range(3)], [A("ACC", 0, 128)], [], 61440, n=3)
+    return ops
+
+
+def depend(ops):
+    def norm(a):
+        return (a[0], 0, 512, 1) if SCRATCH[a[0]][0] == "psum" else a
+
+    def meet(a, b):
+        if a[2] <= b[1] or b[2] <= a[1]:
+            return False
+        return not (a[3] == b[3] and a[3] > 1 and (a[1] - b[1]) % a[3])
+    hist = {}
+    deps = []
+    for i, o in enumerate(ops):
+        d = set()
+        if "after" in o:
+            d.add(o["after"])
+        acc = [(norm(a), SCRATCH[a[0]][0] == "psum") for a in o["r"]] + [(norm(a), True) for a in o["w"]]
+        for a, wr in acc:
+            for (b, bw, j) in hist.get(a[0], []):
+                if (wr or bw) and meet(a, b):
+                    d.add(j)
+        for a, wr in acc:
+            h = hist.setdefault(a[0], [])
+            if wr and a[3] == 1:
+                h[:] = [x for x in h if not (a[1] <= x[0][1] and x[0][2] <= a[2])]
+            h.append((a, wr, i))
+        d.discard(i)
+        deps.append(sorted(d))
+    return deps
+
+
+def schedule(ops, deps, rounds=None):
+    n = len(ops)
+    succ = [[] for _ in range(n)]
+    for i in range(n):
+        for j in deps[i]:
+            succ[j].append(i)
+    alts, lag, bias = [], [], [VBIAS] * n
+    rounds = ROUNDS if rounds is None else rounds
+    for o in ops:
+        e, _, c = o["alts"][0]
+        if e == "X":
+            big = o["link"] > 70000
+            alts.append([("L" if big else None, o["link"] / 5e4)])
+            lag.append(c)
+        elif "dma" in o:
+            alts.append([(e, 0.1 + o["bytes"] / 2.5e5 if e == "Y" else c)])
+            lag.append(2.0 if e == "Y" else 2.5 + o["bytes"] / 1e5)
+        else:
+            alts.append([(a[0], a[2]) for a in o["alts"]])
+            lag.append(LAT)
+
+    def place(seq, pre, back):
+        busy = {e: [] for e in "VSPGYL"}
+        st, fin, ch = [0.0] * n, [0.0] * n, [0] * n
+        for i in seq:
+            r = max([fin[j] + (0.0 if alts[i][0][0] == alts[j][0][0] == "P" else lag[i] if back else lag[j]) for j in pre[i]] + [0.0])
+            best = None
+            for k, (e, c) in enumerate(alts[i]):
+                t, at = r, 0
+                if e:
+                    at = len(busy[e])
+                    for x, (a, b) in enumerate(busy[e]):
+                        if b <= t:
+                            continue
+                        if a >= t + c:
+                            at = x
+                            break
+                        t = b
+                key = t + c + (bias[i] * c if e == "V" and len(alts[i]) > 1 else 0.0)
+                if best is None or key < best[0]:
+                    best = (key, t, k, at)
+            _, t, k, at = best
+            e, c = alts[i][k]
+            st[i], fin[i], ch[i] = t, t + c, k
+            if e:
+                busy[e].insert(at, (t, t + c))
+        return st, fin, ch
+    prio = [0.0] * n
+    for i in range(n - 1, -1, -1):
+        prio[i] = min(a[1] for a in alts[i]) + lag[i] + max([prio[j] for j in succ[i]] + [0.0])
+
+    def replay(order, ch, kg, kp, wait, hop):
+        free = {e: 0.0 for e in "VSPGYL"}
+        fin = [0.0] * n
+        for i in order:
+            e, c = alts[i][ch[i]]
+            t = free[e] if e else 0.0
+            for j in deps[i]:
+                x = fin[j] + (0.0 if e == "P" == alts[j][0][0] else wait if lag[j] == LAT else lag[j] * hop)
+                if x > t:
+                    t = x
+            fin[i] = t + c * (kp if e == "P" else kg if gath[i] else 1.0)
+            if e:
+                free[e] = fin[i]
+        return max(fin)
+
+    def value(pr, turns=0):
+        p = list(pr)
+        for i in range(n - 1, -1, -1):
+            for j in succ[i]:
+                if p[j] + 0.001 > p[i]:
+                    p[i] = p[j] + 0.001
+        st, fin, ch = place(sorted(range(n), key=lambda i: (-p[i], i)), deps, False)
+        for _r in range(turns):
+            fb = place(sorted(range(n), key=lambda i: (-fin[i] - lag[i], -i)), succ, True)[1]
+            pr[:] = fb
+            st, fin, ch = place(sorted(range(n), key=lambda i: (-fb[i], i)), deps, False)
+        order = sorted(range(n), key=lambda i: (st[i], i))
+        v = [max(fin)] + [replay(order, ch, *m) for m in MODELS]
+        return sum(v) / len(v), order, fin, ch, v
+    gath = [bool(o.get("g")) for o in ops]
+    groups = {}
+    for i, o in enumerate(ops):
+        prio[i] += OFFS.get(o["tag"], 0.0)
+        groups.setdefault(o["tag"], []).append(i)
+        groups.setdefault((o["tag"], o["w"][0][0] if o["w"] else ""), []).append(i)
+    groups = list(groups.values())
+    flex = [i for i in range(n) if len(alts[i]) > 1]
+    rng = np.random.default_rng(SEED)
+    best = value(prio, 3)
+    now = best[0]
+    for _ in range(rounds):
+        p, old = list(prio), list(bias)
+        u = rng.random()
+        if u < 0.1:
+            d = float(rng.choice([-0.5, 0.0, 0.5, 1.0, 3.0, 10.0]))
+            for i in groups[int(rng.integers(0, len(groups)))]:
+                bias[i] = d
+        elif u < 0.2:
+            for i in rng.integers(0, n, 3):
+                p[i] += float(rng.normal()) * 3.0
+        elif u < 0.4:
+            for i in rng.choice(flex, int(rng.integers(1, 6))):
+                bias[i] = float(rng.choice([-0.5, 0.0, 0.5, 1.0, 3.0]))
+        else:
+            for _k in range(int(rng.integers(1, 3))):
+                d = float(rng.normal()) * float(rng.choice([1.0, 4.0, 12.0]))
+                for i in groups[int(rng.integers(0, len(groups)))]:
+                    p[i] += d
+        v = value(p, int(rng.random() < TURN))
+        if v[0] <= now + HEAT * (1.0 - _ / rounds) * float(rng.exponential()):
+            now, prio = v[0], p
+            if now < best[0]:
+                best = v
+        else:
+            bias[:] = old
+    PLAN["v"] = best[4]
+    return [(i, best[3][i]) for i in best[1]], best[2]
+
+
+def rank_program(g, core, T, topo):
+    rank = T.rank_of(core)
+    if rank is None:
+        return
+    ops = build(g, T, topo, core, rank)
+    if "order" not in PLAN:
+        PLAN["deps"] = depend(ops)
+        PLAN["order"], PLAN["fin"] = schedule(ops, PLAN["deps"])
+    deps = PLAN["deps"]
+    eng = {"V": g.vector, "S": g.scalar, "P": g.tensor, "G": g, "Y": g.sync}
+    count = {e: 0 for e in "VSPG"}
+    token = {}
+    seen = {e: {} for e in eng}
+    total = {}
+    sent = 0
+    for i, k in PLAN["order"]:
+        o = ops[i]
+        e, f, _ = o["alts"][k]
+        if e == "X":
+            token[i] = (o["arr"], o["n"])
+            total[o["arr"]] = o["n"]
+            continue
+        need = {}
+        for j in deps[i]:
+            if j in token and not (e == "P" and token[j][0] == "sP"):
+                s, v = token[j]
+                need[s] = max(need.get(s, 0), v)
+        for s, v in need.items():
+            if seen[e].get(s, 0) < v:
+                eng[e].wait_ge(T.sem[s], v)
+                seen[e][s] = v
+        ins = f(eng[e])
+        if "send" in o:
+            sent += o["send"]
+        elif "dma" in o:
+            for x in ins:
+                x.then_inc(T.sem[o["dma"]], 16)
+            token[i] = (o["dma"], o["n"])
+            total[o["dma"]] = o["n"]
+        else:
+            for x in ins:
+                x.then_inc(T.sem["s" + e], 1)
+            count[e] += len(ins)
+            token[i] = ("s" + e, count[e])
+            total["s" + e] = count[e]
+    total["sent"] = sent
+    for s, v in total.items():
+        if seen["G"].get(s, 0) < v:
+            g.wait_ge(T.sem[s], v)

@@ -1,74 +1,52 @@
 import numpy as np
-from concourse.bass import DstId, RemoteDMATransfer, IndirectOffsetOnAxis
+from concourse.bass import DstId, RemoteDMATransfer
 from concourse.mybir import AluOpType as ALU, ActivationFunctionType as ACT
 
 NR, NV, NL, NB, L, CAP, NT = 8, 1536, 5120, 2048, 384, 192, 5
 SH = [t * (t + 1) // 2 % 8 for t in range(NT)]
-HF = "float16"
-AOFF = 7 * 4369
-MID = 4.0 * (8 ** 8 - 1) / 7
-BIG = 4096.0
-
-KB_NAMES = ["Z", "E", "BS", "I", "I2", "LS", "FT", "WHI", "WLO", "LVH", "LVL", "PAY", "TRIU", "ONES",
-            "H", "FP", "FM", "LT0", "LT1", "RP", "RM"]
-KH_NAMES = ["CROW", "CROW2", "CONE", "I", "NI", "PW"]
-ONPE = ()
-KF_NAMES = ["I", "H"] + (["NH"] if ONPE else [])
-SCALED = [("I16", "I", 16.0), ("I256", "I", 256.0), ("I4096", "I", 4096.0), ("I22", "I", 2.0 ** 22), ("I44", "I", 2.0 ** 44), ("I66", "I", 2.0 ** 66)]
-SCALED += [("H%d_%d" % (w, i), "H", 2.0 ** (22 * w + 4 * i)) for w in range(4) for i in range(4) if w or i]
-NKB, NKH, NKF = len(KB_NAMES), len(KH_NAMES), len(KF_NAMES)
-NMAT = NKB + NKH + NKF
+F, B, I32, U, HF = "float32", "bfloat16", "int32", "uint16", "float16"
+MAGIC = 1.5 * 2.0 ** 27
+ASC = (0, 1, 4, 7, 10, 13)
+NXC, NXT = 3, 2
 
 
 def _sb(n, d):
     return ("sbuf", [128, n], d)
 
 
-F, B, I32, U = "float32", "bfloat16", "int32", "uint16"
 SCRATCH = {
-    "LF": _sb(NL, B), "IV": _sb(NV, B), "KD": _sb(4 * NV, I32), "BK": _sb(NB, I32), "LVI": _sb(24, I32), "LBI": _sb(120, I32),
-    "PI": _sb(1, I32), "RBI": _sb(12, I32), "RB": _sb(12, F), "S1": _sb(8, F), "XB": _sb(64, F), "X": _sb(16, F),
-    "EB": _sb(64, F), "FB": _sb(64, F), "TM": _sb(128, F), "HB": _sb(96, F), "G3": _sb(24, F), "CC": _sb(16, F),
-    "KT": _sb(16 * (NMAT + 2), F), "KTC": _sb(32, F), "OA": _sb(8 * NMAT, F), "OB": _sb(8 * NMAT, F), "OU": _sb(8 * NMAT, U),
-    "OCA": _sb(8, F), "OCB": _sb(8, F), "OCU": _sb(8, U),
-    "KB": _sb(128 * (NKB + len(SCALED)), B), "KH": _sb(128 * NKH, HF), "KF": _sb(128 * NKF, F), "WC": _sb(128, B),
-    "IOT": _sb(384, F), "CJ": _sb(384, HF), "DJ": _sb(24, HF), "DJ1": _sb(24, F), "JT": _sb(24, F), "ONE": _sb(24, F),
-    "GI": _sb(8, I32), "GF": _sb(8, F), "OUTM": _sb(5 * 208, HF), "CN": _sb(128, HF), "KIX": _sb(4, I32), "KIF": _sb(4, F),
-    "RS": _sb(768, B),
-    "WI": _sb(384, F), "WP": _sb(384, F), "ZO": _sb(6, F), "ZU": _sb(6, U), "NTT": _sb(NV, B), "NTB": _sb(NV, B),
-    "LVU": _sb(24, U), "KA": _sb(384, U), "XC": _sb(16 * L, B), "XA": _sb(16 * L, B), "XT": _sb(32 * CAP, B),
-    "AU": _sb(5 * 1536, U), "AR": _sb(3 * 1536, F), "LT": _sb(5 * 384, B),
-    "LBU": _sb(120, U), "WF": _sb(768, F), "WU": _sb(768, U), "NE": _sb(768, B), "FIT": _sb(384, B), "VAL": _sb(384, HF),
-    "WX": _sb(24, U), "WL": _sb(24, F), "CL": _sb(120, F), "CLJ": _sb(120, F), "IW": _sb(384, B), "FM": _sb(384, B), "OH": _sb(384, B),
-    "P": _sb(2000, F), "KP": _sb(768, F), "MP": _sb(384, HF),
-    "LV": _sb(5 * 24, B), "CAND": _sb(24, B), "CANJ": _sb(24, HF), "CUM": _sb(24, F), "RI": _sb(24, F),
-    "RU": _sb(24, F), "POS": _sb(24, U), "POS2": _sb(24, U), "Z": _sb(1184, F), "ZT": _sb(384, F), "LLU": _sb(80, U),
-    "KL": _sb(192, U), "AF": _sb(1536, F), "AH": _sb(1536, F), "DM": _sb(1536, B), "DP": _sb(1536, B), "BD": _sb(768, B),
-    "KU": _sb(1920, U), "ALU": _sb(800, U), "ZA": _sb(768, F), "ZV": _sb(10, U), "ZW": _sb(16, F), "RESF": _sb(384, B), "ROF": _sb(1920, HF),
-    "NOK": _sb(120, F), "MG": _sb(24, B), "TF": _sb(768, B), "TO": _sb(768, B), "RES": _sb(208, B), "MSG": _sb(4 * 24, B), "RO": _sb(384, HF),
-    "OM": _sb(5 * 128, HF), "OL": _sb(4 * 128, HF), "ACC": _sb(128, F),
-    "DLB": ("dram", [240, 24], I32), "DLT": ("dram", [240, 384], B), "DAU": ("dram", [240, 1536], U),
+    "LF": _sb(NL, B), "IV": _sb(NV, B), "KDI": _sb(NV, I32), "KDF": _sb(NV, F), "KS": _sb(NV, F), "KP": _sb(NV, F), "BK": _sb(NB, I32),
+    "LVI": _sb(24, I32), "LBI": _sb(120, I32), "LVU": _sb(24, U), "LBU": _sb(120, U),
+    "XB": _sb(320, F), "TB": _sb(320, F), "PT": _sb(112, B), "OI": _sb(8, I32), "OU": _sb(8, U), "CC": _sb(16, F), "PK8": _sb(8, B),
+    "HA": _sb(12 * 256, B), "HB": _sb(16 * 128, B), "HFL": _sb(128, F), "KK": _sb(128, B), "PKM": _sb(128, B), "PSM": _sb(128, B),
+    "DW": _sb(768, B), "IOT": _sb(256, B), "RS": _sb(512, B), "RT": _sb(256, B), "MK": _sb(256, B), "SS": _sb(240, B),
+    "EI": _sb(16, F), "EL": _sb(16, U), "WR": _sb(768, B), "W24": _sb(24, B), "ONE": _sb(128, B), "TRI": _sb(128, B),
+    "ID": _sb(5 * 128, B), "FD": _sb(256, B), "FS": _sb(256, B), "CF": _sb(40, B),
+    "RI": _sb(10, I32), "RF": _sb(20, F), "RL": _sb(20, U), "L5F": _sb(8, F), "L5I": _sb(8, I32), "L5": _sb(8, U),
+    "TAU": _sb(NV, B), "SC": _sb(1024, F), "E": _sb(512, HF), "LI": _sb(128, I32), "MU": _sb(96, U), "SG": _sb(NV, B), "SI": _sb(NV, B), "NTB": _sb(NV, B),
+    "KA": _sb(L, U), "NA": _sb(L, B), "AP": _sb(NT * 6 * L, HF), "LT": _sb(NT * L, B),
+    "WU": _sb(NT * L, U), "XC": _sb(NXC * 16 * L, B), "NE": _sb(512, B), "WL": _sb(120, U), "KL": _sb(2 * L, U),
+    "XT": _sb(NXT * 16 * L, B), "BD": _sb(2 * 768, B), "SD": _sb(2 * 768, F),
+    "R1": _sb(128, F), "R2": _sb(128, I32), "V1": _sb(128, F), "V2": _sb(128, I32), "VI": _sb(120, I32), "VB": _sb(480, I32), "VC": _sb(240, I32),
+    "FF": _sb(608, I32), "CD": _sb(24, B), "UU": _sb(120, F), "MG": _sb(160, B), "SB": _sb(24, I32), "FP": _sb(640, HF), "YS": _sb(L, F),
+    "DLB": ("dram", [240, 24], I32),
 }
 for _i in range(8):
     SCRATCH["B%d" % _i] = ("psum", [128, 512], F)
-DMA_SEMS = ["d%d" % _i for _i in range(24)]
-ARR_SEMS = ["a_%s%d" % (k, t) for k in ("lb", "lt", "au", "lv", "om") for t in range(1, NT)]
+DMA_SEMS = ["d%d" % _i for _i in range(10)]
+ARR_SEMS = ["a_%s%d" % (k, t) for k in ("lb", "p0", "pp", "v1", "v2") for t in range(1, NT)]
 SEMAPHORES = ["sV", "sS", "sP", "sG", "sent"] + DMA_SEMS + ARR_SEMS
 
-CY, PCY, GF_, LAT = 1.04e-3, 0.52e-3, 1.56, 0.15
+CY, PCY, GF_, LAT = 0.87e-3, 0.44e-3, 1.56, 0.12
+LINK = 7e4
 VBIAS = 1.0
-AHEAD = (3, 4)
-CORDER = (0, 1, 3, 2, 4)
-ROUNDS, SEED, HEAT, TURN = 3500, 2, 0.4, 0.15
-MODELS = ((0.75, 0.9, 0.1, 0.8), (1.25, 1.0, 0.25, 1.3), (1.0, 1.15, 0.2, 1.0))
-OFFS = {"N": 20, "A": 30}
-PCC, PCT, CH1, CH2 = 96, 96, 32, 96
-CHC = 96
+GCH = 64
+TURNS = 3
 PLAN = {}
 
 
-def A(name, lo, hi, step=1):
-    return (name, lo, hi, step)
+def A(name, lo, hi, step=1, p0=0, p1=128):
+    return (name, lo, hi, step, p0, p1)
 
 
 def cnt(a):
@@ -81,7 +59,7 @@ def build(g, T, topo, core, rank):
     tag = ["K"]
 
     def ap(a):
-        return T[a[0]][:, a[1]:a[2]:a[3]] if a[3] != 1 else T[a[0]][:, a[1]:a[2]]
+        return T[a[0]][a[4]:a[5], a[1]:a[2]:a[3]] if a[3] != 1 else T[a[0]][a[4]:a[5], a[1]:a[2]]
 
     def two(*aps):
         return all(SCRATCH[a[0]][2] in (B, HF, U) for a in aps)
@@ -101,32 +79,30 @@ def build(g, T, topo, core, rank):
     def cost(out, i, off, c=1.0):
         n = cnt(out)
         if off:
-            return 0.06 + n * GF_ * CY
+            return 0.05 + n * GF_ * CY
         return 0.06 + max(64, n * c * (0.5 if two(out, i) else 1.0)) * CY
 
     def okS(*aps):
         return all(SCRATCH[a[0]][2] in (B, F) for a in aps)
 
     def act(out, i, func, bias=0.0, scale=1.0, off=None):
-        c = 0.075 + (cnt(out) * GF_ if off else max(64, cnt(out))) * CY
+        c = 0.065 + (cnt(out) * GF_ if off else max(64, cnt(out))) * CY
         return ("S", lambda e: [e.activation(ap(out), src(i, off), func, bias=sc(bias), scale=sc(scale))], c)
 
-    def ts(out, i, s1, s2, op0, op1=None, s=None):
+    def ts(out, i, s1, s2, op0, op1=None, s=None, off=None):
         def f(e):
             if op1 is None:
-                return [e.tensor_scalar(ap(out), ap(i), sc(s1), None, op0)]
-            return [e.tensor_scalar(ap(out), ap(i), sc(s1), sc(s2), op0, op1)]
-        alts = [("V", f, cost(out, i, None))]
-        if s is None and okS(out, i):
+                return [e.tensor_scalar(ap(out), src(i, off), sc(s1), None, op0)]
+            return [e.tensor_scalar(ap(out), src(i, off), sc(s1), sc(s2), op0, op1)]
+        alts = [("V", f, cost(out, i, off))]
+        if s is None and okS(out, i) and not off:
             if op0 == ALU.mult and op1 is None:
                 s = act(out, i, ACT.Identity, 0.0, s1)
             elif op0 == ALU.mult and op1 == ALU.add:
                 s = act(out, i, ACT.Identity, s2, s1)
-            elif op0 == ALU.add and op1 is None:
-                s = act(out, i, ACT.Identity, s1, 1.0)
         if s:
             alts.append(s)
-        return add(alts, [i, s1, s2], [out])
+        return add(alts, [i, s1, s2, off], [out], g=off)
 
     def cp(out, i, off=None):
         alts = [("V", lambda e: [e.tensor_copy(ap(out), src(i, off))], cost(out, i, off))]
@@ -134,40 +110,50 @@ def build(g, T, topo, core, rank):
             alts.append(act(out, i, ACT.Copy, off=off))
         return add(alts, [i, off], [out], g=off)
 
-    def tt(out, a, b, op):
-        c = 1.0 if a[0][0] == "B" and a[0][1:].isdigit() else 2.0
-        return add([("V", lambda e: [e.tensor_tensor(ap(out), ap(a), ap(b), op)], 0.06 + max(64, cnt(out) * c) * CY)], [a, b], [out])
+    def tt(out, a, b, op, off=None):
+        c = 1.0 if SCRATCH[a[0]][0] == "psum" or SCRATCH[b[0]][0] == "psum" else 2.0
+        c = cost(out, a, off) if off else 0.06 + max(64, cnt(out) * c) * CY
+        return add([("V", lambda e: [e.tensor_tensor(ap(out), src(a, off), ap(b), op)], c)], [a, b, off], [out], g=off)
 
     def ms(out, v):
         return add([("V", lambda e: [e.memset(ap(out), v)], cost(out, out, None))], [], [out])
 
-    def scan(out, d0, d1, op0, op1):
-        return add([("V", lambda e: [e.tensor_tensor_scan(ap(out), ap(d0), ap(d1), 0.0, op0, op1)], cost(out, d1, None))], [d0, d1], [out])
+    def least(out, step, d1):
+        return add([("V", lambda e: [e.tensor_tensor_scan(ap(out), ap(step), ap(d1), 0.0, ALU.add, ALU.min)], cost(out, d1, None))], [step, d1], [out])
 
     def turn(out, i):
         return add([("V", lambda e: [e.transpose(ap(out), ap(i))], cost(out, i, None))], [i], [out])
 
-    def mm(out, pairs):
+    def mg(items, start=True, stop=True):
         def f(e):
-            return [e.matmul(ap(out), ap(a), ap(b), k == 0, k == len(pairs) - 1) for k, (a, b) in enumerate(pairs)]
-        c = 0.04 + sum(max(64, cnt(b)) * (4 if SCRATCH[b[0]][2] == F else 1) for a, b in pairs) * PCY
-        return add([("P", f, c)], [x for p in pairs for x in p], [out])
+            return [e.matmul(ap(o), ap(a), ap(b), start and k == 0, stop and k == len(items) - 1) for k, (o, a, b) in enumerate(items)]
+        c = 0.03 + sum(max(min(64, cnt(a)), cnt(b)) * (4 if SCRATCH[b[0]][2] == F else 1) for o, a, b in items) * PCY
+        return add([("P", f, c)], [x for it in items for x in it[1:]], [it[0] for it in items])
+
+    def mm(out, pairs):
+        return mg([(out, a, b) for a, b in pairs])
 
     def iota(out, pat, base=0, cm=0):
         if SCRATCH[out[0]][2] == I32:
             f = lambda e: [e.iota(ap(out), pat, base, cm)]
         else:
             f = lambda e: [e.iota(ap(out), pat, base, cm, allow_small_or_imprecise_dtypes=True)]
-        return add([("G", f, 0.15 + 2 * cnt(out) * CY)], [], [out])
+        return add([("G", f, 0.13 + 2 * cnt(out) * CY)], [], [out])
 
-    def dma(q, f, reads, writes, nbytes, issue=0.1, n=1):
+    def fill(out, v):
+        return iota(out, [[0, cnt(out)]], v)
+
+    def select(out, i, pat, cmp, other, base, cm):
+        return add([("G", lambda e: [e.affine_select(ap(out), ap(i), pat, cmp, other, base, cm)], 0.17 + 2 * cnt(out) * CY)], [i], [out])
+
+    def dma(f, reads, writes, nbytes, n=1):
         nd[0] += 1
-        return add([(q, f, issue)], reads, writes, dma=DMA_SEMS[nd[0] - 1], n=16 * n, bytes=nbytes)
+        return add([("Y", f, 0.1)], reads, writes, dma=DMA_SEMS[nd[0] - 1], n=16 * n, bytes=nbytes)
 
     def peer(d):
         return T.cores[(rank + d) % NR]
 
-    def send(items, pick, nbytes, lat):
+    def send(items, pick, nbytes, lat=2.5):
         def f(e):
             trs = []
             for k, (s, _, d, land, sem) in enumerate(items):
@@ -181,445 +167,331 @@ def build(g, T, topo, core, rank):
             if trs:
                 e.remote_dma_fused(trs, local_sem=T.sem["sent"])
             return []
-        o = add([("G", f, 0.6)], [it[1] for it in items], [], send=sum(len(pick(k)) for k in range(len(items))))
+        o = add([("G", f, 0.4)], [it[1] for it in items], [], send=sum(len(pick(k)) for k in range(len(items))))
         for k, it in enumerate(items):
             add([("X", None, lat)], [], [it[3]], arr=it[4], n=len(pick(k)), after=o, link=nbytes)
 
-    def K(name, shift=0):
-        names = KB_NAMES + [s[0] for s in SCALED]
-        c = 128 * names.index(name) - shift
-        return A("KB", c, c + 128)
-
-    def KHm(name, shift=0):
-        c = 128 * KH_NAMES.index(name) - shift
-        return A("KH", c, c + 128)
-
-    def KFm(name):
-        c = 128 * KF_NAMES.index(name)
-        return A("KF", c, c + 128)
-
-    def kt(name, lo=0, hi=16, step=1, grp="b"):
-        n = 1 + (KB_NAMES.index(name) if grp == "b" else NKB + KH_NAMES.index(name) if grp == "h" else NKB + NKH + KF_NAMES.index(name))
-        return A("KT", 16 * n + lo, 16 * n + hi, step)
-
-    def bank(i, lo, hi):
-        return A("B%d" % i, lo, hi)
-
-    dma("Y", lambda e: [e.dma_start(T.IV[:], T.iv[:])], [], [A("IV", 0, NV)], 393216)
-    dma("Y", lambda e: [e.dma_start(T.LVI[:], T.lv[:])], [], [A("LVI", 0, 24)], 12288)
-    dma("Y", lambda e: [e.dma_start(T.DLB[0:128, :], T.lb[:]), e.dma_start(T.DLB[128:240, :], T.lb[0:112, :])], [], [A("DLB", 0, 24)], 24576, n=2)
-    dma("Y", lambda e: [e.dma_start(T.KD[:, 0:NV], T.kd[:])], [], [A("KD", 0, NV)], 786432)
-    dma("Y", lambda e: [e.dma_start(T.LF[:], T.lf[:])], [], [A("LF", 0, NL)], 1310720)
-    dma("Y", lambda e: [e.dma_start(T.LBI[:, 0:24], T.lb[:])], [], [A("LBI", 0, 24)], 12288)
-    dma("Y", lambda e: [e.dma_start(T.BK[:], T.bk[:])], [], [A("BK", 0, NB)], 1048576)
-
-    def rows(name, t):
-        r0 = 16 * ((8 - SH[t]) % 8)
-        return T[name][r0:r0 + 128, :]
-
-    send([(rows("DLB", t), A("DLB", 0, 24), t, A("LBI", 24 * t, 24 * t + 24), "a_lb%d" % t) for t in range(1, NT)], lambda k: [2 * k, 2 * k + 1], 12288, 3.0)
-
-    iota(A("PI", 0, 1), [[0, 1]], 0, 1)
-    for b, pat in enumerate(([[0, 8], [1, 2]], [[0, 4], [1, 2], [0, 2]], [[0, 2], [1, 2], [0, 4]], [[1, 2], [0, 8]])):
-        iota(A("XB", 16 * b, 16 * b + 16), pat)
-    iota(A("OCA", 0, 8), [[0, 2], [2, 4]])
-    iota(A("OCB", 0, 8), [[8, 2], [0, 4]], 16)
-    iota(A("X", 0, 16), [[1, 16]])
-    iota(A("OA", 0, 8 * NMAT), [[16, NMAT], [0, 8]], 16)
-    iota(A("OB", 0, 8 * NMAT), [[0, NMAT], [1, 8]])
-    iota(A("IOT", 0, 384), [[1, 384]])
-    iota(A("JT", 0, 24), [[16, 24]], 384)
-    for c, (s, m) in enumerate(((0, 1), (1, 1), (2, 1), (3, 1), (0, 15), (4, 7), (4, 1), (0, 3), (1, 7), (0, 7), (0, 127), (2, 3))):
-        ts(A("RBI", c, c + 1), A("PI", 0, 1), s, m, ALU.logical_shift_right, ALU.bitwise_and)
-    cp(A("RB", 0, 12), A("RBI", 0, 12))
-
-    def rb(c):
-        return A("RB", c, c + 1)
-    r_, g_, g0_, r3_, rh_, r7_, p_ = rb(4), rb(5), rb(6), rb(7), rb(8), rb(9), rb(10)
-    X = A("X", 0, 16)
-    ts(A("S1", 0, 4), A("RB", 0, 4), -2.0, 1.0, ALU.mult, ALU.add)
-    ts(A("S1", 4, 8), A("RB", 0, 4), -2.0, None, ALU.mult)
-
-    def s1(c):
-        return A("S1", c, c + 1)
-
-    def xb(b, n=16):
-        return A("XB", 16 * b, 16 * b + n)
-    for b in range(4):
-        ts(A("EB", 16 * b, 16 * b + 16), xb(b), s1(b), rb(b), ALU.mult, ALU.add)
-    for b, c in enumerate((7.0, 63.0, 4095.0)):
-        ts(A("FB", 16 * b, 16 * b + 16), A("EB", 16 * b, 16 * b + 16), c, 1.0, ALU.mult, ALU.add)
-    ts(A("FB", 48, 64), A("EB", 48, 64), -1.0, 1.0, ALU.mult, ALU.add)
-    tt(A("TM", 0, 16), A("FB", 0, 16), A("FB", 16, 32), ALU.mult)
-    tt(A("TM", 16, 32), A("FB", 32, 48), A("FB", 48, 64), ALU.mult)
-    tt(A("TM", 32, 48), A("TM", 0, 16), A("TM", 16, 32), ALU.mult)
-    ms(A("KTC", 0, 16), 0.0)
-    ts(A("KTC", 16, 32), A("TM", 32, 48), 2.0 ** -24, None, ALU.mult)
-    tt(A("TM", 64, 65), g_, rb(3), ALU.subtract)
-    ts(A("OCA", 0, 8), A("OCA", 0, 8), A("TM", 64, 65), None, ALU.is_equal)
-    ts(A("OCB", 0, 8), A("OCB", 0, 8), r7_, None, ALU.add)
-    tt(A("OCB", 0, 8), A("OCB", 0, 8), A("OCA", 0, 8), ALU.mult)
-    cp(A("OCU", 0, 8), A("OCB", 0, 8))
-    cp(A("WC", 0, 128), A("KTC", 0, 32), A("OCU", 0, 8))
-    iota(A("RS", 0, 768), [[0, 768]])
-    iota(A("RS", 0, 768, 8), [[0, 96]], 2)
-    iota(A("NTT", 3, NV, 4), [[0, 384]])
-    iota(A("KT", 0, 16 * (NMAT + 2)), [[0, 16 * (NMAT + 2)]])
-    ts(kt("WHI"), A("TM", 32, 48), 2.0 ** 24, None, ALU.mult)
-    tt(A("TM", 48, 64), A("FB", 32, 48), A("EB", 48, 64), ALU.mult)
-    tt(kt("WLO"), A("TM", 0, 16), A("TM", 48, 64), ALU.mult)
-    ts(kt("I"), X, r_, None, ALU.is_equal)
-    Ik = kt("I")
-
-    def icol(c):
-        return A("KT", Ik[1] + c, Ik[1] + c + 1)
-    cp(kt("I2"), Ik)
-    cp(kt("I", grp="h"), Ik)
-    cp(kt("I", grp="f"), Ik)
-    ts(kt("NI", grp="h"), Ik, -1.0, None, ALU.mult)
-    ts(kt("CROW", 0, 1, grp="h"), icol(10), -1.0, None, ALU.mult)
-    ts(kt("CROW2", 0, 1, grp="h"), icol(10), -1.0, None, ALU.mult)
-    ts(A("G3", 16, 20), A("X", 0, 4), rb(11), None, ALU.is_equal)
-    ts(A("G3", 20, 24), A("G3", 16, 20), -1.0, None, ALU.mult)
-    cp(kt("E", 0, 2), A("G3", 16, 18))
-    iota(kt("ONES"), [[0, 16]], 1)
-    ts(kt("LS", 0, 16, 2), kt("ONES", 0, 8), A("G3", 20, 21), None, ALU.mult)
-    ts(kt("LS", 1, 16, 2), kt("ONES", 0, 8), A("G3", 21, 22), None, ALU.mult)
-    ts(kt("LVH"), kt("ONES"), A("G3", 22, 23), 2.0 ** 24, ALU.mult, ALU.mult)
-    ts(kt("LVL"), kt("ONES"), A("G3", 23, 24), None, ALU.mult)
-    ts(kt("BS"), X, rh_, None, ALU.is_equal)
-    ts(kt("LT0"), X, r_, -BIG, ALU.is_gt, ALU.mult)
-    ts(kt("LT1"), X, r_, -BIG, ALU.is_ge, ALU.mult)
-    ts(A("TM", 80, 96), Ik, BIG, None, ALU.mult)
-    tt(kt("FT"), kt("LT0"), A("TM", 80, 96), ALU.add)
-    ts(kt("TRIU"), X, r_, -1.0, ALU.is_lt, ALU.mult)
-    for b in range(4):
-        ts(A("HB", 16 * b, 16 * b + 16), xb(b), s1(4 + b), 1.0, ALU.mult, ALU.add)
-    tt(A("HB", 64, 96), A("HB", 0, 32), A("HB", 32, 64), ALU.mult)
-    tt(kt("H"), A("HB", 64, 80), A("HB", 80, 96), ALU.mult)
-    cp(kt("H", grp="f"), kt("H"))
-    if ONPE:
-        ts(kt("NH", grp="f"), kt("H"), -1.0, None, ALU.mult)
-    ts(kt("FP"), kt("H"), 0.5, 0.5, ALU.mult, ALU.add)
-    ts(kt("FM"), kt("H"), -0.5, 0.5, ALU.mult, ALU.add)
-    ts(A("TM", 96, 100), xb(0, 4), s1(2), rb(2), ALU.mult, ALU.add)
-    ts(A("TM", 100, 104), xb(1, 4), s1(3), rb(3), ALU.mult, ALU.add)
-    ts(A("TM", 104, 108), A("TM", 96, 100), 384.0, None, ALU.mult)
-    ts(A("TM", 108, 112), A("TM", 100, 104), 768.0, None, ALU.mult)
-    tt(kt("PAY", 1, 5), A("TM", 104, 108), A("TM", 108, 112), ALU.add)
-    cp(kt("PAY", 7, 8), r_)
-    ts(kt("PAY", 0, 1), r3_, 1536.0, None, ALU.mult)
-    for nm in ("RP", "RM"):
-        iota(kt(nm, 5, 11), [[0, 6]], 1)
-        cp(kt(nm, 8, 9), r_)
-    iota(kt("RM", 9, 10), [[0, 1]], -1)
-    iota(kt("PW", 0, 7, 6, grp="h"), [[0, 2]], 1)
-    iota(kt("CONE", 0, 1, grp="h"), [[0, 1]], 1)
-    allo = 8 * NMAT
-    ts(A("OA", 0, allo), A("OA", 0, allo), r_, None, ALU.add)
-    ts(A("OB", 0, allo), A("OB", 0, allo), g_, None, ALU.is_equal)
-    tt(A("OA", 0, allo), A("OA", 0, allo), A("OB", 0, allo), ALU.mult)
-    cp(A("OU", 0, allo), A("OA", 0, allo))
-    KTW = A("KT", 0, 16 * (NMAT + 2))
-    for m0 in range(0, NKB, 4):
-        m1 = min(NKB, m0 + 4)
-        cp(A("KB", 128 * m0, 128 * m1), KTW, A("OU", 8 * m0, 8 * m1))
-    cp(A("KH", 0, 128 * NKH), KTW, A("OU", 8 * NKB, 8 * (NKB + NKH)))
-    cp(A("KF", 0, 128 * NKF), KTW, A("OU", 8 * (NKB + NKH), allo))
-    for nm, base, v in SCALED:
-        if (len(ONPE) < 2 or nm not in ("I22", "I44", "I66")) and (ONPE or nm[:2] not in ("H1", "H2", "H3")):
-            ts(K(nm), K(base), v, None, ALU.mult)
-    ts(A("CC", 0, 1), icol(5), float(rank + 1), icol(6), ALU.mult, ALU.subtract)
-    ts(A("CC", 6, 7), A("CC", 0, 1), icol(8), icol(9), ALU.add, ALU.add)
-    ts(A("CC", 1, 2), A("CC", 6, 7), icol(10), None, ALU.add)
-    ts(A("CC", 2, 3), r_, 5.0, None, ALU.is_lt)
-    ts(A("CC", 15, 16), icol(0), -1.0, None, ALU.mult)
-    ts(A("CC", 7, 8), r_, 5.0, icol(0), ALU.is_lt, ALU.subtract)
-    ts(A("CJ", 0, 384), A("IOT", 0, 384), A("CC", 7, 8), A("CC", 1, 2), ALU.mult, ALU.add)
-    ts(A("CC", 3, 4), g0_, 16.0, None, ALU.mult)
-    ts(A("DJ", 0, 24), A("JT", 0, 24), r_, A("CC", 3, 4), ALU.add, ALU.add)
-    ts(A("CC", 8, 9), rh_, 32.0, A("CC", 3, 4), ALU.mult, ALU.add)
-    ts(A("CC", 9, 10), rb(0), 192.0, A("CC", 8, 9), ALU.mult, ALU.add)
-    ts(A("ZU", 0, 6), A("X", 0, 6), A("CC", 9, 10), 383.0, ALU.add, ALU.min)
-    ts(A("CC", 10, 11), g0_, s1(0), rb(0), ALU.mult, ALU.add)
-    ts(A("CC", 11, 12), A("CC", 10, 11), 384.0, A("CC", 8, 9), ALU.mult, ALU.add)
-    ts(A("CC", 12, 13), A("CC", 10, 11), g0_, -32.0, ALU.mult, ALU.mult)
-    ts(A("CC", 13, 14), icol(0), g0_, 384.0, ALU.mult, ALU.mult)
-    ts(A("CC", 14, 15), A("CC", 11, 12), A("CC", 12, 13), None, ALU.add)
-    iota(A("ZW", 0, 10), [[1, 5], [256, 2]])
-    ts(A("ZW", 0, 10, 2), A("ZW", 0, 10, 2), A("CC", 13, 14), None, ALU.add)
-    ts(A("ZV", 0, 10), A("ZW", 0, 10), A("CC", 14, 15), 767.0, ALU.add, ALU.min)
-    ts(A("DJ1", 0, 24), A("JT", 0, 24), r_, 1.0, ALU.add, ALU.add)
-    iota(A("ONE", 0, 24), [[0, 24]], 1)
-    iota(A("LV", 0, 24), [[0, 24]], 1)
-    for t in range(NT):
-        ts(A("GI", t, t + 1), A("RBI", 5, 6), float(8 - SH[t]), None, ALU.add)
-    ts(A("GI", 0, 5), A("GI", 0, 5), 7, None, ALU.bitwise_and)
-    ts(A("CC", 4, 5), r_, 76.0, None, ALU.add)
-    ts(A("GF", 0, 5), A("GI", 0, 5), 5.0, A("CC", 4, 5), ALU.mult, ALU.add)
-    ts(A("CC", 5, 6), r_, 10.0, A("CC", 2, 3), ALU.is_lt, ALU.subtract)
-    ts(A("GF", 0, 5), A("GF", 0, 5), A("CC", 5, 6), -1.0, ALU.mult, ALU.add)
-    for t in range(NT):
-        ts(A("OUTM", 208 * t, 208 * t + 208), A("IOT", 0, 208), A("GF", t, t + 1), None, ALU.is_equal)
-    ts(A("CN", 0, 128), A("IOT", 0, 128), 0.0, icol(5), ALU.mult, ALU.subtract)
-    iota(A("Z", 0, 208), [[0, 208]])
-    iota(A("RES", 192, 208), [[0, 16]])
-    ts(A("KIF", 1, 2), s1(0), p_, None, ALU.add)
-    ts(A("KIF", 2, 3), s1(1), 2.0, p_, ALU.mult, ALU.add)
-    ts(A("KIF", 3, 4), A("KIF", 2, 3), s1(0), None, ALU.add)
-    cp(A("KIX", 1, 4), A("KIF", 1, 4))
-    for m in (1, 2, 3):
-        dma("G", lambda e, m=m: [e.indirect_dma_start(T.KD[:, NV * m:NV * m + NV], None, T.kd[:], IndirectOffsetOnAxis(ap=T.KIX[:, m:m + 1], axis=0),
-                                                      bounds_check=127)],
-            [A("KIX", m, m + 1), A("BK", 0, NB)], [A("KD", NV * m, NV * m + NV)], 786432, issue=1.7)
-
-    tag[0] = "N"
-    for i in range(12):
-        bk0, bk1, c0 = (0, 2, 64 * i) if i < 6 else (1, 7, 64 * (i - 6))
-        mm(bank(bk1, c0, c0 + 64), [(A("IV", 128 * i, 128 * i + 128), A("WC", 64, 128))])
-        mm(bank(bk0, c0, c0 + 64), [(A("IV", 128 * i, 128 * i + 128), A("WC", 0, 64))])
-    def cb(n, lo=0, hi=768, step=1):
-        nm, o = {"C1": ("AF", 0), "CA": ("AF", 768), "CB": ("AH", 0), "CD": ("AH", 768), "CM1": ("KP", 0)}[n]
-        return A(nm, o + lo, o + hi, step)
-    for h, (b0, b1) in enumerate(((0, 2), (1, 7))):
-        lo, hi = 384 * h, 384 * h + 384
-        cp(cb("C1", lo, hi), bank(b1, 0, 384))
-        tt(cb("CA", lo, hi), bank(b0, 0, 384), cb("C1", lo, hi), ALU.min)
-        tt(cb("CB", lo, hi), bank(b0, 0, 384), cb("C1", lo, hi), ALU.max)
-        ts(A("WI", 2 + 192 * h, 192 + 192 * h, 4), A("B%d" % b0, 0, 384, 8), 2.0 ** 24, -MID, ALU.mult, ALU.add)
-    ts(A("WI", 3, 384, 4), cb("C1", 0, 768, 8), 2.0 ** 24, -MID, ALU.mult, ALU.add)
-    scan(cb("CM1"), A("RS", 0, 768), cb("CA"), ALU.add, ALU.min)
-    for i in range(8):
-        tt(cb("CD", i, 768, 8), cb("CA", i, 768, 8), cb("CM1", 7, 768, 8), ALU.is_gt)
-    ts(A("WI", 0, 384, 4), cb("CM1", 7, 768, 8), 2.0 ** 24, -MID, ALU.mult, ALU.add)
-    tt(cb("CD"), cb("CD"), cb("CB"), ALU.max)
-    scan(cb("CA"), A("RS", 0, 768), cb("CD"), ALU.add, ALU.min)
-    ts(A("WI", 1, 384, 4), cb("CA", 7, 768, 8), 2.0 ** 24, -MID, ALU.mult, ALU.add)
-    cp(A("NTT", 0, NV, 4), A("WI", 0, 384))
-    tt(A("WP", 0, 384), A("WI", 0, 384), A("NTT", 0, NV, 4), ALU.subtract)
-    cp(A("NTT", 1, NV, 4), A("WP", 0, 384))
-    tt(A("NTT", 2, NV, 4), A("WP", 0, 384), A("NTT", 1, NV, 4), ALU.subtract)
-    for j in range(3):
-        for i in range(4 * j, 4 * j + 4):
-            mm(bank(j, 128 * (i % 4), 128 * (i % 4) + 128), [(A("NTT", 128 * i, 128 * i + 128), K("I"))])
-        cp(A("NTB", 512 * j, 512 * j + 512), bank(j, 0, 512))
-
-    tag[0] = "A"
-    cp(A("LVU", 0, 24), A("LVI", 0, 24))
-    cp(A("KA", 0, 384), A("KD", 0, NV), A("LVU", 0, 24))
-    for c in range(0, 384, CHC):
-        cp(A("XA", 16 * c, 16 * (c + CHC)), A("LF", 0, NL), A("KA", c, c + CHC))
-    for c in range(3):
-        for w in range(4):
-            mm(bank(3 + w, 128 * c, 128 * c + 128),
-               [(K(("I", "I16", "I256", "I4096")[i]), A("XA", 2048 * c + 4 * w + i, 2048 * c + 2048, 16)) for i in range(4)])
-    for w in range(4):
-        ts(A("AU", 384 * w, 384 * w + 384), bank(3 + w, 0, 384), float(AOFF), None, ALU.add)
-        cp(A("AR", 384 * w, 384 * w + 384), bank(3 + w, 0, 384))
-    cp(A("LT", 0, 384), A("NTB", 0, NV), A("LVU", 0, 24))
-    dma("Y", lambda e: [e.dma_start(T.DLT[0:128, :], T.LT[:, 0:384]), e.dma_start(T.DLT[128:240, :], T.LT[0:112, 0:384])],
-        [A("LT", 0, 384)], [A("DLT", 0, 384)], 98304 * 2, n=2)
-    send([(rows("DLT", t), A("DLT", 0, 384), t, A("LT", 384 * t, 384 * t + 384), "a_lt%d" % t) for t in range(1, NT)], lambda k: [2 * k, 2 * k + 1], 98304, 3.0)
-    dma("Y", lambda e: [e.dma_start(T.DAU[0:128, :], T.AU[:, 0:1536]), e.dma_start(T.DAU[128:240, :], T.AU[0:112, 0:1536])],
-        [A("AU", 0, 1536)], [A("DAU", 0, 1536)], 393216 * 2, n=2)
-    for t in range(1, NT):
-        send([(rows("DAU", t), A("DAU", 0, 1536), t, A("AU", 1536 * t, 1536 * t + 1536), "a_au%d" % t)], lambda k: [0, 2, 4, 6], 393216, 3.0)
+    def bank(i, lo, hi, step=1, p1=128):
+        return A("B%d" % i, lo, hi, step, 0, p1)
 
     def nonzero(out, i):
         return ts(out, i, 0.0, None, ALU.not_equal, s=act(out, i, ACT.Abs))
 
-    def iszero(out, i):
-        return ts(out, i, 0.0, None, ALU.is_equal, s=act(out, i, ACT.Relu, 1.0, -1.0))
+    def rot(t):
+        return 16 * ((8 - SH[t]) % 8)
 
-    def first(out, i):
-        return ts(out, i, 1.0 / BIG, 0.0, ALU.mult, ALU.max, s=act(out, i, ACT.Relu, 0.0, 1.0 / BIG))
+    def HAm(i, neg, t):
+        c = 256 * (2 * i + neg) + rot(t)
+        return A("HA", c, c + 128)
 
-    def lessone(out, i):
-        return ts(out, i, A("CC", 15, 16), 0.0, ALU.add, ALU.max, s=act(out, i, ACT.Relu, A("CC", 15, 16), 1.0))
+    def HBm(d):
+        return A("HB", 128 * d, 128 * d + 128) if d else Hb
+
+    def IDm(n):
+        c = 128 * ("I32", "N32", "I512", "I8192", "SGN").index(n)
+        return A("ID", c, c + 128)
+
+    def col(b):
+        return A("TB", 32 * b, 32 * b + 1)
+
+    def cc(c):
+        return A("CC", c, c + 1)
+
+    def slot(t):
+        return (t - 1) % NT
+    Hb = A("HA", 0, 128)
+    HP = A("PT", 16, 32)
+
+    dma(lambda e: [e.dma_start(T.IV[:], T.iv[:])], [], [A("IV", 0, NV)], 393216)
+    dma(lambda e: [e.dma_start(T.DLB[0:128, :], T.lb[:]), e.dma_start(T.DLB[128:240, :], T.lb[0:112, :])], [], [A("DLB", 0, 24)], 24576, n=2)
+    dma(lambda e: [e.dma_start(T.KDI[:], T.kd[:])], [], [A("KDI", 0, NV)], 786432)
+    dma(lambda e: [e.dma_start(T.LVI[:], T.lv[:]), e.dma_start(T.LBI[:, 0:24], T.lb[:])], [], [A("LVI", 0, 24), A("LBI", 0, 24)], 24576, n=2)
+    dma(lambda e: [e.dma_start(T.BK[:], T.bk[:])], [], [A("BK", 0, NB)], 1048576)
+    dma(lambda e: [e.dma_start(T.LF[:], T.lf[:])], [], [A("LF", 0, NL)], 1310720)
+    send([(T.DLB[rot(t):rot(t) + 128, :], A("DLB", 0, 24), t, A("LBI", 24 * t, 24 * t + 24), "a_lb%d" % t) for t in range(1, NT)],
+         lambda k: [2 * k, 2 * k + 1], 12288, 4.0)
+
+    for b in range(4):
+        iota(A("XB", 32 * b, 32 * b + 32), [[0, 16 >> b], [-2, 2]] + ([[0, 1 << b]] if b else []), 1)
+    iota(A("OI", 0, 8), [[-16, 8]], 16, 1)
+    ms(A("PT", 0, 112), 0.0)
+    ms(A("PT", 16, 17), 1.0)
+    turn(A("TB", 0, 128), A("XB", 0, 128))
+    ts(A("OU", 0, 8), A("OI", 0, 8), 32.0, None, ALU.min)
+    for b in range(4):
+        n = 1 << b
+        ts(A("PT", 16 + n, 16 + 2 * n), A("PT", 16, 16 + n), col(b), None, ALU.mult, s=False)
+    cp(Hb, A("PT", 0, 48), A("OU", 0, 8))
+    for b, (m, a) in enumerate(((-8.0, 24.0), (-1.5, 2.5), (-7.5, 8.5), (-127.5, 128.5))):
+        ts(cc(b), col(b), m, a, ALU.mult, ALU.add)
+    ts(cc(4), cc(0), cc(1), cc(2), ALU.mult, ALU.mult)
+    ts(A("KK", 0, 128), Hb, cc(4), cc(3), ALU.mult, ALU.mult)
+    fill(A("RS", 0, 512), 1)
+    fill(A("RS", 0, 512, 16), 1 << 23)
+    iota(A("MK", 0, 256), [[0, 256]], 1)
+    select(A("MK", 0, 256), A("MK", 0, 256), [[0, 32], [-16, 8]], ALU.is_ge, 0.0, 0, 1)
+    select(A("MK", 0, 256), A("MK", 0, 256), [[0, 32], [16, 8]], ALU.is_ge, 0.0, 15, -1)
+    iota(A("EI", 0, 16), [[1, 8], [16, 2]])
+    ts(cc(9), col(3), -4.0, 4.0, ALU.mult, ALU.add)
+    ts(A("EL", 0, 16), A("EI", 0, 16), cc(9), None, ALU.add)
+    iota(A("XB", 128, 160), [[0, 2], [1, 16]])
+    fill(A("XB", 160, 320), 0)
+    for b, rows in ((8, ((0, 680), (1, -8), (2, -32), (4, -128), (8, -512))), (5, [(r, 64 ** r) for r in range(4)]),
+                    (6, [(4 + r, 64 ** r) for r in range(4)]), (7, ((8, 256), (9, 1), (10, 2048))), (9, ((10, 1),))):
+        for r, v in rows:
+            fill(A("XB", 32 * b + r, 32 * b + 32, 16), v)
+    for h in (0, 16):
+        fill(A("XB", 288 + h, 296 + h), -1)
+    turn(A("TB", 128, 160), A("XB", 128, 160))
+    turn(A("TB", 256, 288), A("XB", 256, 288))
+    ms(A("SS", 0, 240), 0.0)
+    ts(A("SS", 112, 128), A("XB", 128, 144), col(4), None, ALU.is_equal)
+    cp(A("HFL", 0, 128), Hb)
+    ts(A("PK8", 0, 8), A("PT", 17, 32, 2), 8.0, None, ALU.mult)
+    tt(A("PT", 48, 56), A("PT", 16, 32, 2), A("PK8", 0, 8), ALU.add)
+    cp(A("PKM", 0, 128), A("PT", 32, 80), A("OU", 0, 8))
+    cp(A("PT", 90, 91), col(8))
+    cp(A("PSM", 0, 128), A("PT", 64, 112), A("OU", 0, 8))
+    iota(A("IOT", 0, 256), [[1, 256]])
+    select(A("IOT", 0, 256), A("IOT", 0, 256), [[0, 256]], ALU.is_gt, 1.0, 0, 1)
+    ms(A("DW", 0, 768), 0.0)
+    iota(A("DW", 8, 768, 16), [[16, 6], [0, 8]])
+    fill(A("DW", 9, 768, 16), 16)
+    for r in range(2):
+        select(A("DW", 8 + r, 768, 16), A("DW", 8 + r, 768, 16), [[0, 48]], ALU.is_equal, 0.0, -r, 1)
+    tag[0] = "K2"
+    turn(A("TB", 160, 256), A("XB", 160, 256))
+    turn(A("TB", 288, 320), A("XB", 288, 320))
+    fill(A("ONE", 0, 128), 1)
+    for n, v in (("I32", 32), ("I512", 512), ("I8192", 8192), ("N32", -32)):
+        fill(IDm(n), v)
+        select(IDm(n), IDm(n), [[-1, 128]], ALU.is_equal, 0.0, 0, 1)
+    ts(IDm("SGN"), IDm("I32"), col(9), None, ALU.mult)
+    select(A("TRI", 0, 128), A("ONE", 0, 128), [[1, 128]], ALU.is_gt, 0.0, 0, -1)
+    select(A("TRI", 0, 128), A("TRI", 0, 128), [[1, 128]], ALU.not_equal, -1024.0, 0, -1)
+    fill(A("RT", 0, 256), 1)
+    fill(A("RT", 0, 256, 32), 1 << 23)
+    fill(A("CF", 0, 40), 0)
+    fill(A("CF", 0, 40, 5), -1)
+    cp(A("HA", 128, 256), Hb)
+    ts(A("HA", 256, 512), A("HA", 0, 256), -1.0, None, ALU.mult)
+    ts(A("HA", 512, 1024), A("HA", 0, 512), 16.0, None, ALU.mult)
+    ts(A("HA", 1024, 1536), A("HA", 512, 1024), 16.0 ** 3, None, ALU.mult)
+    ts(A("HA", 1536, 2560), A("HA", 512, 1536), 16.0 ** 6, None, ALU.mult)
+    ts(A("HA", 2560, 3072), A("HA", 512, 1024), 16.0 ** 12, None, ALU.mult)
+    ts(A("HB", 128, 256), Hb, 16.0, None, ALU.mult)
+    ts(A("HB", 256, 384), Hb, 256.0, None, ALU.mult)
+    ts(A("HB", 384, 640), A("HB", 128, 384), 256.0, None, ALU.mult)
+    ts(A("HB", 640, 1152), A("HB", 128, 640), 16.0 ** 4, None, ALU.mult)
+    ts(A("HB", 1152, 2048), A("HB", 128, 1024), 16.0 ** 8, None, ALU.mult)
+    ts(cc(6), col(7), 2.0 ** -23, None, ALU.mult)
+    for w, c in enumerate((col(5), col(6), cc(6))):
+        ts(A("WR", 256 * w, 256 * w + 256), A("HA", 0, 256), 0.0, c, ALU.not_equal, ALU.mult)
+        cp(A("W24", 8 * w, 8 * w + 8), A("WR", 256 * w, 256 * w + 128, 16))
+    ts(cc(7), A("PT", 31, 32), 64.0, None, ALU.mult)
+    ts(cc(8), A("PT", 31, 32), -64.0, None, ALU.mult)
+    for nm, par, c in (("FD", 1, 7), ("FD", 0, 8), ("FS", 1, 8), ("FS", 0, 7)):
+        out = A(nm, par, 256, 2)
+        ts(out, Hb, cc(c), 0.0, ALU.mult, ALU.max, s=act(out, Hb, ACT.Relu, 0.0, cc(c)))
+    ts(cc(5), col(3), -64.0, 79.0, ALU.mult, ALU.add)
+    for t in range(NT):
+        iota(A("RI", 2 * t, 2 * t + 2), [[0, 2]], SH[t], 1)
+    iota(A("RF", 10, 20), [[0, 5], [256, 2]])
+    ts(A("RI", 0, 10), A("RI", 0, 10), 7, None, ALU.bitwise_and)
+    ts(A("RF", 0, 10), A("RI", 0, 10), 16.0, cc(5), ALU.mult, ALU.add)
+    tt(A("RF", 0, 10), A("RF", 0, 10), A("RF", 10, 20), ALU.add)
+    ts(A("RL", 0, 10), A("RF", 0, 10), 383.0, None, ALU.min)
+    ts(A("RL", 10, 20), A("RL", 0, 10), 2.0, 1.0, ALU.mult, ALU.add)
+    iota(A("L5F", 0, 8), [[16, 8]], -2)
+    ts(A("L5F", 0, 8), A("L5F", 0, 8), col(4), 0.2, ALU.add, ALU.mult)
+    cp(A("L5I", 0, 8), A("L5F", 0, 8))
+    cp(A("L5", 0, 8), A("L5I", 0, 8))
+    fill(A("MG", 0, 160), 0)
+    fill(A("FF", 0, 608), 0)
+    for t in range(NT):
+        fill(A("FF", 120 * slot(t), 120 * slot(t) + 120, 5), (rank + t) % NR + 1)
+
+    def to_list(sb, ncol, top, scale, bits, out):
+        e0, l0 = 256 * sb, 64 * sb
+        ts(A("LI", l0, l0 + ncol), A("SC", 512 * sb + 15, 512 * sb + 16 * ncol, 16), top, scale, ALU.min, ALU.mult)
+        ts(A("LI", l0 + 32, l0 + 32 + ncol), A("LI", l0, l0 + ncol), bits, None, ALU.bitwise_and)
+        tt(A("E", e0, e0 + 256), A("LI", l0 + 32, l0 + 64), A("MK", 0, 256), ALU.mult, off=A("EL", 0, 16))
+        mm(bank(6, 0, ncol), [(A("SS", 112 - 16 * q, 240 - 16 * q), A("E", e0 + 32 * q, e0 + 32 * q + ncol)) for q in range(8)])
+        cp(out, bank(6, 0, ncol))
+
+    tag[0] = "N"
+    cp(A("KDF", 0, NV), A("KDI", 0, NV))
+    for c in range(3):
+        lo, hi = 512 * c, 512 * c + 512
+        mm(bank(c % 2, 0, 512), [(Hb, A("IV", lo, hi))])
+        ts(A("TAU", lo, hi), bank(c % 2, 0, 512), 1.0, -1.0, ALU.min, ALU.max, s=act(A("TAU", lo, hi), bank(c % 2, 0, 512), ACT.Sign))
+        mg([(bank(2 + c % 2, 128 * i, 128 * i + 128), A("TAU", lo + 128 * i, lo + 128 * i + 128), A("KK", 0, 128)) for i in range(4)])
+        least(A("SC", 512 * (c % 2), 512 * (c % 2) + 512), A("RS", 0, 512), bank(2 + c % 2, 0, 512))
+        to_list(c % 2, 32, 2.0 ** 22, 1.0, 15, A("MU", 32 * c, 32 * c + 32))
+        cp(A("SG", lo, hi), HP, A("MU", 32 * c, 32 * c + 32))
+    for c in range(3):
+        lo, hi = 512 * c, 512 * c + 512
+        mm(bank(4 + c % 2, 0, 512), [(A("HFL", 0, 128), A("KDF", lo, hi))])
+        tt(A("KS", lo, hi), bank(4 + c % 2, 0, 512), A("SG", lo, hi), ALU.mult)
+        mm(bank(7, 0, 512), [(A("HFL", 0, 128), A("KS", lo, hi))])
+        ts(A("KP", lo, hi), bank(7, 0, 512), 1.0 / 16, None, ALU.mult)
+        mm(bank(c % 2, 0, 512), [(Hb, A("IV", lo, hi))])
+        tt(A("SI", lo, hi), bank(c % 2, 0, 512), A("SG", lo, hi), ALU.mult)
+        b = 2 + c % 2
+        mg([(bank(b, 0, 512), A("PKM", 0, 128), A("SI", lo, hi)), (bank(b, 0, 512), A("PSM", 0, 128), A("SG", lo, hi))] +
+           [(bank(b, 256 * h, 256 * h + 256), A("DW", 128 * (2 * c + h), 128 * (2 * c + h) + 128), A("IOT", 0, 256)) for h in range(2)])
+        cp(A("NTB", lo, hi), bank(b, 0, 512))
+
+    def spread(buf, x, table, lists, l0):
+        for c in range(0, L, GCH):
+            cp(A(buf, 16 * (L * x + c), 16 * (L * x + c + GCH)), table, A(lists, l0 + c, l0 + c + GCH))
+
+    tag[0] = "A"
+    cp(A("LVU", 0, 24), A("LVI", 0, 24))
+    cp(A("KA", 0, L), A("KP", 0, NV), A("LVU", 0, 24))
+    cp(A("NA", 0, L), A("NTB", 0, NV), A("LVU", 0, 24))
+    spread("XT", 1, A("LF", 0, NL), "KA", 0)
+
+    def xa(d):
+        return A("XT", 16 * L + d, 32 * L, 16)
+    for i in range(6):
+        b = bank((4, 5, 7, 2, 3, 4)[i], 0, L)
+        if i == 0:
+            mm(b, [(IDm("I32"), xa(0)), (IDm("SGN"), A("NA", 0, L))])
+        else:
+            mm(b, [(IDm(n), xa(ASC[i] + j)) for j, n in enumerate(("I32", "I512", "I8192"))])
+        ts(A("AP", L * i, L * i + L), b, 1.0 / 32, None, ALU.mult)
+        if i == 0:
+            send([(ap(A("AP", 0, L)), A("AP", 0, L), t, A("AP", 6 * L * t, 6 * L * t + L), "a_p0%d" % t) for t in range(1, NT)],
+                 lambda k: [2 * k, 2 * k + 1], 98304)
+    for t in range(1, NT):
+        send([(ap(A("AP", L, 6 * L)), A("AP", L, 6 * L), t, A("AP", 6 * L * t + L, 6 * L * t + 6 * L), "a_pp%d" % t)], lambda k: list(range(8)), 491520)
+    mg([(bank(7, 128 * i, 128 * i + 128, 1, 40), A("CF", 0, 40), IDm("I32")) for i in range(3)], stop=False)
+
+    def home(t, out, land, sem):
+        send([(ap(out), out, -t, land, sem)], lambda k: list(range(8)), 12288)
 
     def claims(t):
-        par = t
-        lt0 = 384 * t
-        LTa = A("LT", lt0, lt0 + 384)
-        w0 = 384 * (CORDER.index(t) % 2)
-        cp(A("LBU", 24 * t, 24 * t + 24), A("LBI", 24 * t, 24 * t + 24))
-        cp(A("WF", w0, w0 + 384), A("BK", 0, NB), A("LBU", 24 * t, 24 * t + 24))
-        cp(A("WU", w0, w0 + 384), A("WF", w0, w0 + 384))
-        for c in range(0, 384, CHC):
-            cp(A("XC", 16 * c, 16 * (c + CHC)), A("NTB", 0, NV), A("WU", w0 + c, w0 + c + CHC))
-        for c in range(0, 384, PCC):
-            for h in range(2):
-                mm(bank(h, c, c + PCC), [(K("LS"), A("LT", lt0 + c, lt0 + c + PCC))] +
-                   [(K("E", 2 * k), A("XC", 16 * c + 8 * h + k, 16 * (c + PCC), 16)) for k in range(8)])
-        for h in range(2):
-            nonzero(A("NE", 384 * h, 384 * h + 384), bank(h, 0, 384))
-        b2 = bank(2, 0, 384)
-        mm(b2, [(K("BS"), A("NE", 0, 384)), (K("BS", 8), A("NE", 384, 768))])
-        iszero(A("FIT", 0, 384), b2)
-        mm(b2, [(K("FT"), A("FIT", 0, 384)), (KFm("I"), A("WF", w0, w0 + 384))])
-        ts(A("VAL", 0, 384), b2, 1.0 - BIG, 0.0, ALU.add, ALU.max)
-        bl = bank(2, 384, 408)
-        mm(bl, [(KHm("CONE", l), A("VAL", l, 384, 16)) for l in range(16)])
-        ts(A("WX", 0, 24), bl, -1.0, 0.0, ALU.add, ALU.max)
-        ts(A("CL", 24 * par, 24 * par + 24), bl, 1.0, None, ALU.min)
-        tt(A("CLJ", 24 * par, 24 * par + 24), A("CL", 24 * par, 24 * par + 24), A("DJ1", 0, 24), ALU.mult)
-        iw, win, off = A("IW", 0, 384), A("IV", 0, NV), A("WX", 0, 24)
-        add([("V", lambda e: [e.tensor_scalar(ap(iw), src(win, off), -4.0, None, ALU.add)], cost(iw, win, off)), act(iw, win, ACT.Identity, -4.0, 1.0, off)],
-            [win, off], [iw], g=off)
-        mm(b2, [(K("WHI"), A("IW", 0, 384)), (K("LVH"), LTa), (K("WLO"), A("IW", 0, 384)), (K("LVL"), LTa)])
-        ts(A("FM", 0, 384), b2, 0.0, None, ALU.is_equal)
-        mm(b2, [(K("FT"), A("FM", 0, 384))])
-        first(A("OH", 0, 384), b2)
-        mm(b2, [(KHm("I"), A("CJ", 0, 384)), (KHm("PW"), A("VAL", 0, 384)), (K("PAY"), A("OH", 0, 384))])
-        lessone(A("P", 400 * t, 400 * t + 384), b2)
-        if t in AHEAD:
-            lessone(A("P", 400 * t + 384, 400 * t + 400), bank(2, 0, 16))
-            for h in range(2):
-                turn(A("ZA", 384 * h, 384 * h + 384), A("P", 400 * t + 16 * h, 400 * t + 16 * h + 384))
-            cp(A("ALU", 160 * t, 160 * t + 160), A("ZA", 0, 768), A("ZV", 0, 10))
-            cp(A("KU", 384 * t, 384 * t + 384), A("KD", 0, 4 * NV), A("ALU", 160 * t, 160 * t + 24))
-
-    def ar0(t):
-        return 1536 * (2 if t in AHEAD else t % 2)
-
-    def unpack(t):
-        for w in range(0, 1536, 768):
-            ts(A("AR", ar0(t) + w, ar0(t) + w + 768), A("AU", 1536 * t + w, 1536 * t + w + 768), float(-AOFF), None, ALU.add)
-
-    def tests(t):
-        par = t
-        live = A("LV", 24 * t, 24 * t + 24)
-        Pt = A("P", 400 * t, 400 * t + 384)
-        l24 = lambda n: A(n, 0, 24)
-        tt(l24("CAND"), live, A("CL", 24 * par, 24 * par + 24), ALU.mult)
-        tt(l24("CANJ"), live, A("CLJ", 24 * par, 24 * par + 24), ALU.mult)
-        mm(bank(7, 24, 48), [(K("ONES"), l24("CAND"))])
-        mm(bank(7, 0, 24), [(K("TRIU"), l24("CAND")), (KHm("I"), l24("DJ")), (KHm("NI"), l24("CANJ"))])
-        scan(l24("CUM"), l24("ONE"), bank(7, 24, 48), ALU.mult, ALU.add)
-        tt(l24("RI"), bank(7, 0, 24), l24("CUM"), ALU.add)
-        rot = 16 * (8 - (SH[(t + 1) % NT] - SH[t]) % 8)
-
-        def masked(win, off, other, out=A("RO", 0, 384)):
-            add([("V", lambda e: [e.tensor_tensor(ap(out), src(win, off), ap(other), ALU.mult)], 0.06 + 384 * GF_ * CY)], [win, off, other], [out])
-
-        def hand_on(prs):
-            mm(bank(7, 0, 24), [(K("I", -rot), live)] + prs)
-            m = A("MSG", 24 * t, 24 * t + 24)
-            cp(m, bank(7, 0, 24))
-            send([(ap(m), m, 1, A("LV", 24 * t + 24, 24 * t + 48), "a_lv%d" % (t + 1))], lambda k: [1, 3, 5, 7], 6144, 2.5)
-        if t in AHEAD:
-            if t < NT - 1:
-                ts(l24("RU"), l24("RI"), A("CC", 3, 4), float(CAP), ALU.subtract, ALU.is_lt)
-                tt(l24("MG"), l24("RU"), A("NOK", 24 * t, 24 * t + 24), ALU.mult)
-                hand_on([(K("I", -rot), l24("MG"))])
-            ts(l24("POS2"), l24("RI"), A("CC", 3, 4), float(CAP), ALU.subtract, ALU.is_lt)
-            if t < NT - 1:
-                masked(X, l24("POS2"), A("ROF", 384 * t, 384 * t + 384))
-            else:
-                masked(X, l24("POS2"), Pt, A("MP", 0, 384))
-                for c in (0, 192):
-                    tt(A("RO", c, c + 192), A("RESF", c, c + 192), A("MP", c, c + 192), ALU.mult)
-        else:
-            if t:
-                unpack(t)
-            cp(l24("POS"), l24("RI"))
-            add([("V", lambda e: [e.tensor_copy(T.Z[:, 0:1184].indirect(T.POS[:, 0:24]), ap(Pt))], 0.06 + 384 * 3.8 * CY)], [Pt, l24("POS")], [A("Z", 0, 1184)])
-            ts(l24("POS2"), l24("RI"), A("CC", 3, 4), float(CAP), ALU.subtract, ALU.min)
-            for h in range(2):
-                turn(A("ZT", 192 * h, 192 * h + 192), A("Z", 16 * h, 16 * h + 192))
-            cp(A("LLU", 0, 80), A("ZT", 0, 384), A("ZU", 0, 5))
-            cp(A("KL", 0, 192), A("KD", 0, 4 * NV), A("LLU", 0, 12))
-            batch(t, 0, (3, 4, 7, 7), A("KL", 0, 192), [A("LLU", 16 + 16 * a, 28 + 16 * a) for a in range(4)], A("RES", 0, 192), CH1)
-            masked(A("RES", 0, 208), l24("POS2"), Pt)
-            if t < NT - 1:
-                hand_on([(KHm("CROW", l - rot), A("RO", l, 384, 16)) for l in range(16)])
-        prs = [(A("OUTM", 208 * t + 80 - 40 * i, 208 * t + 208 - 40 * i), A("RO", 128 * i, 128 * i + 128)) for i in range(3)]
-        if t == 0:
-            prs += [(A("OUTM", 80 - 40 * i, 208 - 40 * i), A("CN", 0, 128)) for i in range(3)]
-        mm(bank(7, 384, 512), prs)
-        om = A("OM", 128 * t, 128 * t + 128)
-        cp(om if t else A("ACC", 0, 128), bank(7, 384, 512))
-        if t:
-            land = A("OL", 128 * (t - 1), 128 * t)
-            send([(ap(om), om, -t, land, "a_om%d" % t)], lambda k: [1, 3, 5, 7] if t < NT - 1 else list(range(8)), 32768, 2.5)
-            tt(A("ACC", 0, 128), A("ACC", 0, 128), land, ALU.add)
-
-    def batch(t, x, bk, kl, alists, res, ch):
-        def S(n, lo, hi, step=1):
-            w = SCRATCH[n][1][1] // 2
-            return A(n, w * x + lo, w * x + hi, step)
-        lo, hi, al = bank(bk[3], 0, 192), bank(bk[3], 192, 384), bank(bk[3], 0, 384)
-        for a, off in enumerate(alists):
-            out, win, v = S("AF", 192 * a, 192 * a + 192), A("AR", ar0(t), ar0(t) + 1536), 2.0 ** (22 * a)
-            if x in ONPE and a:
-                add([("V", lambda e, out=out, win=win, off=off, v=v: [e.tensor_scalar(ap(out), src(win, off), v, None, ALU.mult)], cost(out, win, off)),
-                     act(out, win, ACT.Identity, 0.0, v, off)], [win, off], [out], g=off)
-            else:
-                cp(out, win, off)
-        if x in ONPE:
-            for c in range(0, 192, ch):
-                cp(S("XT", 16 * c, 16 * (c + ch)), A("LF", 0, NL), A(kl[0], kl[1] + c, kl[1] + c + ch))
-            al = bank(bk[0], 0, 384)
-            for h in range(2):
-                for y, nm in enumerate(("NH", "H")):
-                    prs = []
-                    for w in (3, 2, 1, 0):
-                        prs.append((KFm(nm), S("AF", 192 * w + 96 * h, 192 * w + 96 * h + 96)))
-                        prs += [(K("H%d_%d" % (w, i) if w or i else "H"), S("XT", 1536 * h + 4 * w + i, 1536 * h + 1536, 16)) for i in range(4)]
-                    mm(bank(bk[0], 192 * y + 96 * h, 192 * y + 96 * h + 96), prs)
-        else:
-            light(S, bk, kl, ch)
-        nonzero(S("BD", 0, 384), al)
-        al = bank(bk[3], 0, 384)
-        mm(lo, [(K("FP"), S("BD", 0, 192)), (K("FM"), S("BD", 192, 384))])
-        mm(hi, [(K("FM"), S("BD", 0, 192)), (K("FP"), S("BD", 192, 384))])
-        iszero(S("TF", 0, 384), al)
-        mm(lo, [(K("FT"), S("TF", 0, 192)), (K("LT0"), S("TF", 192, 384))])
-        mm(hi, [(K("FT"), S("TF", 192, 384)), (K("LT1"), S("TF", 0, 192))])
-        first(S("TO", 0, 384), al)
-        mm(lo, [(K("RP"), S("TO", 0, 192)), (K("RM"), S("TO", 192, 384))])
-        cp(res, lo)
-
-    def light(S, bk, kl, ch):
-        for h in range(2):
-            for w in range(4):
-                mm(bank(bk[2], 96 * w, 96 * w + 96), [(KFm("H"), S("AF", 192 * w + 96 * h, 192 * w + 96 * h + 96))])
-            cp(S("AH", 384 * h, 384 * h + 384), bank(bk[2], 0, 384))
-        for c in range(0, 192, ch):
-            cp(S("XT", 16 * c, 16 * (c + ch)), A("LF", 0, NL), A(kl[0], kl[1] + c, kl[1] + c + ch))
-        for h in range(2):
-            for w in range(4):
-                mm(bank(bk[h], 96 * w, 96 * w + 96),
-                   [(K("H0_%d" % i if i else "H"), S("XT", 1536 * h + 4 * w + i, 1536 * h + 1536, 16)) for i in range(4)])
-            tt(S("DM", 384 * h, 384 * h + 384), bank(bk[h], 0, 384), S("AH", 384 * h, 384 * h + 384), ALU.subtract)
-            tt(S("DP", 384 * h, 384 * h + 384), bank(bk[h], 0, 384), S("AH", 384 * h, 384 * h + 384), ALU.add)
-        wt = ("I", "I22", "I44", "I66")
-        for h in range(2):
-            for y, nm in enumerate(("DM", "DP")):
-                c0 = 192 * y + 96 * h
-                mm(bank(bk[3], c0, c0 + 96), [(K(wt[w]), S(nm, 384 * h + 96 * w, 384 * h + 96 * w + 96)) for w in range(4)])
-
-    def ahead(t):
-        unpack(t)
-        for hb in range(2):
-            c0 = 160 * t + 32 + 12 * hb
-            batch(t, 1, (5, 6, 6, 5), A("KU", 384 * t + 192 * hb, 384 * t + 192 * hb + 192),
-                  [A("ALU", c0 + 32 * a, c0 + 32 * a + 12) for a in range(4)], A("RESF", 192 * hb, 192 * hb + 192), CH2)
-        if t < NT - 1:
-            tt(A("ROF", 384 * t, 384 * t + 384), A("RESF", 0, 384), A("P", 400 * t, 400 * t + 384), ALU.mult)
-            mm(bank(5, 384, 408), [(KHm("CROW2", l), A("ROF", 384 * t + l, 384 * t + 384, 16)) for l in range(16)])
-            cp(A("NOK", 24 * t, 24 * t + 24), bank(5, 384, 408))
-
-    for t in CORDER:
         tag[0] = "C%d" % t
-        claims(t)
-    for t in AHEAD:
-        tag[0] = "H%d" % t
-        ahead(t)
-    for t in range(NT):
+        x, sb = t % NXC, t % 2
+        if t < 2:
+            lo, hi = (0, 24) if t == 0 else (24, 120)
+            cp(A("LBU", lo, hi), A("LBI", lo, hi))
+        cp(A("WU", L * t, L * t + L), A("BK", 0, NB), A("LBU", 24 * t, 24 * t + 24))
+        spread("XC", x, A("NTB", 0, NV), "WU", L * t)
+        ts(A("LT", L * t, L * t + L), A("AP", 6 * L * t, 6 * L * t + L), MAGIC, MAGIC, ALU.add, ALU.subtract)
+        for i in range(3):
+            b = (3 * t + i) % 2
+            x0 = 16 * (L * x + 128 * i)
+
+            def lane(w):
+                return (bank(b, 128 * w, 128 * w + 128), A("LT", L * t + 128 * i, L * t + 128 * i + 128), A("WR", 256 * w + rot(t), 256 * w + rot(t) + 128))
+            mg([lane(0), lane(1)] + [(bank(b, 15 - k, 256, 16), A("XC", x0 + k, x0 + 2048, 16), A("W24", 0, 16)) for k in range(16)])
+            nonzero(A("NE", 256 * b, 256 * b + 256), bank(b, 0, 256))
+            mg([lane(2)] + [(bank(b, 256 + 15 - k, 384, 16), A("XC", x0 + k, x0 + 2048, 16), A("W24", 16, 24)) for k in range(16)] +
+               [(bank(b, 256, 384), IDm("I32"), A("NE", 256 * b + 128 * w, 256 * b + 128 * w + 128)) for w in range(2)])
+            least(A("SC", 512 * sb + 128 * i, 512 * sb + 128 * i + 128), A("RS", 0, 128), bank(b, 256, 384))
+        to_list(sb, 24, 16.0, 2.0 ** 19, 2047, A("WL", 24 * t, 24 * t + 24))
+        out = A("R1", 32 * (t - 1), 32 * t) if t else A("V1", 96, 128)
+        ts(out, A("SC", 512 * sb, 512 * sb + 512), 16.0, 16.0, ALU.min, ALU.subtract, off=A("RL", 2 * t, 2 * t + 2))
+        if t:
+            home(t, A("R1", 32 * (t - 1), 32 * (t - 1) + 24), A("V1", 24 * (t - 1), 24 * t), "a_v1%d" % t)
+
+    def tests(t, n):
         tag[0] = "T%d" % t
-        tests(t)
-    dma("Y", lambda e: [e.dma_start(T.y[:, 128 * i:128 * i + 128], T.ACC[40 * i:40 * i + 40, :]) for i in range(3)], [A("ACC", 0, 128)], [], 61440, n=3)
+        x, a0, d0 = t % NXT, 6 * L * t, 768 * (t % 2)
+        cp(A("KL", L * (t % 2), L * (t % 2) + L), A("KP", 0, NV), A("WL", 24 * t, 24 * t + 24))
+        spread("XT", x, A("LF", 0, NL), "KL", L * (t % 2))
+        for c in range(0, L, n):
+            def kid(d):
+                return (HBm(d), A("XT", 16 * (L * x + c) + d, 16 * (L * x + c + n), 16))
+            for y in range(2):
+                prs = []
+                for i in range(5, 0, -1):
+                    prs.append((HAm(i, 1 - y, t), A("AP", a0 + L * i + c, a0 + L * i + c + n)))
+                    prs += [kid(ASC[i] + j) for j in (2, 1, 0)]
+                prs += [(HAm(0, 1 - y, t), A("AP", a0 + c, a0 + c + n)), (HAm(0, y, t), A("LT", L * t + c, L * t + c + n)), kid(0)]
+                if n == L:
+                    mm(bank(2 + y, 0, L), prs)
+                    nonzero(A("BD", d0 + L * y, d0 + L * y + L), bank(2 + y, 0, L))
+                else:
+                    mm(bank(2 + c // n % 2, n * y, n * y + n), prs)
+            if n < L:
+                nonzero(A("BD", d0 + 2 * c, d0 + 2 * c + 2 * n), bank(2 + c // n % 2, 0, 2 * n))
+        for i in range(3):
+            c0, c1 = (d0 + 128 * i, d0 + L + 128 * i) if n == L else (d0 + 256 * i, d0 + 256 * i + 128)
+            b = bank(4 + (3 * t + i) % 2, 0, 256)
+            mm(b, [(A("BD", c0, c0 + 128), A("FD", 0, 256)), (A("BD", c1, c1 + 128), A("FS", 0, 256))])
+            least(A("SD", d0 + 256 * i, d0 + 256 * i + 256), A("RT", 0, 256), b)
+        out = A("R2", 32 * (t - 1), 32 * t) if t else A("V2", 96, 128)
+        ts(out, A("SD", d0, d0 + 768), 32.0, None, ALU.min, off=A("RL", 10 + 2 * t, 12 + 2 * t))
+        if t:
+            home(t, A("R2", 32 * (t - 1), 32 * (t - 1) + 24), A("V2", 24 * (t - 1), 24 * t), "a_v2%d" % t)
+
+    def v(name, t):
+        return A(name, 24 * slot(t), 24 * slot(t) + 24)
+
+    def tested(t):
+        tag[0] = "L%d" % t
+        if t:
+            mm(bank(6, 64, 88), [(IDm("N32"), A("MG", 32 * s, 32 * s + 24)) for s in range(t)])
+            tt(A("CD", 0, 24), v("V1", t), bank(6, 64, 88), ALU.is_lt)
+        else:
+            ts(A("CD", 0, 24), v("V1", t), 0.0, None, ALU.is_lt)
+        mg([(bank(6, 96, 120), A("TRI", 0, 128), A("CD", 0, 24)), (bank(6, 104, 120), A("ONE", 0, 128), A("CD", 0, 16)),
+            (bank(6, 112, 120), A("ONE", 0, 128), A("CD", 0, 8))])
+        ts(v("UU", t), bank(6, 96, 120), CAP - 1024.0, 32.0, ALU.is_lt, ALU.mult)
+
+    def merged(t):
+        tag[0] = "M%d" % t
+        tt(A("MG", 32 * t, 32 * t + 24), v("V2", t), v("UU", t), ALU.is_lt)
+
+    def fields():
+        tag[0] = "F"
+        ts(A("VI", 0, 120), A("V1", 0, 120), 16.0, 2.0 ** 19, ALU.add, ALU.mult)
+        ts(A("FF", 1, 600, 5), A("VI", 0, 120), 2047, None, ALU.bitwise_and)
+        for b in range(4):
+            ts(A("VB", 120 * b, 120 * b + 120), A("VI", 0, 120), 11 + b, 1 << b, ALU.logical_shift_right, ALU.bitwise_and)
+        tt(A("VC", 0, 240), A("VB", 0, 240), A("VB", 240, 480), ALU.add)
+        tt(A("FF", 2, 600, 5), A("VC", 0, 120), A("VC", 120, 240), ALU.add)
+
+    def store(t):
+        tag[0] = "O%d" % t
+        f0 = 120 * slot(t)
+        ts(A("FF", f0 + 3, f0 + 120, 5), v("V2", t), 1, None, ALU.logical_shift_right)
+        ts(A("SB", 0, 24), v("V2", t), 1, None, ALU.bitwise_and)
+        ts(A("FF", f0 + 4, f0 + 120, 5), A("SB", 0, 24), -2.0, 1.0, ALU.mult, ALU.add)
+        tt(A("FP", 128 * t, 128 * t + 128), A("MG", 32 * t, 32 * t + 32), A("FF", f0, f0 + 128), ALU.mult, off=A("L5", 0, 8))
+        mg([(bank(7, 128 * i, 128 * i + 128, 1, 40), A("FP", 128 * t + 40 * i, 128 * t + 40 * i + 40), IDm("I32")) for i in range(3)],
+           start=False, stop=t == NT - 1)
+
+    claims(0)
+    claims(1)
+    tests(0, L)
+    claims(2)
+    tested(0)
+    tests(1, L)
+    merged(0)
+    claims(3)
+    tested(1)
+    tests(2, L)
+    claims(4)
+    merged(1)
+    tested(2)
+    tests(3, L)
+    fields()
+    merged(2)
+    tested(3)
+    for t in range(3):
+        store(t)
+    tests(4, 128)
+    merged(3)
+    tested(4)
+    store(3)
+    merged(4)
+    store(4)
+    ts(A("YS", 0, L, 1, 0, 40), bank(7, 0, L, 1, 40), 1.0 / 32, None, ALU.mult)
+    dma(lambda e: [e.dma_start(T.y[:], T.YS[0:40, :])], [A("YS", 0, L)], [], 61440)
     return ops
 
 
@@ -644,7 +516,7 @@ def depend(ops):
                     d.add(j)
         for a, wr in acc:
             h = hist.setdefault(a[0], [])
-            if wr and a[3] == 1:
+            if wr and a[3] == 1 and a[4:] in ((), (0, 128)):
                 h[:] = [x for x in h if not (a[1] <= x[0][1] and x[0][2] <= a[2])]
             h.append((a, wr, i))
         d.discard(i)
@@ -652,23 +524,21 @@ def depend(ops):
     return deps
 
 
-def schedule(ops, deps, rounds=None):
+def schedule(ops, deps):
     n = len(ops)
     succ = [[] for _ in range(n)]
     for i in range(n):
         for j in deps[i]:
             succ[j].append(i)
-    alts, lag, bias = [], [], [VBIAS] * n
-    rounds = ROUNDS if rounds is None else rounds
+    alts, lag = [], []
     for o in ops:
         e, _, c = o["alts"][0]
         if e == "X":
-            big = o["link"] > 70000
-            alts.append([("L" if big else None, o["link"] / 5e4)])
+            alts.append([("L", o["link"] / LINK)])
             lag.append(c)
         elif "dma" in o:
-            alts.append([(e, 0.1 + o["bytes"] / 2.5e5 if e == "Y" else c)])
-            lag.append(2.0 if e == "Y" else 2.5 + o["bytes"] / 1e5)
+            alts.append([(e, 0.1 + o["bytes"] / 2.5e5)])
+            lag.append(2.0)
         else:
             alts.append([(a[0], a[2]) for a in o["alts"]])
             lag.append(LAT)
@@ -680,96 +550,33 @@ def schedule(ops, deps, rounds=None):
             r = max([fin[j] + (0.0 if alts[i][0][0] == alts[j][0][0] == "P" else lag[i] if back else lag[j]) for j in pre[i]] + [0.0])
             best = None
             for k, (e, c) in enumerate(alts[i]):
-                t, at = r, 0
-                if e:
-                    at = len(busy[e])
-                    for x, (a, b) in enumerate(busy[e]):
-                        if b <= t:
-                            continue
-                        if a >= t + c:
-                            at = x
-                            break
-                        t = b
-                key = t + c + (bias[i] * c if e == "V" and len(alts[i]) > 1 else 0.0)
+                t, at = r, len(busy[e])
+                for x, (a, b) in enumerate(busy[e]):
+                    if b <= t:
+                        continue
+                    if a >= t + c:
+                        at = x
+                        break
+                    t = b
+                key = t + c + (VBIAS * c if e == "V" and len(alts[i]) > 1 else 0.0)
                 if best is None or key < best[0]:
                     best = (key, t, k, at)
             _, t, k, at = best
             e, c = alts[i][k]
             st[i], fin[i], ch[i] = t, t + c, k
-            if e:
-                busy[e].insert(at, (t, t + c))
+            busy[e].insert(at, (t, t + c))
         return st, fin, ch
     prio = [0.0] * n
     for i in range(n - 1, -1, -1):
         prio[i] = min(a[1] for a in alts[i]) + lag[i] + max([prio[j] for j in succ[i]] + [0.0])
-
-    def replay(order, ch, kg, kp, wait, hop):
-        free = {e: 0.0 for e in "VSPGYL"}
-        fin = [0.0] * n
-        for i in order:
-            e, c = alts[i][ch[i]]
-            t = free[e] if e else 0.0
-            for j in deps[i]:
-                x = fin[j] + (0.0 if e == "P" == alts[j][0][0] else wait if lag[j] == LAT else lag[j] * hop)
-                if x > t:
-                    t = x
-            fin[i] = t + c * (kp if e == "P" else kg if gath[i] else 1.0)
-            if e:
-                free[e] = fin[i]
-        return max(fin)
-
-    def value(pr, turns=0):
-        p = list(pr)
-        for i in range(n - 1, -1, -1):
-            for j in succ[i]:
-                if p[j] + 0.001 > p[i]:
-                    p[i] = p[j] + 0.001
-        st, fin, ch = place(sorted(range(n), key=lambda i: (-p[i], i)), deps, False)
-        for _r in range(turns):
-            fb = place(sorted(range(n), key=lambda i: (-fin[i] - lag[i], -i)), succ, True)[1]
-            pr[:] = fb
-            st, fin, ch = place(sorted(range(n), key=lambda i: (-fb[i], i)), deps, False)
-        order = sorted(range(n), key=lambda i: (st[i], i))
-        v = [max(fin)] + [replay(order, ch, *m) for m in MODELS]
-        return sum(v) / len(v), order, fin, ch, v
-    gath = [bool(o.get("g")) for o in ops]
-    groups = {}
-    for i, o in enumerate(ops):
-        prio[i] += OFFS.get(o["tag"], 0.0)
-        groups.setdefault(o["tag"], []).append(i)
-        groups.setdefault((o["tag"], o["w"][0][0] if o["w"] else ""), []).append(i)
-    groups = list(groups.values())
-    flex = [i for i in range(n) if len(alts[i]) > 1]
-    rng = np.random.default_rng(SEED)
-    best = value(prio, 3)
-    now = best[0]
-    for _ in range(rounds):
-        p, old = list(prio), list(bias)
-        u = rng.random()
-        if u < 0.1:
-            d = float(rng.choice([-0.5, 0.0, 0.5, 1.0, 3.0, 10.0]))
-            for i in groups[int(rng.integers(0, len(groups)))]:
-                bias[i] = d
-        elif u < 0.2:
-            for i in rng.integers(0, n, 3):
-                p[i] += float(rng.normal()) * 3.0
-        elif u < 0.4:
-            for i in rng.choice(flex, int(rng.integers(1, 6))):
-                bias[i] = float(rng.choice([-0.5, 0.0, 0.5, 1.0, 3.0]))
-        else:
-            for _k in range(int(rng.integers(1, 3))):
-                d = float(rng.normal()) * float(rng.choice([1.0, 4.0, 12.0]))
-                for i in groups[int(rng.integers(0, len(groups)))]:
-                    p[i] += d
-        v = value(p, int(rng.random() < TURN))
-        if v[0] <= now + HEAT * (1.0 - _ / rounds) * float(rng.exponential()):
-            now, prio = v[0], p
-            if now < best[0]:
-                best = v
-        else:
-            bias[:] = old
-    PLAN["v"] = best[4]
-    return [(i, best[3][i]) for i in best[1]], best[2]
+    best = None
+    for _r in range(TURNS + 1):
+        st, fin, ch = place(sorted(range(n), key=lambda i: (-prio[i], i)), deps, False)
+        if best is None or max(fin) < max(best[1]):
+            best = (st, fin, ch)
+        prio = place(sorted(range(n), key=lambda i: (-fin[i] - lag[i], -i)), succ, True)[1]
+    st, fin, ch = best
+    return [(i, ch[i]) for i in sorted(range(n), key=lambda i: (st[i], i))], fin
 
 
 def rank_program(g, core, T, topo):

@@ -7,7 +7,7 @@ SH = [t * (t + 1) // 2 % 8 for t in range(NT)]
 F, B, I32, U, HF = "float32", "bfloat16", "int32", "uint16", "float16"
 MAGIC = 1.5 * 2.0 ** 27
 ASC = (0, 1, 4, 7, 10, 13)
-NXC, NXT = 3, 2
+NXC, NXT = 3, 3
 
 
 def _sb(n, d):
@@ -18,15 +18,15 @@ SCRATCH = {
     "LF": _sb(NL, B), "IV": _sb(NV, B), "KDI": _sb(NV, I32), "KDF": _sb(NV, F), "KS": _sb(NV, F), "KP": _sb(NV, F), "BK": _sb(NB, I32),
     "LVI": _sb(24, I32), "LBI": _sb(120, I32), "LVU": _sb(24, U), "LBU": _sb(120, U),
     "XB": _sb(320, F), "TB": _sb(320, F), "PT": _sb(112, B), "OI": _sb(8, I32), "OU": _sb(8, U), "CC": _sb(16, F), "PK8": _sb(8, B),
-    "HA": _sb(12 * 256, B), "HB": _sb(16 * 128, B), "HFL": _sb(128, F), "KK": _sb(128, B), "PKM": _sb(128, B), "PSM": _sb(128, B),
-    "DW": _sb(768, B), "IOT": _sb(256, B), "RS": _sb(512, B), "RT": _sb(256, B), "MK": _sb(256, B), "SS": _sb(240, B),
-    "EI": _sb(16, F), "EL": _sb(16, U), "WR": _sb(768, B), "W24": _sb(24, B), "ONE": _sb(128, B), "TRI": _sb(128, B),
+    "HA": _sb(12 * 256, B), "HB": _sb(8 * 128, B), "PM": _sb(272, F), "KG": _sb(2 * L, F), "XA": _sb(16 * L, B), "HFL": _sb(128, F), "KK": _sb(128, B), "PKM": _sb(128, B), "PSM": _sb(128, B),
+    "DW": _sb(768, B), "IOT": _sb(256, B), "DH": _sb(48, B), "RS": _sb(512, B), "RT": _sb(256, B), "MK": _sb(256, B), "SS": _sb(240, B),
+    "EI": _sb(16, F), "EL": _sb(16, U), "WR": _sb(816, B), "PW": _sb(160, B), "WI": _sb(28, F), "WO": _sb(10, U), "W24": _sb(24, B), "ONE": _sb(128, B), "TRI": _sb(128, B),
     "ID": _sb(5 * 128, B), "FD": _sb(256, B), "FS": _sb(256, B), "CF": _sb(40, B),
     "RI": _sb(10, I32), "RF": _sb(20, F), "RL": _sb(20, U), "L5F": _sb(8, F), "L5I": _sb(8, I32), "L5": _sb(8, U),
     "TAU": _sb(NV, B), "SC": _sb(1024, F), "E": _sb(512, HF), "LI": _sb(128, I32), "MU": _sb(96, U), "SG": _sb(NV, B), "SI": _sb(NV, B), "NTB": _sb(NV, B),
     "KA": _sb(L, U), "NA": _sb(L, B), "AP": _sb(NT * 6 * L, HF), "LT": _sb(NT * L, B),
-    "WU": _sb(NT * L, U), "XC": _sb(NXC * 16 * L, B), "NE": _sb(512, B), "WL": _sb(120, U), "KL": _sb(2 * L, U),
-    "XT": _sb(NXT * 16 * L, B), "BD": _sb(2 * 768, B), "SD": _sb(2 * 768, F),
+    "WU": _sb(NT * L, U), "XC": _sb(NXC * 16 * L, B), "NE": _sb(544, B), "WL": _sb(120, U), "KL": _sb(2 * L, U),
+    "XT": _sb(NXT * 8 * L, B), "BD": _sb(2 * 768, B), "SD": _sb(2 * 768, F),
     "R1": _sb(128, F), "R2": _sb(128, I32), "V1": _sb(128, F), "V2": _sb(128, I32), "VI": _sb(120, I32), "VB": _sb(480, I32), "VC": _sb(240, I32),
     "FF": _sb(608, I32), "CD": _sb(24, B), "UU": _sb(120, F), "MG": _sb(160, B), "SB": _sb(24, I32), "FP": _sb(640, HF), "YS": _sb(L, F),
     "DLB": ("dram", [240, 24], I32),
@@ -39,9 +39,16 @@ SEMAPHORES = ["sV", "sS", "sP", "sG", "sent"] + DMA_SEMS + ARR_SEMS
 
 CY, PCY, GF_, LAT = 0.87e-3, 0.44e-3, 1.56, 0.12
 LINK = 7e4
-VBIAS = 1.0
 GCH = 64
-TURNS = 3
+PARTS = "C0 A C1 T0 C2 T1 C3 T2 C4 T3 T4".split()
+ONV = {"A": (1, 3), "C0": (1, 3), "C1": (1,), "C2": (1, 4), "C3": (1,), "C4": (1,)}
+RANK = "L0 M0 L1 M1 L2 M2 F L3 M3 L4 M4 O0 O1 O2 O3 O4".split() + PARTS
+PACE, SOON, LATE, SLACK = 6.0, 1.5, 3.0, 0.5
+AHEAD, OWN = 0.0, 2.0
+ROUNDS, SEED, HEAT = 24000, 1, 0.2
+MODELS = ((1.0, 1.0, 1.0, LAT, 1.0), (1.3, 1.1, 1.3, 0.25, 1.4))
+EDF = False
+EARLY = -9.0
 PLAN = {}
 
 
@@ -57,6 +64,7 @@ def build(g, T, topo, core, rank):
     ops = []
     nd = [0]
     tag = ["K"]
+    onv = [False]
 
     def ap(a):
         return T[a[0]][a[4]:a[5], a[1]:a[2]:a[3]] if a[3] != 1 else T[a[0]][a[4]:a[5], a[1]:a[2]]
@@ -65,6 +73,8 @@ def build(g, T, topo, core, rank):
         return all(SCRATCH[a[0]][2] in (B, HF, U) for a in aps)
 
     def add(alts, reads, writes, **kw):
+        if tag[0] not in ("K", "K2") and len(alts) > 1:
+            kw["first"] = 0 if onv[0] else 1
         o = {"alts": alts, "r": [a for a in reads if isinstance(a, tuple)], "w": list(writes), "tag": tag[0]}
         o.update(kw)
         ops.append(o)
@@ -120,6 +130,9 @@ def build(g, T, topo, core, rank):
 
     def least(out, step, d1):
         return add([("V", lambda e: [e.tensor_tensor_scan(ap(out), ap(step), ap(d1), 0.0, ALU.add, ALU.min)], cost(out, d1, None))], [step, d1], [out])
+
+    def lastfit(out, miss, d1):
+        return add([("V", lambda e: [e.tensor_tensor_scan(ap(out), ap(miss), ap(d1), 0.0, ALU.min, ALU.max)], cost(out, d1, None))], [miss, d1], [out])
 
     def turn(out, i):
         return add([("V", lambda e: [e.transpose(ap(out), ap(i))], cost(out, i, None))], [i], [out])
@@ -226,18 +239,18 @@ def build(g, T, topo, core, rank):
         ts(cc(b), col(b), m, a, ALU.mult, ALU.add)
     ts(cc(4), cc(0), cc(1), cc(2), ALU.mult, ALU.mult)
     ts(A("KK", 0, 128), Hb, cc(4), cc(3), ALU.mult, ALU.mult)
-    fill(A("RS", 0, 512), 1)
-    fill(A("RS", 0, 512, 16), 1 << 23)
-    iota(A("MK", 0, 256), [[0, 256]], 1)
+    ms(A("RS", 0, 512), 1.0)
+    ms(A("RS", 0, 512, 16), 2.0 ** 23)
+    ms(A("MK", 0, 256), 1.0)
     select(A("MK", 0, 256), A("MK", 0, 256), [[0, 32], [-16, 8]], ALU.is_ge, 0.0, 0, 1)
     select(A("MK", 0, 256), A("MK", 0, 256), [[0, 32], [16, 8]], ALU.is_ge, 0.0, 15, -1)
     iota(A("EI", 0, 16), [[1, 8], [16, 2]])
     ts(cc(9), col(3), -4.0, 4.0, ALU.mult, ALU.add)
     ts(A("EL", 0, 16), A("EI", 0, 16), cc(9), None, ALU.add)
     iota(A("XB", 128, 160), [[0, 2], [1, 16]])
-    fill(A("XB", 160, 320), 0)
+    ms(A("XB", 160, 320), 0.0)
     for b, rows in ((8, ((0, 680), (1, -8), (2, -32), (4, -128), (8, -512))), (5, [(r, 64 ** r) for r in range(4)]),
-                    (6, [(4 + r, 64 ** r) for r in range(4)]), (7, ((8, 256), (9, 1), (10, 2048))), (9, ((10, 1),))):
+                    (6, [(4 + r, 64 ** r) for r in range(4)]), (7, ((8, 256), (9, 1), (10, 2048))), (9, ((10, 1), (11, 1)))):
         for r, v in rows:
             fill(A("XB", 32 * b + r, 32 * b + 32, 16), v)
     for h in (0, 16):
@@ -251,14 +264,14 @@ def build(g, T, topo, core, rank):
     tt(A("PT", 48, 56), A("PT", 16, 32, 2), A("PK8", 0, 8), ALU.add)
     cp(A("PKM", 0, 128), A("PT", 32, 80), A("OU", 0, 8))
     cp(A("PT", 90, 91), col(8))
+    ts(A("PT", 91, 92), col(4), 0.0, 16.0, ALU.is_equal, ALU.mult)
     cp(A("PSM", 0, 128), A("PT", 64, 112), A("OU", 0, 8))
     iota(A("IOT", 0, 256), [[1, 256]])
-    select(A("IOT", 0, 256), A("IOT", 0, 256), [[0, 256]], ALU.is_gt, 1.0, 0, 1)
+    ms(A("IOT", 0, 256, 1, 0, 1), 1.0)
     ms(A("DW", 0, 768), 0.0)
-    iota(A("DW", 8, 768, 16), [[16, 6], [0, 8]])
-    fill(A("DW", 9, 768, 16), 16)
-    for r in range(2):
-        select(A("DW", 8 + r, 768, 16), A("DW", 8 + r, 768, 16), [[0, 48]], ALU.is_equal, 0.0, -r, 1)
+    iota(A("DH", 0, 48), [[16, 6], [0, 8]])
+    cp(A("DW", 8, 768, 16, 0, 1), A("DH", 0, 48, 1, 0, 1))
+    ms(A("DW", 9, 768, 16, 64, 65), 16.0)
     tag[0] = "K2"
     turn(A("TB", 160, 256), A("XB", 160, 256))
     turn(A("TB", 288, 320), A("XB", 288, 320))
@@ -279,29 +292,43 @@ def build(g, T, topo, core, rank):
     ts(A("HA", 1024, 1536), A("HA", 512, 1024), 16.0 ** 3, None, ALU.mult)
     ts(A("HA", 1536, 2560), A("HA", 512, 1536), 16.0 ** 6, None, ALU.mult)
     ts(A("HA", 2560, 3072), A("HA", 512, 1024), 16.0 ** 12, None, ALU.mult)
-    ts(A("HB", 128, 256), Hb, 16.0, None, ALU.mult)
-    ts(A("HB", 256, 384), Hb, 256.0, None, ALU.mult)
-    ts(A("HB", 384, 640), A("HB", 128, 384), 256.0, None, ALU.mult)
-    ts(A("HB", 640, 1152), A("HB", 128, 640), 16.0 ** 4, None, ALU.mult)
-    ts(A("HB", 1152, 2048), A("HB", 128, 1024), 16.0 ** 8, None, ALU.mult)
-    ts(cc(6), col(7), 2.0 ** -23, None, ALU.mult)
+    ts(A("HB", 128, 256), Hb, 256.0, None, ALU.mult)
+    ts(A("HB", 256, 384), Hb, 256.0 ** 2, None, ALU.mult)
+    ts(A("HB", 384, 640), A("HB", 128, 384), 256.0 ** 2, None, ALU.mult)
+    ts(A("HB", 640, 1024), A("HB", 128, 512), 256.0 ** 4, None, ALU.mult)
+    fill(A("PM", 0, 272), 0)
+    for y in range(2):
+        select(A("PM", 136 * y + 8, 136 * y + 136), A("ONE", 0, 128), [[-16, 8], [1024, 2], [-2, 8]], ALU.is_equal, 0.0, y - 1, 1)
+    ts(cc(6), col(7), 2.0 ** -27, None, ALU.mult)
+    ts(cc(10), col(4), 11.0, 1.0 / 256, ALU.is_equal, ALU.mult)
+    fill(A("PW", 0, 160), 0)
+    iota(A("WI", 0, 17), [[-1, 17]], 16)
+    iota(A("WI", 18, 27), [[16, 9]], 16, 1)
+    iota(A("WI", 27, 28), [[0, 1]], 0, 1)
+    ts(cc(11), A("WI", 27, 28), col(4), -33.0 / 16, ALU.subtract, ALU.mult)
+    ts(A("WO", 0, 9), A("WI", 18, 27), cc(11), 33.0, ALU.add, ALU.min)
     for w, c in enumerate((col(5), col(6), cc(6))):
-        ts(A("WR", 256 * w, 256 * w + 256), A("HA", 0, 256), 0.0, c, ALU.not_equal, ALU.mult)
-        cp(A("W24", 8 * w, 8 * w + 8), A("WR", 256 * w, 256 * w + 128, 16))
+        if w < 2:
+            ts(A("PW", 48 * w + 17, 48 * w + 33), A("ONE", 0, 16), c, None, ALU.mult)
+        else:
+            ts(A("PW", 113, 129), A("WI", 1, 17), cc(10), c, ALU.mult, ALU.add)
+            ts(A("PW", 112, 113), cc(10), 16.0, None, ALU.mult)
+        cp(A("WR", 272 * w, 272 * w + 144), A("PW", 48 * w, 48 * w + 48), A("WO", 0, 9))
+        cp(A("WR", 272 * w + 136, 272 * w + 272), A("WR", 272 * w, 272 * w + 136))
+        ts(A("W24", 8 * w, 8 * w + 8), A("HA", 0, 128, 16), c, None, ALU.mult)
     ts(cc(7), A("PT", 31, 32), 64.0, None, ALU.mult)
     ts(cc(8), A("PT", 31, 32), -64.0, None, ALU.mult)
     for nm, par, c in (("FD", 1, 7), ("FD", 0, 8), ("FS", 1, 8), ("FS", 0, 7)):
         out = A(nm, par, 256, 2)
         ts(out, Hb, cc(c), 0.0, ALU.mult, ALU.max, s=act(out, Hb, ACT.Relu, 0.0, cc(c)))
-    ts(cc(5), col(3), -64.0, 79.0, ALU.mult, ALU.add)
     for t in range(NT):
         iota(A("RI", 2 * t, 2 * t + 2), [[0, 2]], SH[t], 1)
-    iota(A("RF", 10, 20), [[0, 5], [256, 2]])
+    iota(A("RF", 10, 20), [[0, 5], [16, 2]])
     ts(A("RI", 0, 10), A("RI", 0, 10), 7, None, ALU.bitwise_and)
-    ts(A("RF", 0, 10), A("RI", 0, 10), 16.0, cc(5), ALU.mult, ALU.add)
-    tt(A("RF", 0, 10), A("RF", 0, 10), A("RF", 10, 20), ALU.add)
-    ts(A("RL", 0, 10), A("RF", 0, 10), 383.0, None, ALU.min)
-    ts(A("RL", 10, 20), A("RL", 0, 10), 2.0, 1.0, ALU.mult, ALU.add)
+    tt(A("RF", 0, 10), A("RI", 0, 10), A("RF", 10, 20), ALU.add)
+    ts(A("RF", 10, 20), A("RF", 0, 10), cc(9), 23.0, ALU.add, ALU.min)
+    ts(A("RL", 0, 10), A("RF", 10, 20), 17.0, 16.0, ALU.mult, ALU.add)
+    ts(A("RL", 10, 20), A("RF", 10, 20), 32.0, 31.0, ALU.mult, ALU.add)
     iota(A("L5F", 0, 8), [[16, 8]], -2)
     ts(A("L5F", 0, 8), A("L5F", 0, 8), col(4), 0.2, ALU.add, ALU.mult)
     cp(A("L5I", 0, 8), A("L5F", 0, 8))
@@ -311,49 +338,51 @@ def build(g, T, topo, core, rank):
     for t in range(NT):
         fill(A("FF", 120 * slot(t), 120 * slot(t) + 120, 5), (rank + t) % NR + 1)
 
-    def to_list(sb, ncol, top, scale, bits, out):
+    def to_list(sb, ncol, run, scale, bits, out):
         e0, l0 = 256 * sb, 64 * sb
-        ts(A("LI", l0, l0 + ncol), A("SC", 512 * sb + 15, 512 * sb + 16 * ncol, 16), top, scale, ALU.min, ALU.mult)
+        ts(A("LI", l0, l0 + ncol), A("SC", 512 * sb + run - 1, 512 * sb + run * ncol, run), scale, None, ALU.mult)
         ts(A("LI", l0 + 32, l0 + 32 + ncol), A("LI", l0, l0 + ncol), bits, None, ALU.bitwise_and)
         tt(A("E", e0, e0 + 256), A("LI", l0 + 32, l0 + 64), A("MK", 0, 256), ALU.mult, off=A("EL", 0, 16))
-        mm(bank(6, 0, ncol), [(A("SS", 112 - 16 * q, 240 - 16 * q), A("E", e0 + 32 * q, e0 + 32 * q + ncol)) for q in range(8)])
-        cp(out, bank(6, 0, ncol))
+        b = bank(6, 32 * sb, 32 * sb + ncol)
+        mm(b, [(A("SS", 112 - 16 * q, 240 - 16 * q), A("E", e0 + 32 * q, e0 + 32 * q + ncol)) for q in range(8)])
+        cp(out, b)
 
     tag[0] = "N"
-    cp(A("KDF", 0, NV), A("KDI", 0, NV))
     for c in range(3):
         lo, hi = 512 * c, 512 * c + 512
-        mm(bank(c % 2, 0, 512), [(Hb, A("IV", lo, hi))])
-        ts(A("TAU", lo, hi), bank(c % 2, 0, 512), 1.0, -1.0, ALU.min, ALU.max, s=act(A("TAU", lo, hi), bank(c % 2, 0, 512), ACT.Sign))
-        mg([(bank(2 + c % 2, 128 * i, 128 * i + 128), A("TAU", lo + 128 * i, lo + 128 * i + 128), A("KK", 0, 128)) for i in range(4)])
-        least(A("SC", 512 * (c % 2), 512 * (c % 2) + 512), A("RS", 0, 512), bank(2 + c % 2, 0, 512))
-        to_list(c % 2, 32, 2.0 ** 22, 1.0, 15, A("MU", 32 * c, 32 * c + 32))
+        select(A("KDF", lo, hi), A("KDI", lo, hi), [[0, 512]], ALU.is_ge, 0.0, 0, 0)
+        mm(bank(c, 0, 512), [(Hb, A("IV", lo, hi))])
+        ts(A("TAU", lo, hi), bank(c, 0, 512), 1.0, -1.0, ALU.min, ALU.max, s=act(A("TAU", lo, hi), bank(c, 0, 512), ACT.Sign))
+        mg([(bank(7, 128 * i, 128 * i + 128), A("TAU", lo + 128 * i, lo + 128 * i + 128), A("KK", 0, 128)) for i in range(4)])
+        least(A("SC", 512 * (c % 2), 512 * (c % 2) + 512), A("RS", 0, 512), bank(7, 0, 512))
+        to_list(c % 2, 32, 16, 1.0, 15, A("MU", 32 * c, 32 * c + 32))
         cp(A("SG", lo, hi), HP, A("MU", 32 * c, 32 * c + 32))
+        mm(bank(3 + c, 0, 512), [(A("HFL", 0, 128), A("KDF", lo, hi))])
     for c in range(3):
         lo, hi = 512 * c, 512 * c + 512
-        mm(bank(4 + c % 2, 0, 512), [(A("HFL", 0, 128), A("KDF", lo, hi))])
-        tt(A("KS", lo, hi), bank(4 + c % 2, 0, 512), A("SG", lo, hi), ALU.mult)
-        mm(bank(7, 0, 512), [(A("HFL", 0, 128), A("KS", lo, hi))])
-        ts(A("KP", lo, hi), bank(7, 0, 512), 1.0 / 16, None, ALU.mult)
-        mm(bank(c % 2, 0, 512), [(Hb, A("IV", lo, hi))])
-        tt(A("SI", lo, hi), bank(c % 2, 0, 512), A("SG", lo, hi), ALU.mult)
-        b = 2 + c % 2
-        mg([(bank(b, 0, 512), A("PKM", 0, 128), A("SI", lo, hi)), (bank(b, 0, 512), A("PSM", 0, 128), A("SG", lo, hi))] +
-           [(bank(b, 256 * h, 256 * h + 256), A("DW", 128 * (2 * c + h), 128 * (2 * c + h) + 128), A("IOT", 0, 256)) for h in range(2)])
-        cp(A("NTB", lo, hi), bank(b, 0, 512))
+        tt(A("SI", lo, hi), bank(c, 0, 512), A("SG", lo, hi), ALU.mult)
+        mg([(bank(c, 0, 512), A("PSM", 0, 128), A("SG", lo, hi))] +
+           [(bank(c, 256 * h, 256 * h + 256), A("DW", 128 * (2 * c + h), 128 * (2 * c + h) + 128), A("IOT", 0, 256)) for h in range(2)] +
+           [(bank(c, 0, 512), A("PKM", 0, 128), A("SI", lo, hi))])
+        cp(A("NTB", lo, hi), bank(c, 0, 512))
+        tt(A("KS", lo, hi), bank(3 + c, 0, 512), A("SG", lo, hi), ALU.mult)
+        mm(bank(3 + c, 0, 512), [(A("HFL", 0, 128), A("KS", lo, hi))])
+        ts(A("KP", lo, hi), bank(3 + c, 0, 512), 1.0 / 16, None, ALU.mult)
 
     def spread(buf, x, table, lists, l0):
         for c in range(0, L, GCH):
+            onv[0] = c // GCH in ONV[tag[0]]
             cp(A(buf, 16 * (L * x + c), 16 * (L * x + c + GCH)), table, A(lists, l0 + c, l0 + c + GCH))
+        onv[0] = False
 
     tag[0] = "A"
     cp(A("LVU", 0, 24), A("LVI", 0, 24))
     cp(A("KA", 0, L), A("KP", 0, NV), A("LVU", 0, 24))
     cp(A("NA", 0, L), A("NTB", 0, NV), A("LVU", 0, 24))
-    spread("XT", 1, A("LF", 0, NL), "KA", 0)
+    spread("XA", 0, A("LF", 0, NL), "KA", 0)
 
     def xa(d):
-        return A("XT", 16 * L + d, 32 * L, 16)
+        return A("XA", d, 16 * L, 16)
     for i in range(6):
         b = bank((4, 5, 7, 2, 3, 4)[i], 0, L)
         if i == 0:
@@ -379,50 +408,51 @@ def build(g, T, topo, core, rank):
             cp(A("LBU", lo, hi), A("LBI", lo, hi))
         cp(A("WU", L * t, L * t + L), A("BK", 0, NB), A("LBU", 24 * t, 24 * t + 24))
         spread("XC", x, A("NTB", 0, NV), "WU", L * t)
-        ts(A("LT", L * t, L * t + L), A("AP", 6 * L * t, 6 * L * t + L), MAGIC, MAGIC, ALU.add, ALU.subtract)
+        if t:
+            ts(A("LT", L * t, L * t + L), A("AP", 6 * L * t, 6 * L * t + L), MAGIC, MAGIC, ALU.add, ALU.subtract)
+        else:
+            ts(A("LT", 0, L), A("NA", 0, L), col(9), None, ALU.mult)
         for i in range(3):
             b = (3 * t + i) % 2
             x0 = 16 * (L * x + 128 * i)
-
-            def lane(w):
-                return (bank(b, 128 * w, 128 * w + 128), A("LT", L * t + 128 * i, L * t + 128 * i + 128), A("WR", 256 * w + rot(t), 256 * w + rot(t) + 128))
-            mg([lane(0), lane(1)] + [(bank(b, 15 - k, 256, 16), A("XC", x0 + k, x0 + 2048, 16), A("W24", 0, 16)) for k in range(16)])
-            nonzero(A("NE", 256 * b, 256 * b + 256), bank(b, 0, 256))
-            mg([lane(2)] + [(bank(b, 256 + 15 - k, 384, 16), A("XC", x0 + k, x0 + 2048, 16), A("W24", 16, 24)) for k in range(16)] +
-               [(bank(b, 256, 384), IDm("I32"), A("NE", 256 * b + 128 * w, 256 * b + 128 * w + 128)) for w in range(2)])
-            least(A("SC", 512 * sb + 128 * i, 512 * sb + 128 * i + 128), A("RS", 0, 128), bank(b, 256, 384))
-        to_list(sb, 24, 16.0, 2.0 ** 19, 2047, A("WL", 24 * t, 24 * t + 24))
+            r0, n0 = 17 * rot(t) // 16, 272 * b
+            mg([(bank(b, 136 * w, 136 * w + 136), A("LT", L * t + 128 * i, L * t + 128 * i + 128), A("WR", 272 * w + r0, 272 * w + r0 + 136)) for w in range(3)] +
+               [(bank(b, 16 - k, 408, 17), A("XC", x0 + k, x0 + 2048, 16), A("W24", 0, 24)) for k in range(16)])
+            ts(A("NE", n0, n0 + 136), bank(b, 136, 272), 2.0 ** 30, None, ALU.mult)
+            tt(A("NE", n0 + 136, n0 + 272), bank(b, 0, 136), A("NE", n0, n0 + 136), ALU.not_equal)
+            lastfit(A("SC", 512 * sb + 136 * i, 512 * sb + 136 * i + 136), A("NE", n0 + 136, n0 + 272), bank(b, 272, 408))
+        to_list(sb, 24, 17, 2.0 ** 23, 2047, A("WL", 24 * t, 24 * t + 24))
         out = A("R1", 32 * (t - 1), 32 * t) if t else A("V1", 96, 128)
-        ts(out, A("SC", 512 * sb, 512 * sb + 512), 16.0, 16.0, ALU.min, ALU.subtract, off=A("RL", 2 * t, 2 * t + 2))
+        win, off = A("SC", 512 * sb, 512 * sb + 512), A("RL", 2 * t, 2 * t + 2)
+        ts(out, win, -1.0, None, ALU.add, off=off, s=act(out, win, ACT.Identity, -1.0, 1.0, off))
         if t:
             home(t, A("R1", 32 * (t - 1), 32 * (t - 1) + 24), A("V1", 24 * (t - 1), 24 * t), "a_v1%d" % t)
 
-    def tests(t, n):
+    def tests(t, n=128):
         tag[0] = "T%d" % t
         x, a0, d0 = t % NXT, 6 * L * t, 768 * (t % 2)
-        cp(A("KL", L * (t % 2), L * (t % 2) + L), A("KP", 0, NV), A("WL", 24 * t, 24 * t + 24))
-        spread("XT", x, A("LF", 0, NL), "KL", L * (t % 2))
+        k0, x0, lf = L * (t % 2), 8 * L * x, A("LF", 0, NL)
+        cp(A("KG", k0, k0 + L), A("KP", 0, NV), A("WL", 24 * t, 24 * t + 24))
+        mg([(bank(5, 128 + 192 * y, 320 + 192 * y), A("PM", 136 * y + 8 - 8 * h, 136 * y + 136 - 8 * h), A("KG", k0 + h, k0 + L, 2))
+            for y in range(2) for h in range(2)])
+        cp(A("KL", k0, k0 + L), bank(5, 128, 512))
+        for c in range(0, L, 2 * GCH):
+            out, off = A("XT", x0 + 8 * c, x0 + 8 * c + 16 * GCH), A("KL", k0 + c // 2, k0 + c // 2 + GCH)
+            ts(out, lf, 16.0, None, ALU.mult, off=off, s=act(out, lf, ACT.Identity, 0.0, 16.0, off))
+            tt(out, lf, out, ALU.add, off=A("KL", k0 + 192 + c // 2, k0 + 192 + c // 2 + GCH))
         for c in range(0, L, n):
-            def kid(d):
-                return (HBm(d), A("XT", 16 * (L * x + c) + d, 16 * (L * x + c + n), 16))
+            def two_kids(i):
+                return (HBm(i), A("XT", x0 + 8 * c + i, x0 + 8 * (c + n), 8))
             for y in range(2):
-                prs = []
-                for i in range(5, 0, -1):
-                    prs.append((HAm(i, 1 - y, t), A("AP", a0 + L * i + c, a0 + L * i + c + n)))
-                    prs += [kid(ASC[i] + j) for j in (2, 1, 0)]
-                prs += [(HAm(0, 1 - y, t), A("AP", a0 + c, a0 + c + n)), (HAm(0, y, t), A("LT", L * t + c, L * t + c + n)), kid(0)]
-                if n == L:
-                    mm(bank(2 + y, 0, L), prs)
-                    nonzero(A("BD", d0 + L * y, d0 + L * y + L), bank(2 + y, 0, L))
-                else:
-                    mm(bank(2 + c // n % 2, n * y, n * y + n), prs)
-            if n < L:
-                nonzero(A("BD", d0 + 2 * c, d0 + 2 * c + 2 * n), bank(2 + c // n % 2, 0, 2 * n))
-        for i in range(3):
-            c0, c1 = (d0 + 128 * i, d0 + L + 128 * i) if n == L else (d0 + 256 * i, d0 + 256 * i + 128)
-            b = bank(4 + (3 * t + i) % 2, 0, 256)
-            mm(b, [(A("BD", c0, c0 + 128), A("FD", 0, 256)), (A("BD", c1, c1 + 128), A("FS", 0, 256))])
-            least(A("SD", d0 + 256 * i, d0 + 256 * i + 256), A("RT", 0, 256), b)
+                def piece(i):
+                    return (HAm(i, 1 - y, t), A("AP", a0 + L * i + c, a0 + L * i + c + n))
+                prs = [piece(5), two_kids(7), two_kids(6), piece(4), two_kids(5), piece(3), two_kids(4), two_kids(3), piece(2), two_kids(2),
+                       piece(1), two_kids(1), piece(0), (HAm(0, y, t), A("LT", L * t + c, L * t + c + n)), two_kids(0)]
+                mm(bank(2 + c // n, n * y, n * y + n), prs)
+            c0, b = d0 + 2 * c, bank(2 + c // n, 256, 512)
+            nonzero(A("BD", c0, c0 + 256), bank(2 + c // n, 0, 256))
+            mm(b, [(A("BD", c0, c0 + 128), A("FD", 0, 256)), (A("BD", c0 + 128, c0 + 256), A("FS", 0, 256))])
+            least(A("SD", c0, c0 + 256), A("RT", 0, 256), b)
         out = A("R2", 32 * (t - 1), 32 * t) if t else A("V2", 96, 128)
         ts(out, A("SD", d0, d0 + 768), 32.0, None, ALU.min, off=A("RL", 10 + 2 * t, 12 + 2 * t))
         if t:
@@ -434,13 +464,13 @@ def build(g, T, topo, core, rank):
     def tested(t):
         tag[0] = "L%d" % t
         if t:
-            mm(bank(6, 64, 88), [(IDm("N32"), A("MG", 32 * s, 32 * s + 24)) for s in range(t)])
-            tt(A("CD", 0, 24), v("V1", t), bank(6, 64, 88), ALU.is_lt)
+            mm(bank(5, 64, 88), [(IDm("N32"), A("MG", 32 * s, 32 * s + 24)) for s in range(t)])
+            tt(A("CD", 0, 24), v("V1", t), bank(5, 64, 88), ALU.is_lt)
         else:
             ts(A("CD", 0, 24), v("V1", t), 0.0, None, ALU.is_lt)
-        mg([(bank(6, 96, 120), A("TRI", 0, 128), A("CD", 0, 24)), (bank(6, 104, 120), A("ONE", 0, 128), A("CD", 0, 16)),
-            (bank(6, 112, 120), A("ONE", 0, 128), A("CD", 0, 8))])
-        ts(v("UU", t), bank(6, 96, 120), CAP - 1024.0, 32.0, ALU.is_lt, ALU.mult)
+        mg([(bank(5, 96, 120), A("TRI", 0, 128), A("CD", 0, 24)), (bank(5, 104, 120), A("ONE", 0, 128), A("CD", 0, 16)),
+            (bank(5, 112, 120), A("ONE", 0, 128), A("CD", 0, 8))])
+        ts(v("UU", t), bank(5, 96, 120), CAP - 1024.0, 32.0, ALU.is_lt, ALU.mult)
 
     def merged(t):
         tag[0] = "M%d" % t
@@ -448,7 +478,7 @@ def build(g, T, topo, core, rank):
 
     def fields():
         tag[0] = "F"
-        ts(A("VI", 0, 120), A("V1", 0, 120), 16.0, 2.0 ** 19, ALU.add, ALU.mult)
+        ts(A("VI", 0, 120), A("V1", 0, 120), 1.0, 2.0 ** 23, ALU.add, ALU.mult)
         ts(A("FF", 1, 600, 5), A("VI", 0, 120), 2047, None, ALU.bitwise_and)
         for b in range(4):
             ts(A("VB", 120 * b, 120 * b + 120), A("VI", 0, 120), 11 + b, 1 << b, ALU.logical_shift_right, ALU.bitwise_and)
@@ -465,40 +495,21 @@ def build(g, T, topo, core, rank):
         mg([(bank(7, 128 * i, 128 * i + 128, 1, 40), A("FP", 128 * t + 40 * i, 128 * t + 40 * i + 40), IDm("I32")) for i in range(3)],
            start=False, stop=t == NT - 1)
 
-    claims(0)
-    claims(1)
-    tests(0, L)
-    claims(2)
-    tested(0)
-    tests(1, L)
-    merged(0)
-    claims(3)
-    tested(1)
-    tests(2, L)
-    claims(4)
-    merged(1)
-    tested(2)
-    tests(3, L)
+    for part in PARTS:
+        if part != "A":
+            (claims if part[0] == "C" else tests)(int(part[1]))
     fields()
-    merged(2)
-    tested(3)
-    for t in range(3):
+    for t in range(NT):
+        tested(t)
+        merged(t)
+    for t in range(NT):
         store(t)
-    tests(4, 128)
-    merged(3)
-    tested(4)
-    store(3)
-    merged(4)
-    store(4)
     ts(A("YS", 0, L, 1, 0, 40), bank(7, 0, L, 1, 40), 1.0 / 32, None, ALU.mult)
     dma(lambda e: [e.dma_start(T.y[:], T.YS[0:40, :])], [A("YS", 0, L)], [], 61440)
     return ops
 
 
 def depend(ops):
-    def norm(a):
-        return (a[0], 0, 512, 1) if SCRATCH[a[0]][0] == "psum" else a
-
     def meet(a, b):
         if a[2] <= b[1] or b[2] <= a[1]:
             return False
@@ -509,7 +520,7 @@ def depend(ops):
         d = set()
         if "after" in o:
             d.add(o["after"])
-        acc = [(norm(a), SCRATCH[a[0]][0] == "psum") for a in o["r"]] + [(norm(a), True) for a in o["w"]]
+        acc = [(a, False) for a in o["r"]] + [(a, True) for a in o["w"]]
         for a, wr in acc:
             for (b, bw, j) in hist.get(a[0], []):
                 if (wr or bw) and meet(a, b):
@@ -543,40 +554,156 @@ def schedule(ops, deps):
             alts.append([(a[0], a[2]) for a in o["alts"]])
             lag.append(LAT)
 
-    def place(seq, pre, back):
-        busy = {e: [] for e in "VSPGYL"}
-        st, fin, ch = [0.0] * n, [0.0] * n, [0] * n
-        for i in seq:
-            r = max([fin[j] + (0.0 if alts[i][0][0] == alts[j][0][0] == "P" else lag[i] if back else lag[j]) for j in pre[i]] + [0.0])
-            best = None
-            for k, (e, c) in enumerate(alts[i]):
-                t, at = r, len(busy[e])
-                for x, (a, b) in enumerate(busy[e]):
-                    if b <= t:
-                        continue
-                    if a >= t + c:
-                        at = x
-                        break
-                    t = b
-                key = t + c + (VBIAS * c if e == "V" and len(alts[i]) > 1 else 0.0)
-                if best is None or key < best[0]:
-                    best = (key, t, k, at)
-            _, t, k, at = best
-            e, c = alts[i][k]
-            st[i], fin[i], ch[i] = t, t + c, k
-            busy[e].insert(at, (t, t + c))
-        return st, fin, ch
-    prio = [0.0] * n
+    due, seen = [1e9] * n, {}
+    for i, o in enumerate(ops):
+        part = o["tag"] if o["tag"] in PARTS else "T" + o["tag"][1:] if o["tag"][0] in "LMO" else "C4" if o["tag"] == "F" else None
+        if part:
+            long_ = bool(o.get("g")) and alts[i][0][1] > 0.6
+            seen[part] = seen.get(part, 0) + (cnt(o["w"][0]) if long_ else 0)
+            due[i] = PACE * (PARTS.index(part) + (seen[part] / (16.0 * L) if long_ else SOON if part == o["tag"] else LATE))
+        elif "dma" in o or "send" in o:
+            due[i] = i - 1e3 if "dma" in o else EARLY
     for i in range(n - 1, -1, -1):
-        prio[i] = min(a[1] for a in alts[i]) + lag[i] + max([prio[j] for j in succ[i]] + [0.0])
-    best = None
-    for _r in range(TURNS + 1):
-        st, fin, ch = place(sorted(range(n), key=lambda i: (-prio[i], i)), deps, False)
-        if best is None or max(fin) < max(best[1]):
-            best = (st, fin, ch)
-        prio = place(sorted(range(n), key=lambda i: (-fin[i] - lag[i], -i)), succ, True)[1]
-    st, fin, ch = best
-    return [(i, ch[i]) for i in sorted(range(n), key=lambda i: (st[i], i))], fin
+        slack = SLACK if ops[i]["tag"] in RANK and alts[i][0][0] == "V" else 0.0
+        if "dma" in ops[i]:
+            continue
+        due[i] = min([due[i]] + [due[j] - lag[i] - slack for j in succ[i]]) - min(a[1] for a in alts[i])
+    left = [len(d) for d in deps]
+    ready = {i: 0.0 for i in range(n) if not left[i]}
+    free = {e: 0.0 for e in "VSPGYL"}
+    st, fin, ch = [0.0] * n, [0.0] * n, [0] * n
+
+    def key(x):
+        i, k = x
+        if ops[i]["tag"] not in RANK:
+            return (2, -due[i] - (OWN if k == 0 and len(alts[i]) > 1 else 0.0), -i)
+        if EDF:
+            return (1, -due[i], -i)
+        return (alts[i][k][1] < 1, -RANK.index(ops[i]["tag"]), -i)
+    banks = [{a[0] for a in o["r"] + o["w"] if SCRATCH[a[0]][0] == "psum"} for o in ops]
+    held = {}
+    while ready:
+        best = None
+        for i in ready:
+            for b in banks[i]:
+                if b in held:
+                    j = held[b]
+                    ready[i] = max(ready[i], fin[j] + (0.0 if alts[i][0][0] == alts[j][0][0] == "P" else lag[j]))
+        for e in free:
+            mine = [(i, k) for i in ready for k, a in enumerate(alts[i]) if a[0] == e and ops[i].get("first", k) == k]
+            if mine:
+                t = max(free[e], min(ready[i] for i, k in mine))
+                if best is None or t < best[0]:
+                    best = (t, e, mine)
+        t, e, mine = best
+        i, k = max(((i, k) for i, k in mine if ready[i] <= t + (AHEAD if alts[i][k][1] < 1 else 0.0)), key=key)
+        st[i], ch[i] = max(t, ready.pop(i)), k
+        fin[i] = free[e] = st[i] + alts[i][k][1]
+        for b in banks[i]:
+            held[b] = i
+        for j in succ[i]:
+            left[j] -= 1
+            if not left[j]:
+                ready[j] = max(fin[x] + (0.0 if alts[x][0][0] == alts[j][0][0] == "P" else lag[x]) for x in deps[j])
+
+    ispe = [a[0][0] == "P" for a in alts]
+    banks = [sorted(b) for b in banks]
+    models = []
+    for kc, kg, kp, wait, hop in MODELS:
+        cs = [[c * (kp if e == "P" else hop if e in "YL" else kc * (kg if ops[i].get("g") else 1.0)) for e, c in alts[i]] for i in range(n)]
+        lg = [wait if x == LAT else x * hop for x in lag]
+        models.append((cs, [[(j, 0.0 if ispe[i] and ispe[j] else lg[j]) for j in deps[i]] for i in range(n)], wait))
+
+    def replay(order, ch, model):
+        cs, pre, wait = model
+        free, last, fin, why = dict.fromkeys("VSPGYL", 0.0), {}, [0.0] * n, [-1] * n
+        for i in order:
+            e = alts[i][ch[i]][0]
+            t, y = free[e], last.get(e, -1)
+            for j, x in pre[i]:
+                if fin[j] + x > t:
+                    t, y = fin[j] + x, j
+            for b in banks[i]:
+                j = last.get(b, -1)
+                if j >= 0 and fin[j] + (0.0 if ispe[i] and ispe[j] else wait) > t:
+                    t, y = fin[j] + (0.0 if ispe[i] and ispe[j] else wait), j
+                last[b] = i
+            fin[i] = free[e] = t + cs[i][ch[i]]
+            last[e], why[i] = i, y
+        return fin, why
+
+    def value(p, ch):
+        for i in range(n):
+            for j in deps[i]:
+                if p[j] >= p[i]:
+                    p[i] = p[j] + 1e-4
+        order = sorted(range(n), key=lambda i: p[i])
+        runs = [replay(order, ch, m) for m in models]
+        return sum(max(r[0]) / m[0] for r, m in zip(runs, MODELS)) / len(runs), order, runs[0]
+    groups = {}
+    for i, o in enumerate(ops):
+        groups.setdefault(o["tag"], []).append(i)
+        groups.setdefault((o["tag"], o["w"][0][0] if o["w"] else ""), []).append(i)
+    groups = list(groups.values())
+    flex = [i for i in range(n) if len(alts[i]) > 1]
+    rng = np.random.default_rng(SEED)
+    now = best = value(list(st), ch) + (list(ch),)
+    for r in range(ROUNDS):
+        fin, why = now[2]
+        p, c = [fin[i] - models[0][0][i][now[3][i]] for i in range(n)], list(now[3])
+        for x, i in enumerate(now[1]):
+            p[i] += 1e-7 * x
+        path, i = [], max(range(n), key=lambda j: fin[j])
+        while i >= 0:
+            path.append(i)
+            i = why[i]
+        u = float(rng.random())
+        i = path[int(rng.integers(0, len(path)))]
+        if u < 0.35:
+            j = why[i]
+            if j < 0 or j in deps[i]:
+                continue
+            if u < 0.2:
+                back(p, deps, i, p[j] - 1e-5)
+            else:
+                p[j] = p[i] + 1e-5
+        elif u < 0.5:
+            i = i if len(alts[i]) > 1 else flex[int(rng.integers(0, len(flex)))]
+            c[i] = 1 - c[i]
+            if u < 0.45:
+                j = flex[int(rng.integers(0, len(flex)))]
+                if c[j] == c[i] and j != i and abs(alts[j][0][1] - alts[i][0][1]) < 0.3:
+                    c[j] = 1 - c[j]
+        elif u < 0.75:
+            i = i if u < 0.65 else int(rng.integers(0, n))
+            back(p, deps, i, p[i] + float(rng.normal()) * 2.0)
+        else:
+            d = float(rng.normal()) * float(rng.choice([0.5, 2.0, 6.0]))
+            for i in groups[int(rng.integers(0, len(groups)))]:
+                back(p, deps, i, p[i] + d)
+        v = value(p, c) + (c,)
+        if v[0] <= now[0] + HEAT * (1.0 - r / ROUNDS) * float(rng.exponential()):
+            now = v
+            if v[0] < best[0]:
+                best = v
+    PLAN["v"] = best[0]
+    last = {}
+    for i in best[1]:
+        for b in banks[i]:
+            if b in last and last[b] not in deps[i]:
+                deps[i].append(last[b])
+            last[b] = i
+    return [(i, best[3][i]) for i in best[1]], best[2][0]
+
+
+def back(p, deps, i, t):
+    todo = [(i, t)]
+    p[i] = t + 1.0 if t > p[i] else p[i]
+    while todo:
+        j, x = todo.pop()
+        if p[j] > x:
+            p[j] = x
+            todo += [(k, x - 1e-5) for k in deps[j]]
 
 
 def rank_program(g, core, T, topo):

@@ -28,7 +28,7 @@ SCRATCH = {
     "WU": _sb(NT * L, U), "XC": _sb(NXC * 16 * L, B), "NE": _sb(544, B), "WL": _sb(120, U), "KL": _sb(2 * L, U),
     "XT": _sb(NXT * 8 * L, B), "BD": _sb(2 * 768, B), "SD": _sb(2 * 768, F),
     "R1": _sb(128, F), "R2": _sb(128, I32), "V1": _sb(128, F), "V2": _sb(128, I32), "VI": _sb(120, I32), "VB": _sb(480, I32), "VC": _sb(240, I32),
-    "FF": _sb(608, I32), "CD": _sb(24, B), "UU": _sb(120, F), "MG": _sb(160, B), "SB": _sb(24, I32), "FP": _sb(640, HF), "YS": _sb(L, F),
+    "FF": _sb(608, I32), "CD": _sb(24, B), "UU": _sb(120, F), "MG": _sb(160, B), "SB": _sb(120, I32), "FP": _sb(640, HF), "YS": _sb(L, F),
     "DLB": ("dram", [240, 24], I32),
 }
 for _i in range(8):
@@ -38,15 +38,19 @@ ARR_SEMS = ["a_%s%d" % (k, t) for k in ("lb", "p0", "pp", "v1", "v2") for t in r
 SEMAPHORES = ["sV", "sS", "sP", "sG", "sent"] + DMA_SEMS + ARR_SEMS
 
 CY, PCY, GF_, LAT = 0.87e-3, 0.44e-3, 1.56, 0.12
-LINK = 7e4
-GCH = 64
-PARTS = "C0 A C1 T0 C2 T1 C3 T2 C4 T3 T4".split()
-ONV = {"A": (1, 3), "C0": (1, 3), "C1": (1,), "C2": (1, 4), "C3": (1,), "C4": (1,)}
+LINK = 6e4
+GCH = 128
+PARTS = "C0 A C1 T0 C2 T1 C3 C4 T2 T3 T4".split()
+ONV = {"A": (1,), "C0": (1,), "C1": (1,), "C2": (1,), "C3": (), "C4": (1,)}
 RANK = "L0 M0 L1 M1 L2 M2 F L3 M3 L4 M4 O0 O1 O2 O3 O4".split() + PARTS
 PACE, SOON, LATE, SLACK = 6.0, 1.5, 3.0, 0.5
 AHEAD, OWN = 0.0, 2.0
-ROUNDS, SEED, HEAT = 24000, 1, 0.2
-MODELS = ((1.0, 1.0, 1.0, LAT, 1.0), (1.3, 1.1, 1.3, 0.25, 1.4))
+ROUNDS, SEED, HEAT = 50000, 2, 0.15
+MODELS = ((1.0, 1.0, 1.0, LAT, 1.0),)
+FILL = 0.05
+WV, WS = 0.3, 0.1
+SPLIT = ()
+TWICE = (0, 1)
 EDF = False
 EARLY = -9.0
 PLAN = {}
@@ -159,6 +163,9 @@ def build(g, T, topo, core, rank):
     def select(out, i, pat, cmp, other, base, cm):
         return add([("G", lambda e: [e.affine_select(ap(out), ap(i), pat, cmp, other, base, cm)], 0.17 + 2 * cnt(out) * CY)], [i], [out])
 
+    def gcp(out, i):
+        return select(out, i, [[0, cnt(out)]], ALU.is_ge, 0.0, 0, 0)
+
     def dma(f, reads, writes, nbytes, n=1):
         nd[0] += 1
         return add([("Y", f, 0.1)], reads, writes, dma=DMA_SEMS[nd[0] - 1], n=16 * n, bytes=nbytes)
@@ -215,7 +222,8 @@ def build(g, T, topo, core, rank):
     Hb = A("HA", 0, 128)
     HP = A("PT", 16, 32)
 
-    dma(lambda e: [e.dma_start(T.IV[:], T.iv[:])], [], [A("IV", 0, NV)], 393216)
+    for lo, hi in ((0, 512), (512, NV)):
+        dma(lambda e, lo=lo, hi=hi: [e.dma_start(T.IV[:, lo:hi], T.iv[:, lo:hi])], [], [A("IV", lo, hi)], 256 * (hi - lo))
     dma(lambda e: [e.dma_start(T.DLB[0:128, :], T.lb[:]), e.dma_start(T.DLB[128:240, :], T.lb[0:112, :])], [], [A("DLB", 0, 24)], 24576, n=2)
     dma(lambda e: [e.dma_start(T.KDI[:], T.kd[:])], [], [A("KDI", 0, NV)], 786432)
     dma(lambda e: [e.dma_start(T.LVI[:], T.lv[:]), e.dma_start(T.LBI[:, 0:24], T.lb[:])], [], [A("LVI", 0, 24), A("LBI", 0, 24)], 24576, n=2)
@@ -231,9 +239,10 @@ def build(g, T, topo, core, rank):
     ms(A("PT", 16, 17), 1.0)
     turn(A("TB", 0, 128), A("XB", 0, 128))
     ts(A("OU", 0, 8), A("OI", 0, 8), 32.0, None, ALU.min)
-    for b in range(4):
-        n = 1 << b
-        ts(A("PT", 16 + n, 16 + 2 * n), A("PT", 16, 16 + n), col(b), None, ALU.mult, s=False)
+    for b, n in ((0, 1), (2, 4)):
+        ts(A("PT", 16 + n, 16 + 2 * n), A("PT", 16, 16 + n), col(b), None, ALU.mult)
+        ts(A("PT", 16 + 2 * n, 16 + 3 * n), A("PT", 16, 16 + n), col(b + 1), None, ALU.mult)
+        ts(A("PT", 16 + 3 * n, 16 + 4 * n), A("PT", 16, 16 + n), col(b), col(b + 1), ALU.mult, ALU.mult)
     cp(Hb, A("PT", 0, 48), A("OU", 0, 8))
     for b, (m, a) in enumerate(((-8.0, 24.0), (-1.5, 2.5), (-7.5, 8.5), (-127.5, 128.5))):
         ts(cc(b), col(b), m, a, ALU.mult, ALU.add)
@@ -307,14 +316,15 @@ def build(g, T, topo, core, rank):
     iota(A("WI", 27, 28), [[0, 1]], 0, 1)
     ts(cc(11), A("WI", 27, 28), col(4), -33.0 / 16, ALU.subtract, ALU.mult)
     ts(A("WO", 0, 9), A("WI", 18, 27), cc(11), 33.0, ALU.add, ALU.min)
-    for w, c in enumerate((col(5), col(6), cc(6))):
+    ts(cc(5), col(5), 2.0 ** 26, None, ALU.mult)
+    for w, c in enumerate((cc(5), col(6), cc(6))):
         if w < 2:
             ts(A("PW", 48 * w + 17, 48 * w + 33), A("ONE", 0, 16), c, None, ALU.mult)
         else:
             ts(A("PW", 113, 129), A("WI", 1, 17), cc(10), c, ALU.mult, ALU.add)
             ts(A("PW", 112, 113), cc(10), 16.0, None, ALU.mult)
         cp(A("WR", 272 * w, 272 * w + 144), A("PW", 48 * w, 48 * w + 48), A("WO", 0, 9))
-        cp(A("WR", 272 * w + 136, 272 * w + 272), A("WR", 272 * w, 272 * w + 136))
+        gcp(A("WR", 272 * w + 136, 272 * w + 272), A("WR", 272 * w, 272 * w + 136))
         ts(A("W24", 8 * w, 8 * w + 8), A("HA", 0, 128, 16), c, None, ALU.mult)
     ts(cc(7), A("PT", 31, 32), 64.0, None, ALU.mult)
     ts(cc(8), A("PT", 31, 32), -64.0, None, ALU.mult)
@@ -332,7 +342,7 @@ def build(g, T, topo, core, rank):
     iota(A("L5F", 0, 8), [[16, 8]], -2)
     ts(A("L5F", 0, 8), A("L5F", 0, 8), col(4), 0.2, ALU.add, ALU.mult)
     cp(A("L5I", 0, 8), A("L5F", 0, 8))
-    cp(A("L5", 0, 8), A("L5I", 0, 8))
+    gcp(A("L5", 0, 8), A("L5I", 0, 8))
     fill(A("MG", 0, 160), 0)
     fill(A("FF", 0, 608), 0)
     for t in range(NT):
@@ -350,7 +360,7 @@ def build(g, T, topo, core, rank):
     tag[0] = "N"
     for c in range(3):
         lo, hi = 512 * c, 512 * c + 512
-        select(A("KDF", lo, hi), A("KDI", lo, hi), [[0, 512]], ALU.is_ge, 0.0, 0, 0)
+        gcp(A("KDF", lo, hi), A("KDI", lo, hi))
         mm(bank(c, 0, 512), [(Hb, A("IV", lo, hi))])
         ts(A("TAU", lo, hi), bank(c, 0, 512), 1.0, -1.0, ALU.min, ALU.max, s=act(A("TAU", lo, hi), bank(c, 0, 512), ACT.Sign))
         mg([(bank(7, 128 * i, 128 * i + 128), A("TAU", lo + 128 * i, lo + 128 * i + 128), A("KK", 0, 128)) for i in range(4)])
@@ -376,7 +386,7 @@ def build(g, T, topo, core, rank):
         onv[0] = False
 
     tag[0] = "A"
-    cp(A("LVU", 0, 24), A("LVI", 0, 24))
+    gcp(A("LVU", 0, 24), A("LVI", 0, 24))
     cp(A("KA", 0, L), A("KP", 0, NV), A("LVU", 0, 24))
     cp(A("NA", 0, L), A("NTB", 0, NV), A("LVU", 0, 24))
     spread("XA", 0, A("LF", 0, NL), "KA", 0)
@@ -405,7 +415,7 @@ def build(g, T, topo, core, rank):
         x, sb = t % NXC, t % 2
         if t < 2:
             lo, hi = (0, 24) if t == 0 else (24, 120)
-            cp(A("LBU", lo, hi), A("LBI", lo, hi))
+            gcp(A("LBU", lo, hi), A("LBI", lo, hi))
         cp(A("WU", L * t, L * t + L), A("BK", 0, NB), A("LBU", 24 * t, 24 * t + 24))
         spread("XC", x, A("NTB", 0, NV), "WU", L * t)
         if t:
@@ -416,11 +426,22 @@ def build(g, T, topo, core, rank):
             b = (3 * t + i) % 2
             x0 = 16 * (L * x + 128 * i)
             r0, n0 = 17 * rot(t) // 16, 272 * b
-            mg([(bank(b, 136 * w, 136 * w + 136), A("LT", L * t + 128 * i, L * t + 128 * i + 128), A("WR", 272 * w + r0, 272 * w + r0 + 136)) for w in range(3)] +
-               [(bank(b, 16 - k, 408, 17), A("XC", x0 + k, x0 + 2048, 16), A("W24", 0, 24)) for k in range(16)])
-            ts(A("NE", n0, n0 + 136), bank(b, 136, 272), 2.0 ** 30, None, ALU.mult)
-            tt(A("NE", n0 + 136, n0 + 272), bank(b, 0, 136), A("NE", n0, n0 + 136), ALU.not_equal)
-            lastfit(A("SC", 512 * sb + 136 * i, 512 * sb + 136 * i + 136), A("NE", n0 + 136, n0 + 272), bank(b, 272, 408))
+
+            def lane(w, c0):
+                return (bank(b, c0, c0 + 136), A("LT", L * t + 128 * i, L * t + 128 * i + 128), A("WR", 272 * w + r0, 272 * w + r0 + 136))
+
+            def slots(hi, w0, w1):
+                return [(bank(b, 16 - k, hi, 17), A("XC", x0 + k, x0 + 2048, 16), A("W24", w0, w1)) for k in range(16)]
+            out = A("SC", 512 * sb + 136 * i, 512 * sb + 136 * i + 136)
+            if t in TWICE:
+                mg([lane(0, 0)] + slots(136, 0, 8) + [lane(1, 0), lane(2, 136)] + slots(272, 8, 24))
+                nonzero(A("NE", n0, n0 + 136), bank(b, 0, 136))
+                lastfit(out, A("NE", n0, n0 + 136), bank(b, 136, 272))
+            else:
+                mg([lane(w, 136 * w) for w in range(3)] + slots(408, 0, 24))
+                cp(A("NE", n0, n0 + 136), bank(b, 0, 136))
+                tt(A("NE", n0 + 136, n0 + 272), bank(b, 136, 272), A("NE", n0, n0 + 136), ALU.not_equal)
+                lastfit(out, A("NE", n0 + 136, n0 + 272), bank(b, 272, 408))
         to_list(sb, 24, 17, 2.0 ** 23, 2047, A("WL", 24 * t, 24 * t + 24))
         out = A("R1", 32 * (t - 1), 32 * t) if t else A("V1", 96, 128)
         win, off = A("SC", 512 * sb, 512 * sb + 512), A("RL", 2 * t, 2 * t + 2)
@@ -428,7 +449,7 @@ def build(g, T, topo, core, rank):
         if t:
             home(t, A("R1", 32 * (t - 1), 32 * (t - 1) + 24), A("V1", 24 * (t - 1), 24 * t), "a_v1%d" % t)
 
-    def tests(t, n=128):
+    def tests(t):
         tag[0] = "T%d" % t
         x, a0, d0 = t % NXT, 6 * L * t, 768 * (t % 2)
         k0, x0, lf = L * (t % 2), 8 * L * x, A("LF", 0, NL)
@@ -436,23 +457,29 @@ def build(g, T, topo, core, rank):
         mg([(bank(5, 128 + 192 * y, 320 + 192 * y), A("PM", 136 * y + 8 - 8 * h, 136 * y + 136 - 8 * h), A("KG", k0 + h, k0 + L, 2))
             for y in range(2) for h in range(2)])
         cp(A("KL", k0, k0 + L), bank(5, 128, 512))
-        for c in range(0, L, 2 * GCH):
-            out, off = A("XT", x0 + 8 * c, x0 + 8 * c + 16 * GCH), A("KL", k0 + c // 2, k0 + c // 2 + GCH)
+        for c, n in [(0, 128), (128, 128)] + ([(256, 128)] if t < NT - 1 else [(256, 64), (320, 64)]):
+            out, off, even = A("XT", x0 + 8 * c, x0 + 8 * (c + n)), A("KL", k0 + c // 2, k0 + (c + n) // 2), A("KL", k0 + 192 + c // 2, k0 + 192 + (c + n) // 2)
             ts(out, lf, 16.0, None, ALU.mult, off=off, s=act(out, lf, ACT.Identity, 0.0, 16.0, off))
-            tt(out, lf, out, ALU.add, off=A("KL", k0 + 192 + c // 2, k0 + 192 + c // 2 + GCH))
-        for c in range(0, L, n):
+            apart = (t, c) in SPLIT
+            if apart:
+                cp(A("XA", 8 * c, 8 * (c + n)), lf, even)
+            else:
+                tt(out, lf, out, ALU.add, off=even)
+
             def two_kids(i):
-                return (HBm(i), A("XT", x0 + 8 * c + i, x0 + 8 * (c + n), 8))
+                return [(HBm(i), A("XT", x0 + 8 * c + i, x0 + 8 * (c + n), 8))] + ([(HBm(i), A("XA", 8 * c + i, 8 * (c + n), 8))] if apart else [])
+            b = 2 + c // 128
             for y in range(2):
                 def piece(i):
-                    return (HAm(i, 1 - y, t), A("AP", a0 + L * i + c, a0 + L * i + c + n))
-                prs = [piece(5), two_kids(7), two_kids(6), piece(4), two_kids(5), piece(3), two_kids(4), two_kids(3), piece(2), two_kids(2),
-                       piece(1), two_kids(1), piece(0), (HAm(0, y, t), A("LT", L * t + c, L * t + c + n)), two_kids(0)]
-                mm(bank(2 + c // n, n * y, n * y + n), prs)
-            c0, b = d0 + 2 * c, bank(2 + c // n, 256, 512)
-            nonzero(A("BD", c0, c0 + 256), bank(2 + c // n, 0, 256))
-            mm(b, [(A("BD", c0, c0 + 128), A("FD", 0, 256)), (A("BD", c0 + 128, c0 + 256), A("FS", 0, 256))])
-            least(A("SD", c0, c0 + 256), A("RT", 0, 256), b)
+                    return [(HAm(i, 1 - y, t), A("AP", a0 + L * i + c, a0 + L * i + c + n))]
+                mm(bank(b, 128 * y + c % 128, 128 * y + c % 128 + n),
+                   piece(5) + two_kids(7) + two_kids(6) + piece(4) + two_kids(5) + piece(3) + two_kids(4) + two_kids(3) + piece(2) + two_kids(2) +
+                   piece(1) + two_kids(1) + piece(0) + [(HAm(0, y, t), A("LT", L * t + c, L * t + c + n))] + two_kids(0))
+            if (c + n) % 128 == 0:
+                c0 = d0 + 256 * (c // 128)
+                nonzero(A("BD", c0, c0 + 256), bank(b, 0, 256))
+                mm(bank(b, 256, 512), [(A("BD", c0, c0 + 128), A("FD", 0, 256)), (A("BD", c0 + 128, c0 + 256), A("FS", 0, 256))])
+                least(A("SD", c0, c0 + 256), A("RT", 0, 256), bank(b, 256, 512))
         out = A("R2", 32 * (t - 1), 32 * t) if t else A("V2", 96, 128)
         ts(out, A("SD", d0, d0 + 768), 32.0, None, ALU.min, off=A("RL", 10 + 2 * t, 12 + 2 * t))
         if t:
@@ -488,9 +515,12 @@ def build(g, T, topo, core, rank):
     def store(t):
         tag[0] = "O%d" % t
         f0 = 120 * slot(t)
-        ts(A("FF", f0 + 3, f0 + 120, 5), v("V2", t), 1, None, ALU.logical_shift_right)
-        ts(A("SB", 0, 24), v("V2", t), 1, None, ALU.bitwise_and)
-        ts(A("FF", f0 + 4, f0 + 120, 5), A("SB", 0, 24), -2.0, 1.0, ALU.mult, ALU.add)
+        if t not in (2, 3):
+            n = 72 if t == 1 else 24
+            v2, sb = A("V2", 24 * slot(t), 24 * slot(t) + n), A("SB", 24 * slot(t), 24 * slot(t) + n)
+            ts(A("FF", f0 + 3, f0 + 5 * n, 5), v2, 1, None, ALU.logical_shift_right)
+            ts(sb, v2, 1, None, ALU.bitwise_and)
+            ts(A("FF", f0 + 4, f0 + 5 * n, 5), sb, -2.0, 1.0, ALU.mult, ALU.add)
         tt(A("FP", 128 * t, 128 * t + 128), A("MG", 32 * t, 32 * t + 32), A("FF", f0, f0 + 128), ALU.mult, off=A("L5", 0, 8))
         mg([(bank(7, 128 * i, 128 * i + 128, 1, 40), A("FP", 128 * t + 40 * i, 128 * t + 40 * i + 40), IDm("I32")) for i in range(3)],
            start=False, stop=t == NT - 1)
@@ -639,7 +669,8 @@ def schedule(ops, deps):
                     p[i] = p[j] + 1e-4
         order = sorted(range(n), key=lambda i: p[i])
         runs = [replay(order, ch, m) for m in models]
-        return sum(max(r[0]) / m[0] for r, m in zip(runs, MODELS)) / len(runs), order, runs[0]
+        onv = sum(alts[i][0][1] for i in flex if not ch[i])
+        return sum(max(r[0]) / m[0] for r, m in zip(runs, MODELS)) / len(runs) + WV * onv + WS * sum(runs[0][0]) / n, order, runs[0]
     groups = {}
     for i, o in enumerate(ops):
         groups.setdefault(o["tag"], []).append(i)
@@ -659,7 +690,20 @@ def schedule(ops, deps):
             i = why[i]
         u = float(rng.random())
         i = path[int(rng.integers(0, len(path)))]
-        if u < 0.35:
+        if rng.random() < FILL:
+            e = "VSP"[int(rng.integers(0, 5)) % 3]
+            mine = [j for j in now[1] if alts[j][c[j]][0] == e]
+            gaps = [(fin[a], p[b]) for a, b in zip(mine, mine[1:]) if p[b] - fin[a] > 0.1]
+            if not gaps:
+                continue
+            a, b = gaps[int(rng.integers(0, len(gaps)))]
+            fits = [j for j in now[1] if p[j] > b and any(x[0] == e for x in alts[j]) and all(fin[k] + x < b for k, x in models[0][1][j])][:6]
+            if not fits:
+                continue
+            j = fits[int(rng.integers(0, len(fits)))]
+            c[j] = [x[0] for x in alts[j]].index(e)
+            p[j] = b - 1e-5
+        elif u < 0.35:
             j = why[i]
             if j < 0 or j in deps[i]:
                 continue

@@ -7,7 +7,8 @@ SH = [t * (t + 1) // 2 % 8 for t in range(NT)]
 F, B, I32, U, HF = "float32", "bfloat16", "int32", "uint16", "float16"
 MAGIC = 1.5 * 2.0 ** 27
 ASC = (0, 1, 4, 7, 10, 13)
-NXC, NXT = 3, 3
+NONE = 17.0 * 2 ** 19
+SCANINT = True
 
 
 def _sb(n, d):
@@ -17,42 +18,45 @@ def _sb(n, d):
 SCRATCH = {
     "LF": _sb(NL, B), "IV": _sb(NV, B), "KDI": _sb(NV, I32), "KDF": _sb(NV, F), "KS": _sb(NV, F), "KP": _sb(NV, F), "BK": _sb(NB, I32),
     "LVI": _sb(24, I32), "LBI": _sb(120, I32), "LVU": _sb(24, U), "LBU": _sb(120, U),
-    "XB": _sb(320, F), "TB": _sb(320, F), "PT": _sb(112, B), "OI": _sb(8, I32), "OU": _sb(8, U), "CC": _sb(16, F), "PK8": _sb(8, B),
-    "HA": _sb(12 * 256, B), "HB": _sb(8 * 128, B), "PM": _sb(272, F), "KG": _sb(2 * L, F), "XA": _sb(16 * L, B), "HFL": _sb(128, F), "KK": _sb(128, B), "PKM": _sb(128, B), "PSM": _sb(128, B),
-    "DW": _sb(768, B), "IOT": _sb(256, B), "DH": _sb(48, B), "RS": _sb(512, B), "RT": _sb(256, B), "MK": _sb(256, B), "SS": _sb(240, B),
-    "EI": _sb(16, F), "EL": _sb(16, U), "WR": _sb(816, B), "PW": _sb(160, B), "WI": _sb(28, F), "WO": _sb(10, U), "W24": _sb(24, B), "ONE": _sb(128, B), "TRI": _sb(128, B),
+    "XB": _sb(704, F), "TB": _sb(704, F), "PT": _sb(112, B), "OI": _sb(8, I32), "OU": _sb(8, U), "CC": _sb(8, F), "PK8": _sb(8, B),
+    "HA": _sb(6 * 256, B), "HB": _sb(5 * 128, B), "XA": _sb(16 * L, B), "HFL": _sb(128, F), "KK": _sb(128, B), "PKM": _sb(128, B), "PSM": _sb(128, B),
+    "RS": _sb(512, B), "RT": _sb(256, B), "MI": _sb(448, B), "MK": _sb(448, B), "SS": _sb(480, B), "ZR": _sb(136, B), "SW": _sb(136, B),
+    "EI": _sb(28, F), "EL": _sb(28, U), "WR": _sb(816, B), "WI": _sb(272, B), "W24": _sb(24, B), "NON": _sb(128, B), "TRI": _sb(128, B), "CM": _sb(24, B),
     "ID": _sb(5 * 128, B), "FD": _sb(256, B), "FS": _sb(256, B), "CF": _sb(40, B),
     "RI": _sb(10, I32), "RF": _sb(20, F), "RL": _sb(20, U), "L5F": _sb(8, F), "L5I": _sb(8, I32), "L5": _sb(8, U),
-    "TAU": _sb(NV, B), "SC": _sb(1024, F), "E": _sb(512, HF), "LI": _sb(128, I32), "MU": _sb(96, U), "SG": _sb(NV, B), "SI": _sb(NV, B), "NTB": _sb(NV, B),
+    "TAU": _sb(NV, B), "SN": _sb(1024, I32 if SCANINT else F), "SC": _sb(1024, F), "E": _sb(512, HF), "LI": _sb(128, I32), "MU": _sb(96, U),
+    "SG": _sb(NV, B), "SI": _sb(NV, B), "NTB": _sb(NV, B),
     "KA": _sb(L, U), "NA": _sb(L, B), "AP": _sb(NT * 6 * L, HF), "LT": _sb(NT * L, B),
-    "WU": _sb(NT * L, U), "XC": _sb(NXC * 16 * L, B), "NE": _sb(544, B), "WL": _sb(120, U), "KL": _sb(2 * L, U),
-    "XT": _sb(NXT * 8 * L, B), "BD": _sb(2 * 768, B), "SD": _sb(2 * 768, F),
-    "R1": _sb(128, F), "R2": _sb(128, I32), "V1": _sb(128, F), "V2": _sb(128, I32), "VI": _sb(120, I32), "VB": _sb(480, I32), "VC": _sb(240, I32),
-    "FF": _sb(608, I32), "CD": _sb(24, B), "UU": _sb(120, F), "MG": _sb(160, B), "SB": _sb(120, I32), "FP": _sb(640, HF), "YS": _sb(L, F),
-    "DLB": ("dram", [240, 24], I32),
+    "WU": _sb(NT * L, U), "WF": _sb(NT * L, HF), "XC": _sb(NT * 16 * L, B), "NE": _sb(816, B), "WL": _sb(120, U), "KG": _sb(NT * L, U), "KL": _sb(NT * L, U),
+    "XT": _sb(2 * 8 * L, B), "BD": _sb(2 * 768, B), "SD": _sb(2 * 768, F),
+    "R1": _sb(128, I32), "R2": _sb(128, B), "V1": _sb(128, I32), "V2": _sb(128, B), "VB": _sb(240, I32),
+    "FF": _sb(608, I32), "CD": _sb(24, B), "MG": _sb(160, B), "FP": _sb(640, HF), "YS": _sb(L, F),
+    "DLB": ("dram", [240, 24], I32), "DK": ("dram", [16 * NT, 8 * L], U),
 }
 for _i in range(8):
     SCRATCH["B%d" % _i] = ("psum", [128, 512], F)
-DMA_SEMS = ["d%d" % _i for _i in range(10)]
+DMA_SEMS = ["d%d" % _i for _i in range(18)]
 ARR_SEMS = ["a_%s%d" % (k, t) for k in ("lb", "p0", "pp", "v1", "v2") for t in range(1, NT)]
-SEMAPHORES = ["sV", "sS", "sP", "sG", "sent"] + DMA_SEMS + ARR_SEMS
+SEMAPHORES = ["sV", "sS", "sP", "sG", "sent", "relay"] + DMA_SEMS + ARR_SEMS
 
 CY, PCY, GF_, LAT = 0.87e-3, 0.44e-3, 1.56, 0.12
-LINK = 6e4
+LINK, NEAR = 6e4, 1.5e5
 GCH = 128
-PARTS = "C0 A C1 T0 C2 T1 C3 C4 T2 T3 T4".split()
-ONV = {"A": (1,), "C0": (1,), "C1": (1,), "C2": (1,), "C3": (), "C4": (1,)}
+PARTS = "A C0 T0 C1 C2 C3 T1 C4 T2 T3 T4".split()
+ONV = {"A": (1,), "C0": (1,), "C1": (1,), "C2": (1,), "C3": (1,), "C4": ()}
 RANK = "L0 M0 L1 M1 L2 M2 F L3 M3 L4 M4 O0 O1 O2 O3 O4".split() + PARTS
 PACE, SOON, LATE, SLACK = 6.0, 1.5, 3.0, 0.5
 AHEAD, OWN = 0.0, 2.0
-ROUNDS, SEED, HEAT = 50000, 2, 0.15
+ROUNDS, SEED, HEAT = 22000, 3, 0.08
 MODELS = ((1.0, 1.0, 1.0, LAT, 1.0),)
 FILL = 0.05
-WV, WS = 0.3, 0.1
-SPLIT = ()
-TWICE = (0, 1)
-EDF = False
+WV, WS, WX = 0.2, 0.1, 0.1
 EARLY = -9.0
+SPLIT = ()
+CRIT, WH = 0.3, 0.3
+HLAG, DLAG, NH = 4.5, 2.6, 2
+CB = (0, 1, 5)
+TWICE = (0, 1, 2)
 PLAN = {}
 
 
@@ -118,11 +122,19 @@ def build(g, T, topo, core, rank):
             alts.append(s)
         return add(alts, [i, s1, s2, off], [out], g=off)
 
-    def cp(out, i, off=None):
+    def keep(out, i):
+        return ("G", lambda e: [e.affine_select(ap(out), ap(i), [[0, cnt(out)]], ALU.is_ge, 0.0, 0, 0)], 0.17 + 2 * cnt(out) * CY)
+
+    def cp(out, i, off=None, gp=False):
         alts = [("V", lambda e: [e.tensor_copy(ap(out), src(i, off))], cost(out, i, off))]
         if okS(out, i):
             alts.append(act(out, i, ACT.Copy, off=off))
+        if gp:
+            alts.append(keep(out, i))
         return add(alts, [i, off], [out], g=off)
+
+    def gcp(out, i):
+        return add([keep(out, i)], [i], [out])
 
     def tt(out, a, b, op, off=None):
         c = 1.0 if SCRATCH[a[0]][0] == "psum" or SCRATCH[b[0]][0] == "psum" else 2.0
@@ -130,7 +142,9 @@ def build(g, T, topo, core, rank):
         return add([("V", lambda e: [e.tensor_tensor(ap(out), src(a, off), ap(b), op)], c)], [a, b, off], [out], g=off)
 
     def ms(out, v):
-        return add([("V", lambda e: [e.memset(ap(out), v)], cost(out, out, None))], [], [out])
+        alts = [("V", lambda e: [e.memset(ap(out), v)], cost(out, out, None)),
+                ("G", lambda e: [e.iota(ap(out), [[0, cnt(out)]], int(v), 0, allow_small_or_imprecise_dtypes=True)], 0.13 + 2 * cnt(out) * CY)]
+        return add(alts, [], [out])
 
     def least(out, step, d1):
         return add([("V", lambda e: [e.tensor_tensor_scan(ap(out), ap(step), ap(d1), 0.0, ALU.add, ALU.min)], cost(out, d1, None))], [step, d1], [out])
@@ -138,7 +152,8 @@ def build(g, T, topo, core, rank):
     def lastfit(out, miss, d1):
         return add([("V", lambda e: [e.tensor_tensor_scan(ap(out), ap(miss), ap(d1), 0.0, ALU.min, ALU.max)], cost(out, d1, None))], [miss, d1], [out])
 
-    def turn(out, i):
+    def turn(b0, b1):
+        out, i = A("TB", 32 * b0, 32 * b1), A("XB", 32 * b0, 32 * b1)
         return add([("V", lambda e: [e.transpose(ap(out), ap(i))], cost(out, i, None))], [i], [out])
 
     def mg(items, start=True, stop=True):
@@ -163,8 +178,8 @@ def build(g, T, topo, core, rank):
     def select(out, i, pat, cmp, other, base, cm):
         return add([("G", lambda e: [e.affine_select(ap(out), ap(i), pat, cmp, other, base, cm)], 0.17 + 2 * cnt(out) * CY)], [i], [out])
 
-    def gcp(out, i):
-        return select(out, i, [[0, cnt(out)]], ALU.is_ge, 0.0, 0, 0)
+    def put(out, v):
+        return select(out, out, [[0, cnt(out)]], ALU.is_gt, v, 0, 0)
 
     def dma(f, reads, writes, nbytes, n=1):
         nd[0] += 1
@@ -189,7 +204,7 @@ def build(g, T, topo, core, rank):
             return []
         o = add([("G", f, 0.4)], [it[1] for it in items], [], send=sum(len(pick(k)) for k in range(len(items))))
         for k, it in enumerate(items):
-            add([("X", None, lat)], [], [it[3]], arr=it[4], n=len(pick(k)), after=o, link=nbytes)
+            add([("X", None, lat)], [A(name, 0, 1) for name, _ in LOADS], [it[3]], arr=it[4], n=len(pick(k)), after=o, link=nbytes)
 
     def bank(i, lo, hi, step=1, p1=128):
         return A("B%d" % i, lo, hi, step, 0, p1)
@@ -201,179 +216,184 @@ def build(g, T, topo, core, rank):
         return 16 * ((8 - SH[t]) % 8)
 
     def HAm(i, neg, t):
-        c = 256 * (2 * i + neg) + rot(t)
+        c = 256 * (2 * (i // 2) + neg) + rot(t)
         return A("HA", c, c + 128)
 
     def HBm(d):
-        return A("HB", 128 * d, 128 * d + 128) if d else Hb
+        if d % 3 == 0:
+            return A("HA", 512 * (d // 3), 512 * (d // 3) + 128)
+        c = 128 * (d - 1 - d // 3)
+        return A("HB", c, c + 128)
 
     def IDm(n):
-        c = 128 * ("I32", "N32", "I512", "I8192", "SGN").index(n)
+        c = 128 * ("I1", "I16", "I256", "NEG", "SGN").index(n)
         return A("ID", c, c + 128)
 
-    def col(b):
-        return A("TB", 32 * b, 32 * b + 1)
+    def row(b, lo=0, hi=32, step=1, p0=0, p1=128):
+        return A("XB", 32 * b + lo, 32 * b + hi, step, p0, p1)
 
-    def cc(c):
-        return A("CC", c, c + 1)
+    def col(b, p1=128):
+        return A("TB", 32 * b, 32 * b + 1, 1, 0, p1)
 
     def slot(t):
         return (t - 1) % NT
     Hb = A("HA", 0, 128)
     HP = A("PT", 16, 32)
+    P16, Q16, P8, PSW, Q32, H16, B8, HEAVY, LIGHT, PAY, TOP, SIGN, YSC = range(8, 21)
 
     for lo, hi in ((0, 512), (512, NV)):
         dma(lambda e, lo=lo, hi=hi: [e.dma_start(T.IV[:, lo:hi], T.iv[:, lo:hi])], [], [A("IV", lo, hi)], 256 * (hi - lo))
     dma(lambda e: [e.dma_start(T.DLB[0:128, :], T.lb[:]), e.dma_start(T.DLB[128:240, :], T.lb[0:112, :])], [], [A("DLB", 0, 24)], 24576, n=2)
-    dma(lambda e: [e.dma_start(T.KDI[:], T.kd[:])], [], [A("KDI", 0, NV)], 786432)
     dma(lambda e: [e.dma_start(T.LVI[:], T.lv[:]), e.dma_start(T.LBI[:, 0:24], T.lb[:])], [], [A("LVI", 0, 24), A("LBI", 0, 24)], 24576, n=2)
-    dma(lambda e: [e.dma_start(T.BK[:], T.bk[:])], [], [A("BK", 0, NB)], 1048576)
-    dma(lambda e: [e.dma_start(T.LF[:], T.lf[:])], [], [A("LF", 0, NL)], 1310720)
+    for name, nbytes in LOADS:
+        dma(lambda e, name=name: [e.dma_start(T[name][:], T[name[:2].lower()][:])], [], [A(name, 0, SCRATCH[name][1][1])], nbytes)
     send([(T.DLB[rot(t):rot(t) + 128, :], A("DLB", 0, 24), t, A("LBI", 24 * t, 24 * t + 24), "a_lb%d" % t) for t in range(1, NT)],
          lambda k: [2 * k, 2 * k + 1], 12288, 4.0)
 
+    def bit(b, lo, hi):
+        return [[0, 16 >> b], [hi - lo, 2]] + ([[0, 1 << b]] if b else []), lo
     for b in range(4):
-        iota(A("XB", 32 * b, 32 * b + 32), [[0, 16 >> b], [-2, 2]] + ([[0, 1 << b]] if b else []), 1)
+        iota(row(b), *bit(b, 1, -1))
     iota(A("OI", 0, 8), [[-16, 8]], 16, 1)
     ms(A("PT", 0, 112), 0.0)
     ms(A("PT", 16, 17), 1.0)
-    turn(A("TB", 0, 128), A("XB", 0, 128))
+    turn(0, 4)
     ts(A("OU", 0, 8), A("OI", 0, 8), 32.0, None, ALU.min)
     for b, n in ((0, 1), (2, 4)):
         ts(A("PT", 16 + n, 16 + 2 * n), A("PT", 16, 16 + n), col(b), None, ALU.mult)
         ts(A("PT", 16 + 2 * n, 16 + 3 * n), A("PT", 16, 16 + n), col(b + 1), None, ALU.mult)
         ts(A("PT", 16 + 3 * n, 16 + 4 * n), A("PT", 16, 16 + n), col(b), col(b + 1), ALU.mult, ALU.mult)
     cp(Hb, A("PT", 0, 48), A("OU", 0, 8))
-    for b, (m, a) in enumerate(((-8.0, 24.0), (-1.5, 2.5), (-7.5, 8.5), (-127.5, 128.5))):
-        ts(cc(b), col(b), m, a, ALU.mult, ALU.add)
-    ts(cc(4), cc(0), cc(1), cc(2), ALU.mult, ALU.mult)
-    ts(A("KK", 0, 128), Hb, cc(4), cc(3), ALU.mult, ALU.mult)
+    for b, (lo, hi) in enumerate(((16, 32), (1, 4), (1, 16), (1, 256))):
+        iota(row(4 + b), *bit(b, lo, hi))
+    turn(4, 8)
+    ts(A("CC", 0, 1), col(4), col(5), col(6), ALU.mult, ALU.mult)
+    ts(A("KK", 0, 128), Hb, A("CC", 0, 1), col(7), ALU.mult, ALU.mult)
     ms(A("RS", 0, 512), 1.0)
     ms(A("RS", 0, 512, 16), 2.0 ** 23)
-    ms(A("MK", 0, 256), 1.0)
-    select(A("MK", 0, 256), A("MK", 0, 256), [[0, 32], [-16, 8]], ALU.is_ge, 0.0, 0, 1)
-    select(A("MK", 0, 256), A("MK", 0, 256), [[0, 32], [16, 8]], ALU.is_ge, 0.0, 15, -1)
-    iota(A("EI", 0, 16), [[1, 8], [16, 2]])
-    ts(cc(9), col(3), -4.0, 4.0, ALU.mult, ALU.add)
-    ts(A("EL", 0, 16), A("EI", 0, 16), cc(9), None, ALU.add)
-    iota(A("XB", 128, 160), [[0, 2], [1, 16]])
-    ms(A("XB", 160, 320), 0.0)
-    for b, rows in ((8, ((0, 680), (1, -8), (2, -32), (4, -128), (8, -512))), (5, [(r, 64 ** r) for r in range(4)]),
-                    (6, [(4 + r, 64 ** r) for r in range(4)]), (7, ((8, 256), (9, 1), (10, 2048))), (9, ((10, 1), (11, 1)))):
-        for r, v in rows:
-            fill(A("XB", 32 * b + r, 32 * b + 32, 16), v)
-    for h in (0, 16):
-        fill(A("XB", 288 + h, 296 + h), -1)
-    turn(A("TB", 128, 160), A("XB", 128, 160))
-    turn(A("TB", 256, 288), A("XB", 256, 288))
+    iota(row(P16), [[0, 2], [1, 16]])
+    iota(row(Q16), [[16, 2], [0, 16]], 0, 1)
+    iota(row(P8), [[0, 4], [1, 8]])
+    ms(row(PSW), 0.0)
+    for r, v in ((0, 680), (1, -8), (4, -32), (2, -128), (8, -512)):
+        fill(row(PSW, r, 32, 16), v)
+    turn(P16, Q32)
+    iota(A("MI", 0, 256), [[0, 4], [16, 8], [0, 8]])
+    ts(A("MK", 0, 256), A("MI", 0, 256), col(Q16), None, ALU.is_equal)
+    iota(A("EI", 0, 16), [[8, 4], [0, 4]])
+    iota(A("EI", 16, 28), [[0, 2], [8, 3], [0, 2]])
+    ts(A("EL", 0, 28), A("EI", 0, 28), col(P8), None, ALU.add)
     ms(A("SS", 0, 240), 0.0)
-    ts(A("SS", 112, 128), A("XB", 128, 144), col(4), None, ALU.is_equal)
-    cp(A("HFL", 0, 128), Hb)
+    ts(A("SS", 112, 128), row(P16, 0, 16), col(P16), None, ALU.is_equal)
+    cp(A("HFL", 0, 128), Hb, gp=True)
     ts(A("PK8", 0, 8), A("PT", 17, 32, 2), 8.0, None, ALU.mult)
     tt(A("PT", 48, 56), A("PT", 16, 32, 2), A("PK8", 0, 8), ALU.add)
     cp(A("PKM", 0, 128), A("PT", 32, 80), A("OU", 0, 8))
-    cp(A("PT", 90, 91), col(8))
-    ts(A("PT", 91, 92), col(4), 0.0, 16.0, ALU.is_equal, ALU.mult)
+    cp(A("PT", 90, 91), col(PSW), gp=True)
+    ts(A("PT", 91, 92), col(P16), 0.0, 16.0, ALU.is_equal, ALU.mult)
     cp(A("PSM", 0, 128), A("PT", 64, 112), A("OU", 0, 8))
-    iota(A("IOT", 0, 256), [[1, 256]])
-    ms(A("IOT", 0, 256, 1, 0, 1), 1.0)
-    ms(A("DW", 0, 768), 0.0)
-    iota(A("DH", 0, 48), [[16, 6], [0, 8]])
-    cp(A("DW", 8, 768, 16, 0, 1), A("DH", 0, 48, 1, 0, 1))
-    ms(A("DW", 9, 768, 16, 64, 65), 16.0)
     tag[0] = "K2"
-    turn(A("TB", 160, 256), A("XB", 160, 256))
-    turn(A("TB", 288, 320), A("XB", 288, 320))
-    fill(A("ONE", 0, 128), 1)
-    for n, v in (("I32", 32), ("I512", 512), ("I8192", 8192), ("N32", -32)):
-        fill(IDm(n), v)
-        select(IDm(n), IDm(n), [[-1, 128]], ALU.is_equal, 0.0, 0, 1)
-    ts(IDm("SGN"), IDm("I32"), col(9), None, ALU.mult)
-    select(A("TRI", 0, 128), A("ONE", 0, 128), [[1, 128]], ALU.is_gt, 0.0, 0, -1)
-    select(A("TRI", 0, 128), A("TRI", 0, 128), [[1, 128]], ALU.not_equal, -1024.0, 0, -1)
-    fill(A("RT", 0, 256), 1)
+    iota(row(Q32), [[0, 16], [128, 2]], 0, 1)
+    iota(row(H16), [[1, 16], [0, 2]])
+    iota(row(B8), *bit(3, 0, 8))
+    ms(A("XB", 32 * HEAVY, 32 * YSC), 0.0)
+    for r in range(4):
+        put(row(HEAVY, r, 32, 16), 64.0 ** r * 2.0 ** 26)
+        fill(row(LIGHT, 4 + r, 32, 16), 64 ** r)
+    for b, r, v in ((PAY, 10, 2.0 ** -17), (PAY, 11, 2.0 ** -9), (TOP, 10, 2.0 ** -17)):
+        put(row(b, r, 32, 16), v)
+    for b, r in ((TOP, 11), (SIGN, 10), (SIGN, 11)):
+        fill(row(b, r, 32, 16), 1)
+    for h in (0, 16):
+        fill(row(SIGN, h, h + 8), -1)
+    fill(row(YSC), 1)
+    for p in (0, 32):
+        out = row(YSC, (3 - p) % 5, 32, 5)
+        select(out, out, [[0, cnt(out)]], ALU.not_equal, 0.25, -p, 1)
+    turn(Q32, YSC + 1)
+    for z in range(2):
+        iota(A("MI", 256 + 96 * z, 352 + 96 * z), [[0, 3], [32, 4], [0, 8]], 128 * z)
+    ts(A("MK", 256, 448), A("MI", 256, 448), col(Q32), None, ALU.is_equal)
+    ms(A("SS", 240, 480), 0.0)
+    ts(A("SS", 352, 368), row(P16, 0, 16), col(H16), None, ALU.is_equal)
+    fill(A("ZR", 0, 136), 0)
+    for n, v in (("I1", 1.0), ("I16", 16.0), ("I256", 256.0), ("NEG", -2.0 ** 24)):
+        select(IDm(n), A("ZR", 0, 128), [[-1, 128]], ALU.not_equal, v, 0, 1)
+    fill(A("NON", 0, 128), -64)
+    select(A("TRI", 0, 128), A("NON", 0, 128), [[1, 128]], ALU.is_gt, 0.0, 0, -1)
+    select(A("TRI", 0, 128), A("TRI", 0, 128), [[1, 128]], ALU.not_equal, 64.0 * CAP, 0, -1)
+    select(A("CM", 0, 24), A("ZR", 0, 24), [[0, 24]], ALU.is_gt, 2.0 ** -12, 0, 0)
+    fill(A("RT", 0, 256), -2)
     fill(A("RT", 0, 256, 32), 1 << 23)
     fill(A("CF", 0, 40), 0)
     fill(A("CF", 0, 40, 5), -1)
-    cp(A("HA", 128, 256), Hb)
+    cp(A("HA", 128, 256), Hb, gp=True)
     ts(A("HA", 256, 512), A("HA", 0, 256), -1.0, None, ALU.mult)
-    ts(A("HA", 512, 1024), A("HA", 0, 512), 16.0, None, ALU.mult)
-    ts(A("HA", 1024, 1536), A("HA", 512, 1024), 16.0 ** 3, None, ALU.mult)
-    ts(A("HA", 1536, 2560), A("HA", 512, 1536), 16.0 ** 6, None, ALU.mult)
-    ts(A("HA", 2560, 3072), A("HA", 512, 1024), 16.0 ** 12, None, ALU.mult)
-    ts(A("HB", 128, 256), Hb, 256.0, None, ALU.mult)
-    ts(A("HB", 256, 384), Hb, 256.0 ** 2, None, ALU.mult)
-    ts(A("HB", 384, 640), A("HB", 128, 384), 256.0 ** 2, None, ALU.mult)
-    ts(A("HB", 640, 1024), A("HB", 128, 512), 256.0 ** 4, None, ALU.mult)
-    fill(A("PM", 0, 272), 0)
-    for y in range(2):
-        select(A("PM", 136 * y + 8, 136 * y + 136), A("ONE", 0, 128), [[-16, 8], [1024, 2], [-2, 8]], ALU.is_equal, 0.0, y - 1, 1)
-    ts(cc(6), col(7), 2.0 ** -27, None, ALU.mult)
-    ts(cc(10), col(4), 11.0, 1.0 / 256, ALU.is_equal, ALU.mult)
-    fill(A("PW", 0, 160), 0)
-    iota(A("WI", 0, 17), [[-1, 17]], 16)
-    iota(A("WI", 18, 27), [[16, 9]], 16, 1)
-    iota(A("WI", 27, 28), [[0, 1]], 0, 1)
-    ts(cc(11), A("WI", 27, 28), col(4), -33.0 / 16, ALU.subtract, ALU.mult)
-    ts(A("WO", 0, 9), A("WI", 18, 27), cc(11), 33.0, ALU.add, ALU.min)
-    ts(cc(5), col(5), 2.0 ** 26, None, ALU.mult)
-    for w, c in enumerate((cc(5), col(6), cc(6))):
-        if w < 2:
-            ts(A("PW", 48 * w + 17, 48 * w + 33), A("ONE", 0, 16), c, None, ALU.mult)
-        else:
-            ts(A("PW", 113, 129), A("WI", 1, 17), cc(10), c, ALU.mult, ALU.add)
-            ts(A("PW", 112, 113), cc(10), 16.0, None, ALU.mult)
-        cp(A("WR", 272 * w, 272 * w + 144), A("PW", 48 * w, 48 * w + 48), A("WO", 0, 9))
-        gcp(A("WR", 272 * w + 136, 272 * w + 272), A("WR", 272 * w, 272 * w + 136))
-        ts(A("W24", 8 * w, 8 * w + 8), A("HA", 0, 128, 16), c, None, ALU.mult)
-    ts(cc(7), A("PT", 31, 32), 64.0, None, ALU.mult)
-    ts(cc(8), A("PT", 31, 32), -64.0, None, ALU.mult)
-    for nm, par, c in (("FD", 1, 7), ("FD", 0, 8), ("FS", 1, 8), ("FS", 0, 7)):
-        out = A(nm, par, 256, 2)
-        ts(out, Hb, cc(c), 0.0, ALU.mult, ALU.max, s=act(out, Hb, ACT.Relu, 0.0, cc(c)))
+    ts(A("HA", 512, 1024), A("HA", 0, 512), 256.0 ** 3, None, ALU.mult)
+    ts(A("HA", 1024, 1536), A("HA", 0, 512), 256.0 ** 6, None, ALU.mult)
+    ts(HBm(1), Hb, 256.0, None, ALU.mult)
+    ts(HBm(2), Hb, 256.0 ** 2, None, ALU.mult)
+    ts(A("HB", 256, 512), A("HB", 0, 256), 256.0 ** 3, None, ALU.mult)
+    ts(HBm(7), HBm(1), 256.0 ** 6, None, ALU.mult)
+    iota(A("WI", 0, 272), [[0, 16], [-1, 17]], 17)
+    select(A("WI", 0, 272), A("WI", 0, 272), [[0, 2], [-16, 8], [0, 17]], ALU.is_ge, 0.0, 0, 1)
+    select(A("WI", 0, 272), A("WI", 0, 272), [[0, 2], [16, 8], [0, 17]], ALU.is_ge, 0.0, 15, -1)
+    for w, b in enumerate((HEAVY, LIGHT)):
+        ts(A("WR", 272 * w, 272 * w + 272), A("WI", 0, 272), 1.0, col(b), ALU.min, ALU.mult)
+    ts(A("WR", 544, 816), A("WI", 0, 272), col(PAY), col(TOP), ALU.mult, ALU.min)
+    fill(A("WR", 0, 544, 17), 0)
+    for w in range(2):
+        gcp(A("W24", 8 * w, 8 * w + 8), A("WR", 272 * w + 1, 272 * w + 136, 17))
+    select(A("W24", 16, 24), A("WR", 545, 680, 17), [[-16, 8]], ALU.not_equal, 0.0, -11, 1)
+    select(A("SW", 0, 136), A("ZR", 0, 136), [[-16, 8], [1, 17]], ALU.not_equal, 2.0 ** -24, -16, 1)
+    for par, c in ((0, 2.0 ** 18), (1, -2.0 ** 18)):
+        out = A("FD", par, 256, 2)
+        ts(out, Hb, c, 0.0, ALU.mult, ALU.max, s=act(out, Hb, ACT.Relu, 0.0, c))
+        cp(A("FS", 1 - par, 256, 2), out, gp=True)
     for t in range(NT):
         iota(A("RI", 2 * t, 2 * t + 2), [[0, 2]], SH[t], 1)
     iota(A("RF", 10, 20), [[0, 5], [16, 2]])
     ts(A("RI", 0, 10), A("RI", 0, 10), 7, None, ALU.bitwise_and)
     tt(A("RF", 0, 10), A("RI", 0, 10), A("RF", 10, 20), ALU.add)
-    ts(A("RF", 10, 20), A("RF", 0, 10), cc(9), 23.0, ALU.add, ALU.min)
+    ts(A("RF", 10, 20), A("RF", 0, 10), col(B8), 23.0, ALU.add, ALU.min)
     ts(A("RL", 0, 10), A("RF", 10, 20), 17.0, 16.0, ALU.mult, ALU.add)
     ts(A("RL", 10, 20), A("RF", 10, 20), 32.0, 31.0, ALU.mult, ALU.add)
     iota(A("L5F", 0, 8), [[16, 8]], -2)
-    ts(A("L5F", 0, 8), A("L5F", 0, 8), col(4), 0.2, ALU.add, ALU.mult)
-    cp(A("L5I", 0, 8), A("L5F", 0, 8))
+    ts(A("L5I", 0, 8), A("L5F", 0, 8), col(P16), 0.2, ALU.add, ALU.mult)
     gcp(A("L5", 0, 8), A("L5I", 0, 8))
     fill(A("MG", 0, 160), 0)
     fill(A("FF", 0, 608), 0)
     for t in range(NT):
         fill(A("FF", 120 * slot(t), 120 * slot(t) + 120, 5), (rank + t) % NR + 1)
 
-    def to_list(sb, ncol, run, scale, bits, out):
-        e0, l0 = 256 * sb, 64 * sb
-        ts(A("LI", l0, l0 + ncol), A("SC", 512 * sb + run - 1, 512 * sb + run * ncol, run), scale, None, ALU.mult)
-        ts(A("LI", l0 + 32, l0 + 32 + ncol), A("LI", l0, l0 + ncol), bits, None, ALU.bitwise_and)
-        tt(A("E", e0, e0 + 256), A("LI", l0 + 32, l0 + 64), A("MK", 0, 256), ALU.mult, off=A("EL", 0, 16))
-        b = bank(6, 32 * sb, 32 * sb + ncol)
-        mm(b, [(A("SS", 112 - 16 * q, 240 - 16 * q), A("E", e0 + 32 * q, e0 + 32 * q + ncol)) for q in range(8)])
+    def to_list(sb, words, bits, lanes, shift, out):
+        n, e0, l0 = cnt(words), 256 * sb, 64 * sb
+        ts(A("LI", l0, l0 + n), words, bits, None, ALU.bitwise_and)
+        tt(A("E", e0, e0 + 8 * n), A("LI", l0, l0 + n), A("MK", 256 * lanes, 256 * lanes + 8 * n), ALU.mult, off=A("EL", 16 * lanes, 16 * lanes + n // 2))
+        b = bank(6, 32 * sb, 32 * sb + n)
+        s0 = [240 * lanes + 112 - 16 * ((q + shift) % 8) for q in range(8)]
+        mm(b, [(A("SS", s0[q], s0[q] + 128), A("E", e0 + q, e0 + 8 * n, 8)) for q in range(8)])
         cp(out, b)
 
     tag[0] = "N"
     for c in range(3):
-        lo, hi = 512 * c, 512 * c + 512
+        lo, hi, sb = 512 * c, 512 * c + 512, c % 2
         gcp(A("KDF", lo, hi), A("KDI", lo, hi))
         mm(bank(c, 0, 512), [(Hb, A("IV", lo, hi))])
         ts(A("TAU", lo, hi), bank(c, 0, 512), 1.0, -1.0, ALU.min, ALU.max, s=act(A("TAU", lo, hi), bank(c, 0, 512), ACT.Sign))
         mg([(bank(7, 128 * i, 128 * i + 128), A("TAU", lo + 128 * i, lo + 128 * i + 128), A("KK", 0, 128)) for i in range(4)])
-        least(A("SC", 512 * (c % 2), 512 * (c % 2) + 512), A("RS", 0, 512), bank(7, 0, 512))
-        to_list(c % 2, 32, 16, 1.0, 15, A("MU", 32 * c, 32 * c + 32))
+        least(A("SN", 512 * sb, 512 * sb + 512), A("RS", 0, 512), bank(7, 0, 512))
+        words = A("SN", 512 * sb + 15, 512 * sb + 512, 16)
+        if not SCANINT:
+            cp(A("LI", 64 * sb + 32, 64 * sb + 64), words)
+            words = A("LI", 64 * sb + 32, 64 * sb + 64)
+        to_list(sb, words, 15, 0, 0, A("MU", 32 * c, 32 * c + 32))
         cp(A("SG", lo, hi), HP, A("MU", 32 * c, 32 * c + 32))
         mm(bank(3 + c, 0, 512), [(A("HFL", 0, 128), A("KDF", lo, hi))])
     for c in range(3):
         lo, hi = 512 * c, 512 * c + 512
         tt(A("SI", lo, hi), bank(c, 0, 512), A("SG", lo, hi), ALU.mult)
-        mg([(bank(c, 0, 512), A("PSM", 0, 128), A("SG", lo, hi))] +
-           [(bank(c, 256 * h, 256 * h + 256), A("DW", 128 * (2 * c + h), 128 * (2 * c + h) + 128), A("IOT", 0, 256)) for h in range(2)] +
-           [(bank(c, 0, 512), A("PKM", 0, 128), A("SI", lo, hi))])
+        mm(bank(c, 0, 512), [(A("PSM", 0, 128), A("SG", lo, hi)), (A("PKM", 0, 128), A("SI", lo, hi))])
         cp(A("NTB", lo, hi), bank(c, 0, 512))
         tt(A("KS", lo, hi), bank(3 + c, 0, 512), A("SG", lo, hi), ALU.mult)
         mm(bank(3 + c, 0, 512), [(A("HFL", 0, 128), A("KS", lo, hi))])
@@ -388,86 +408,95 @@ def build(g, T, topo, core, rank):
     tag[0] = "A"
     gcp(A("LVU", 0, 24), A("LVI", 0, 24))
     cp(A("KA", 0, L), A("KP", 0, NV), A("LVU", 0, 24))
-    cp(A("NA", 0, L), A("NTB", 0, NV), A("LVU", 0, 24))
+    ts(A("LT", 0, L), A("NTB", 0, NV), col(SIGN), None, ALU.mult, off=A("LVU", 0, 24),
+       s=act(A("LT", 0, L), A("NTB", 0, NV), ACT.Identity, 0.0, col(SIGN), A("LVU", 0, 24)))
     spread("XA", 0, A("LF", 0, NL), "KA", 0)
 
     def xa(d):
         return A("XA", d, 16 * L, 16)
     for i in range(6):
-        b = bank((4, 5, 7, 2, 3, 4)[i], 0, L)
+        b = bank(2 + i % 3, 0, L)
         if i == 0:
-            mm(b, [(IDm("I32"), xa(0)), (IDm("SGN"), A("NA", 0, L))])
+            mm(b, [(IDm("I1"), xa(0)), (IDm("I1"), A("LT", 0, L))])
         else:
-            mm(b, [(IDm(n), xa(ASC[i] + j)) for j, n in enumerate(("I32", "I512", "I8192"))])
-        ts(A("AP", L * i, L * i + L), b, 1.0 / 32, None, ALU.mult)
+            mm(b, [(IDm(n), xa(ASC[i] + j)) for j, n in enumerate(("I1", "I16", "I256"))])
+        ts(A("AP", L * i, L * i + L), b, 16.0 ** ASC[i] / 256.0 ** (3 * (i // 2)), None, ALU.mult)
         if i == 0:
             send([(ap(A("AP", 0, L)), A("AP", 0, L), t, A("AP", 6 * L * t, 6 * L * t + L), "a_p0%d" % t) for t in range(1, NT)],
                  lambda k: [2 * k, 2 * k + 1], 98304)
+    def to_helper(e):
+        h = helpers(T, topo, rank)[0]
+        rid, pid, _se = topo.addr(h)
+        e.remote_dma(T.AP[:, L:6 * L], T.AP[:, L:6 * L], T.sem["relay"], T.sem["sent"], pid, rid, sum(1 << x for x in topo.engines(core, h)[-8:]))
+        return []
+    o = add([("G", to_helper, 0.4)], [A("AP", L, 6 * L)], [], send=8)
+    o = add([("X", None, HLAG)], [], [], arr=None, after=o, link=491520 * LINK / NEAR, via="R")
     for t in range(1, NT):
-        send([(ap(A("AP", L, 6 * L)), A("AP", L, 6 * L), t, A("AP", 6 * L * t + L, 6 * L * t + 6 * L), "a_pp%d" % t)], lambda k: list(range(8)), 491520)
-    mg([(bank(7, 128 * i, 128 * i + 128, 1, 40), A("CF", 0, 40), IDm("I32")) for i in range(3)], stop=False)
+        o = add([("X", None, 2.5)], [], [A("AP", 6 * L * t + L, 6 * L * t + 6 * L)], arr="a_pp%d" % t, n=8, after=o, link=491520, via="H")
+    mg([(bank(7, 128 * i, 128 * i + 128, 1, 40), A("CF", 0, 40), IDm("I1")) for i in range(3)], stop=False)
 
-    def home(t, out, land, sem):
-        send([(ap(out), out, -t, land, sem)], lambda k: list(range(8)), 12288)
+    def home(t, out, land, sem, nbytes):
+        send([(ap(out), out, -t, land, sem)], lambda k: list(range(8)), nbytes)
 
     def claims(t):
         tag[0] = "C%d" % t
-        x, sb = t % NXC, t % 2
+        sb = t % 2
         if t < 2:
             lo, hi = (0, 24) if t == 0 else (24, 120)
             gcp(A("LBU", lo, hi), A("LBI", lo, hi))
         cp(A("WU", L * t, L * t + L), A("BK", 0, NB), A("LBU", 24 * t, 24 * t + 24))
-        spread("XC", x, A("NTB", 0, NV), "WU", L * t)
+        gcp(A("WF", L * t, L * t + L), A("WU", L * t, L * t + L))
+        spread("XC", t, A("NTB", 0, NV), "WU", L * t)
         if t:
             ts(A("LT", L * t, L * t + L), A("AP", 6 * L * t, 6 * L * t + L), MAGIC, MAGIC, ALU.add, ALU.subtract)
-        else:
-            ts(A("LT", 0, L), A("NA", 0, L), col(9), None, ALU.mult)
         for i in range(3):
-            b = (3 * t + i) % 2
-            x0 = 16 * (L * x + 128 * i)
-            r0, n0 = 17 * rot(t) // 16, 272 * b
+            b = CB[(3 * t + i) % len(CB)]
+            x0, l0, r0 = 16 * (L * t + 128 * i), L * t + 128 * i, 17 * rot(t) // 16
 
             def lane(w, c0):
-                return (bank(b, c0, c0 + 136), A("LT", L * t + 128 * i, L * t + 128 * i + 128), A("WR", 272 * w + r0, 272 * w + r0 + 136))
+                return (bank(b, c0, c0 + 136), A("LT", l0, l0 + 128), A("WR", 272 * w + r0, 272 * w + r0 + 136))
 
             def slots(hi, w0, w1):
                 return [(bank(b, 16 - k, hi, 17), A("XC", x0 + k, x0 + 2048, 16), A("W24", w0, w1)) for k in range(16)]
-            out = A("SC", 512 * sb + 136 * i, 512 * sb + 136 * i + 136)
+            def nodes(c0):
+                return (bank(b, c0, c0 + 136), A("WF", l0, l0 + 128), A("SW", 0, 136))
+            out, ne = A("SC", 512 * sb + 136 * i, 512 * sb + 136 * i + 136), A("NE", 272 * i, 272 * i + 136)
             if t in TWICE:
-                mg([lane(0, 0)] + slots(136, 0, 8) + [lane(1, 0), lane(2, 136)] + slots(272, 8, 24))
-                nonzero(A("NE", n0, n0 + 136), bank(b, 0, 136))
-                lastfit(out, A("NE", n0, n0 + 136), bank(b, 136, 272))
+                mg([lane(0, 0)] + slots(136, 0, 8) + [lane(1, 0), lane(2, 136), nodes(136)] + slots(272, 8, 24))
+                nonzero(ne, bank(b, 0, 136))
+                lastfit(out, ne, bank(b, 136, 272))
             else:
-                mg([lane(w, 136 * w) for w in range(3)] + slots(408, 0, 24))
-                cp(A("NE", n0, n0 + 136), bank(b, 0, 136))
-                tt(A("NE", n0 + 136, n0 + 272), bank(b, 136, 272), A("NE", n0, n0 + 136), ALU.not_equal)
-                lastfit(out, A("NE", n0 + 136, n0 + 272), bank(b, 272, 408))
-        to_list(sb, 24, 17, 2.0 ** 23, 2047, A("WL", 24 * t, 24 * t + 24))
-        out = A("R1", 32 * (t - 1), 32 * t) if t else A("V1", 96, 128)
-        win, off = A("SC", 512 * sb, 512 * sb + 512), A("RL", 2 * t, 2 * t + 2)
-        ts(out, win, -1.0, None, ALU.add, off=off, s=act(out, win, ACT.Identity, -1.0, 1.0, off))
+                mg([lane(w, 136 * w) for w in range(3)] + [nodes(272)] + slots(408, 0, 24))
+                cp(ne, bank(b, 0, 136))
+                both = A("NE", 272 * i + 136, 272 * i + 272)
+                tt(both, bank(b, 136, 272), ne, ALU.not_equal)
+                lastfit(out, both, bank(b, 272, 408))
+        r0 = 32 * (t - 1) if t else 96
+        name = "R1" if t else "V1"
+        ts(A(name, r0, r0 + 32), A("SC", 512 * sb, 512 * sb + 408), 2.0 ** 24, -NONE, ALU.mult, ALU.add, off=A("RL", 2 * t, 2 * t + 2))
         if t:
-            home(t, A("R1", 32 * (t - 1), 32 * (t - 1) + 24), A("V1", 24 * (t - 1), 24 * t), "a_v1%d" % t)
+            home(t, A("R1", r0, r0 + 24), A("V1", 24 * (t - 1), 24 * t), "a_v1%d" % t, 12288)
+        to_list(sb, A(name, r0, r0 + 24), 2047, 1, SH[t], A("WL", 24 * t, 24 * t + 24))
 
     def tests(t):
         tag[0] = "T%d" % t
-        x, a0, d0 = t % NXT, 6 * L * t, 768 * (t % 2)
-        k0, x0, lf = L * (t % 2), 8 * L * x, A("LF", 0, NL)
+        a0, d0 = 6 * L * t, 768 * (t % 2)
+        k0, x0, lf = L * t, 8 * L * (t % 2), A("LF", 0, NL)
         cp(A("KG", k0, k0 + L), A("KP", 0, NV), A("WL", 24 * t, 24 * t + 24))
-        mg([(bank(5, 128 + 192 * y, 320 + 192 * y), A("PM", 136 * y + 8 - 8 * h, 136 * y + 136 - 8 * h), A("KG", k0 + h, k0 + L, 2))
-            for y in range(2) for h in range(2)])
-        cp(A("KL", k0, k0 + L), bank(5, 128, 512))
+        dma(lambda e: [e.dma_start(T.DK[16 * t + z:16 * t + 16:2, :], T.KG[:, k0 + 192 * z:k0 + 192 * z + 192]) for z in range(2)],
+            [A("KG", k0, k0 + L)], [A("DK", t, t + 1)], 98304, n=2)
+        dma(lambda e: [e.dma_start(T.KL[:, k0:k0 + L], T.DK[16 * t:16 * t + 16, :])], [A("DK", t, t + 1)], [A("KL", k0, k0 + L)], 98304)
         for c, n in [(0, 128), (128, 128)] + ([(256, 128)] if t < NT - 1 else [(256, 64), (320, 64)]):
-            out, off, even = A("XT", x0 + 8 * c, x0 + 8 * (c + n)), A("KL", k0 + c // 2, k0 + (c + n) // 2), A("KL", k0 + 192 + c // 2, k0 + 192 + (c + n) // 2)
-            ts(out, lf, 16.0, None, ALU.mult, off=off, s=act(out, lf, ACT.Identity, 0.0, 16.0, off))
-            apart = (t, c) in SPLIT
+            out, even, odd = A("XT", x0 + 8 * c, x0 + 8 * (c + n)), A("KL", k0 + c // 2, k0 + (c + n) // 2), A("KL", k0 + 192 + c // 2, k0 + 192 + (c + n) // 2)
+            ts(out, lf, 16.0, None, ALU.mult, off=odd, s=act(out, lf, ACT.Identity, 0.0, 16.0, odd))
+            apart, y0 = (t, c) in SPLIT, 8 * L * (t % 2)
             if apart:
-                cp(A("XA", 8 * c, 8 * (c + n)), lf, even)
+                cp(A("XA", y0 + 8 * c, y0 + 8 * (c + n)), lf, even)
             else:
                 tt(out, lf, out, ALU.add, off=even)
 
             def two_kids(i):
-                return [(HBm(i), A("XT", x0 + 8 * c + i, x0 + 8 * (c + n), 8))] + ([(HBm(i), A("XA", 8 * c + i, 8 * (c + n), 8))] if apart else [])
+                return [(HBm(i), A("XT", x0 + 8 * c + i, x0 + 8 * (c + n), 8))] + ([(HBm(i), A("XA", y0 + 8 * c + i, y0 + 8 * (c + n), 8))] if apart else [])
             b = 2 + c // 128
             for y in range(2):
                 def piece(i):
@@ -481,9 +510,9 @@ def build(g, T, topo, core, rank):
                 mm(bank(b, 256, 512), [(A("BD", c0, c0 + 128), A("FD", 0, 256)), (A("BD", c0 + 128, c0 + 256), A("FS", 0, 256))])
                 least(A("SD", c0, c0 + 256), A("RT", 0, 256), bank(b, 256, 512))
         out = A("R2", 32 * (t - 1), 32 * t) if t else A("V2", 96, 128)
-        ts(out, A("SD", d0, d0 + 768), 32.0, None, ALU.min, off=A("RL", 10 + 2 * t, 12 + 2 * t))
+        ts(out, A("SD", d0, d0 + 768), 61.0, 2.0 ** 20, ALU.add, ALU.min, off=A("RL", 10 + 2 * t, 12 + 2 * t))
         if t:
-            home(t, A("R2", 32 * (t - 1), 32 * (t - 1) + 24), A("V2", 24 * (t - 1), 24 * t), "a_v2%d" % t)
+            home(t, A("R2", 32 * (t - 1), 32 * (t - 1) + 24), A("V2", 24 * (t - 1), 24 * t), "a_v2%d" % t, 6144)
 
     def v(name, t):
         return A(name, 24 * slot(t), 24 * slot(t) + 24)
@@ -491,38 +520,34 @@ def build(g, T, topo, core, rank):
     def tested(t):
         tag[0] = "L%d" % t
         if t:
-            mm(bank(5, 64, 88), [(IDm("N32"), A("MG", 32 * s, 32 * s + 24)) for s in range(t)])
-            tt(A("CD", 0, 24), v("V1", t), bank(5, 64, 88), ALU.is_lt)
+            mm(bank(6, 64, 88), [(IDm("NEG"), A("MG", 32 * s, 32 * s + 24)) for s in range(t)])
+            tt(A("CD", 0, 24), v("V1", t), bank(6, 64, 88), ALU.is_lt)
         else:
             ts(A("CD", 0, 24), v("V1", t), 0.0, None, ALU.is_lt)
-        mg([(bank(5, 96, 120), A("TRI", 0, 128), A("CD", 0, 24)), (bank(5, 104, 120), A("ONE", 0, 128), A("CD", 0, 16)),
-            (bank(5, 112, 120), A("ONE", 0, 128), A("CD", 0, 8))])
-        ts(v("UU", t), bank(5, 96, 120), CAP - 1024.0, 32.0, ALU.is_lt, ALU.mult)
+        mg([(bank(6, 96, 120), A("NON", 0, 128), A("CM", 0, 24)), (bank(6, 96, 120), A("TRI", 0, 128), A("CD", 0, 24)),
+            (bank(6, 104, 120), A("NON", 0, 128), A("CD", 0, 16)), (bank(6, 112, 120), A("NON", 0, 128), A("CD", 0, 8))])
 
     def merged(t):
         tag[0] = "M%d" % t
-        tt(A("MG", 32 * t, 32 * t + 24), v("V2", t), v("UU", t), ALU.is_lt)
+        tt(A("MG", 32 * t, 32 * t + 24), v("V2", t), bank(6, 96, 120), ALU.is_lt)
 
     def fields():
         tag[0] = "F"
-        ts(A("VI", 0, 120), A("V1", 0, 120), 1.0, 2.0 ** 23, ALU.add, ALU.mult)
-        ts(A("FF", 1, 600, 5), A("VI", 0, 120), 2047, None, ALU.bitwise_and)
-        for b in range(4):
-            ts(A("VB", 120 * b, 120 * b + 120), A("VI", 0, 120), 11 + b, 1 << b, ALU.logical_shift_right, ALU.bitwise_and)
-        tt(A("VC", 0, 240), A("VB", 0, 240), A("VB", 240, 480), ALU.add)
-        tt(A("FF", 2, 600, 5), A("VC", 0, 120), A("VC", 120, 240), ALU.add)
+        ts(A("FF", 1, 600, 5), A("V1", 0, 120), 2047, None, ALU.bitwise_and)
+        for b in range(2):
+            ts(A("VB", 120 * b, 120 * b + 120), A("V1", 0, 120), 11 + 3 * b, 5 << b, ALU.logical_shift_right, ALU.bitwise_and)
+        tt(A("FF", 2, 600, 5), A("VB", 0, 120), A("VB", 120, 240), ALU.add)
 
     def store(t):
         tag[0] = "O%d" % t
         f0 = 120 * slot(t)
         if t not in (2, 3):
             n = 72 if t == 1 else 24
-            v2, sb = A("V2", 24 * slot(t), 24 * slot(t) + n), A("SB", 24 * slot(t), 24 * slot(t) + n)
-            ts(A("FF", f0 + 3, f0 + 5 * n, 5), v2, 1, None, ALU.logical_shift_right)
-            ts(sb, v2, 1, None, ALU.bitwise_and)
-            ts(A("FF", f0 + 4, f0 + 5 * n, 5), sb, -2.0, 1.0, ALU.mult, ALU.add)
+            v2 = A("V2", 24 * slot(t), 24 * slot(t) + n)
+            ts(A("FF", f0 + 3, f0 + 5 * n, 5), v2, MAGIC / 4, MAGIC / 4, ALU.add, ALU.subtract)
+            tt(A("FF", f0 + 4, f0 + 5 * n, 5), A("FF", f0 + 3, f0 + 5 * n, 5), v2, ALU.subtract)
         tt(A("FP", 128 * t, 128 * t + 128), A("MG", 32 * t, 32 * t + 32), A("FF", f0, f0 + 128), ALU.mult, off=A("L5", 0, 8))
-        mg([(bank(7, 128 * i, 128 * i + 128, 1, 40), A("FP", 128 * t + 40 * i, 128 * t + 40 * i + 40), IDm("I32")) for i in range(3)],
+        mg([(bank(7, 128 * i, 128 * i + 128, 1, 40), A("FP", 128 * t + 40 * i, 128 * t + 40 * i + 40), IDm("I1")) for i in range(3)],
            start=False, stop=t == NT - 1)
 
     for part in PARTS:
@@ -534,9 +559,12 @@ def build(g, T, topo, core, rank):
         merged(t)
     for t in range(NT):
         store(t)
-    ts(A("YS", 0, L, 1, 0, 40), bank(7, 0, L, 1, 40), 1.0 / 32, None, ALU.mult)
+    ts(A("YS", 0, L, 1, 0, 40), bank(7, 0, L, 1, 40), col(YSC, 40), None, ALU.mult)
     dma(lambda e: [e.dma_start(T.y[:], T.YS[0:40, :])], [A("YS", 0, L)], [], 61440)
     return ops
+
+
+LOADS = (("BK", 1048576), ("KDI", 786432), ("LF", 1310720))
 
 
 def depend(ops):
@@ -607,8 +635,6 @@ def schedule(ops, deps):
         i, k = x
         if ops[i]["tag"] not in RANK:
             return (2, -due[i] - (OWN if k == 0 and len(alts[i]) > 1 else 0.0), -i)
-        if EDF:
-            return (1, -due[i], -i)
         return (alts[i][k][1] < 1, -RANK.index(ops[i]["tag"]), -i)
     banks = [{a[0] for a in o["r"] + o["w"] if SCRATCH[a[0]][0] == "psum"} for o in ops]
     held = {}
@@ -713,11 +739,12 @@ def schedule(ops, deps):
                 p[j] = p[i] + 1e-5
         elif u < 0.5:
             i = i if len(alts[i]) > 1 else flex[int(rng.integers(0, len(flex)))]
-            c[i] = 1 - c[i]
+            was = c[i]
+            c[i] = (was + int(rng.integers(1, len(alts[i])))) % len(alts[i])
             if u < 0.45:
                 j = flex[int(rng.integers(0, len(flex)))]
-                if c[j] == c[i] and j != i and abs(alts[j][0][1] - alts[i][0][1]) < 0.3:
-                    c[j] = 1 - c[j]
+                if c[j] == c[i] and j != i and was < len(alts[j]) and abs(alts[j][0][1] - alts[i][0][1]) < 0.3:
+                    c[j] = was
         elif u < 0.75:
             i = i if u < 0.65 else int(rng.integers(0, n))
             back(p, deps, i, p[i] + float(rng.normal()) * 2.0)
@@ -750,9 +777,193 @@ def back(p, deps, i, t):
             todo += [(k, x - 1e-5) for k in deps[j]]
 
 
+def place(order, links, alts, banks, fixed):
+    n = len(alts)
+    st, fin, ch = [0.0] * n, [0.0] * n, [0] * n
+    busy = {e: ([], [], 0.0) for e in "VSPGYLHR"}
+    busy.update({"B%d" % b: ([], [], LAT) for b in range(8)})
+    for i in order:
+        t0 = 0.0
+        for j, x in links[i]:
+            if fin[j] + x > t0:
+                t0 = fin[j] + x
+        best = 1e9
+        for k in (fixed[i],) if fixed[i] >= 0 else range(len(alts[i])):
+            e, c = alts[i][k]
+            res = [busy[e]] + [busy[b] for b in banks[i]]
+            t, moved = t0, True
+            while moved:
+                moved = False
+                for a, z, w in res:
+                    x = y = len(z)
+                    while x and z[x - 1] > t:
+                        x -= 1
+                    w += c - 1e-9
+                    while x < y and a[x] < t + w:
+                        t, x, moved = z[x], x + 1, len(res) > 1
+            v = t + 2 * c if e == "V" else t + c
+            if v < best:
+                best, st[i], fin[i], ch[i], took = v, t, t + c, k, res
+        t = st[i]
+        for a, z, w in took:
+            x = len(a)
+            while x and a[x - 1] > t:
+                x -= 1
+            a.insert(x, t)
+            z.insert(x, fin[i] + w)
+    return st, fin, ch
+
+
+def schedule(ops, deps):
+    n = len(ops)
+    alts, lag = [], []
+    for o in ops:
+        e, _, c = o["alts"][0]
+        if e == "X":
+            alts.append([(o.get("via", "L"), o["link"] / LINK)])
+            lag.append(c)
+        elif "dma" in o:
+            alts.append([(e, 0.1 + o["bytes"] / 2.5e5)])
+            lag.append(2.0 if o["tag"] == "K" else DLAG)
+        else:
+            alts.append([(a[0], a[2]) for a in o["alts"]])
+            lag.append(LAT)
+    banks = [sorted({a[0] for a in o["r"] + o["w"] if SCRATCH[a[0]][0] == "psum"}) for o in ops]
+    pre, suc, before = [], [[] for _ in range(n)], []
+    for i in range(n):
+        m = 0
+        for j in deps[i]:
+            m |= before[j]
+        pre.append([(j, 0.0 if alts[i][0][0] == alts[j][0][0] in "PH" else lag[j]) for j in deps[i] if not m >> j & 1])
+        for j, x in pre[i]:
+            suc[j].append((i, x))
+        before.append(m | sum(1 << j for j in deps[i]))
+
+    def justify(s, fixed):
+        s = place(sorted(range(n), key=lambda i: (-s[1][i], -i)), suc, alts, banks, fixed)
+        return place(sorted(range(n), key=lambda i: (-s[1][i], i)), pre, alts, banks, fixed)
+
+    def value(s):
+        return max(s[1]) + WS * sum(s[1]) / n + WV * sum(alts[i][0][1] for i in flex if not s[2][i]) + WX * sum(s[1][i] for i in moves) / len(moves) + WH * s[1][relay]
+    relay = [i for i in range(n) if alts[i][0][0] == "R"][0]
+
+    def blocked(s):
+        st, fin, ch = s
+        ends = {}
+        for j in range(n):
+            for r in [alts[j][ch[j]][0]] + banks[j]:
+                ends[(r, round(fin[j] + (LAT if len(r) > 1 else 0.0), 6))] = j
+        pairs, i = [], max(range(n), key=lambda j: fin[j])
+        while st[i] > 1e-9:
+            j = [j for j, x in pre[i] if fin[j] + x > st[i] - 1e-7]
+            if not j:
+                j = [ends[k] for k in [(r, round(st[i], 6)) for r in [alts[i][ch[i]][0]] + banks[i]] if k in ends]
+                if not j:
+                    break
+                pairs.append((i, j[0]))
+            i = j[0]
+        return pairs
+    held = [None, None]
+    moves = [i for i in range(n) if alts[i][0][0] in "LYH"]
+    groups = {}
+    for i, o in enumerate(ops):
+        groups.setdefault(o["tag"], []).append(i)
+        groups.setdefault((o["tag"], o["w"][0][0] if o["w"] else ""), []).append(i)
+    groups = list(groups.values())
+    flex = [i for i in range(n) if len(alts[i]) > 1]
+    rng = np.random.default_rng(SEED)
+    fixed = [o.get("first", -1 if len(o["alts"]) > 1 else 0) for o in ops]
+    s = place(range(n), pre, alts, banks, fixed)
+    for _ in range(8):
+        s = justify(s, fixed)
+    now = best = (value(s), s, fixed)
+    for r in range(ROUNDS):
+        p, ch, fixed = list(now[1][0]), now[1][2], list(now[2])
+        u = rng.random()
+        if rng.random() < CRIT:
+            if held[0] is not now:
+                held[:] = [now, blocked(now[1])]
+            if not held[1]:
+                continue
+            i, j = held[1][int(rng.integers(0, len(held[1])))]
+            if u < 0.4:
+                p[i] = p[j] - 1e-4 - (rng.exponential() if u < 0.2 else 0.0)
+            elif u < 0.8 or len(alts[j]) == 1:
+                p[j] = p[i] + 1e-4 + (rng.exponential() if u < 0.6 else 0.0)
+                for k in range(j, n):
+                    for m, x in pre[k]:
+                        if p[k] <= p[m]:
+                            p[k] = p[m] + 1e-6
+            else:
+                fixed[j] = (ch[j] + int(rng.integers(1, len(alts[j])))) % len(alts[j])
+        elif u < 0.3:
+            for i in rng.integers(0, n, int(rng.integers(1, 4))):
+                p[i] += rng.normal() * 3.0
+        elif u < 0.55:
+            d = rng.normal() * rng.choice([1.0, 3.0, 8.0])
+            for i in groups[int(rng.integers(0, len(groups)))]:
+                p[i] += d
+        elif u < 0.8:
+            i = flex[int(rng.integers(0, len(flex)))]
+            fixed[i] = (ch[i] + int(rng.integers(1, len(alts[i])))) % len(alts[i])
+            like = [j for j in flex if ch[j] == fixed[i] and ch[i] < len(alts[j]) and abs(alts[j][0][1] - alts[i][0][1]) < 0.3 and abs(p[j] - p[i]) < 15]
+            if u < 0.7 and like:
+                fixed[like[int(rng.integers(0, len(like)))]] = ch[i]
+        else:
+            t0, w = rng.random() * max(now[1][1]), rng.choice([2.0, 8.0])
+            for i in range(n):
+                if t0 < p[i] < t0 + w:
+                    p[i] += rng.normal() * w / 8
+        for i in range(n - 1, -1, -1):
+            for j, x in pre[i]:
+                if p[j] >= p[i]:
+                    p[j] = p[i] - 1e-6
+        s = place(sorted(range(n), key=lambda i: p[i]), pre, alts, banks, fixed)
+        if rng.random() < 0.2:
+            s = justify(s, fixed)
+        v = value(s)
+        if v <= now[0] + HEAT * (1.0 - r / ROUNDS) * rng.exponential():
+            now = (v, s, fixed)
+            if v < best[0]:
+                best = now
+    PLAN["v"] = best[0]
+    st, fin, ch = best[1]
+    order = sorted(range(n), key=lambda i: (st[i], i))
+    last = {}
+    for i in order:
+        for b in banks[i]:
+            if b in last and last[b] not in deps[i]:
+                deps[i].append(last[b])
+            last[b] = i
+    return [(i, ch[i]) for i in order], fin
+
+
+def helpers(T, topo, rank):
+    c = T.cores[rank]
+    return [h for h in topo.cores_of(c) if h not in T.cores and topo.die(h) == topo.die(c)
+            and all(topo.may_write(h, T.cores[(rank + t) % NR]) for t in range(1, NT))][:NH]
+
+
+def hand_on(g, core, T, topo, rank):
+    hs = helpers(T, topo, rank)
+    k = hs.index(core)
+    to = [(T.cores[(rank + t) % NR], 6 * L * t, "a_pp%d" % t) for t in range(1 + k, NT, len(hs))]
+    to[1:1] = [(h, 0, "relay") for h in hs[k + 1:k + 2]]
+    g.wait_ge(T.sem["relay"], 8)
+    for c, c0, sem in to:
+        rid, pid, _se = topo.addr(c)
+        en = topo.engines(core, c)
+        g.remote_dma(T.AP[:, c0 + L:c0 + 6 * L], T.AP[:, L:6 * L], T.sem[sem], T.sem["sent"], pid, rid,
+                     sum(1 << x for x in (en[-8:] if sem == "relay" else en[:8])))
+    g.wait_ge(T.sem["sent"], 8 * len(to))
+
+
 def rank_program(g, core, T, topo):
     rank = T.rank_of(core)
     if rank is None:
+        for r in range(NR):
+            if core in helpers(T, topo, r):
+                hand_on(g, core, T, topo, r)
         return
     ops = build(g, T, topo, core, rank)
     if "order" not in PLAN:
@@ -761,7 +972,7 @@ def rank_program(g, core, T, topo):
     deps = PLAN["deps"]
     eng = {"V": g.vector, "S": g.scalar, "P": g.tensor, "G": g, "Y": g.sync}
     count = {e: 0 for e in "VSPG"}
-    token = {}
+    token, known, born = {}, {}, {}
     seen = {e: {} for e in eng}
     total = {}
     sent = 0
@@ -769,18 +980,22 @@ def rank_program(g, core, T, topo):
         o = ops[i]
         e, f, _ = o["alts"][k]
         if e == "X":
-            token[i] = (o["arr"], o["n"])
-            total[o["arr"]] = o["n"]
+            if o["arr"]:
+                token[i] = (o["arr"], o["n"])
+                total[o["arr"]] = o["n"]
+                born[token[i]] = len(born)
             continue
         need = {}
         for j in deps[i]:
             if j in token and not (e == "P" and token[j][0] == "sP"):
                 s, v = token[j]
                 need[s] = max(need.get(s, 0), v)
-        for s, v in need.items():
+        for s, v in sorted(need.items(), key=lambda x: -born[x]):
             if seen[e].get(s, 0) < v:
                 eng[e].wait_ge(T.sem[s], v)
                 seen[e][s] = v
+                for s2, v2 in known.get((s, v), {}).items():
+                    seen[e][s2] = max(seen[e].get(s2, 0), v2)
         ins = f(eng[e])
         if "send" in o:
             sent += o["send"]
@@ -795,6 +1010,8 @@ def rank_program(g, core, T, topo):
             count[e] += len(ins)
             token[i] = ("s" + e, count[e])
             total["s" + e] = count[e]
+        if i in token:
+            known[token[i]], born[token[i]] = dict(seen[e]), len(born)
     total["sent"] = sent
     for s, v in total.items():
         if seen["G"].get(s, 0) < v:

@@ -1,3 +1,4 @@
+import math
 import numpy as np
 from concourse.bass import DstId, RemoteDMATransfer
 from concourse.mybir import AluOpType as ALU, ActivationFunctionType as ACT
@@ -5,10 +6,12 @@ from concourse.mybir import AluOpType as ALU, ActivationFunctionType as ACT
 NR, NV, NL, NB, L, CAP, NT = 8, 1536, 5120, 2048, 384, 192, 5
 SH = [t * (t + 1) // 2 % 8 for t in range(NT)]
 F, B, I32, U, HF = "float32", "bfloat16", "int32", "uint16", "float16"
-MAGIC = 1.5 * 2.0 ** 27
-ASC = (0, 1, 4, 7, 10, 13)
+MAGIC = 1.5 * 2.0 ** 23
 NONE = 17.0 * 2 ** 19
-SCANINT = True
+XCN, XTN = 3, 3
+LONG = 6 * L
+AT = {1: 0, 3: L, 5: 2 * L, 0: 3 * L, 2: 4 * L, 4: 5 * L}
+PARCELS = ((0, 3 * L), (3 * L, LONG))
 
 
 def _sb(n, d):
@@ -17,46 +20,41 @@ def _sb(n, d):
 
 SCRATCH = {
     "LF": _sb(NL, B), "IV": _sb(NV, B), "KDI": _sb(NV, I32), "KDF": _sb(NV, F), "KS": _sb(NV, F), "KP": _sb(NV, F), "BK": _sb(NB, I32),
-    "LVI": _sb(24, I32), "LBI": _sb(120, I32), "LVU": _sb(24, U), "LBU": _sb(120, U),
+    "LVI": _sb(24, I32), "LBI": _sb(24, I32), "LVU": _sb(24, U), "LBU": _sb(120, U),
     "XB": _sb(704, F), "TB": _sb(704, F), "PT": _sb(112, B), "OI": _sb(8, I32), "OU": _sb(8, U), "CC": _sb(8, F), "PK8": _sb(8, B),
-    "HA": _sb(6 * 256, B), "HB": _sb(5 * 128, B), "XA": _sb(16 * L, B), "HFL": _sb(128, F), "KK": _sb(128, B), "PKM": _sb(128, B), "PSM": _sb(128, B),
-    "RS": _sb(512, B), "RT": _sb(256, B), "MI": _sb(448, B), "MK": _sb(448, B), "SS": _sb(480, B), "ZR": _sb(136, B), "SW": _sb(136, B),
-    "EI": _sb(28, F), "EL": _sb(28, U), "WR": _sb(816, B), "WI": _sb(272, B), "W24": _sb(24, B), "NON": _sb(128, B), "TRI": _sb(128, B), "CM": _sb(24, B),
-    "ID": _sb(5 * 128, B), "FD": _sb(256, B), "FS": _sb(256, B), "CF": _sb(40, B),
-    "RI": _sb(10, I32), "RF": _sb(20, F), "RL": _sb(20, U), "L5F": _sb(8, F), "L5I": _sb(8, I32), "L5": _sb(8, U),
-    "TAU": _sb(NV, B), "SN": _sb(1024, I32 if SCANINT else F), "SC": _sb(1024, F), "E": _sb(512, HF), "LI": _sb(128, I32), "MU": _sb(96, U),
+    "HM": _sb(2304, B), "HFL": _sb(128, F), "KK": _sb(128, B), "PKM": _sb(128, B), "PSM": _sb(128, B),
+    "RS": _sb(640, B), "RT": _sb(768, B), "MI": _sb(512, B), "MK": _sb(512, B), "SS": _sb(240, B), "ZR": _sb(272, B), "SW": _sb(272, B),
+    "EI": _sb(32, F), "EL": _sb(32, U), "WR": _sb(408, B), "WI": _sb(136, B), "PK": _sb(136, B), "WS": _sb(48, B), "NON": _sb(128, B), "TRI": _sb(128, B), "CM": _sb(24, B),
+    "ID": _sb(4 * 128, B), "FD": _sb(512, B), "CF": _sb(40, B), "L5F": _sb(38, F), "L5I": _sb(38, I32), "L5": _sb(38, U),
+    "TAU": _sb(NV, B), "SN": _sb(NV, I32), "SC": _sb(1024, F), "E": _sb(640, HF), "LI": _sb(128, I32), "MU": _sb(96, U),
     "SG": _sb(NV, B), "SI": _sb(NV, B), "NTB": _sb(NV, B),
-    "KA": _sb(L, U), "NA": _sb(L, B), "AP": _sb(NT * 6 * L, HF), "LT": _sb(NT * L, B),
-    "WU": _sb(NT * L, U), "WF": _sb(NT * L, HF), "XC": _sb(NT * 16 * L, B), "NE": _sb(816, B), "WL": _sb(120, U), "KG": _sb(NT * L, U), "KL": _sb(NT * L, U),
-    "XT": _sb(2 * 8 * L, B), "BD": _sb(2 * 768, B), "SD": _sb(2 * 768, F),
+    "KA": _sb(L, U), "CT": _sb(NT * 128, HF), "LC": _sb(NT * L, HF), "PL": _sb(NT * LONG, HF), "LT": _sb(L, B),
+    "WU": _sb(NT * L, U), "WF": _sb(NT * L, HF), "XC": _sb(XCN * 16 * L, B), "NE": _sb(816, B), "NH": _sb(816, B), "W40": _sb(40 * NT, B), "WL": _sb(120, U), "KG": _sb(NT * L, U), "KL": _sb(NT * L, U),
+    "XT": _sb(XTN * 8 * L, B), "BD": _sb(2 * 768, B), "SD": _sb(2 * 768, F),
     "R1": _sb(128, I32), "R2": _sb(128, B), "V1": _sb(128, I32), "V2": _sb(128, B), "VB": _sb(240, I32),
     "FF": _sb(608, I32), "CD": _sb(24, B), "MG": _sb(160, B), "FP": _sb(640, HF), "YS": _sb(L, F),
-    "DLB": ("dram", [240, 24], I32), "DK": ("dram", [16 * NT, 8 * L], U),
+    "DLB": ("dram", [240, 24], U),
+    "PS": ("psum", [128, 4096], F),
 }
-for _i in range(8):
-    SCRATCH["B%d" % _i] = ("psum", [128, 512], F)
-DMA_SEMS = ["d%d" % _i for _i in range(18)]
-ARR_SEMS = ["a_%s%d" % (k, t) for k in ("lb", "p0", "pp", "v1", "v2") for t in range(1, NT)]
-SEMAPHORES = ["sV", "sS", "sP", "sG", "sent", "relay"] + DMA_SEMS + ARR_SEMS
+DMA_SEMS = ["d%d" % _i for _i in range(24)]
+ARR_SEMS = ["a_%s%d" % (k, t) for k in ("lb", "ct", "pl", "v1", "v2") for t in range(1, NT)]
+HAND_SEMS = ["own%d" % _i for _i in range(len(PARCELS))] + ["far%d_%d" % (_k, _i) for _k in range(NT) for _i in range(len(PARCELS))]
+SEMAPHORES = ["sV", "sS", "sP", "sG", "sent"] + DMA_SEMS + ARR_SEMS + HAND_SEMS
 
 CY, PCY, GF_, LAT = 0.87e-3, 0.44e-3, 1.56, 0.12
-LINK, NEAR = 6e4, 1.5e5
-GCH = 128
-PARTS = "A C0 T0 C1 C2 C3 T1 C4 T2 T3 T4".split()
-ONV = {"A": (1,), "C0": (1,), "C1": (1,), "C2": (1,), "C3": (1,), "C4": ()}
-RANK = "L0 M0 L1 M1 L2 M2 F L3 M3 L4 M4 O0 O1 O2 O3 O4".split() + PARTS
-PACE, SOON, LATE, SLACK = 6.0, 1.5, 3.0, 0.5
-AHEAD, OWN = 0.0, 2.0
-ROUNDS, SEED, HEAT = 22000, 3, 0.08
-MODELS = ((1.0, 1.0, 1.0, LAT, 1.0),)
-FILL = 0.05
-WV, WS, WX = 0.2, 0.1, 0.1
-EARLY = -9.0
-SPLIT = ()
-CRIT, WH = 0.3, 0.3
-HLAG, DLAG, NH = 4.5, 2.6, 2
-CB = (0, 1, 5)
-TWICE = (0, 1, 2)
+LINK, NEAR, HBM = 6e4, 1.5e5, 2.5e5
+HOP, DLAG = 2.5, 2.6
+CUT_P = (0, 512, 1024, NV)
+CUT_N = (0, 1024, NV)
+CUT_O = (0, 4, 5)
+CUT_A = (0, 192, 384)
+CUT_C = 5 * [(0, 128, 256, 320, 384)]
+CUT_T = 5 * [(0, 128, 256, 384)]
+JOIN_T = 2 * [(0, 3)] + 3 * [(0, 2, 3)]
+JOIN_W = ((0, 1), (1, 3), (3, 5))
+LOADS = ("bk", "kd", "lf")
+JOIN_D = 5 * [(0, 2, 3)]
+BOTH, KG_WIDE, ONCE = True, (3, 4), ()
 PLAN = {}
 
 
@@ -68,11 +66,22 @@ def cnt(a):
     return (a[2] - a[1] + a[3] - 1) // a[3]
 
 
+def part(a, i, j):
+    return (a[0], a[1] + i * a[3], min(a[2], a[1] + j * a[3]), a[3], a[4], a[5])
+
+
+def banks_of(a):
+    return range(a[1] // 512, (a[1] + (cnt(a) - 1) * a[3]) // 512 + 1) if a[0] == "PS" else ()
+
+
+def pairs(cut):
+    return list(zip(cut, cut[1:]))
+
+
 def build(g, T, topo, core, rank):
     ops = []
     nd = [0]
     tag = ["K"]
-    onv = [False]
 
     def ap(a):
         return T[a[0]][a[4]:a[5], a[1]:a[2]:a[3]] if a[3] != 1 else T[a[0]][a[4]:a[5], a[1]:a[2]]
@@ -81,8 +90,6 @@ def build(g, T, topo, core, rank):
         return all(SCRATCH[a[0]][2] in (B, HF, U) for a in aps)
 
     def add(alts, reads, writes, **kw):
-        if tag[0] not in ("K", "K2") and len(alts) > 1:
-            kw["first"] = 0 if onv[0] else 1
         o = {"alts": alts, "r": [a for a in reads if isinstance(a, tuple)], "w": list(writes), "tag": tag[0]}
         o.update(kw)
         ops.append(o)
@@ -113,11 +120,11 @@ def build(g, T, topo, core, rank):
                 return [e.tensor_scalar(ap(out), src(i, off), sc(s1), None, op0)]
             return [e.tensor_scalar(ap(out), src(i, off), sc(s1), sc(s2), op0, op1)]
         alts = [("V", f, cost(out, i, off))]
-        if s is None and okS(out, i) and not off:
+        if s is None and okS(out, i):
             if op0 == ALU.mult and op1 is None:
-                s = act(out, i, ACT.Identity, 0.0, s1)
+                s = act(out, i, ACT.Identity, 0.0, s1, off)
             elif op0 == ALU.mult and op1 == ALU.add:
-                s = act(out, i, ACT.Identity, s2, s1)
+                s = act(out, i, ACT.Identity, s2, s1, off)
         if s:
             alts.append(s)
         return add(alts, [i, s1, s2, off], [out], g=off)
@@ -137,7 +144,7 @@ def build(g, T, topo, core, rank):
         return add([keep(out, i)], [i], [out])
 
     def tt(out, a, b, op, off=None):
-        c = 1.0 if SCRATCH[a[0]][0] == "psum" or SCRATCH[b[0]][0] == "psum" else 2.0
+        c = 1.0 if "PS" in (a[0], b[0]) else 2.0
         c = cost(out, a, off) if off else 0.06 + max(64, cnt(out) * c) * CY
         return add([("V", lambda e: [e.tensor_tensor(ap(out), src(a, off), ap(b), op)], c)], [a, b, off], [out], g=off)
 
@@ -157,13 +164,21 @@ def build(g, T, topo, core, rank):
         return add([("V", lambda e: [e.transpose(ap(out), ap(i))], cost(out, i, None))], [i], [out])
 
     def mg(items, start=True, stop=True):
+        cut = []
+        for o, a, b in items:
+            n = cnt(o)
+            x = min(n, (512 * (o[1] // 512 + 1) - o[1] + o[3] - 1) // o[3])
+            cut += [(part(o, i, j), a, part(b, i, j)) for i, j in ((0, x), (x, n)) if j > i]
+        where = [o[1] // 512 for o, a, b in cut]
+
         def f(e):
-            return [e.matmul(ap(o), ap(a), ap(b), start and k == 0, stop and k == len(items) - 1) for k, (o, a, b) in enumerate(items)]
-        c = 0.03 + sum(max(min(64, cnt(a)), cnt(b)) * (4 if SCRATCH[b[0]][2] == F else 1) for o, a, b in items) * PCY
+            return [e.matmul(ap(o), ap(a), ap(b), start and where[k] not in where[:k], stop and where[k] not in where[k + 1:])
+                    for k, (o, a, b) in enumerate(cut)]
+        c = 0.03 + sum(max(min(64, cnt(a)), cnt(b)) * (4 if SCRATCH[b[0]][2] == F else 1) for o, a, b in cut) * PCY
         return add([("P", f, c)], [x for it in items for x in it[1:]], [it[0] for it in items])
 
-    def mm(out, pairs):
-        return mg([(out, a, b) for a, b in pairs])
+    def mm(out, prs):
+        return mg([(out, a, b) for a, b in prs])
 
     def iota(out, pat, base=0, cm=0):
         if SCRATCH[out[0]][2] == I32:
@@ -181,14 +196,23 @@ def build(g, T, topo, core, rank):
     def put(out, v):
         return select(out, out, [[0, cnt(out)]], ALU.is_gt, v, 0, 0)
 
+    def join(first):
+        some = ops[first:]
+        del ops[first:]
+        add([(some[0]["alts"][0][0], lambda e: [x for o in some for x in o["alts"][0][1](e)], sum(o["alts"][0][2] for o in some))],
+            [a for o in some for a in o["r"]], [a for o in some for a in o["w"]])
+
     def dma(f, reads, writes, nbytes, n=1):
         nd[0] += 1
-        return add([("Y", f, 0.1)], reads, writes, dma=DMA_SEMS[nd[0] - 1], n=16 * n, bytes=nbytes)
+        return add([("Y", f, 0.1 + nbytes / HBM)], reads, writes, dma=DMA_SEMS[nd[0] - 1], n=16 * n, lag=2.0 if tag[0] == "K" else DLAG)
+
+    def way(via, us, after, writes=(), reads=(), arr=None, n=0, lag=HOP):
+        return add([(via, None, us)], reads, writes, arr=arr, n=n, after=list(after), lag=lag)
 
     def peer(d):
         return T.cores[(rank + d) % NR]
 
-    def send(items, pick, nbytes, lat=2.5):
+    def send(items, pick, nbytes, behind=()):
         def f(e):
             trs = []
             for k, (s, _, d, land, sem) in enumerate(items):
@@ -204,10 +228,10 @@ def build(g, T, topo, core, rank):
             return []
         o = add([("G", f, 0.4)], [it[1] for it in items], [], send=sum(len(pick(k)) for k in range(len(items))))
         for k, it in enumerate(items):
-            add([("X", None, lat)], [A(name, 0, 1) for name, _ in LOADS], [it[3]], arr=it[4], n=len(pick(k)), after=o, link=nbytes)
+            way("L", nbytes / LINK, [o], [it[3]], behind, it[4], len(pick(k)))
 
-    def bank(i, lo, hi, step=1, p1=128):
-        return A("B%d" % i, lo, hi, step, 0, p1)
+    def ps(lo, hi, step=1, p1=128):
+        return A("PS", lo, hi, step, 0, p1)
 
     def nonzero(out, i):
         return ts(out, i, 0.0, None, ALU.not_equal, s=act(out, i, ACT.Abs))
@@ -216,17 +240,15 @@ def build(g, T, topo, core, rank):
         return 16 * ((8 - SH[t]) % 8)
 
     def HAm(i, neg, t):
-        c = 256 * (2 * (i // 2) + neg) + rot(t)
-        return A("HA", c, c + 128)
+        c = 256 + 768 * (i // 2) + 256 * neg + rot(t)
+        return A("HM", c, c + 128)
 
     def HBm(d):
-        if d % 3 == 0:
-            return A("HA", 512 * (d // 3), 512 * (d // 3) + 128)
-        c = 128 * (d - 1 - d // 3)
-        return A("HB", c, c + 128)
+        c = (128, 256, 768)[d % 3] + 768 * (d // 3) if d else 0
+        return A("HM", c, c + 128)
 
     def IDm(n):
-        c = 128 * ("I1", "I16", "I256", "NEG", "SGN").index(n)
+        c = 128 * ("I1", "I16", "I256", "NEG").index(n)
         return A("ID", c, c + 128)
 
     def row(b, lo=0, hi=32, step=1, p0=0, p1=128):
@@ -235,26 +257,34 @@ def build(g, T, topo, core, rank):
     def col(b, p1=128):
         return A("TB", 32 * b, 32 * b + 1, 1, 0, p1)
 
-    def slot(t):
-        return (t - 1) % NT
-    Hb = A("HA", 0, 128)
+    Hb = A("HM", 0, 128)
     HP = A("PT", 16, 32)
-    P16, Q16, P8, PSW, Q32, H16, B8, HEAVY, LIGHT, PAY, TOP, SIGN, YSC = range(8, 21)
+    P16, Q16, P8, PSW, YSC = range(8, 13)
+    SMALL, ROWS, KEYS = 3584, 2048, 2048
 
-    for lo, hi in ((0, 512), (512, NV)):
+    for lo, hi in ((0, CUT_P[1]), (CUT_P[1], NV)):
         dma(lambda e, lo=lo, hi=hi: [e.dma_start(T.IV[:, lo:hi], T.iv[:, lo:hi])], [], [A("IV", lo, hi)], 256 * (hi - lo))
-    dma(lambda e: [e.dma_start(T.DLB[0:128, :], T.lb[:]), e.dma_start(T.DLB[128:240, :], T.lb[0:112, :])], [], [A("DLB", 0, 24)], 24576, n=2)
-    dma(lambda e: [e.dma_start(T.LVI[:], T.lv[:]), e.dma_start(T.LBI[:, 0:24], T.lb[:])], [], [A("LVI", 0, 24), A("LBI", 0, 24)], 24576, n=2)
-    for name, nbytes in LOADS:
-        dma(lambda e, name=name: [e.dma_start(T[name][:], T[name[:2].lower()][:])], [], [A(name, 0, SCRATCH[name][1][1])], nbytes)
-    send([(T.DLB[rot(t):rot(t) + 128, :], A("DLB", 0, 24), t, A("LBI", 24 * t, 24 * t + 24), "a_lb%d" % t) for t in range(1, NT)],
-         lambda k: [2 * k, 2 * k + 1], 12288, 4.0)
+    dma(lambda e: [e.dma_start(T.LVI[:], T.lv[:]), e.dma_start(T.LBI[:], T.lb[:])], [], [A("LVI", 0, 24), A("LBI", 0, 24)], 24576, n=2)
+    gcp(A("LBU", 0, 24), A("LBI", 0, 24))
+    dma(lambda e: [e.dma_start(T.DLB[0:128, :], T.LBU[:, 0:24]), e.dma_start(T.DLB[128:240, :], T.LBU[0:112, 0:24])], [A("LBU", 0, 24)], [A("DLB", 0, 24)], 12288, n=2)
+    for name in LOADS:
+        if name == "kd":
+            for lo in range(0, NV, 512):
+                dma(lambda e, lo=lo: [e.dma_start(T.KDI[:, lo:lo + 512], T.kd[:, lo:lo + 512])], [], [A("KDI", lo, lo + 512)], 262144)
+        elif name == "lf":
+            dma(lambda e: [e.dma_start(T.LF[:], T.lf[:])], [], [A("LF", 0, NL)], 256 * NL)
+        else:
+            dma(lambda e: [e.dma_start(T.BK[:], T.bk[:])], [], [A("BK", 0, NB)], 512 * NB)
+    send([(T.DLB[rot(t):rot(t) + 128, :], A("DLB", 0, 24), t, A("LBU", 24 * t, 24 * t + 24), "a_lb%d" % t) for t in range(1, NT)],
+         lambda k: [2 * k, 2 * k + 1], 6144, [A("LF", 0, 1), A("BK", 0, 1)])
 
     def bit(b, lo, hi):
         return [[0, 16 >> b], [hi - lo, 2]] + ([[0, 1 << b]] if b else []), lo
+    first = len(ops)
     for b in range(4):
         iota(row(b), *bit(b, 1, -1))
     iota(A("OI", 0, 8), [[-16, 8]], 16, 1)
+    join(first)
     ms(A("PT", 0, 112), 0.0)
     ms(A("PT", 16, 17), 1.0)
     turn(0, 4)
@@ -264,25 +294,35 @@ def build(g, T, topo, core, rank):
         ts(A("PT", 16 + 2 * n, 16 + 3 * n), A("PT", 16, 16 + n), col(b + 1), None, ALU.mult)
         ts(A("PT", 16 + 3 * n, 16 + 4 * n), A("PT", 16, 16 + n), col(b), col(b + 1), ALU.mult, ALU.mult)
     cp(Hb, A("PT", 0, 48), A("OU", 0, 8))
-    for b, (lo, hi) in enumerate(((16, 32), (1, 4), (1, 16), (1, 256))):
+    first = len(ops)
+    for b, (lo, hi) in enumerate(((16, 32), (1, 4), (1, 256), (1, 16))):
         iota(row(4 + b), *bit(b, lo, hi))
+    join(first)
     turn(4, 8)
     ts(A("CC", 0, 1), col(4), col(5), col(6), ALU.mult, ALU.mult)
     ts(A("KK", 0, 128), Hb, A("CC", 0, 1), col(7), ALU.mult, ALU.mult)
-    ms(A("RS", 0, 512), 1.0)
-    ms(A("RS", 0, 512, 16), 2.0 ** 23)
+    most = max(hi - lo for lo, hi in pairs(CUT_P))
+    ms(A("RS", 0, most), 1.0)
+    ms(A("RS", 0, most, 16), 2.0 ** 23)
+    first = len(ops)
     iota(row(P16), [[0, 2], [1, 16]])
     iota(row(Q16), [[16, 2], [0, 16]], 0, 1)
     iota(row(P8), [[0, 4], [1, 8]])
+    join(first)
+    turn(P16, PSW)
     ms(row(PSW), 0.0)
+    first = len(ops)
     for r, v in ((0, 680), (1, -8), (4, -32), (2, -128), (8, -512)):
         fill(row(PSW, r, 32, 16), v)
-    turn(P16, Q32)
-    iota(A("MI", 0, 256), [[0, 4], [16, 8], [0, 8]])
-    ts(A("MK", 0, 256), A("MI", 0, 256), col(Q16), None, ALU.is_equal)
-    iota(A("EI", 0, 16), [[8, 4], [0, 4]])
-    iota(A("EI", 16, 28), [[0, 2], [8, 3], [0, 2]])
-    ts(A("EL", 0, 28), A("EI", 0, 28), col(P8), None, ALU.add)
+    join(first)
+    turn(PSW, YSC)
+    iota(A("MI", 0, most // 2), [[0, most // 128], [16, 8], [0, 8]])
+    ts(A("MK", 0, most // 2), A("MI", 0, most // 2), col(Q16), None, ALU.is_equal)
+    first = len(ops)
+    iota(A("EI", 0, 20), [[8, 5], [0, 4]])
+    iota(A("EI", 20, 32), [[0, 2], [8, 3], [0, 2]])
+    join(first)
+    ts(A("EL", 0, 32), A("EI", 0, 32), col(P8), None, ALU.add)
     ms(A("SS", 0, 240), 0.0)
     ts(A("SS", 112, 128), row(P16, 0, 16), col(P16), None, ALU.is_equal)
     cp(A("HFL", 0, 128), Hb, gp=True)
@@ -290,246 +330,267 @@ def build(g, T, topo, core, rank):
     tt(A("PT", 48, 56), A("PT", 16, 32, 2), A("PK8", 0, 8), ALU.add)
     cp(A("PKM", 0, 128), A("PT", 32, 80), A("OU", 0, 8))
     cp(A("PT", 90, 91), col(PSW), gp=True)
-    ts(A("PT", 91, 92), col(P16), 0.0, 16.0, ALU.is_equal, ALU.mult)
+    ts(A("PT", 81, 91, 2), A("TB", 32 * P16, 32 * P16 + 5), 0.0, -512.0, ALU.is_equal, ALU.mult)
     cp(A("PSM", 0, 128), A("PT", 64, 112), A("OU", 0, 8))
     tag[0] = "K2"
-    iota(row(Q32), [[0, 16], [128, 2]], 0, 1)
-    iota(row(H16), [[1, 16], [0, 2]])
-    iota(row(B8), *bit(3, 0, 8))
-    ms(A("XB", 32 * HEAVY, 32 * YSC), 0.0)
+
+    def spot(out, pat, r, c):
+        return select(out, out, pat, ALU.not_equal, c, -r, 1)
+    first = len(ops)
+    fill(A("PK", 0, 136), 0)
+    fill(A("WS", 0, 48), 0)
+    fill(A("ZR", 0, 272), 0)
+    iota(A("WI", 0, 136), [[0, 8], [-1, 17]], 17)
+    join(first)
+    for par in range(2):
+        first = len(ops)
+        for q in range(4):
+            spot(A("PK", 2 + 3 * q, 122, 15), [[-16, 8]], 2 * q + par, (-1.0 / 16, -4.0)[par])
+        if par:
+            spot(A("PK", 14, 122, 15), [[-16, 8]], 10, 1.0 / 16)
+            spot(A("PK", 122, 123), [[0, 1]], 9, -2.0 ** -14)
+        join(first)
+    select(A("WR", 272, 408), A("WI", 0, 136), [[0, 136]], ALU.is_equal, 0.0, -40, 1)
+    fill(A("WR", 0, 272), 0)
+    for q in range(2):
+        first = len(ops)
+        spot(A("WR", 0, 136), [[-5, 8], [0, 17]], q, 4096.0 ** q * 2.0 ** 30)
+        spot(A("WR", 136, 272), [[-5, 8], [0, 17]], 2 + q, 4096.0 ** q * 16)
+        if q:
+            spot(A("WR", 272, 408), [[-5, 8], [0, 17]], 4, 2.0 ** -13)
+        join(first)
+    fill(A("WR", 0, 272, 17), 0)
     for r in range(4):
-        put(row(HEAVY, r, 32, 16), 64.0 ** r * 2.0 ** 26)
-        fill(row(LIGHT, 4 + r, 32, 16), 64 ** r)
-    for b, r, v in ((PAY, 10, 2.0 ** -17), (PAY, 11, 2.0 ** -9), (TOP, 10, 2.0 ** -17)):
-        put(row(b, r, 32, 16), v)
-    for b, r in ((TOP, 11), (SIGN, 10), (SIGN, 11)):
-        fill(row(b, r, 32, 16), 1)
-    for h in (0, 16):
-        fill(row(SIGN, h, h + 8), -1)
-    fill(row(YSC), 1)
-    for p in (0, 32):
-        out = row(YSC, (3 - p) % 5, 32, 5)
-        select(out, out, [[0, cnt(out)]], ALU.not_equal, 0.25, -p, 1)
-    turn(Q32, YSC + 1)
+        first = len(ops)
+        spot(A("WS", 0, 16), [[0, 2], [-16, 8]], r, 64.0 ** r * 2.0 ** 26)
+        spot(A("WS", 16, 32), [[0, 2], [-16, 8]], 4 + r, 64.0 ** r)
+        if r == 0:
+            spot(A("WS", 32, 48), [[0, 2], [-16, 8]], 10, 2.0 ** -17)
+        join(first)
+    select(A("SW", 0, 272), A("ZR", 0, 272), [[0, 2], [-16, 8], [1, 17]], ALU.not_equal, 2.0 ** -24, -16, 1)
+    first = len(ops)
     for z in range(2):
-        iota(A("MI", 256 + 96 * z, 352 + 96 * z), [[0, 3], [32, 4], [0, 8]], 128 * z)
-    ts(A("MK", 256, 448), A("MI", 256, 448), col(Q32), None, ALU.is_equal)
-    ms(A("SS", 240, 480), 0.0)
-    ts(A("SS", 352, 368), row(P16, 0, 16), col(H16), None, ALU.is_equal)
-    fill(A("ZR", 0, 136), 0)
-    for n, v in (("I1", 1.0), ("I16", 16.0), ("I256", 256.0), ("NEG", -2.0 ** 24)):
+        iota(A("MI", 320 + 96 * z, 416 + 96 * z), [[0, 3], [16, 4], [0, 8]], 64 * z)
+    join(first)
+    ts(A("MK", 320, 512), A("MI", 320, 512), col(Q16), None, ALU.is_equal)
+    for n, v in (("I1", 1.0), ("I16", 16.0), ("I256", 256.0)):
         select(IDm(n), A("ZR", 0, 128), [[-1, 128]], ALU.not_equal, v, 0, 1)
+    tag[0] = "K3"
+    cp(A("HM", 128, 256), Hb, gp=True)
+    for lo, n, c in ((256, 256, 256.0), (512, 256, -256.0), (768, 128, 256.0 ** 2), (896, 128, 256.0 ** 3)):
+        ts(A("HM", lo, lo + n), A("HM", 0, n), c, None, ALU.mult)
+    ts(A("HM", 1024, 1792), A("HM", 256, 1024), 256.0 ** 3, None, ALU.mult)
+    ts(A("HM", 1792, 2304), A("HM", 256, 768), 256.0 ** 6, None, ALU.mult)
+    out = A("FD", 0, 512)
+    ts(out, A("HM", 256, 768), 2.0 ** 10, 0.0, ALU.mult, ALU.max, s=act(out, A("HM", 256, 768), ACT.Relu, 0.0, 2.0 ** 10))
+    wide = 256 * max(j - i for cut in JOIN_T for i, j in pairs(cut))
+    fill(A("RT", 0, wide), -2)
+    fill(A("RT", 0, wide, 32), 1 << 23)
+    tag[0] = "K4"
+    select(IDm("NEG"), A("ZR", 0, 128), [[-1, 128]], ALU.not_equal, -2.0 ** 24, 0, 1)
     fill(A("NON", 0, 128), -64)
     select(A("TRI", 0, 128), A("NON", 0, 128), [[1, 128]], ALU.is_gt, 0.0, 0, -1)
     select(A("TRI", 0, 128), A("TRI", 0, 128), [[1, 128]], ALU.not_equal, 64.0 * CAP, 0, -1)
     select(A("CM", 0, 24), A("ZR", 0, 24), [[0, 24]], ALU.is_gt, 2.0 ** -12, 0, 0)
-    fill(A("RT", 0, 256), -2)
-    fill(A("RT", 0, 256, 32), 1 << 23)
     fill(A("CF", 0, 40), 0)
     fill(A("CF", 0, 40, 5), -1)
-    cp(A("HA", 128, 256), Hb, gp=True)
-    ts(A("HA", 256, 512), A("HA", 0, 256), -1.0, None, ALU.mult)
-    ts(A("HA", 512, 1024), A("HA", 0, 512), 256.0 ** 3, None, ALU.mult)
-    ts(A("HA", 1024, 1536), A("HA", 0, 512), 256.0 ** 6, None, ALU.mult)
-    ts(HBm(1), Hb, 256.0, None, ALU.mult)
-    ts(HBm(2), Hb, 256.0 ** 2, None, ALU.mult)
-    ts(A("HB", 256, 512), A("HB", 0, 256), 256.0 ** 3, None, ALU.mult)
-    ts(HBm(7), HBm(1), 256.0 ** 6, None, ALU.mult)
-    iota(A("WI", 0, 272), [[0, 16], [-1, 17]], 17)
-    select(A("WI", 0, 272), A("WI", 0, 272), [[0, 2], [-16, 8], [0, 17]], ALU.is_ge, 0.0, 0, 1)
-    select(A("WI", 0, 272), A("WI", 0, 272), [[0, 2], [16, 8], [0, 17]], ALU.is_ge, 0.0, 15, -1)
-    for w, b in enumerate((HEAVY, LIGHT)):
-        ts(A("WR", 272 * w, 272 * w + 272), A("WI", 0, 272), 1.0, col(b), ALU.min, ALU.mult)
-    ts(A("WR", 544, 816), A("WI", 0, 272), col(PAY), col(TOP), ALU.mult, ALU.min)
-    fill(A("WR", 0, 544, 17), 0)
-    for w in range(2):
-        gcp(A("W24", 8 * w, 8 * w + 8), A("WR", 272 * w + 1, 272 * w + 136, 17))
-    select(A("W24", 16, 24), A("WR", 545, 680, 17), [[-16, 8]], ALU.not_equal, 0.0, -11, 1)
-    select(A("SW", 0, 136), A("ZR", 0, 136), [[-16, 8], [1, 17]], ALU.not_equal, 2.0 ** -24, -16, 1)
-    for par, c in ((0, 2.0 ** 18), (1, -2.0 ** 18)):
-        out = A("FD", par, 256, 2)
-        ts(out, Hb, c, 0.0, ALU.mult, ALU.max, s=act(out, Hb, ACT.Relu, 0.0, c))
-        cp(A("FS", 1 - par, 256, 2), out, gp=True)
+    fill(row(YSC), 1)
+    for p in (0, 32):
+        out = row(YSC, (3 - p) % 5, 32, 5)
+        select(out, out, [[0, cnt(out)]], ALU.not_equal, 0.25, -p, 1)
+    turn(YSC, YSC + 1)
+    iota(A("L5F", 0, 38), [[16, 38]], -2)
+    ts(A("L5I", 0, 38), A("L5F", 0, 38), col(P16), 0.2, ALU.add, ALU.mult)
+    gcp(A("L5", 0, 38), A("L5I", 0, 38))
+    first = len(ops)
+    fill(A("MG", 0, 128), 0)
+    fill(A("FF", 600, 608), 0)
     for t in range(NT):
-        iota(A("RI", 2 * t, 2 * t + 2), [[0, 2]], SH[t], 1)
-    iota(A("RF", 10, 20), [[0, 5], [16, 2]])
-    ts(A("RI", 0, 10), A("RI", 0, 10), 7, None, ALU.bitwise_and)
-    tt(A("RF", 0, 10), A("RI", 0, 10), A("RF", 10, 20), ALU.add)
-    ts(A("RF", 10, 20), A("RF", 0, 10), col(B8), 23.0, ALU.add, ALU.min)
-    ts(A("RL", 0, 10), A("RF", 10, 20), 17.0, 16.0, ALU.mult, ALU.add)
-    ts(A("RL", 10, 20), A("RF", 10, 20), 32.0, 31.0, ALU.mult, ALU.add)
-    iota(A("L5F", 0, 8), [[16, 8]], -2)
-    ts(A("L5I", 0, 8), A("L5F", 0, 8), col(P16), 0.2, ALU.add, ALU.mult)
-    gcp(A("L5", 0, 8), A("L5I", 0, 8))
-    fill(A("MG", 0, 160), 0)
-    fill(A("FF", 0, 608), 0)
-    for t in range(NT):
-        fill(A("FF", 120 * slot(t), 120 * slot(t) + 120, 5), (rank + t) % NR + 1)
+        fill(A("FF", 120 * t, 120 * t + 120, 5), (rank + t) % NR + 1)
+    join(first)
 
     def to_list(sb, words, bits, lanes, shift, out):
-        n, e0, l0 = cnt(words), 256 * sb, 64 * sb
+        n, e0, l0 = cnt(words), 320 * sb, 64 * sb
         ts(A("LI", l0, l0 + n), words, bits, None, ALU.bitwise_and)
-        tt(A("E", e0, e0 + 8 * n), A("LI", l0, l0 + n), A("MK", 256 * lanes, 256 * lanes + 8 * n), ALU.mult, off=A("EL", 16 * lanes, 16 * lanes + n // 2))
-        b = bank(6, 32 * sb, 32 * sb + n)
-        s0 = [240 * lanes + 112 - 16 * ((q + shift) % 8) for q in range(8)]
+        tt(A("E", e0, e0 + 8 * n), A("LI", l0, l0 + n), A("MK", 320 * lanes, 320 * lanes + 8 * n), ALU.mult, off=A("EL", 20 * lanes, 20 * lanes + n // 2))
+        b = ps(SMALL + 40 * sb, SMALL + 40 * sb + n)
+        s0 = [112 - 16 * ((q + shift) % 8) for q in range(8)]
         mm(b, [(A("SS", s0[q], s0[q] + 128), A("E", e0 + q, e0 + 8 * n, 8)) for q in range(8)])
         cp(out, b)
 
     tag[0] = "N"
-    for c in range(3):
-        lo, hi, sb = 512 * c, 512 * c + 512, c % 2
-        gcp(A("KDF", lo, hi), A("KDI", lo, hi))
-        mm(bank(c, 0, 512), [(Hb, A("IV", lo, hi))])
-        ts(A("TAU", lo, hi), bank(c, 0, 512), 1.0, -1.0, ALU.min, ALU.max, s=act(A("TAU", lo, hi), bank(c, 0, 512), ACT.Sign))
-        mg([(bank(7, 128 * i, 128 * i + 128), A("TAU", lo + 128 * i, lo + 128 * i + 128), A("KK", 0, 128)) for i in range(4)])
-        least(A("SN", 512 * sb, 512 * sb + 512), A("RS", 0, 512), bank(7, 0, 512))
-        words = A("SN", 512 * sb + 15, 512 * sb + 512, 16)
-        if not SCANINT:
-            cp(A("LI", 64 * sb + 32, 64 * sb + 64), words)
-            words = A("LI", 64 * sb + 32, 64 * sb + 64)
-        to_list(sb, words, 15, 0, 0, A("MU", 32 * c, 32 * c + 32))
-        cp(A("SG", lo, hi), HP, A("MU", 32 * c, 32 * c + 32))
-        mm(bank(3 + c, 0, 512), [(A("HFL", 0, 128), A("KDF", lo, hi))])
+    for c, (lo, hi) in enumerate(pairs(CUT_P)):
+        mm(ps(lo, hi), [(Hb, A("IV", lo, hi))])
+        ts(A("TAU", lo, hi), ps(lo, hi), 1.0, -1.0, ALU.min, ALU.max, s=act(A("TAU", lo, hi), ps(lo, hi), ACT.Sign))
+        mg([(ps(KEYS + i, KEYS + i + 128), A("TAU", i, i + 128), A("KK", 0, 128)) for i in range(lo, hi, 128)])
+        least(A("SN", lo, hi), A("RS", 0, hi - lo), ps(KEYS + lo, KEYS + hi))
+        to_list(c % 2, A("SN", lo + 15, hi, 16), 15, 0, 0, A("MU", lo // 16, hi // 16))
+        cp(A("SG", lo, hi), HP, A("MU", lo // 16, hi // 16))
+        tt(A("SI", lo, hi), ps(lo, hi), A("SG", lo, hi), ALU.mult)
+        mm(ps(lo, hi), [(A("PSM", 0, 128), A("SG", lo, hi)), (A("PKM", 0, 128), A("SI", lo, hi))])
+    for lo, hi in pairs(CUT_N):
+        cp(A("NTB", lo, hi), ps(lo, hi))
+    tag[0] = "N2"
     for c in range(3):
         lo, hi = 512 * c, 512 * c + 512
-        tt(A("SI", lo, hi), bank(c, 0, 512), A("SG", lo, hi), ALU.mult)
-        mm(bank(c, 0, 512), [(A("PSM", 0, 128), A("SG", lo, hi)), (A("PKM", 0, 128), A("SI", lo, hi))])
-        cp(A("NTB", lo, hi), bank(c, 0, 512))
-        tt(A("KS", lo, hi), bank(3 + c, 0, 512), A("SG", lo, hi), ALU.mult)
-        mm(bank(3 + c, 0, 512), [(A("HFL", 0, 128), A("KS", lo, hi))])
-        ts(A("KP", lo, hi), bank(3 + c, 0, 512), 1.0 / 16, None, ALU.mult)
+        cp(A("KDF", lo, hi), A("KDI", lo, hi), gp=True)
+        mm(ps(NV + lo, NV + hi), [(A("HFL", 0, 128), A("KDF", lo, hi))])
+        tt(A("KS", lo, hi), ps(NV + lo, NV + hi), A("SG", lo, hi), ALU.mult)
+        mm(ps(NV + lo, NV + hi), [(A("HFL", 0, 128), A("KS", lo, hi))])
+    for lo, hi in pairs(CUT_N):
+        ts(A("KP", lo, hi), ps(NV + lo, NV + hi), 1.0 / 16, None, ALU.mult)
 
-    def spread(buf, x, table, lists, l0):
-        for c in range(0, L, GCH):
-            onv[0] = c // GCH in ONV[tag[0]]
-            cp(A(buf, 16 * (L * x + c), 16 * (L * x + c + GCH)), table, A(lists, l0 + c, l0 + c + GCH))
-        onv[0] = False
-
-    tag[0] = "A"
+    tag[0] = "C0"
     gcp(A("LVU", 0, 24), A("LVI", 0, 24))
+    cp(A("LT", 0, L), A("NTB", 0, NV), A("LVU", 0, 24))
+    mm(ps(SMALL + 128, SMALL + 256), [(A("PK", 2 - i, 130 - i), A("LT", 128 * i, 128 * i + 128)) for i in range(3)])
+    cp(A("CT", 0, 128), ps(SMALL + 128, SMALL + 256))
+    send([(ap(A("CT", 0, 128)), A("CT", 0, 128), t, A("CT", 128 * t, 128 * t + 128), "a_ct%d" % t) for t in range(1, NT)], lambda k: [2 * k, 2 * k + 1],
+         32768, [A("LF", 0, 1), A("BK", 0, 1)])
+    tag[0] = "A"
     cp(A("KA", 0, L), A("KP", 0, NV), A("LVU", 0, 24))
-    ts(A("LT", 0, L), A("NTB", 0, NV), col(SIGN), None, ALU.mult, off=A("LVU", 0, 24),
-       s=act(A("LT", 0, L), A("NTB", 0, NV), ACT.Identity, 0.0, col(SIGN), A("LVU", 0, 24)))
-    spread("XA", 0, A("LF", 0, NL), "KA", 0)
+    for lo, hi in pairs(CUT_A):
+        cp(A("XT", 16 * lo, 16 * hi), A("LF", 0, NL), A("KA", lo, hi))
 
     def xa(d):
-        return A("XA", d, 16 * L, 16)
-    for i in range(6):
-        b = bank(2 + i % 3, 0, L)
-        if i == 0:
-            mm(b, [(IDm("I1"), xa(0)), (IDm("I1"), A("LT", 0, L))])
-        else:
-            mm(b, [(IDm(n), xa(ASC[i] + j)) for j, n in enumerate(("I1", "I16", "I256"))])
-        ts(A("AP", L * i, L * i + L), b, 16.0 ** ASC[i] / 256.0 ** (3 * (i // 2)), None, ALU.mult)
-        if i == 0:
-            send([(ap(A("AP", 0, L)), A("AP", 0, L), t, A("AP", 6 * L * t, 6 * L * t + L), "a_p0%d" % t) for t in range(1, NT)],
-                 lambda k: [2 * k, 2 * k + 1], 98304)
-    def to_helper(e):
-        h = helpers(T, topo, rank)[0]
-        rid, pid, _se = topo.addr(h)
-        e.remote_dma(T.AP[:, L:6 * L], T.AP[:, L:6 * L], T.sem["relay"], T.sem["sent"], pid, rid, sum(1 << x for x in topo.engines(core, h)[-8:]))
-        return []
-    o = add([("G", to_helper, 0.4)], [A("AP", L, 6 * L)], [], send=8)
-    o = add([("X", None, HLAG)], [], [], arr=None, after=o, link=491520 * LINK / NEAR, via="R")
-    for t in range(1, NT):
-        o = add([("X", None, 2.5)], [], [A("AP", 6 * L * t + L, 6 * L * t + 6 * L)], arr="a_pp%d" % t, n=8, after=o, link=491520, via="H")
-    mg([(bank(7, 128 * i, 128 * i + 128, 1, 40), A("CF", 0, 40), IDm("I1")) for i in range(3)], stop=False)
+        return A("XT", d, 16 * L, 16)
+    legs, last = [], []
+    for n, (lo, hi) in enumerate(PARCELS):
+        back = 256 * n
+        for some in (((1, 3, 5),), ((2, 4), (0,)))[n]:
+            mg([(ps(AT[i] - back, AT[i] + L - back), IDm(m), xa(3 * i + j)) for i in some for j, m in enumerate(("I1", "I16", "I256")) if 3 * i + j < 16])
+        ts(A("PL", lo, hi), ps(lo - back, hi - back), (16.0, 2.0 ** -8)[n], None, ALU.mult)
+
+        def to_helper(e, n=n, lo=lo, hi=hi):
+            h = helpers(T, topo, rank)[0]
+            rid, pid, _se = topo.addr(h)
+            en = topo.engines(core, h)
+            e.remote_dma(T.PL[:, lo:hi], T.PL[:, lo:hi], T.sem["own%d" % n], T.sem["sent"], pid, rid, sum(1 << x for x in en[-8:]))
+            return []
+        o = add([("G", to_helper, 0.4)], [A("PL", lo, hi)], [], send=8)
+        legs.append(way("R", 256 * (hi - lo) / NEAR, [o], lag=HOP + 1.0))
+    for t in range(1, NT, 2):
+        for n, (lo, hi) in enumerate(PARCELS):
+            o = way("H", 256 * (hi - lo) / LINK, [legs[n]], lag=HOP + 1.0)
+            last[n:] = [way("F", 256 * (hi - lo) / NEAR, [o])]
+        for x in (t, t + 1):
+            way("Z", 0.0, last, [A("PL", LONG * x, LONG * x + LONG)], (), "a_pl%d" % x, 8 * len(PARCELS), 0.0)
 
     def home(t, out, land, sem, nbytes):
         send([(ap(out), out, -t, land, sem)], lambda k: list(range(8)), nbytes)
 
     def claims(t):
         tag[0] = "C%d" % t
-        sb = t % 2
-        if t < 2:
-            lo, hi = (0, 24) if t == 0 else (24, 120)
-            gcp(A("LBU", lo, hi), A("LBI", lo, hi))
-        cp(A("WU", L * t, L * t + L), A("BK", 0, NB), A("LBU", 24 * t, 24 * t + 24))
+        sb, xc = t % 2, 16 * L * (t % XCN)
+        for lo, hi in JOIN_W:
+            if lo == t:
+                cp(A("WU", L * lo, L * hi), A("BK", 0, NB), A("LBU", 24 * lo, 24 * hi))
+        dma(lambda e: [e.dma_start(T.LC[0:41, L * t + 128 * i:L * t + 128 * i + 128], T.CT[i:123:3, 128 * t:128 * t + 128]) for i in range(3)],
+            [A("CT", 128 * t, 128 * t + 128)] + ([] if t else [A("LF", 0, 1)]), [A("LC", L * t, L * t + L)], 30720, n=3)
         gcp(A("WF", L * t, L * t + L), A("WU", L * t, L * t + L))
-        spread("XC", t, A("NTB", 0, NV), "WU", L * t)
-        if t:
-            ts(A("LT", L * t, L * t + L), A("AP", 6 * L * t, 6 * L * t + L), MAGIC, MAGIC, ALU.add, ALU.subtract)
+        first = len(ops)
+        for c, w in enumerate((2, 1, 0, 1, 2)):
+            gcp(A("W40", 40 * t + 8 * c, 40 * t + 8 * c + 8), A("WS", 16 * w + SH[t], 16 * w + SH[t] + 8))
+        join(first)
+        for lo, hi in pairs(CUT_C[t]):
+            cp(A("XC", xc + 16 * lo, xc + 16 * hi), A("NTB", 0, NV), A("WU", L * t + lo, L * t + hi))
+        n0, runs = 408 * sb, 3 if t in ONCE else 2
+
+        def at(i, r):
+            return ROWS + (512 * i + 136 * r if i else 376 - 136 * r)
         for i in range(3):
-            b = CB[(3 * t + i) % len(CB)]
-            x0, l0, r0 = 16 * (L * t + 128 * i), L * t + 128 * i, 17 * rot(t) // 16
+            x0, l0, lo = xc + 2048 * i, L * t + 128 * i, min(at(i, 0), at(i, runs - 1))
 
-            def lane(w, c0):
-                return (bank(b, c0, c0 + 136), A("LT", l0, l0 + 128), A("WR", 272 * w + r0, 272 * w + r0 + 136))
+            def lane(w, r):
+                return (ps(at(i, r), at(i, r) + 136), A("LC", l0, l0 + 128, 1, 0, 41), A("WR", 136 * w, 136 * w + 136, 1, 0, 41))
 
-            def slots(hi, w0, w1):
-                return [(bank(b, 16 - k, hi, 17), A("XC", x0 + k, x0 + 2048, 16), A("W24", w0, w1)) for k in range(16)]
-            def nodes(c0):
-                return (bank(b, c0, c0 + 136), A("WF", l0, l0 + 128), A("SW", 0, 136))
-            out, ne = A("SC", 512 * sb + 136 * i, 512 * sb + 136 * i + 136), A("NE", 272 * i, 272 * i + 136)
-            if t in TWICE:
-                mg([lane(0, 0)] + slots(136, 0, 8) + [lane(1, 0), lane(2, 136), nodes(136)] + slots(272, 8, 24))
-                nonzero(ne, bank(b, 0, 136))
-                lastfit(out, ne, bank(b, 136, 272))
+            def slots(c0, w0, n):
+                return [(ps(c0 + 16 - k, c0 + 17 * n, 17), A("XC", x0 + k, x0 + 2048, 16), A("W40", 40 * t + w0, 40 * t + w0 + n)) for k in range(16)]
+            nodes = (ps(at(i, runs - 1), at(i, runs - 1) + 136), A("WF", l0, l0 + 128), A("SW", 17 * SH[t], 17 * SH[t] + 136))
+            if t in ONCE:
+                mg([lane(0, 0), lane(1, 1), lane(2, 2), nodes] + slots(lo, 16 if i else 0, 24))
             else:
-                mg([lane(w, 136 * w) for w in range(3)] + [nodes(272)] + slots(408, 0, 24))
-                cp(ne, bank(b, 0, 136))
-                both = A("NE", 272 * i + 136, 272 * i + 272)
-                tt(both, bank(b, 136, 272), ne, ALU.not_equal)
-                lastfit(out, both, bank(b, 272, 408))
-        r0 = 32 * (t - 1) if t else 96
-        name = "R1" if t else "V1"
-        ts(A(name, r0, r0 + 32), A("SC", 512 * sb, 512 * sb + 408), 2.0 ** 24, -NONE, ALU.mult, ALU.add, off=A("RL", 2 * t, 2 * t + 2))
+                mg([lane(0, 0)] + slots(at(i, 0), 16, 8) + [lane(1, 0), lane(2, 1), nodes] + slots(lo, 24 if i else 0, 16))
+        for i0, i1 in pairs(JOIN_D[t]):
+            first = ps(at(i0, 0), at(i0, 0) + 136 * (i1 - i0))
+            if t in ONCE:
+                cp(A("NH", n0 + 136 * i0, n0 + 136 * i1), first)
+            else:
+                nonzero(A("NE", n0 + 136 * i0, n0 + 136 * i1), first)
+        for i in range(3):
+            ne = A("NE", n0 + 136 * i, n0 + 136 * i + 136)
+            if t in ONCE:
+                tt(ne, ps(at(i, 1), at(i, 1) + 136), A("NH", n0 + 136 * i, n0 + 136 * i + 136), ALU.not_equal)
+            lastfit(A("SC", n0 + 136 * i, n0 + 136 * i + 136), ne, ps(at(i, runs - 1), at(i, runs - 1) + 136))
+        out = v("R1" if t else "V1", t)
+        ts(out, A("SC", n0 + 16, n0 + 408, 17), 2.0 ** 24, -NONE, ALU.mult, ALU.add)
         if t:
-            home(t, A("R1", r0, r0 + 24), A("V1", 24 * (t - 1), 24 * t), "a_v1%d" % t, 12288)
-        to_list(sb, A(name, r0, r0 + 24), 2047, 1, SH[t], A("WL", 24 * t, 24 * t + 24))
+            home(t, out, v("V1", t), "a_v1%d" % t, 12288)
+        to_list(sb, out, 2047, 1, SH[t], A("WL", 24 * t, 24 * t + 24))
 
     def tests(t):
         tag[0] = "T%d" % t
-        a0, d0 = 6 * L * t, 768 * (t % 2)
-        k0, x0, lf = L * t, 8 * L * (t % 2), A("LF", 0, NL)
-        cp(A("KG", k0, k0 + L), A("KP", 0, NV), A("WL", 24 * t, 24 * t + 24))
-        dma(lambda e: [e.dma_start(T.DK[16 * t + z:16 * t + 16:2, :], T.KG[:, k0 + 192 * z:k0 + 192 * z + 192]) for z in range(2)],
-            [A("KG", k0, k0 + L)], [A("DK", t, t + 1)], 98304, n=2)
-        dma(lambda e: [e.dma_start(T.KL[:, k0:k0 + L], T.DK[16 * t:16 * t + 16, :])], [A("DK", t, t + 1)], [A("KL", k0, k0 + L)], 98304)
-        for c, n in [(0, 128), (128, 128)] + ([(256, 128)] if t < NT - 1 else [(256, 64), (320, 64)]):
-            out, even, odd = A("XT", x0 + 8 * c, x0 + 8 * (c + n)), A("KL", k0 + c // 2, k0 + (c + n) // 2), A("KL", k0 + 192 + c // 2, k0 + 192 + (c + n) // 2)
-            ts(out, lf, 16.0, None, ALU.mult, off=odd, s=act(out, lf, ACT.Identity, 0.0, 16.0, odd))
-            apart, y0 = (t, c) in SPLIT, 8 * L * (t % 2)
-            if apart:
-                cp(A("XA", y0 + 8 * c, y0 + 8 * (c + n)), lf, even)
-            else:
-                tt(out, lf, out, ALU.add, off=even)
+        d0, k0, x0, lf = 768 * (t % 2), L * t, 8 * L * ((t + 2) % XTN), A("LF", 0, NL)
+        if t in KG_WIDE:
+            wide = A("KS", L * (t % 2), L * (t % 2) + L)
+            cp(wide, A("KP", 0, NV), A("WL", 24 * t, 24 * t + 24))
+            gcp(A("KG", k0, k0 + L), wide)
+        else:
+            cp(A("KG", k0, k0 + L), A("KP", 0, NV), A("WL", 24 * t, 24 * t + 24))
+        dma(lambda e: [e.dma_start(T.KL[z:128:2, k0 + 192 * y:k0 + 192 * y + 192], T.KG[y:128:2, k0 + 192 * z:k0 + 192 * z + 192])
+                       for y in (1, 0) for z in range(2)], [A("KG", k0, k0 + L)], [A("KL", k0, k0 + L)], 98304, n=4)
+        for lo, hi in pairs(CUT_T[t]):
+            out = A("XT", x0 + 8 * lo, x0 + 8 * hi)
+            ts(out, lf, 16.0, None, ALU.mult, off=A("KL", k0 + 192 + lo // 2, k0 + 192 + hi // 2))
+            tt(out, lf, out, ALU.add, off=A("KL", k0 + lo // 2, k0 + hi // 2))
 
-            def two_kids(i):
-                return [(HBm(i), A("XT", x0 + 8 * c + i, x0 + 8 * (c + n), 8))] + ([(HBm(i), A("XA", y0 + 8 * c + i, y0 + 8 * (c + n), 8))] if apart else [])
-            b = 2 + c // 128
-            for y in range(2):
-                def piece(i):
-                    return [(HAm(i, 1 - y, t), A("AP", a0 + L * i + c, a0 + L * i + c + n))]
-                mm(bank(b, 128 * y + c % 128, 128 * y + c % 128 + n),
-                   piece(5) + two_kids(7) + two_kids(6) + piece(4) + two_kids(5) + piece(3) + two_kids(4) + two_kids(3) + piece(2) + two_kids(2) +
-                   piece(1) + two_kids(1) + piece(0) + [(HAm(0, y, t), A("LT", L * t + c, L * t + c + n))] + two_kids(0))
-            if (c + n) % 128 == 0:
-                c0 = d0 + 256 * (c // 128)
-                nonzero(A("BD", c0, c0 + 256), bank(b, 0, 256))
-                mm(bank(b, 256, 512), [(A("BD", c0, c0 + 128), A("FD", 0, 256)), (A("BD", c0 + 128, c0 + 256), A("FS", 0, 256))])
-                least(A("SD", c0, c0 + 256), A("RT", 0, 256), bank(b, 256, 512))
-        out = A("R2", 32 * (t - 1), 32 * t) if t else A("V2", 96, 128)
-        ts(out, A("SD", d0, d0 + 768), 61.0, 2.0 ** 20, ALU.add, ALU.min, off=A("RL", 10 + 2 * t, 12 + 2 * t))
+        def place(i):
+            return 256 * ((3 * t + i) % 8)
+        for i0, i1 in pairs(JOIN_T[t]):
+            for lo in range(128 * i0, 128 * i1, 128):
+                steps = []
+                for y in range(2):
+                    c, hi = place(lo // 128) + 128 * y, lo + 128
+
+                    def mine(i):
+                        return [(ps(c, c + 128), HAm(i, 1 - y, t), A("PL", LONG * t + AT[i] + lo, LONG * t + AT[i] + hi))]
+
+                    def theirs(i):
+                        return [(ps(c + 64 * z, c + 64 * z + 64), HBm(i), A("XT", x0 + 8 * lo + 2 * i + z, x0 + 8 * hi, 16)) for z in range(2)]
+                    steps += (mine(5) + theirs(7) + mine(4) + theirs(6) + theirs(5) +
+                              mine(3) + theirs(4) + mine(2) + theirs(3) + theirs(2) + mine(1) + theirs(1) + mine(0) + theirs(0))
+                    if y or not BOTH:
+                        mg(steps)
+                        steps = []
+            both, c0, n = ps(place(i0), place(i0) + 256 * (i1 - i0)), d0 + 256 * i0, 256 * (i1 - i0)
+            nonzero(A("BD", c0, c0 + n), both)
+            for i in range(i0, i1):
+                c, f0 = d0 + 256 * i, 16 * SH[t]
+                mg([(ps(place(i) + s, place(i) + 256, 2), A("BD", c + 128 * y, c + 128 * y + 128), A("FD", 256 * (s ^ y) + f0, 256 * (s ^ y) + f0 + 128))
+                    for s in range(2) for y in range(2)])
+            least(A("SD", c0, c0 + n), A("RT", 0, n), both)
+        out = v("R2" if t else "V2", t)
+        ts(out, A("SD", d0 + 31, d0 + 768, 32), 61.0, 2.0 ** 20, ALU.add, ALU.min)
         if t:
-            home(t, A("R2", 32 * (t - 1), 32 * (t - 1) + 24), A("V2", 24 * (t - 1), 24 * t), "a_v2%d" % t, 6144)
+            home(t, out, v("V2", t), "a_v2%d" % t, 6144)
 
     def v(name, t):
-        return A(name, 24 * slot(t), 24 * slot(t) + 24)
+        return A(name, 24 * t, 24 * t + 24)
 
     def tested(t):
         tag[0] = "L%d" % t
+        dead, n = ps(SMALL + 80, SMALL + 104), SMALL + 104
         if t:
-            mm(bank(6, 64, 88), [(IDm("NEG"), A("MG", 32 * s, 32 * s + 24)) for s in range(t)])
-            tt(A("CD", 0, 24), v("V1", t), bank(6, 64, 88), ALU.is_lt)
+            mm(dead, [(IDm("NEG"), v("MG", s)) for s in range(t)])
+            tt(A("CD", 0, 24), v("V1", t), dead, ALU.is_lt)
         else:
             ts(A("CD", 0, 24), v("V1", t), 0.0, None, ALU.is_lt)
-        mg([(bank(6, 96, 120), A("NON", 0, 128), A("CM", 0, 24)), (bank(6, 96, 120), A("TRI", 0, 128), A("CD", 0, 24)),
-            (bank(6, 104, 120), A("NON", 0, 128), A("CD", 0, 16)), (bank(6, 112, 120), A("NON", 0, 128), A("CD", 0, 8))])
+        mg([(ps(n, n + 24), A("NON", 0, 128), A("CM", 0, 24)), (ps(n, n + 24), A("TRI", 0, 128), A("CD", 0, 24)),
+            (ps(n + 8, n + 24), A("NON", 0, 128), A("CD", 0, 16)), (ps(n + 16, n + 24), A("NON", 0, 128), A("CD", 0, 8))])
 
     def merged(t):
         tag[0] = "M%d" % t
-        tt(A("MG", 32 * t, 32 * t + 24), v("V2", t), bank(6, 96, 120), ALU.is_lt)
+        tt(v("MG", t), v("V2", t), ps(SMALL + 104, SMALL + 128), ALU.is_lt)
 
     def fields():
         tag[0] = "F"
@@ -537,34 +598,31 @@ def build(g, T, topo, core, rank):
         for b in range(2):
             ts(A("VB", 120 * b, 120 * b + 120), A("V1", 0, 120), 11 + 3 * b, 5 << b, ALU.logical_shift_right, ALU.bitwise_and)
         tt(A("FF", 2, 600, 5), A("VB", 0, 120), A("VB", 120, 240), ALU.add)
+        mg([(ps(ROWS + 128 * i, ROWS + 128 * i + 128, 1, 40), A("CF", 0, 40), IDm("I1")) for i in range(3)], stop=False)
 
-    def store(t):
-        tag[0] = "O%d" % t
-        f0 = 120 * slot(t)
-        if t not in (2, 3):
-            n = 72 if t == 1 else 24
-            v2 = A("V2", 24 * slot(t), 24 * slot(t) + n)
-            ts(A("FF", f0 + 3, f0 + 5 * n, 5), v2, MAGIC / 4, MAGIC / 4, ALU.add, ALU.subtract)
-            tt(A("FF", f0 + 4, f0 + 5 * n, 5), A("FF", f0 + 3, f0 + 5 * n, 5), v2, ALU.subtract)
-        tt(A("FP", 128 * t, 128 * t + 128), A("MG", 32 * t, 32 * t + 32), A("FF", f0, f0 + 128), ALU.mult, off=A("L5", 0, 8))
-        mg([(bank(7, 128 * i, 128 * i + 128, 1, 40), A("FP", 128 * t + 40 * i, 128 * t + 40 * i + 40), IDm("I1")) for i in range(3)],
-           start=False, stop=t == NT - 1)
+    def store(t0, t1):
+        tag[0] = "O%d" % (t1 - 1)
+        lo, hi, end = 24 * t0, 24 * t1, -(-120 * t1 // 16) * 16
+        ts(A("FF", 5 * lo + 3, 5 * hi, 5), A("V2", lo, hi), 4 * MAGIC, 4 * MAGIC, ALU.add, ALU.subtract)
+        tt(A("FF", 5 * lo + 4, 5 * hi, 5), A("FF", 5 * lo + 3, 5 * hi, 5), A("V2", lo, hi), ALU.subtract)
+        tt(A("FP", 5 * lo, end), A("MG", 0, -(-end // 5)), A("FF", 5 * lo, end), ALU.mult, off=A("L5", 5 * lo // 16, end // 16))
+        mg([(ps(ROWS + 128 * (i % 3), ROWS + 128 * (i % 3) + 128, 1, 40), A("FP", 40 * i, 40 * i + 40), IDm("I1")) for i in range(3 * t0, 3 * t1)],
+           start=False, stop=t1 == NT)
 
-    for part in PARTS:
-        if part != "A":
-            (claims if part[0] == "C" else tests)(int(part[1]))
+    for t in range(NT):
+        claims(t)
+    for t in range(NT):
+        tests(t)
     fields()
     for t in range(NT):
         tested(t)
         merged(t)
-    for t in range(NT):
-        store(t)
-    ts(A("YS", 0, L, 1, 0, 40), bank(7, 0, L, 1, 40), col(YSC, 40), None, ALU.mult)
+        for t0, t1 in pairs(CUT_O):
+            if t1 == t + 1:
+                store(t0, t1)
+    ts(A("YS", 0, L, 1, 0, 40), ps(ROWS, ROWS + L, 1, 40), col(YSC, 40), None, ALU.mult)
     dma(lambda e: [e.dma_start(T.y[:], T.YS[0:40, :])], [A("YS", 0, L)], [], 61440)
     return ops
-
-
-LOADS = (("BK", 1048576), ("KDI", 786432), ("LF", 1310720))
 
 
 def depend(ops):
@@ -575,9 +633,7 @@ def depend(ops):
     hist = {}
     deps = []
     for i, o in enumerate(ops):
-        d = set()
-        if "after" in o:
-            d.add(o["after"])
+        d = set(o.get("after", ()))
         acc = [(a, False) for a in o["r"]] + [(a, True) for a in o["w"]]
         for a, wr in acc:
             for (b, bw, j) in hist.get(a[0], []):
@@ -593,203 +649,45 @@ def depend(ops):
     return deps
 
 
-def schedule(ops, deps):
-    n = len(ops)
-    succ = [[] for _ in range(n)]
-    for i in range(n):
-        for j in deps[i]:
-            succ[j].append(i)
-    alts, lag = [], []
-    for o in ops:
-        e, _, c = o["alts"][0]
-        if e == "X":
-            alts.append([("L", o["link"] / LINK)])
-            lag.append(c)
-        elif "dma" in o:
-            alts.append([(e, 0.1 + o["bytes"] / 2.5e5)])
-            lag.append(2.0)
-        else:
-            alts.append([(a[0], a[2]) for a in o["alts"]])
-            lag.append(LAT)
+QUEUES = "VSPGYLRHFZ"
+PACES = ((1.0, 1.15, 1.15, 1.15, 0.15, 1.1, 1.1), (1.0, 1.0, 1.0, 1.0, 0.12, 1.0, 1.0), (0.8, 1.25, 1.25, 1.25, 0.15, 1.1, 1.2), (1.3, 1.1, 1.1, 1.1, 0.2, 1.3, 1.5))
+PARTS = "C0 A C1 T0 C2 C3 T1 C4 T2 T3 T4".split()
+ONV = [("A", "XT", 0)] + [("C%d" % t, "XC", k) for t in range(4) for k in (2, 3)] + [("C%d" % t, "NE", 1) for t in range(NT)]
+TABLES = {"K": -400.0, "N": -400.0, "N2": -390.0, "K2": -100.0, "K3": -95.0, "K4": -90.0}
+HOLD, OWN, FIRST, STEP = 0.2, 1.0, 200.0, 0.02
+SHARES = (0.25, 0.25, 0.25, 0.25)
+TRIES, ROUNDS, SEED, WARM, HEAT, MEAN = 28000, 18000, 2, 0.08, 0.02, 0.02
+JUST, AGAIN, SWAP, WP = 8, 0.2, 0.15, 0.0
+WV, WS, WX, WH, CRIT = 0.2, 0.1, 0.1, 0.3, 0.3
 
-    due, seen = [1e9] * n, {}
-    for i, o in enumerate(ops):
-        part = o["tag"] if o["tag"] in PARTS else "T" + o["tag"][1:] if o["tag"][0] in "LMO" else "C4" if o["tag"] == "F" else None
-        if part:
-            long_ = bool(o.get("g")) and alts[i][0][1] > 0.6
-            seen[part] = seen.get(part, 0) + (cnt(o["w"][0]) if long_ else 0)
-            due[i] = PACE * (PARTS.index(part) + (seen[part] / (16.0 * L) if long_ else SOON if part == o["tag"] else LATE))
-        elif "dma" in o or "send" in o:
-            due[i] = i - 1e3 if "dma" in o else EARLY
-    for i in range(n - 1, -1, -1):
-        slack = SLACK if ops[i]["tag"] in RANK and alts[i][0][0] == "V" else 0.0
-        if "dma" in ops[i]:
-            continue
-        due[i] = min([due[i]] + [due[j] - lag[i] - slack for j in succ[i]]) - min(a[1] for a in alts[i])
-    left = [len(d) for d in deps]
-    ready = {i: 0.0 for i in range(n) if not left[i]}
-    free = {e: 0.0 for e in "VSPGYL"}
+
+def place(order, links, eng, cs, banks, fixed):
+    n, nq = len(eng), len(QUEUES)
     st, fin, ch = [0.0] * n, [0.0] * n, [0] * n
-
-    def key(x):
-        i, k = x
-        if ops[i]["tag"] not in RANK:
-            return (2, -due[i] - (OWN if k == 0 and len(alts[i]) > 1 else 0.0), -i)
-        return (alts[i][k][1] < 1, -RANK.index(ops[i]["tag"]), -i)
-    banks = [{a[0] for a in o["r"] + o["w"] if SCRATCH[a[0]][0] == "psum"} for o in ops]
-    held = {}
-    while ready:
-        best = None
-        for i in ready:
-            for b in banks[i]:
-                if b in held:
-                    j = held[b]
-                    ready[i] = max(ready[i], fin[j] + (0.0 if alts[i][0][0] == alts[j][0][0] == "P" else lag[j]))
-        for e in free:
-            mine = [(i, k) for i in ready for k, a in enumerate(alts[i]) if a[0] == e and ops[i].get("first", k) == k]
-            if mine:
-                t = max(free[e], min(ready[i] for i, k in mine))
-                if best is None or t < best[0]:
-                    best = (t, e, mine)
-        t, e, mine = best
-        i, k = max(((i, k) for i, k in mine if ready[i] <= t + (AHEAD if alts[i][k][1] < 1 else 0.0)), key=key)
-        st[i], ch[i] = max(t, ready.pop(i)), k
-        fin[i] = free[e] = st[i] + alts[i][k][1]
-        for b in banks[i]:
-            held[b] = i
-        for j in succ[i]:
-            left[j] -= 1
-            if not left[j]:
-                ready[j] = max(fin[x] + (0.0 if alts[x][0][0] == alts[j][0][0] == "P" else lag[x]) for x in deps[j])
-
-    ispe = [a[0][0] == "P" for a in alts]
-    banks = [sorted(b) for b in banks]
-    models = []
-    for kc, kg, kp, wait, hop in MODELS:
-        cs = [[c * (kp if e == "P" else hop if e in "YL" else kc * (kg if ops[i].get("g") else 1.0)) for e, c in alts[i]] for i in range(n)]
-        lg = [wait if x == LAT else x * hop for x in lag]
-        models.append((cs, [[(j, 0.0 if ispe[i] and ispe[j] else lg[j]) for j in deps[i]] for i in range(n)], wait))
-
-    def replay(order, ch, model):
-        cs, pre, wait = model
-        free, last, fin, why = dict.fromkeys("VSPGYL", 0.0), {}, [0.0] * n, [-1] * n
-        for i in order:
-            e = alts[i][ch[i]][0]
-            t, y = free[e], last.get(e, -1)
-            for j, x in pre[i]:
-                if fin[j] + x > t:
-                    t, y = fin[j] + x, j
-            for b in banks[i]:
-                j = last.get(b, -1)
-                if j >= 0 and fin[j] + (0.0 if ispe[i] and ispe[j] else wait) > t:
-                    t, y = fin[j] + (0.0 if ispe[i] and ispe[j] else wait), j
-                last[b] = i
-            fin[i] = free[e] = t + cs[i][ch[i]]
-            last[e], why[i] = i, y
-        return fin, why
-
-    def value(p, ch):
-        for i in range(n):
-            for j in deps[i]:
-                if p[j] >= p[i]:
-                    p[i] = p[j] + 1e-4
-        order = sorted(range(n), key=lambda i: p[i])
-        runs = [replay(order, ch, m) for m in models]
-        onv = sum(alts[i][0][1] for i in flex if not ch[i])
-        return sum(max(r[0]) / m[0] for r, m in zip(runs, MODELS)) / len(runs) + WV * onv + WS * sum(runs[0][0]) / n, order, runs[0]
-    groups = {}
-    for i, o in enumerate(ops):
-        groups.setdefault(o["tag"], []).append(i)
-        groups.setdefault((o["tag"], o["w"][0][0] if o["w"] else ""), []).append(i)
-    groups = list(groups.values())
-    flex = [i for i in range(n) if len(alts[i]) > 1]
-    rng = np.random.default_rng(SEED)
-    now = best = value(list(st), ch) + (list(ch),)
-    for r in range(ROUNDS):
-        fin, why = now[2]
-        p, c = [fin[i] - models[0][0][i][now[3][i]] for i in range(n)], list(now[3])
-        for x, i in enumerate(now[1]):
-            p[i] += 1e-7 * x
-        path, i = [], max(range(n), key=lambda j: fin[j])
-        while i >= 0:
-            path.append(i)
-            i = why[i]
-        u = float(rng.random())
-        i = path[int(rng.integers(0, len(path)))]
-        if rng.random() < FILL:
-            e = "VSP"[int(rng.integers(0, 5)) % 3]
-            mine = [j for j in now[1] if alts[j][c[j]][0] == e]
-            gaps = [(fin[a], p[b]) for a, b in zip(mine, mine[1:]) if p[b] - fin[a] > 0.1]
-            if not gaps:
-                continue
-            a, b = gaps[int(rng.integers(0, len(gaps)))]
-            fits = [j for j in now[1] if p[j] > b and any(x[0] == e for x in alts[j]) and all(fin[k] + x < b for k, x in models[0][1][j])][:6]
-            if not fits:
-                continue
-            j = fits[int(rng.integers(0, len(fits)))]
-            c[j] = [x[0] for x in alts[j]].index(e)
-            p[j] = b - 1e-5
-        elif u < 0.35:
-            j = why[i]
-            if j < 0 or j in deps[i]:
-                continue
-            if u < 0.2:
-                back(p, deps, i, p[j] - 1e-5)
-            else:
-                p[j] = p[i] + 1e-5
-        elif u < 0.5:
-            i = i if len(alts[i]) > 1 else flex[int(rng.integers(0, len(flex)))]
-            was = c[i]
-            c[i] = (was + int(rng.integers(1, len(alts[i])))) % len(alts[i])
-            if u < 0.45:
-                j = flex[int(rng.integers(0, len(flex)))]
-                if c[j] == c[i] and j != i and was < len(alts[j]) and abs(alts[j][0][1] - alts[i][0][1]) < 0.3:
-                    c[j] = was
-        elif u < 0.75:
-            i = i if u < 0.65 else int(rng.integers(0, n))
-            back(p, deps, i, p[i] + float(rng.normal()) * 2.0)
-        else:
-            d = float(rng.normal()) * float(rng.choice([0.5, 2.0, 6.0]))
-            for i in groups[int(rng.integers(0, len(groups)))]:
-                back(p, deps, i, p[i] + d)
-        v = value(p, c) + (c,)
-        if v[0] <= now[0] + HEAT * (1.0 - r / ROUNDS) * float(rng.exponential()):
-            now = v
-            if v[0] < best[0]:
-                best = v
-    PLAN["v"] = best[0]
-    last = {}
-    for i in best[1]:
-        for b in banks[i]:
-            if b in last and last[b] not in deps[i]:
-                deps[i].append(last[b])
-            last[b] = i
-    return [(i, best[3][i]) for i in best[1]], best[2][0]
-
-
-def back(p, deps, i, t):
-    todo = [(i, t)]
-    p[i] = t + 1.0 if t > p[i] else p[i]
-    while todo:
-        j, x = todo.pop()
-        if p[j] > x:
-            p[j] = x
-            todo += [(k, x - 1e-5) for k in deps[j]]
-
-
-def place(order, links, alts, banks, fixed):
-    n = len(alts)
-    st, fin, ch = [0.0] * n, [0.0] * n, [0] * n
-    busy = {e: ([], [], 0.0) for e in "VSPGYLHR"}
-    busy.update({"B%d" % b: ([], [], LAT) for b in range(8)})
+    busy = [([], [], 0.0 if r < nq else LAT) for r in range(nq + 8)]
     for i in order:
         t0 = 0.0
         for j, x in links[i]:
             if fin[j] + x > t0:
                 t0 = fin[j] + x
+        k = fixed[i]
+        if k >= 0 and not banks[i]:
+            a, z, _ = busy[eng[i][k]]
+            c = cs[i][k]
+            x = y = len(z)
+            while x and z[x - 1] > t0:
+                x -= 1
+            w = c - 1e-9
+            while x < y and a[x] < t0 + w:
+                t0 = z[x]
+                x += 1
+            st[i], fin[i], ch[i] = t0, t0 + c, k
+            a.insert(x, t0)
+            z.insert(x, t0 + c)
+            continue
         best = 1e9
-        for k in (fixed[i],) if fixed[i] >= 0 else range(len(alts[i])):
-            e, c = alts[i][k]
+        for k in (k,) if k >= 0 else range(len(eng[i])):
+            e, c = eng[i][k], cs[i][k]
             res = [busy[e]] + [busy[b] for b in banks[i]]
             t, moved = t0, True
             while moved:
@@ -801,7 +699,7 @@ def place(order, links, alts, banks, fixed):
                     w += c - 1e-9
                     while x < y and a[x] < t + w:
                         t, x, moved = z[x], x + 1, len(res) > 1
-            v = t + 2 * c if e == "V" else t + c
+            v = t + c if e else t + 2 * c
             if v < best:
                 best, st[i], fin[i], ch[i], took = v, t, t + c, k, res
         t = st[i]
@@ -814,70 +712,53 @@ def place(order, links, alts, banks, fixed):
     return st, fin, ch
 
 
-def schedule(ops, deps):
-    n = len(ops)
-    alts, lag = [], []
-    for o in ops:
-        e, _, c = o["alts"][0]
-        if e == "X":
-            alts.append([(o.get("via", "L"), o["link"] / LINK)])
-            lag.append(c)
-        elif "dma" in o:
-            alts.append([(e, 0.1 + o["bytes"] / 2.5e5)])
-            lag.append(2.0 if o["tag"] == "K" else DLAG)
-        else:
-            alts.append([(a[0], a[2]) for a in o["alts"]])
-            lag.append(LAT)
-    banks = [sorted({a[0] for a in o["r"] + o["w"] if SCRATCH[a[0]][0] == "psum"}) for o in ops]
-    pre, suc, before = [], [[] for _ in range(n)], []
+def fill_gaps(ops, order, ch, pre, eng, cs, banks, rng):
+    n, nq = len(ops), len(QUEUES)
+    suc = [[] for _ in range(n)]
     for i in range(n):
-        m = 0
-        for j in deps[i]:
-            m |= before[j]
-        pre.append([(j, 0.0 if alts[i][0][0] == alts[j][0][0] in "PH" else lag[j]) for j in deps[i] if not m >> j & 1])
         for j, x in pre[i]:
             suc[j].append((i, x))
-        before.append(m | sum(1 << j for j in deps[i]))
 
     def justify(s, fixed):
-        s = place(sorted(range(n), key=lambda i: (-s[1][i], -i)), suc, alts, banks, fixed)
-        return place(sorted(range(n), key=lambda i: (-s[1][i], i)), pre, alts, banks, fixed)
+        s = place(sorted(range(n), key=lambda i: (-s[1][i], -i)), suc, eng, cs, banks, fixed)
+        return place(sorted(range(n), key=lambda i: (-s[1][i], i)), pre, eng, cs, banks, fixed)
 
     def value(s):
-        return max(s[1]) + WS * sum(s[1]) / n + WV * sum(alts[i][0][1] for i in flex if not s[2][i]) + WX * sum(s[1][i] for i in moves) / len(moves) + WH * s[1][relay]
-    relay = [i for i in range(n) if alts[i][0][0] == "R"][0]
+        return max(s[1]) + WS * sum(s[1]) / n + WV * sum(cs[i][0] for i in flex if not s[2][i]) + WX * sum(s[1][i] for i in moves) / len(moves) + WH * s[1][relay] + WP * sum(s[1][i] for i in tensor) / len(tensor)
+    tensor = [i for i in range(n) if eng[i][0] == 2 and cs[i][0] > 1.5]
+    big = [i for i in range(n) if eng[i][0] < 2 and cs[i][0] > 1.3]
 
     def blocked(s):
         st, fin, ch = s
         ends = {}
         for j in range(n):
-            for r in [alts[j][ch[j]][0]] + banks[j]:
-                ends[(r, round(fin[j] + (LAT if len(r) > 1 else 0.0), 6))] = j
-        pairs, i = [], max(range(n), key=lambda j: fin[j])
+            for r in (eng[j][ch[j]],) + banks[j]:
+                ends[(r, round(fin[j] + (LAT if r >= nq else 0.0), 6))] = j
+        found, i = [], max(range(n), key=lambda j: fin[j])
         while st[i] > 1e-9:
             j = [j for j, x in pre[i] if fin[j] + x > st[i] - 1e-7]
             if not j:
-                j = [ends[k] for k in [(r, round(st[i], 6)) for r in [alts[i][ch[i]][0]] + banks[i]] if k in ends]
+                j = [ends[k] for k in [(r, round(st[i], 6)) for r in (eng[i][ch[i]],) + banks[i]] if k in ends]
                 if not j:
                     break
-                pairs.append((i, j[0]))
+                found.append((i, j[0]))
             i = j[0]
-        return pairs
+        return found
     held = [None, None]
-    moves = [i for i in range(n) if alts[i][0][0] in "LYH"]
+    relay = [i for i in range(n) if QUEUES[eng[i][0]] == "R"][-1]
+    moves = [i for i in range(n) if QUEUES[eng[i][0]] in "LYH"]
     groups = {}
     for i, o in enumerate(ops):
         groups.setdefault(o["tag"], []).append(i)
         groups.setdefault((o["tag"], o["w"][0][0] if o["w"] else ""), []).append(i)
     groups = list(groups.values())
-    flex = [i for i in range(n) if len(alts[i]) > 1]
-    rng = np.random.default_rng(SEED)
-    fixed = [o.get("first", -1 if len(o["alts"]) > 1 else 0) for o in ops]
-    s = place(range(n), pre, alts, banks, fixed)
-    for _ in range(8):
+    flex = [i for i in range(n) if len(eng[i]) > 1]
+    fixed = [-1 if len(eng[i]) > 1 and o["tag"][0] == "K" else ch[i] for i, o in enumerate(ops)]
+    s = place(order, pre, eng, cs, banks, fixed)
+    for _ in range(JUST):
         s = justify(s, fixed)
     now = best = (value(s), s, fixed)
-    for r in range(ROUNDS):
+    for r in range(TRIES):
         p, ch, fixed = list(now[1][0]), now[1][2], list(now[2])
         u = rng.random()
         if rng.random() < CRIT:
@@ -888,14 +769,25 @@ def schedule(ops, deps):
             i, j = held[1][int(rng.integers(0, len(held[1])))]
             if u < 0.4:
                 p[i] = p[j] - 1e-4 - (rng.exponential() if u < 0.2 else 0.0)
-            elif u < 0.8 or len(alts[j]) == 1:
+            elif u < 0.8 or len(eng[j]) == 1:
                 p[j] = p[i] + 1e-4 + (rng.exponential() if u < 0.6 else 0.0)
                 for k in range(j, n):
                     for m, x in pre[k]:
                         if p[k] <= p[m]:
                             p[k] = p[m] + 1e-6
             else:
-                fixed[j] = (ch[j] + int(rng.integers(1, len(alts[j])))) % len(alts[j])
+                fixed[j] = (ch[j] + int(rng.integers(1, len(eng[j])))) % len(eng[j])
+        elif u < SWAP:
+            i = big[int(rng.integers(0, len(big)))]
+            near = [j for j in big if j != i and abs(p[j] - p[i]) < 12]
+            j = near[int(rng.integers(0, len(near)))]
+            p[i], p[j] = p[j], p[i]
+            if len(eng[i]) > 1 and len(eng[j]) > 1:
+                fixed[i], fixed[j] = ch[j], ch[i]
+            for k in range(min(i, j), n):
+                for m, x in pre[k]:
+                    if p[k] <= p[m] and m in (i, j):
+                        p[k] = p[m] + 1e-6
         elif u < 0.3:
             for i in rng.integers(0, n, int(rng.integers(1, 4))):
                 p[i] += rng.normal() * 3.0
@@ -905,8 +797,8 @@ def schedule(ops, deps):
                 p[i] += d
         elif u < 0.8:
             i = flex[int(rng.integers(0, len(flex)))]
-            fixed[i] = (ch[i] + int(rng.integers(1, len(alts[i])))) % len(alts[i])
-            like = [j for j in flex if ch[j] == fixed[i] and ch[i] < len(alts[j]) and abs(alts[j][0][1] - alts[i][0][1]) < 0.3 and abs(p[j] - p[i]) < 15]
+            fixed[i] = (ch[i] + int(rng.integers(1, len(eng[i])))) % len(eng[i])
+            like = [j for j in flex if ch[j] == fixed[i] and ch[i] < len(eng[j]) and abs(cs[j][0] - cs[i][0]) < 0.3 and abs(p[j] - p[i]) < 15]
             if u < 0.7 and like:
                 fixed[like[int(rng.integers(0, len(like)))]] = ch[i]
         else:
@@ -918,44 +810,235 @@ def schedule(ops, deps):
             for j, x in pre[i]:
                 if p[j] >= p[i]:
                     p[j] = p[i] - 1e-6
-        s = place(sorted(range(n), key=lambda i: p[i]), pre, alts, banks, fixed)
-        if rng.random() < 0.2:
+        s = place(sorted(range(n), key=lambda i: p[i]), pre, eng, cs, banks, fixed)
+        if rng.random() < AGAIN:
             s = justify(s, fixed)
         v = value(s)
-        if v <= now[0] + HEAT * (1.0 - r / ROUNDS) * rng.exponential():
+        if v <= now[0] + WARM * (1.0 - r / TRIES) * rng.exponential():
             now = (v, s, fixed)
             if v < best[0]:
                 best = now
-    PLAN["v"] = best[0]
     st, fin, ch = best[1]
-    order = sorted(range(n), key=lambda i: (st[i], i))
+    return sorted(range(n), key=lambda i: (st[i], i)), ch
+
+
+def schedule(ops, deps):
+    n, nq = len(ops), len(QUEUES)
+    eng = [[QUEUES.index(a[0]) for a in o["alts"]] for o in ops]
+    banks = [tuple(sorted({nq + b for a in o["r"] + o["w"] for b in banks_of(a)})) for o in ops]
+    pre, suc, before = [], [[] for _ in range(n)], []
+    for i in range(n):
+        m = 0
+        for j in deps[i]:
+            m |= before[j]
+        pre.append([j for j in deps[i] if not m >> j & 1])
+        for j in pre[i]:
+            suc[j].append(i)
+        before.append(m | sum(1 << j for j in deps[i]))
+    paces = []
+    for gf, kc, kp, kg, wait, hop, link in PACES:
+        cs = [[c * (kp if e == "P" else kg if e == "G" else link if e not in "VS" else gf if o.get("g") else kc) for e, _, c in o["alts"]] for o in ops]
+        lag = [o["lag"] * hop if "lag" in o else wait for o in ops]
+        paces.append((cs, [[(j, 0.0 if eng[i][0] == eng[j][0] == 2 else lag[j]) for j in pre[i]] for i in range(n)], wait))
+
+    def replay(order, ch, pace):
+        cs, links, wait = pace
+        free, pe, fin = [0.0] * (nq + 8), [False] * (nq + 8), [0.0] * n
+        for i in order:
+            k = ch[i]
+            e = eng[i][k]
+            t = free[e]
+            for j, x in links[i]:
+                x += fin[j]
+                if x > t:
+                    t = x
+            if banks[i]:
+                for b in banks[i]:
+                    x = free[b] if e == 2 and pe[b] else free[b] + wait
+                    if x > t:
+                        t = x
+                t += cs[i][k]
+                for b in banks[i]:
+                    free[b], pe[b] = t, e == 2
+            else:
+                t += cs[i][k]
+            fin[i] = free[e] = t
+        return fin
+
+    def value(order, ch):
+        v = 0.0
+        for pace, w in zip(paces, weight):
+            fin = replay(order, ch, pace)
+            v += (max(fin) + MEAN * sum(fin) / n) * w
+        return v
+
+    cs, links, wait = paces[0]
+    long_ = [bool(o.get("g")) and cs[i][0] > 0.7 and o["tag"] in PARTS and o["w"][0][0] in ("XT", "XC") for i, o in enumerate(ops)]
+
+    plain, t, begin = [0.0] * n, 0.0, {}
+    for p in PARTS:
+        begin[p] = t
+        for i in range(n):
+            if ops[i]["tag"] == p and eng[i][0] < 2:
+                plain[i] = t
+                t += cs[i][0] / 2
+    for i, o in enumerate(ops):
+        tg = o["tag"]
+        if tg in TABLES:
+            plain[i] = TABLES[tg] + i * STEP
+        elif not long_[i]:
+            plain[i] = begin[tg if tg in begin else "T" + (tg + "4")[1]] + i * 1e-3 - (0.0 if eng[i][0] == 2 and cs[i][0] > 0.4 else FIRST)
+    kinds = [i if long_[i] or "dma" in o or o["tag"] in TABLES else (o["tag"], o["w"][0][0] if o["w"] else "") for i, o in enumerate(ops)]
+    keys = sorted(set(kinds), key=str)
+    kinds = [keys.index(k) for k in kinds]
+
+    def dues(shift):
+        return [plain[i] + shift[kinds[i]] for i in range(n)]
+
+    def dispatch(due, own, onv):
+        left = [len(p) for p in pre]
+        can = [e if len(e) == 1 or ops[i]["tag"][0] == "K" else [e[0 if i in onv else -1]] for i, e in enumerate(eng)]
+        ready = [[] for _ in range(nq)]
+        at, fin, ch, order = [0.0] * n, [0.0] * n, [0] * n, []
+        free, pe = [0.0] * (nq + 8), [False] * (nq + 8)
+        for i in range(n):
+            if not left[i]:
+                for e in can[i]:
+                    ready[e].append(i)
+        for _ in range(n):
+            best, be = 1e9, -1
+            for e in range(nq):
+                if ready[e] and free[e] < best:
+                    t = 1e9
+                    for i in ready[e]:
+                        x = at[i]
+                        for b in banks[i]:
+                            y = free[b] if e == 2 and pe[b] else free[b] + wait
+                            if y > x:
+                                x = at[i] = y
+                        if x < t:
+                            t = x
+                    t = max(t, free[e])
+                    if t < best:
+                        best, be = t, e
+            i = min((i for i in ready[be] if at[i] <= best + (0.0 if long_[i] else HOLD)),
+                    key=lambda i: due[i] + (own if be == 0 and len(eng[i]) > 1 else 0.0))
+            k = ch[i] = eng[i].index(be)
+            fin[i] = free[be] = max(best, at[i]) + cs[i][k]
+            for b in banks[i]:
+                free[b], pe[b] = fin[i], be == 2
+            for e in can[i]:
+                ready[e].remove(i)
+            order.append(i)
+            for j in suc[i]:
+                left[j] -= 1
+                if not left[j]:
+                    at[j] = max(fin[x] + y for x, y in links[j])
+                    for e in can[j]:
+                        ready[e].append(j)
+        return order, ch
+
+    rng = np.random.default_rng(SEED)
+    both = [i for i in range(n) if len(eng[i]) > 1 and ops[i]["tag"][0] != "K"]
+    onv = {i for p, b, k in ONV for i in [i for i in both if ops[i]["tag"] == p and ops[i]["w"][0][0] == b][k:k + 1]}
+    order, ch = dispatch(dues([0.0] * len(keys)), OWN, onv)
+    weight = [1.0 / max(replay(order, ch, pace)) for pace in paces]
+    weight = [w / weight[0] * s for w, s in zip(weight, SHARES)]
+    flex = [i for i in range(n) if len(eng[i]) > 1]
+    order, ch = fill_gaps(ops, order, ch, links, eng, cs, banks, rng)
+    PLAN["first"] = [max(replay(order, ch, pace)) for pace in paces]
+    now = best = (value(order, ch), order, ch)
+    draw = rng.random((ROUNDS, 5)).tolist()
+    for r in range(ROUNDS):
+        u, a, b, c, d = draw[r]
+        order, ch = now[1], now[2]
+        if u < 0.2:
+            i = flex[int(a * len(flex))]
+            ch = list(ch)
+            was = ch[i]
+            ch[i] = (was + 1 + int(b * (len(eng[i]) - 1))) % len(eng[i])
+            if u < 0.1:
+                p = order.index(i)
+                near = [j for j in order[max(0, p - 30):p + 30] if j != i and ch[j] == ch[i] and len(eng[j]) > max(was, 1)]
+                if near:
+                    ch[near[int(c * len(near))]] = was
+        else:
+            p = int(a * n)
+            far = 1 + int(-math.log(1.0 - b) * (4.0, 12.0, 40.0)[int(c * 3)])
+            step, q, kin = (-1, max(0, p - far), pre) if u < 0.6 else (1, min(n - 1, p + far), suc)
+            take, need = {order[p]}, set(kin[order[p]])
+            for x in range(p + step, q + step, step):
+                if order[x] in need:
+                    take.add(order[x])
+                    need.update(kin[order[x]])
+            lo, hi = min(p, q), max(p, q) + 1
+            moved, rest = [j for j in order[lo:hi] if j in take], [j for j in order[lo:hi] if j not in take]
+            order = order[:lo] + (moved + rest if step < 0 else rest + moved) + order[hi:]
+        x = value(order, ch)
+        if x <= now[0] - HEAT * (1.0 - r / ROUNDS) * math.log(1.0 - d):
+            now = (x, order, ch)
+            if x < best[0]:
+                best = now
+    _, order, ch = best
+    PLAN["last"] = [max(replay(order, ch, pace)) for pace in paces]
     last = {}
     for i in order:
         for b in banks[i]:
             if b in last and last[b] not in deps[i]:
                 deps[i].append(last[b])
             last[b] = i
-    return [(i, ch[i]) for i in order], fin
+    return [(i, ch[i]) for i in order], replay(order, ch, paces[0])
 
 
 def helpers(T, topo, rank):
     c = T.cores[rank]
-    return [h for h in topo.cores_of(c) if h not in T.cores and topo.die(h) == topo.die(c)
-            and all(topo.may_write(h, T.cores[(rank + t) % NR]) for t in range(1, NT))][:NH]
+    return [h for h in topo.cores_of(c) if h not in T.cores and topo.die(h) == topo.die(c)][:2]
+
+
+def routes(T, topo, rank):
+    c, out = T.cores[rank], {}
+    for t in range(1, NT):
+        out.setdefault(topo.chip(T.cores[(rank + t) % NR]), []).append(t)
+    res = []
+    for chip, visits in out.items():
+        gate = [r for r in range(NR) if topo.chip(T.cores[r]) == chip and topo.die(T.cores[r]) == topo.die(c)]
+        if chip != topo.chip(c) and len(visits) > 1 and gate:
+            res.append((visits, helpers(T, topo, gate[0])[1]))
+        else:
+            res += [([t], None) for t in visits]
+    return res
 
 
 def hand_on(g, core, T, topo, rank):
-    hs = helpers(T, topo, rank)
-    k = hs.index(core)
-    to = [(T.cores[(rank + t) % NR], 6 * L * t, "a_pp%d" % t) for t in range(1 + k, NT, len(hs))]
-    to[1:1] = [(h, 0, "relay") for h in hs[k + 1:k + 2]]
-    g.wait_ge(T.sem["relay"], 8)
-    for c, c0, sem in to:
-        rid, pid, _se = topo.addr(c)
-        en = topo.engines(core, c)
-        g.remote_dma(T.AP[:, c0 + L:c0 + 6 * L], T.AP[:, L:6 * L], T.sem[sem], T.sem["sent"], pid, rid,
-                     sum(1 << x for x in (en[-8:] if sem == "relay" else en[:8])))
-    g.wait_ge(T.sem["sent"], 8 * len(to))
+    sent = [0]
+
+    def write(to, t_to, t_from, n, sem, last):
+        lo, hi = PARCELS[n]
+        rid, pid, _se = topo.addr(to)
+        en = topo.engines(core, to)
+        g.remote_dma(T.PL[:, LONG * t_to + lo:LONG * t_to + hi], T.PL[:, LONG * t_from + lo:LONG * t_from + hi], T.sem[sem], T.sem["sent"], pid, rid,
+                     sum(1 << x for x in (en[-8:] if last else en[:8])))
+        sent[0] += 8
+    if core == helpers(T, topo, rank)[0]:
+        legs = [(k, n) for k in range(len(routes(T, topo, rank))) for n in range(len(PARCELS))]
+        here = 0
+        for k, n in legs:
+            visits, gate = routes(T, topo, rank)[k]
+            while here <= n:
+                g.wait_ge(T.sem["own%d" % here], 8)
+                here += 1
+            if gate is None:
+                write(T.cores[(rank + visits[0]) % NR], visits[0], 0, n, "a_pl%d" % visits[0], True)
+            else:
+                write(gate, visits[0], 0, n, "far%d_%d" % (visits[0], n), True)
+    else:
+        for visits, r in sorted((visits, r) for r in range(NR) for visits, gate in routes(T, topo, r) if gate == core):
+            for n in range(len(PARCELS)):
+                g.wait_ge(T.sem["far%d_%d" % (visits[0], n)], 8)
+                for k, t in enumerate(visits):
+                    write(T.cores[(r + t) % NR], t, visits[0], n, "a_pl%d" % t, k % 2)
+    if sent[0]:
+        g.wait_ge(T.sem["sent"], sent[0])
 
 
 def rank_program(g, core, T, topo):
@@ -979,7 +1062,7 @@ def rank_program(g, core, T, topo):
     for i, k in PLAN["order"]:
         o = ops[i]
         e, f, _ = o["alts"][k]
-        if e == "X":
+        if f is None:
             if o["arr"]:
                 token[i] = (o["arr"], o["n"])
                 total[o["arr"]] = o["n"]

import math
import numpy as np
from concourse.bass import DstId, RemoteDMATransfer
from concourse.mybir import AluOpType as ALU, ActivationFunctionType as ACT

NR, NV, NL, NB, L, CAP, NT = 8, 1536, 5120, 2048, 384, 192, 5
SH = [t * (t + 1) // 2 % 8 for t in range(NT)]
F, B, I32, U, HF = "float32", "bfloat16", "int32", "uint16", "float16"
MAGIC = 1.5 * 2.0 ** 23
NONE = 17.0 * 2 ** 19
XCN, XTN = 3, 3
LONG = 6 * L
AT = {1: 0, 3: L, 5: 2 * L, 0: 3 * L, 2: 4 * L, 4: 5 * L}
PARCELS = ((0, 3 * L), (3 * L, LONG))


def _sb(n, d):
    return ("sbuf", [128, n], d)


SCRATCH = {
    "LF": _sb(NL, B), "IV": _sb(NV, B), "KDI": _sb(NV, I32), "KDF": _sb(NV, F), "KS": _sb(NV, F), "KP": _sb(NV, F), "BK": _sb(NB, I32),
    "LVI": _sb(24, I32), "LBI": _sb(24, I32), "LVU": _sb(24, U), "LBU": _sb(120, U),
    "XB": _sb(704, F), "TB": _sb(704, F), "PT": _sb(112, B), "OI": _sb(8, I32), "OU": _sb(8, U), "CC": _sb(8, F), "PK8": _sb(8, B),
    "HM": _sb(2304, B), "HFL": _sb(128, F), "KK": _sb(128, B), "PKM": _sb(128, B), "PSM": _sb(128, B),
    "RS": _sb(640, B), "RT": _sb(768, B), "MI": _sb(512, B), "MK": _sb(512, B), "SS": _sb(240, B), "ZR": _sb(272, B), "SW": _sb(272, B),
    "EI": _sb(32, F), "EL": _sb(32, U), "WR": _sb(408, B), "WI": _sb(136, B), "PK": _sb(136, B), "WS": _sb(48, B), "NON": _sb(128, B), "TRI": _sb(128, B), "CM": _sb(24, B),
    "ID": _sb(4 * 128, B), "FD": _sb(512, B), "CF": _sb(40, B), "L5F": _sb(38, F), "L5I": _sb(38, I32), "L5": _sb(38, U),
    "TAU": _sb(NV, B), "SN": _sb(NV, I32), "SC": _sb(1024, F), "E": _sb(640, HF), "LI": _sb(128, I32), "MU": _sb(96, U),
    "SG": _sb(NV, B), "SI": _sb(NV, B), "NTB": _sb(NV, B),
    "KA": _sb(L, U), "CT": _sb(NT * 128, HF), "LC": _sb(NT * L, HF), "PL": _sb(NT * LONG, HF), "LT": _sb(L, B),
    "WU": _sb(NT * L, U), "WF": _sb(NT * L, HF), "XC": _sb(XCN * 16 * L, B), "NE": _sb(816, B), "NH": _sb(816, B), "W40": _sb(40 * NT, B), "WL": _sb(120, U), "KG": _sb(NT * L, U), "KL": _sb(NT * L, U),
    "XT": _sb(XTN * 8 * L, B), "BD": _sb(2 * 768, B), "SD": _sb(2 * 768, F),
    "R1": _sb(128, I32), "R2": _sb(128, B), "V1": _sb(128, I32), "V2": _sb(128, B), "VB": _sb(240, I32),
    "FF": _sb(608, I32), "CD": _sb(24, B), "MG": _sb(160, B), "FP": _sb(640, HF), "YS": _sb(L, F),
    "DLB": ("dram", [240, 24], U),
    "PS": ("psum", [128, 4096], F),
}
DMA_SEMS = ["d%d" % _i for _i in range(24)]
ARR_SEMS = ["a_%s%d" % (k, t) for k in ("lb", "ct", "pl", "v1", "v2") for t in range(1, NT)]
HAND_SEMS = ["own%d" % _i for _i in range(len(PARCELS))] + ["far%d_%d" % (_k, _i) for _k in range(NT) for _i in range(len(PARCELS))]
SEMAPHORES = ["sV", "sS", "sP", "sG", "sent"] + DMA_SEMS + ARR_SEMS + HAND_SEMS

CY, PCY, GF_, LAT = 0.87e-3, 0.44e-3, 1.56, 0.12
LINK, NEAR, HBM = 6e4, 1.5e5, 2.5e5
HOP, DLAG = 2.5, 2.6
CUT_P = (0, 512, 1024, NV)
CUT_N = (0, 1024, NV)
CUT_O = (0, 4, 5)
CUT_A = (0, 192, 384)
CUT_C = 5 * [(0, 128, 256, 320, 384)]
CUT_T = 5 * [(0, 128, 256, 384)]
JOIN_T = 2 * [(0, 3)] + 3 * [(0, 2, 3)]
JOIN_W = ((0, 1), (1, 3), (3, 5))
LOADS = ("bk", "kd", "lf")
JOIN_D = 5 * [(0, 2, 3)]
BOTH, KG_WIDE, ONCE = True, (3, 4), ()
PLAN = {}


def A(name, lo, hi, step=1, p0=0, p1=128):
    return (name, lo, hi, step, p0, p1)


def cnt(a):
    return (a[2] - a[1] + a[3] - 1) // a[3]


def part(a, i, j):
    return (a[0], a[1] + i * a[3], min(a[2], a[1] + j * a[3]), a[3], a[4], a[5])


def banks_of(a):
    return range(a[1] // 512, (a[1] + (cnt(a) - 1) * a[3]) // 512 + 1) if a[0] == "PS" else ()


def pairs(cut):
    return list(zip(cut, cut[1:]))


def build(g, T, topo, core, rank):
    ops = []
    nd = [0]
    tag = ["K"]

    def ap(a):
        return T[a[0]][a[4]:a[5], a[1]:a[2]:a[3]] if a[3] != 1 else T[a[0]][a[4]:a[5], a[1]:a[2]]

    def two(*aps):
        return all(SCRATCH[a[0]][2] in (B, HF, U) for a in aps)

    def add(alts, reads, writes, **kw):
        o = {"alts": alts, "r": [a for a in reads if isinstance(a, tuple)], "w": list(writes), "tag": tag[0]}
        o.update(kw)
        ops.append(o)
        return len(ops) - 1

    def sc(x):
        return ap(x) if isinstance(x, tuple) else x

    def src(i, off):
        return ap(i).indirect(ap(off)) if off else ap(i)

    def cost(out, i, off, c=1.0):
        n = cnt(out)
        if off:
            return 0.05 + n * GF_ * CY
        return 0.06 + max(64, n * c * (0.5 if two(out, i) else 1.0)) * CY

    def okS(*aps):
        return all(SCRATCH[a[0]][2] in (B, F) for a in aps)

    def act(out, i, func, bias=0.0, scale=1.0, off=None):
        c = 0.065 + (cnt(out) * GF_ if off else max(64, cnt(out))) * CY
        return ("S", lambda e: [e.activation(ap(out), src(i, off), func, bias=sc(bias), scale=sc(scale))], c)

    def ts(out, i, s1, s2, op0, op1=None, s=None, off=None):
        def f(e):
            if op1 is None:
                return [e.tensor_scalar(ap(out), src(i, off), sc(s1), None, op0)]
            return [e.tensor_scalar(ap(out), src(i, off), sc(s1), sc(s2), op0, op1)]
        alts = [("V", f, cost(out, i, off))]
        if s is None and okS(out, i):
            if op0 == ALU.mult and op1 is None:
                s = act(out, i, ACT.Identity, 0.0, s1, off)
            elif op0 == ALU.mult and op1 == ALU.add:
                s = act(out, i, ACT.Identity, s2, s1, off)
        if s:
            alts.append(s)
        return add(alts, [i, s1, s2, off], [out], g=off)

    def keep(out, i):
        return ("G", lambda e: [e.affine_select(ap(out), ap(i), [[0, cnt(out)]], ALU.is_ge, 0.0, 0, 0)], 0.17 + 2 * cnt(out) * CY)

    def cp(out, i, off=None, gp=False):
        alts = [("V", lambda e: [e.tensor_copy(ap(out), src(i, off))], cost(out, i, off))]
        if okS(out, i):
            alts.append(act(out, i, ACT.Copy, off=off))
        if gp:
            alts.append(keep(out, i))
        return add(alts, [i, off], [out], g=off)

    def gcp(out, i):
        return add([keep(out, i)], [i], [out])

    def tt(out, a, b, op, off=None):
        c = 1.0 if "PS" in (a[0], b[0]) else 2.0
        c = cost(out, a, off) if off else 0.06 + max(64, cnt(out) * c) * CY
        return add([("V", lambda e: [e.tensor_tensor(ap(out), src(a, off), ap(b), op)], c)], [a, b, off], [out], g=off)

    def ms(out, v):
        alts = [("V", lambda e: [e.memset(ap(out), v)], cost(out, out, None)),
                ("G", lambda e: [e.iota(ap(out), [[0, cnt(out)]], int(v), 0, allow_small_or_imprecise_dtypes=True)], 0.13 + 2 * cnt(out) * CY)]
        return add(alts, [], [out])

    def least(out, step, d1):
        return add([("V", lambda e: [e.tensor_tensor_scan(ap(out), ap(step), ap(d1), 0.0, ALU.add, ALU.min)], cost(out, d1, None))], [step, d1], [out])

    def lastfit(out, miss, d1):
        return add([("V", lambda e: [e.tensor_tensor_scan(ap(out), ap(miss), ap(d1), 0.0, ALU.min, ALU.max)], cost(out, d1, None))], [miss, d1], [out])

    def turn(b0, b1):
        out, i = A("TB", 32 * b0, 32 * b1), A("XB", 32 * b0, 32 * b1)
        return add([("V", lambda e: [e.transpose(ap(out), ap(i))], cost(out, i, None))], [i], [out])

    def mg(items, start=True, stop=True):
        cut = []
        for o, a, b in items:
            n = cnt(o)
            x = min(n, (512 * (o[1] // 512 + 1) - o[1] + o[3] - 1) // o[3])
            cut += [(part(o, i, j), a, part(b, i, j)) for i, j in ((0, x), (x, n)) if j > i]
        where = [o[1] // 512 for o, a, b in cut]

        def f(e):
            return [e.matmul(ap(o), ap(a), ap(b), start and where[k] not in where[:k], stop and where[k] not in where[k + 1:])
                    for k, (o, a, b) in enumerate(cut)]
        c = 0.03 + sum(max(min(64, cnt(a)), cnt(b)) * (4 if SCRATCH[b[0]][2] == F else 1) for o, a, b in cut) * PCY
        return add([("P", f, c)], [x for it in items for x in it[1:]], [it[0] for it in items])

    def mm(out, prs):
        return mg([(out, a, b) for a, b in prs])

    def iota(out, pat, base=0, cm=0):
        if SCRATCH[out[0]][2] == I32:
            f = lambda e: [e.iota(ap(out), pat, base, cm)]
        else:
            f = lambda e: [e.iota(ap(out), pat, base, cm, allow_small_or_imprecise_dtypes=True)]
        return add([("G", f, 0.13 + 2 * cnt(out) * CY)], [], [out])

    def fill(out, v):
        return iota(out, [[0, cnt(out)]], v)

    def select(out, i, pat, cmp, other, base, cm):
        return add([("G", lambda e: [e.affine_select(ap(out), ap(i), pat, cmp, other, base, cm)], 0.17 + 2 * cnt(out) * CY)], [i], [out])

    def put(out, v):
        return select(out, out, [[0, cnt(out)]], ALU.is_gt, v, 0, 0)

    def join(first):
        some = ops[first:]
        del ops[first:]
        add([(some[0]["alts"][0][0], lambda e: [x for o in some for x in o["alts"][0][1](e)], sum(o["alts"][0][2] for o in some))],
            [a for o in some for a in o["r"]], [a for o in some for a in o["w"]])

    def dma(f, reads, writes, nbytes, n=1):
        nd[0] += 1
        return add([("Y", f, 0.1 + nbytes / HBM)], reads, writes, dma=DMA_SEMS[nd[0] - 1], n=16 * n, lag=2.0 if tag[0] == "K" else DLAG)

    def way(via, us, after, writes=(), reads=(), arr=None, n=0, lag=HOP):
        return add([(via, None, us)], reads, writes, arr=arr, n=n, after=list(after), lag=lag)

    def peer(d):
        return T.cores[(rank + d) % NR]

    def send(items, pick, nbytes, behind=()):
        def f(e):
            trs = []
            for k, (s, _, d, land, sem) in enumerate(items):
                rid, pid, _se = topo.addr(peer(d))
                en = topo.engines(core, peer(d))
                m = sum(1 << en[j] for j in pick(k))
                if len(items) == 1:
                    e.remote_dma(ap(land), s, T.sem[sem], T.sem["sent"], pid, rid, m)
                else:
                    trs.append(RemoteDMATransfer(dst_ids=[DstId(rid=rid, pnc=pid)], dma_engine_mask=m, remote_sem=T.sem[sem], src=s, dst=ap(land)))
            if trs:
                e.remote_dma_fused(trs, local_sem=T.sem["sent"])
            return []
        o = add([("G", f, 0.4)], [it[1] for it in items], [], send=sum(len(pick(k)) for k in range(len(items))))
        for k, it in enumerate(items):
            way("L", nbytes / LINK, [o], [it[3]], behind, it[4], len(pick(k)))

    def ps(lo, hi, step=1, p1=128):
        return A("PS", lo, hi, step, 0, p1)

    def nonzero(out, i):
        return ts(out, i, 0.0, None, ALU.not_equal, s=act(out, i, ACT.Abs))

    def rot(t):
        return 16 * ((8 - SH[t]) % 8)

    def HAm(i, neg, t):
        c = 256 + 768 * (i // 2) + 256 * neg + rot(t)
        return A("HM", c, c + 128)

    def HBm(d):
        c = (128, 256, 768)[d % 3] + 768 * (d // 3) if d else 0
        return A("HM", c, c + 128)

    def IDm(n):
        c = 128 * ("I1", "I16", "I256", "NEG").index(n)
        return A("ID", c, c + 128)

    def row(b, lo=0, hi=32, step=1, p0=0, p1=128):
        return A("XB", 32 * b + lo, 32 * b + hi, step, p0, p1)

    def col(b, p1=128):
        return A("TB", 32 * b, 32 * b + 1, 1, 0, p1)

    Hb = A("HM", 0, 128)
    HP = A("PT", 16, 32)
    P16, Q16, P8, PSW, YSC = range(8, 13)
    SMALL, ROWS, KEYS = 3584, 2048, 2048

    for lo, hi in ((0, CUT_P[1]), (CUT_P[1], NV)):
        dma(lambda e, lo=lo, hi=hi: [e.dma_start(T.IV[:, lo:hi], T.iv[:, lo:hi])], [], [A("IV", lo, hi)], 256 * (hi - lo))
    dma(lambda e: [e.dma_start(T.LVI[:], T.lv[:]), e.dma_start(T.LBI[:], T.lb[:])], [], [A("LVI", 0, 24), A("LBI", 0, 24)], 24576, n=2)
    gcp(A("LBU", 0, 24), A("LBI", 0, 24))
    dma(lambda e: [e.dma_start(T.DLB[0:128, :], T.LBU[:, 0:24]), e.dma_start(T.DLB[128:240, :], T.LBU[0:112, 0:24])], [A("LBU", 0, 24)], [A("DLB", 0, 24)], 12288, n=2)
    for name in LOADS:
        if name == "kd":
            for lo in range(0, NV, 512):
                dma(lambda e, lo=lo: [e.dma_start(T.KDI[:, lo:lo + 512], T.kd[:, lo:lo + 512])], [], [A("KDI", lo, lo + 512)], 262144)
        elif name == "lf":
            dma(lambda e: [e.dma_start(T.LF[:], T.lf[:])], [], [A("LF", 0, NL)], 256 * NL)
        else:
            dma(lambda e: [e.dma_start(T.BK[:], T.bk[:])], [], [A("BK", 0, NB)], 512 * NB)
    send([(T.DLB[rot(t):rot(t) + 128, :], A("DLB", 0, 24), t, A("LBU", 24 * t, 24 * t + 24), "a_lb%d" % t) for t in range(1, NT)],
         lambda k: [2 * k, 2 * k + 1], 6144, [A("LF", 0, 1), A("BK", 0, 1)])

    def bit(b, lo, hi):
        return [[0, 16 >> b], [hi - lo, 2]] + ([[0, 1 << b]] if b else []), lo
    first = len(ops)
    for b in range(4):
        iota(row(b), *bit(b, 1, -1))
    iota(A("OI", 0, 8), [[-16, 8]], 16, 1)
    join(first)
    ms(A("PT", 0, 112), 0.0)
    ms(A("PT", 16, 17), 1.0)
    turn(0, 4)
    ts(A("OU", 0, 8), A("OI", 0, 8), 32.0, None, ALU.min)
    for b, n in ((0, 1), (2, 4)):
        ts(A("PT", 16 + n, 16 + 2 * n), A("PT", 16, 16 + n), col(b), None, ALU.mult)
        ts(A("PT", 16 + 2 * n, 16 + 3 * n), A("PT", 16, 16 + n), col(b + 1), None, ALU.mult)
        ts(A("PT", 16 + 3 * n, 16 + 4 * n), A("PT", 16, 16 + n), col(b), col(b + 1), ALU.mult, ALU.mult)
    cp(Hb, A("PT", 0, 48), A("OU", 0, 8))
    first = len(ops)
    for b, (lo, hi) in enumerate(((16, 32), (1, 4), (1, 256), (1, 16))):
        iota(row(4 + b), *bit(b, lo, hi))
    join(first)
    turn(4, 8)
    ts(A("CC", 0, 1), col(4), col(5), col(6), ALU.mult, ALU.mult)
    ts(A("KK", 0, 128), Hb, A("CC", 0, 1), col(7), ALU.mult, ALU.mult)
    most = max(hi - lo for lo, hi in pairs(CUT_P))
    ms(A("RS", 0, most), 1.0)
    ms(A("RS", 0, most, 16), 2.0 ** 23)
    first = len(ops)
    iota(row(P16), [[0, 2], [1, 16]])
    iota(row(Q16), [[16, 2], [0, 16]], 0, 1)
    iota(row(P8), [[0, 4], [1, 8]])
    join(first)
    turn(P16, PSW)
    ms(row(PSW), 0.0)
    first = len(ops)
    for r, v in ((0, 680), (1, -8), (4, -32), (2, -128), (8, -512)):
        fill(row(PSW, r, 32, 16), v)
    join(first)
    turn(PSW, YSC)
    iota(A("MI", 0, most // 2), [[0, most // 128], [16, 8], [0, 8]])
    ts(A("MK", 0, most // 2), A("MI", 0, most // 2), col(Q16), None, ALU.is_equal)
    first = len(ops)
    iota(A("EI", 0, 20), [[8, 5], [0, 4]])
    iota(A("EI", 20, 32), [[0, 2], [8, 3], [0, 2]])
    join(first)
    ts(A("EL", 0, 32), A("EI", 0, 32), col(P8), None, ALU.add)
    ms(A("SS", 0, 240), 0.0)
    ts(A("SS", 112, 128), row(P16, 0, 16), col(P16), None, ALU.is_equal)
    cp(A("HFL", 0, 128), Hb, gp=True)
    ts(A("PK8", 0, 8), A("PT", 17, 32, 2), 8.0, None, ALU.mult)
    tt(A("PT", 48, 56), A("PT", 16, 32, 2), A("PK8", 0, 8), ALU.add)
    cp(A("PKM", 0, 128), A("PT", 32, 80), A("OU", 0, 8))
    cp(A("PT", 90, 91), col(PSW), gp=True)
    ts(A("PT", 81, 91, 2), A("TB", 32 * P16, 32 * P16 + 5), 0.0, -512.0, ALU.is_equal, ALU.mult)
    cp(A("PSM", 0, 128), A("PT", 64, 112), A("OU", 0, 8))
    tag[0] = "K2"

    def spot(out, pat, r, c):
        return select(out, out, pat, ALU.not_equal, c, -r, 1)
    first = len(ops)
    fill(A("PK", 0, 136), 0)
    fill(A("WS", 0, 48), 0)
    fill(A("ZR", 0, 272), 0)
    iota(A("WI", 0, 136), [[0, 8], [-1, 17]], 17)
    join(first)
    for par in range(2):
        first = len(ops)
        for q in range(4):
            spot(A("PK", 2 + 3 * q, 122, 15), [[-16, 8]], 2 * q + par, (-1.0 / 16, -4.0)[par])
        if par:
            spot(A("PK", 14, 122, 15), [[-16, 8]], 10, 1.0 / 16)
            spot(A("PK", 122, 123), [[0, 1]], 9, -2.0 ** -14)
        join(first)
    select(A("WR", 272, 408), A("WI", 0, 136), [[0, 136]], ALU.is_equal, 0.0, -40, 1)
    fill(A("WR", 0, 272), 0)
    for q in range(2):
        first = len(ops)
        spot(A("WR", 0, 136), [[-5, 8], [0, 17]], q, 4096.0 ** q * 2.0 ** 30)
        spot(A("WR", 136, 272), [[-5, 8], [0, 17]], 2 + q, 4096.0 ** q * 16)
        if q:
            spot(A("WR", 272, 408), [[-5, 8], [0, 17]], 4, 2.0 ** -13)
        join(first)
    fill(A("WR", 0, 272, 17), 0)
    for r in range(4):
        first = len(ops)
        spot(A("WS", 0, 16), [[0, 2], [-16, 8]], r, 64.0 ** r * 2.0 ** 26)
        spot(A("WS", 16, 32), [[0, 2], [-16, 8]], 4 + r, 64.0 ** r)
        if r == 0:
            spot(A("WS", 32, 48), [[0, 2], [-16, 8]], 10, 2.0 ** -17)
        join(first)
    select(A("SW", 0, 272), A("ZR", 0, 272), [[0, 2], [-16, 8], [1, 17]], ALU.not_equal, 2.0 ** -24, -16, 1)
    first = len(ops)
    for z in range(2):
        iota(A("MI", 320 + 96 * z, 416 + 96 * z), [[0, 3], [16, 4], [0, 8]], 64 * z)
    join(first)
    ts(A("MK", 320, 512), A("MI", 320, 512), col(Q16), None, ALU.is_equal)
    for n, v in (("I1", 1.0), ("I16", 16.0), ("I256", 256.0)):
        select(IDm(n), A("ZR", 0, 128), [[-1, 128]], ALU.not_equal, v, 0, 1)
    tag[0] = "K3"
    cp(A("HM", 128, 256), Hb, gp=True)
    for lo, n, c in ((256, 256, 256.0), (512, 256, -256.0), (768, 128, 256.0 ** 2), (896, 128, 256.0 ** 3)):
        ts(A("HM", lo, lo + n), A("HM", 0, n), c, None, ALU.mult)
    ts(A("HM", 1024, 1792), A("HM", 256, 1024), 256.0 ** 3, None, ALU.mult)
    ts(A("HM", 1792, 2304), A("HM", 256, 768), 256.0 ** 6, None, ALU.mult)
    out = A("FD", 0, 512)
    ts(out, A("HM", 256, 768), 2.0 ** 10, 0.0, ALU.mult, ALU.max, s=act(out, A("HM", 256, 768), ACT.Relu, 0.0, 2.0 ** 10))
    wide = 256 * max(j - i for cut in JOIN_T for i, j in pairs(cut))
    fill(A("RT", 0, wide), -2)
    fill(A("RT", 0, wide, 32), 1 << 23)
    tag[0] = "K4"
    select(IDm("NEG"), A("ZR", 0, 128), [[-1, 128]], ALU.not_equal, -2.0 ** 24, 0, 1)
    fill(A("NON", 0, 128), -64)
    select(A("TRI", 0, 128), A("NON", 0, 128), [[1, 128]], ALU.is_gt, 0.0, 0, -1)
    select(A("TRI", 0, 128), A("TRI", 0, 128), [[1, 128]], ALU.not_equal, 64.0 * CAP, 0, -1)
    select(A("CM", 0, 24), A("ZR", 0, 24), [[0, 24]], ALU.is_gt, 2.0 ** -12, 0, 0)
    fill(A("CF", 0, 40), 0)
    fill(A("CF", 0, 40, 5), -1)
    fill(row(YSC), 1)
    for p in (0, 32):
        out = row(YSC, (3 - p) % 5, 32, 5)
        select(out, out, [[0, cnt(out)]], ALU.not_equal, 0.25, -p, 1)
    turn(YSC, YSC + 1)
    iota(A("L5F", 0, 38), [[16, 38]], -2)
    ts(A("L5I", 0, 38), A("L5F", 0, 38), col(P16), 0.2, ALU.add, ALU.mult)
    gcp(A("L5", 0, 38), A("L5I", 0, 38))
    first = len(ops)
    fill(A("MG", 0, 128), 0)
    fill(A("FF", 600, 608), 0)
    for t in range(NT):
        fill(A("FF", 120 * t, 120 * t + 120, 5), (rank + t) % NR + 1)
    join(first)

    def to_list(sb, words, bits, lanes, shift, out):
        n, e0, l0 = cnt(words), 320 * sb, 64 * sb
        ts(A("LI", l0, l0 + n), words, bits, None, ALU.bitwise_and)
        tt(A("E", e0, e0 + 8 * n), A("LI", l0, l0 + n), A("MK", 320 * lanes, 320 * lanes + 8 * n), ALU.mult, off=A("EL", 20 * lanes, 20 * lanes + n // 2))
        b = ps(SMALL + 40 * sb, SMALL + 40 * sb + n)
        s0 = [112 - 16 * ((q + shift) % 8) for q in range(8)]
        mm(b, [(A("SS", s0[q], s0[q] + 128), A("E", e0 + q, e0 + 8 * n, 8)) for q in range(8)])
        cp(out, b)

    tag[0] = "N"
    for c, (lo, hi) in enumerate(pairs(CUT_P)):
        mm(ps(lo, hi), [(Hb, A("IV", lo, hi))])
        ts(A("TAU", lo, hi), ps(lo, hi), 1.0, -1.0, ALU.min, ALU.max, s=act(A("TAU", lo, hi), ps(lo, hi), ACT.Sign))
        mg([(ps(KEYS + i, KEYS + i + 128), A("TAU", i, i + 128), A("KK", 0, 128)) for i in range(lo, hi, 128)])
        least(A("SN", lo, hi), A("RS", 0, hi - lo), ps(KEYS + lo, KEYS + hi))
        to_list(c % 2, A("SN", lo + 15, hi, 16), 15, 0, 0, A("MU", lo // 16, hi // 16))
        cp(A("SG", lo, hi), HP, A("MU", lo // 16, hi // 16))
        tt(A("SI", lo, hi), ps(lo, hi), A("SG", lo, hi), ALU.mult)
        mm(ps(lo, hi), [(A("PSM", 0, 128), A("SG", lo, hi)), (A("PKM", 0, 128), A("SI", lo, hi))])
    for lo, hi in pairs(CUT_N):
        cp(A("NTB", lo, hi), ps(lo, hi))
    tag[0] = "N2"
    for c in range(3):
        lo, hi = 512 * c, 512 * c + 512
        cp(A("KDF", lo, hi), A("KDI", lo, hi), gp=True)
        mm(ps(NV + lo, NV + hi), [(A("HFL", 0, 128), A("KDF", lo, hi))])
        tt(A("KS", lo, hi), ps(NV + lo, NV + hi), A("SG", lo, hi), ALU.mult)
        mm(ps(NV + lo, NV + hi), [(A("HFL", 0, 128), A("KS", lo, hi))])
    for lo, hi in pairs(CUT_N):
        ts(A("KP", lo, hi), ps(NV + lo, NV + hi), 1.0 / 16, None, ALU.mult)

    tag[0] = "C0"
    gcp(A("LVU", 0, 24), A("LVI", 0, 24))
    cp(A("LT", 0, L), A("NTB", 0, NV), A("LVU", 0, 24))
    mm(ps(SMALL + 128, SMALL + 256), [(A("PK", 2 - i, 130 - i), A("LT", 128 * i, 128 * i + 128)) for i in range(3)])
    cp(A("CT", 0, 128), ps(SMALL + 128, SMALL + 256))
    send([(ap(A("CT", 0, 128)), A("CT", 0, 128), t, A("CT", 128 * t, 128 * t + 128), "a_ct%d" % t) for t in range(1, NT)], lambda k: [2 * k, 2 * k + 1],
         32768, [A("LF", 0, 1), A("BK", 0, 1)])
    tag[0] = "A"
    cp(A("KA", 0, L), A("KP", 0, NV), A("LVU", 0, 24))
    for lo, hi in pairs(CUT_A):
        cp(A("XT", 16 * lo, 16 * hi), A("LF", 0, NL), A("KA", lo, hi))

    def xa(d):
        return A("XT", d, 16 * L, 16)
    legs, last = [], []
    for n, (lo, hi) in enumerate(PARCELS):
        back = 256 * n
        for some in (((1, 3, 5),), ((2, 4), (0,)))[n]:
            mg([(ps(AT[i] - back, AT[i] + L - back), IDm(m), xa(3 * i + j)) for i in some for j, m in enumerate(("I1", "I16", "I256")) if 3 * i + j < 16])
        ts(A("PL", lo, hi), ps(lo - back, hi - back), (16.0, 2.0 ** -8)[n], None, ALU.mult)

        def to_helper(e, n=n, lo=lo, hi=hi):
            h = helpers(T, topo, rank)[0]
            rid, pid, _se = topo.addr(h)
            en = topo.engines(core, h)
            e.remote_dma(T.PL[:, lo:hi], T.PL[:, lo:hi], T.sem["own%d" % n], T.sem["sent"], pid, rid, sum(1 << x for x in en[-8:]))
            return []
        o = add([("G", to_helper, 0.4)], [A("PL", lo, hi)], [], send=8)
        legs.append(way("R", 256 * (hi - lo) / NEAR, [o], lag=HOP + 1.0))
    for t in range(1, NT, 2):
        for n, (lo, hi) in enumerate(PARCELS):
            o = way("H", 256 * (hi - lo) / LINK, [legs[n]], lag=HOP + 1.0)
            last[n:] = [way("F", 256 * (hi - lo) / NEAR, [o])]
        for x in (t, t + 1):
            way("Z", 0.0, last, [A("PL", LONG * x, LONG * x + LONG)], (), "a_pl%d" % x, 8 * len(PARCELS), 0.0)

    def home(t, out, land, sem, nbytes):
        send([(ap(out), out, -t, land, sem)], lambda k: list(range(8)), nbytes)

    def claims(t):
        tag[0] = "C%d" % t
        sb, xc = t % 2, 16 * L * (t % XCN)
        for lo, hi in JOIN_W:
            if lo == t:
                cp(A("WU", L * lo, L * hi), A("BK", 0, NB), A("LBU", 24 * lo, 24 * hi))
        dma(lambda e: [e.dma_start(T.LC[0:41, L * t + 128 * i:L * t + 128 * i + 128], T.CT[i:123:3, 128 * t:128 * t + 128]) for i in range(3)],
            [A("CT", 128 * t, 128 * t + 128)] + ([] if t else [A("LF", 0, 1)]), [A("LC", L * t, L * t + L)], 30720, n=3)
        gcp(A("WF", L * t, L * t + L), A("WU", L * t, L * t + L))
        first = len(ops)
        for c, w in enumerate((2, 1, 0, 1, 2)):
            gcp(A("W40", 40 * t + 8 * c, 40 * t + 8 * c + 8), A("WS", 16 * w + SH[t], 16 * w + SH[t] + 8))
        join(first)
        for lo, hi in pairs(CUT_C[t]):
            cp(A("XC", xc + 16 * lo, xc + 16 * hi), A("NTB", 0, NV), A("WU", L * t + lo, L * t + hi))
        n0, runs = 408 * sb, 3 if t in ONCE else 2

        def at(i, r):
            return ROWS + (512 * i + 136 * r if i else 376 - 136 * r)
        for i in range(3):
            x0, l0, lo = xc + 2048 * i, L * t + 128 * i, min(at(i, 0), at(i, runs - 1))

            def lane(w, r):
                return (ps(at(i, r), at(i, r) + 136), A("LC", l0, l0 + 128, 1, 0, 41), A("WR", 136 * w, 136 * w + 136, 1, 0, 41))

            def slots(c0, w0, n):
                return [(ps(c0 + 16 - k, c0 + 17 * n, 17), A("XC", x0 + k, x0 + 2048, 16), A("W40", 40 * t + w0, 40 * t + w0 + n)) for k in range(16)]
            nodes = (ps(at(i, runs - 1), at(i, runs - 1) + 136), A("WF", l0, l0 + 128), A("SW", 17 * SH[t], 17 * SH[t] + 136))
            if t in ONCE:
                mg([lane(0, 0), lane(1, 1), lane(2, 2), nodes] + slots(lo, 16 if i else 0, 24))
            else:
                mg([lane(0, 0)] + slots(at(i, 0), 16, 8) + [lane(1, 0), lane(2, 1), nodes] + slots(lo, 24 if i else 0, 16))
        for i0, i1 in pairs(JOIN_D[t]):
            first = ps(at(i0, 0), at(i0, 0) + 136 * (i1 - i0))
            if t in ONCE:
                cp(A("NH", n0 + 136 * i0, n0 + 136 * i1), first)
            else:
                nonzero(A("NE", n0 + 136 * i0, n0 + 136 * i1), first)
        for i in range(3):
            ne = A("NE", n0 + 136 * i, n0 + 136 * i + 136)
            if t in ONCE:
                tt(ne, ps(at(i, 1), at(i, 1) + 136), A("NH", n0 + 136 * i, n0 + 136 * i + 136), ALU.not_equal)
            lastfit(A("SC", n0 + 136 * i, n0 + 136 * i + 136), ne, ps(at(i, runs - 1), at(i, runs - 1) + 136))
        out = v("R1" if t else "V1", t)
        ts(out, A("SC", n0 + 16, n0 + 408, 17), 2.0 ** 24, -NONE, ALU.mult, ALU.add)
        if t:
            home(t, out, v("V1", t), "a_v1%d" % t, 12288)
        to_list(sb, out, 2047, 1, SH[t], A("WL", 24 * t, 24 * t + 24))

    def tests(t):
        tag[0] = "T%d" % t
        d0, k0, x0, lf = 768 * (t % 2), L * t, 8 * L * ((t + 2) % XTN), A("LF", 0, NL)
        if t in KG_WIDE:
            wide = A("KS", L * (t % 2), L * (t % 2) + L)
            cp(wide, A("KP", 0, NV), A("WL", 24 * t, 24 * t + 24))
            gcp(A("KG", k0, k0 + L), wide)
        else:
            cp(A("KG", k0, k0 + L), A("KP", 0, NV), A("WL", 24 * t, 24 * t + 24))
        dma(lambda e: [e.dma_start(T.KL[z:128:2, k0 + 192 * y:k0 + 192 * y + 192], T.KG[y:128:2, k0 + 192 * z:k0 + 192 * z + 192])
                       for y in (1, 0) for z in range(2)], [A("KG", k0, k0 + L)], [A("KL", k0, k0 + L)], 98304, n=4)
        for lo, hi in pairs(CUT_T[t]):
            out = A("XT", x0 + 8 * lo, x0 + 8 * hi)
            ts(out, lf, 16.0, None, ALU.mult, off=A("KL", k0 + 192 + lo // 2, k0 + 192 + hi // 2))
            tt(out, lf, out, ALU.add, off=A("KL", k0 + lo // 2, k0 + hi // 2))

        def place(i):
            return 256 * ((3 * t + i) % 8)
        for i0, i1 in pairs(JOIN_T[t]):
            for lo in range(128 * i0, 128 * i1, 128):
                steps = []
                for y in range(2):
                    c, hi = place(lo // 128) + 128 * y, lo + 128

                    def mine(i):
                        return [(ps(c, c + 128), HAm(i, 1 - y, t), A("PL", LONG * t + AT[i] + lo, LONG * t + AT[i] + hi))]

                    def theirs(i):
                        return [(ps(c + 64 * z, c + 64 * z + 64), HBm(i), A("XT", x0 + 8 * lo + 2 * i + z, x0 + 8 * hi, 16)) for z in range(2)]
                    steps += (mine(5) + theirs(7) + mine(4) + theirs(6) + theirs(5) +
                              mine(3) + theirs(4) + mine(2) + theirs(3) + theirs(2) + mine(1) + theirs(1) + mine(0) + theirs(0))
                    if y or not BOTH:
                        mg(steps)
                        steps = []
            both, c0, n = ps(place(i0), place(i0) + 256 * (i1 - i0)), d0 + 256 * i0, 256 * (i1 - i0)
            nonzero(A("BD", c0, c0 + n), both)
            for i in range(i0, i1):
                c, f0 = d0 + 256 * i, 16 * SH[t]
                mg([(ps(place(i) + s, place(i) + 256, 2), A("BD", c + 128 * y, c + 128 * y + 128), A("FD", 256 * (s ^ y) + f0, 256 * (s ^ y) + f0 + 128))
                    for s in range(2) for y in range(2)])
            least(A("SD", c0, c0 + n), A("RT", 0, n), both)
        out = v("R2" if t else "V2", t)
        ts(out, A("SD", d0 + 31, d0 + 768, 32), 61.0, 2.0 ** 20, ALU.add, ALU.min)
        if t:
            home(t, out, v("V2", t), "a_v2%d" % t, 6144)

    def v(name, t):
        return A(name, 24 * t, 24 * t + 24)

    def tested(t):
        tag[0] = "L%d" % t
        dead, n = ps(SMALL + 80, SMALL + 104), SMALL + 104
        if t:
            mm(dead, [(IDm("NEG"), v("MG", s)) for s in range(t)])
            tt(A("CD", 0, 24), v("V1", t), dead, ALU.is_lt)
        else:
            ts(A("CD", 0, 24), v("V1", t), 0.0, None, ALU.is_lt)
        mg([(ps(n, n + 24), A("NON", 0, 128), A("CM", 0, 24)), (ps(n, n + 24), A("TRI", 0, 128), A("CD", 0, 24)),
            (ps(n + 8, n + 24), A("NON", 0, 128), A("CD", 0, 16)), (ps(n + 16, n + 24), A("NON", 0, 128), A("CD", 0, 8))])

    def merged(t):
        tag[0] = "M%d" % t
        tt(v("MG", t), v("V2", t), ps(SMALL + 104, SMALL + 128), ALU.is_lt)

    def fields():
        tag[0] = "F"
        ts(A("FF", 1, 600, 5), A("V1", 0, 120), 2047, None, ALU.bitwise_and)
        for b in range(2):
            ts(A("VB", 120 * b, 120 * b + 120), A("V1", 0, 120), 11 + 3 * b, 5 << b, ALU.logical_shift_right, ALU.bitwise_and)
        tt(A("FF", 2, 600, 5), A("VB", 0, 120), A("VB", 120, 240), ALU.add)
        mg([(ps(ROWS + 128 * i, ROWS + 128 * i + 128, 1, 40), A("CF", 0, 40), IDm("I1")) for i in range(3)], stop=False)

    def store(t0, t1):
        tag[0] = "O%d" % (t1 - 1)
        lo, hi, end = 24 * t0, 24 * t1, -(-120 * t1 // 16) * 16
        ts(A("FF", 5 * lo + 3, 5 * hi, 5), A("V2", lo, hi), 4 * MAGIC, 4 * MAGIC, ALU.add, ALU.subtract)
        tt(A("FF", 5 * lo + 4, 5 * hi, 5), A("FF", 5 * lo + 3, 5 * hi, 5), A("V2", lo, hi), ALU.subtract)
        tt(A("FP", 5 * lo, end), A("MG", 0, -(-end // 5)), A("FF", 5 * lo, end), ALU.mult, off=A("L5", 5 * lo // 16, end // 16))
        mg([(ps(ROWS + 128 * (i % 3), ROWS + 128 * (i % 3) + 128, 1, 40), A("FP", 40 * i, 40 * i + 40), IDm("I1")) for i in range(3 * t0, 3 * t1)],
           start=False, stop=t1 == NT)

    for t in range(NT):
        claims(t)
    for t in range(NT):
        tests(t)
    fields()
    for t in range(NT):
        tested(t)
        merged(t)
        for t0, t1 in pairs(CUT_O):
            if t1 == t + 1:
                store(t0, t1)
    ts(A("YS", 0, L, 1, 0, 40), ps(ROWS, ROWS + L, 1, 40), col(YSC, 40), None, ALU.mult)
    dma(lambda e: [e.dma_start(T.y[:], T.YS[0:40, :])], [A("YS", 0, L)], [], 61440)
    return ops


def depend(ops):
    def meet(a, b):
        if a[2] <= b[1] or b[2] <= a[1]:
            return False
        return not (a[3] == b[3] and a[3] > 1 and (a[1] - b[1]) % a[3])
    hist = {}
    deps = []
    for i, o in enumerate(ops):
        d = set(o.get("after", ()))
        acc = [(a, False) for a in o["r"]] + [(a, True) for a in o["w"]]
        for a, wr in acc:
            for (b, bw, j) in hist.get(a[0], []):
                if (wr or bw) and meet(a, b):
                    d.add(j)
        for a, wr in acc:
            h = hist.setdefault(a[0], [])
            if wr and a[3] == 1 and a[4:] in ((), (0, 128)):
                h[:] = [x for x in h if not (a[1] <= x[0][1] and x[0][2] <= a[2])]
            h.append((a, wr, i))
        d.discard(i)
        deps.append(sorted(d))
    return deps


QUEUES = "VSPGYLRHFZ"
PACES = ((1.0, 1.15, 1.15, 1.15, 0.15, 1.1, 1.1), (1.0, 1.0, 1.0, 1.0, 0.12, 1.0, 1.0), (0.8, 1.25, 1.25, 1.25, 0.15, 1.1, 1.2), (1.3, 1.1, 1.1, 1.1, 0.2, 1.3, 1.5))
PARTS = "C0 A C1 T0 C2 C3 T1 C4 T2 T3 T4".split()
ONV = [("A", "XT", 0)] + [("C%d" % t, "XC", k) for t in range(4) for k in (2, 3)] + [("C%d" % t, "NE", 1) for t in range(NT)]
TABLES = {"K": -400.0, "N": -400.0, "N2": -390.0, "K2": -100.0, "K3": -95.0, "K4": -90.0}
HOLD, OWN, FIRST, STEP = 0.2, 1.0, 200.0, 0.02
SHARES = (0.25, 0.25, 0.25, 0.25)
TRIES, ROUNDS, SEED, WARM, HEAT, MEAN = 28000, 18000, 2, 0.08, 0.02, 0.02
JUST, AGAIN, SWAP, WP = 8, 0.2, 0.15, 0.0
WV, WS, WX, WH, CRIT = 0.2, 0.1, 0.1, 0.3, 0.3


def place(order, links, eng, cs, banks, fixed):
    n, nq = len(eng), len(QUEUES)
    st, fin, ch = [0.0] * n, [0.0] * n, [0] * n
    busy = [([], [], 0.0 if r < nq else LAT) for r in range(nq + 8)]
    for i in order:
        t0 = 0.0
        for j, x in links[i]:
            if fin[j] + x > t0:
                t0 = fin[j] + x
        k = fixed[i]
        if k >= 0 and not banks[i]:
            a, z, _ = busy[eng[i][k]]
            c = cs[i][k]
            x = y = len(z)
            while x and z[x - 1] > t0:
                x -= 1
            w = c - 1e-9
            while x < y and a[x] < t0 + w:
                t0 = z[x]
                x += 1
            st[i], fin[i], ch[i] = t0, t0 + c, k
            a.insert(x, t0)
            z.insert(x, t0 + c)
            continue
        best = 1e9
        for k in (k,) if k >= 0 else range(len(eng[i])):
            e, c = eng[i][k], cs[i][k]
            res = [busy[e]] + [busy[b] for b in banks[i]]
            t, moved = t0, True
            while moved:
                moved = False
                for a, z, w in res:
                    x = y = len(z)
                    while x and z[x - 1] > t:
                        x -= 1
                    w += c - 1e-9
                    while x < y and a[x] < t + w:
                        t, x, moved = z[x], x + 1, len(res) > 1
            v = t + c if e else t + 2 * c
            if v < best:
                best, st[i], fin[i], ch[i], took = v, t, t + c, k, res
        t = st[i]
        for a, z, w in took:
            x = len(a)
            while x and a[x - 1] > t:
                x -= 1
            a.insert(x, t)
            z.insert(x, fin[i] + w)
    return st, fin, ch


def fill_gaps(ops, order, ch, pre, eng, cs, banks, rng):
    n, nq = len(ops), len(QUEUES)
    suc = [[] for _ in range(n)]
    for i in range(n):
        for j, x in pre[i]:
            suc[j].append((i, x))

    def justify(s, fixed):
        s = place(sorted(range(n), key=lambda i: (-s[1][i], -i)), suc, eng, cs, banks, fixed)
        return place(sorted(range(n), key=lambda i: (-s[1][i], i)), pre, eng, cs, banks, fixed)

    def value(s):
        return max(s[1]) + WS * sum(s[1]) / n + WV * sum(cs[i][0] for i in flex if not s[2][i]) + WX * sum(s[1][i] for i in moves) / len(moves) + WH * s[1][relay] + WP * sum(s[1][i] for i in tensor) / len(tensor)
    tensor = [i for i in range(n) if eng[i][0] == 2 and cs[i][0] > 1.5]
    big = [i for i in range(n) if eng[i][0] < 2 and cs[i][0] > 1.3]

    def blocked(s):
        st, fin, ch = s
        ends = {}
        for j in range(n):
            for r in (eng[j][ch[j]],) + banks[j]:
                ends[(r, round(fin[j] + (LAT if r >= nq else 0.0), 6))] = j
        found, i = [], max(range(n), key=lambda j: fin[j])
        while st[i] > 1e-9:
            j = [j for j, x in pre[i] if fin[j] + x > st[i] - 1e-7]
            if not j:
                j = [ends[k] for k in [(r, round(st[i], 6)) for r in (eng[i][ch[i]],) + banks[i]] if k in ends]
                if not j:
                    break
                found.append((i, j[0]))
            i = j[0]
        return found
    held = [None, None]
    relay = [i for i in range(n) if QUEUES[eng[i][0]] == "R"][-1]
    moves = [i for i in range(n) if QUEUES[eng[i][0]] in "LYH"]
    groups = {}
    for i, o in enumerate(ops):
        groups.setdefault(o["tag"], []).append(i)
        groups.setdefault((o["tag"], o["w"][0][0] if o["w"] else ""), []).append(i)
    groups = list(groups.values())
    flex = [i for i in range(n) if len(eng[i]) > 1]
    fixed = [-1 if len(eng[i]) > 1 and o["tag"][0] == "K" else ch[i] for i, o in enumerate(ops)]
    s = place(order, pre, eng, cs, banks, fixed)
    for _ in range(JUST):
        s = justify(s, fixed)
    now = best = (value(s), s, fixed)
    for r in range(TRIES):
        p, ch, fixed = list(now[1][0]), now[1][2], list(now[2])
        u = rng.random()
        if rng.random() < CRIT:
            if held[0] is not now:
                held[:] = [now, blocked(now[1])]
            if not held[1]:
                continue
            i, j = held[1][int(rng.integers(0, len(held[1])))]
            if u < 0.4:
                p[i] = p[j] - 1e-4 - (rng.exponential() if u < 0.2 else 0.0)
            elif u < 0.8 or len(eng[j]) == 1:
                p[j] = p[i] + 1e-4 + (rng.exponential() if u < 0.6 else 0.0)
                for k in range(j, n):
                    for m, x in pre[k]:
                        if p[k] <= p[m]:
                            p[k] = p[m] + 1e-6
            else:
                fixed[j] = (ch[j] + int(rng.integers(1, len(eng[j])))) % len(eng[j])
        elif u < SWAP:
            i = big[int(rng.integers(0, len(big)))]
            near = [j for j in big if j != i and abs(p[j] - p[i]) < 12]
            j = near[int(rng.integers(0, len(near)))]
            p[i], p[j] = p[j], p[i]
            if len(eng[i]) > 1 and len(eng[j]) > 1:
                fixed[i], fixed[j] = ch[j], ch[i]
            for k in range(min(i, j), n):
                for m, x in pre[k]:
                    if p[k] <= p[m] and m in (i, j):
                        p[k] = p[m] + 1e-6
        elif u < 0.3:
            for i in rng.integers(0, n, int(rng.integers(1, 4))):
                p[i] += rng.normal() * 3.0
        elif u < 0.55:
            d = rng.normal() * rng.choice([1.0, 3.0, 8.0])
            for i in groups[int(rng.integers(0, len(groups)))]:
                p[i] += d
        elif u < 0.8:
            i = flex[int(rng.integers(0, len(flex)))]
            fixed[i] = (ch[i] + int(rng.integers(1, len(eng[i])))) % len(eng[i])
            like = [j for j in flex if ch[j] == fixed[i] and ch[i] < len(eng[j]) and abs(cs[j][0] - cs[i][0]) < 0.3 and abs(p[j] - p[i]) < 15]
            if u < 0.7 and like:
                fixed[like[int(rng.integers(0, len(like)))]] = ch[i]
        else:
            t0, w = rng.random() * max(now[1][1]), rng.choice([2.0, 8.0])
            for i in range(n):
                if t0 < p[i] < t0 + w:
                    p[i] += rng.normal() * w / 8
        for i in range(n - 1, -1, -1):
            for j, x in pre[i]:
                if p[j] >= p[i]:
                    p[j] = p[i] - 1e-6
        s = place(sorted(range(n), key=lambda i: p[i]), pre, eng, cs, banks, fixed)
        if rng.random() < AGAIN:
            s = justify(s, fixed)
        v = value(s)
        if v <= now[0] + WARM * (1.0 - r / TRIES) * rng.exponential():
            now = (v, s, fixed)
            if v < best[0]:
                best = now
    st, fin, ch = best[1]
    return sorted(range(n), key=lambda i: (st[i], i)), ch


def schedule(ops, deps):
    n, nq = len(ops), len(QUEUES)
    eng = [[QUEUES.index(a[0]) for a in o["alts"]] for o in ops]
    banks = [tuple(sorted({nq + b for a in o["r"] + o["w"] for b in banks_of(a)})) for o in ops]
    pre, suc, before = [], [[] for _ in range(n)], []
    for i in range(n):
        m = 0
        for j in deps[i]:
            m |= before[j]
        pre.append([j for j in deps[i] if not m >> j & 1])
        for j in pre[i]:
            suc[j].append(i)
        before.append(m | sum(1 << j for j in deps[i]))
    paces = []
    for gf, kc, kp, kg, wait, hop, link in PACES:
        cs = [[c * (kp if e == "P" else kg if e == "G" else link if e not in "VS" else gf if o.get("g") else kc) for e, _, c in o["alts"]] for o in ops]
        lag = [o["lag"] * hop if "lag" in o else wait for o in ops]
        paces.append((cs, [[(j, 0.0 if eng[i][0] == eng[j][0] == 2 else lag[j]) for j in pre[i]] for i in range(n)], wait))

    def replay(order, ch, pace):
        cs, links, wait = pace
        free, pe, fin = [0.0] * (nq + 8), [False] * (nq + 8), [0.0] * n
        for i in order:
            k = ch[i]
            e = eng[i][k]
            t = free[e]
            for j, x in links[i]:
                x += fin[j]
                if x > t:
                    t = x
            if banks[i]:
                for b in banks[i]:
                    x = free[b] if e == 2 and pe[b] else free[b] + wait
                    if x > t:
                        t = x
                t += cs[i][k]
                for b in banks[i]:
                    free[b], pe[b] = t, e == 2
            else:
                t += cs[i][k]
            fin[i] = free[e] = t
        return fin

    def value(order, ch):
        v = 0.0
        for pace, w in zip(paces, weight):
            fin = replay(order, ch, pace)
            v += (max(fin) + MEAN * sum(fin) / n) * w
        return v

    cs, links, wait = paces[0]
    long_ = [bool(o.get("g")) and cs[i][0] > 0.7 and o["tag"] in PARTS and o["w"][0][0] in ("XT", "XC") for i, o in enumerate(ops)]

    plain, t, begin = [0.0] * n, 0.0, {}
    for p in PARTS:
        begin[p] = t
        for i in range(n):
            if ops[i]["tag"] == p and eng[i][0] < 2:
                plain[i] = t
                t += cs[i][0] / 2
    for i, o in enumerate(ops):
        tg = o["tag"]
        if tg in TABLES:
            plain[i] = TABLES[tg] + i * STEP
        elif not long_[i]:
            plain[i] = begin[tg if tg in begin else "T" + (tg + "4")[1]] + i * 1e-3 - (0.0 if eng[i][0] == 2 and cs[i][0] > 0.4 else FIRST)
    kinds = [i if long_[i] or "dma" in o or o["tag"] in TABLES else (o["tag"], o["w"][0][0] if o["w"] else "") for i, o in enumerate(ops)]
    keys = sorted(set(kinds), key=str)
    kinds = [keys.index(k) for k in kinds]

    def dues(shift):
        return [plain[i] + shift[kinds[i]] for i in range(n)]

    def dispatch(due, own, onv):
        left = [len(p) for p in pre]
        can = [e if len(e) == 1 or ops[i]["tag"][0] == "K" else [e[0 if i in onv else -1]] for i, e in enumerate(eng)]
        ready = [[] for _ in range(nq)]
        at, fin, ch, order = [0.0] * n, [0.0] * n, [0] * n, []
        free, pe = [0.0] * (nq + 8), [False] * (nq + 8)
        for i in range(n):
            if not left[i]:
                for e in can[i]:
                    ready[e].append(i)
        for _ in range(n):
            best, be = 1e9, -1
            for e in range(nq):
                if ready[e] and free[e] < best:
                    t = 1e9
                    for i in ready[e]:
                        x = at[i]
                        for b in banks[i]:
                            y = free[b] if e == 2 and pe[b] else free[b] + wait
                            if y > x:
                                x = at[i] = y
                        if x < t:
                            t = x
                    t = max(t, free[e])
                    if t < best:
                        best, be = t, e
            i = min((i for i in ready[be] if at[i] <= best + (0.0 if long_[i] else HOLD)),
                    key=lambda i: due[i] + (own if be == 0 and len(eng[i]) > 1 else 0.0))
            k = ch[i] = eng[i].index(be)
            fin[i] = free[be] = max(best, at[i]) + cs[i][k]
            for b in banks[i]:
                free[b], pe[b] = fin[i], be == 2
            for e in can[i]:
                ready[e].remove(i)
            order.append(i)
            for j in suc[i]:
                left[j] -= 1
                if not left[j]:
                    at[j] = max(fin[x] + y for x, y in links[j])
                    for e in can[j]:
                        ready[e].append(j)
        return order, ch

    rng = np.random.default_rng(SEED)
    both = [i for i in range(n) if len(eng[i]) > 1 and ops[i]["tag"][0] != "K"]
    onv = {i for p, b, k in ONV for i in [i for i in both if ops[i]["tag"] == p and ops[i]["w"][0][0] == b][k:k + 1]}
    order, ch = dispatch(dues([0.0] * len(keys)), OWN, onv)
    weight = [1.0 / max(replay(order, ch, pace)) for pace in paces]
    weight = [w / weight[0] * s for w, s in zip(weight, SHARES)]
    flex = [i for i in range(n) if len(eng[i]) > 1]
    order, ch = fill_gaps(ops, order, ch, links, eng, cs, banks, rng)
    PLAN["first"] = [max(replay(order, ch, pace)) for pace in paces]
    now = best = (value(order, ch), order, ch)
    draw = rng.random((ROUNDS, 5)).tolist()
    for r in range(ROUNDS):
        u, a, b, c, d = draw[r]
        order, ch = now[1], now[2]
        if u < 0.2:
            i = flex[int(a * len(flex))]
            ch = list(ch)
            was = ch[i]
            ch[i] = (was + 1 + int(b * (len(eng[i]) - 1))) % len(eng[i])
            if u < 0.1:
                p = order.index(i)
                near = [j for j in order[max(0, p - 30):p + 30] if j != i and ch[j] == ch[i] and len(eng[j]) > max(was, 1)]
                if near:
                    ch[near[int(c * len(near))]] = was
        else:
            p = int(a * n)
            far = 1 + int(-math.log(1.0 - b) * (4.0, 12.0, 40.0)[int(c * 3)])
            step, q, kin = (-1, max(0, p - far), pre) if u < 0.6 else (1, min(n - 1, p + far), suc)
            take, need = {order[p]}, set(kin[order[p]])
            for x in range(p + step, q + step, step):
                if order[x] in need:
                    take.add(order[x])
                    need.update(kin[order[x]])
            lo, hi = min(p, q), max(p, q) + 1
            moved, rest = [j for j in order[lo:hi] if j in take], [j for j in order[lo:hi] if j not in take]
            order = order[:lo] + (moved + rest if step < 0 else rest + moved) + order[hi:]
        x = value(order, ch)
        if x <= now[0] - HEAT * (1.0 - r / ROUNDS) * math.log(1.0 - d):
            now = (x, order, ch)
            if x < best[0]:
                best = now
    _, order, ch = best
    PLAN["last"] = [max(replay(order, ch, pace)) for pace in paces]
    last = {}
    for i in order:
        for b in banks[i]:
            if b in last and last[b] not in deps[i]:
                deps[i].append(last[b])
            last[b] = i
    return [(i, ch[i]) for i in order], replay(order, ch, paces[0])


def helpers(T, topo, rank):
    c = T.cores[rank]
    return [h for h in topo.cores_of(c) if h not in T.cores and topo.die(h) == topo.die(c)][:2]


def routes(T, topo, rank):
    c, out = T.cores[rank], {}
    for t in range(1, NT):
        out.setdefault(topo.chip(T.cores[(rank + t) % NR]), []).append(t)
    res = []
    for chip, visits in out.items():
        gate = [r for r in range(NR) if topo.chip(T.cores[r]) == chip and topo.die(T.cores[r]) == topo.die(c)]
        if chip != topo.chip(c) and len(visits) > 1 and gate:
            res.append((visits, helpers(T, topo, gate[0])[1]))
        else:
            res += [([t], None) for t in visits]
    return res


def hand_on(g, core, T, topo, rank):
    sent = [0]

    def write(to, t_to, t_from, n, sem, last):
        lo, hi = PARCELS[n]
        rid, pid, _se = topo.addr(to)
        en = topo.engines(core, to)
        g.remote_dma(T.PL[:, LONG * t_to + lo:LONG * t_to + hi], T.PL[:, LONG * t_from + lo:LONG * t_from + hi], T.sem[sem], T.sem["sent"], pid, rid,
                     sum(1 << x for x in (en[-8:] if last else en[:8])))
        sent[0] += 8
    if core == helpers(T, topo, rank)[0]:
        legs = [(k, n) for k in range(len(routes(T, topo, rank))) for n in range(len(PARCELS))]
        here = 0
        for k, n in legs:
            visits, gate = routes(T, topo, rank)[k]
            while here <= n:
                g.wait_ge(T.sem["own%d" % here], 8)
                here += 1
            if gate is None:
                write(T.cores[(rank + visits[0]) % NR], visits[0], 0, n, "a_pl%d" % visits[0], True)
            else:
                write(gate, visits[0], 0, n, "far%d_%d" % (visits[0], n), True)
    else:
        for visits, r in sorted((visits, r) for r in range(NR) for visits, gate in routes(T, topo, r) if gate == core):
            for n in range(len(PARCELS)):
                g.wait_ge(T.sem["far%d_%d" % (visits[0], n)], 8)
                for k, t in enumerate(visits):
                    write(T.cores[(r + t) % NR], t, visits[0], n, "a_pl%d" % t, k % 2)
    if sent[0]:
        g.wait_ge(T.sem["sent"], sent[0])


def rank_program(g, core, T, topo):
    rank = T.rank_of(core)
    if rank is None:
        for r in range(NR):
            if core in helpers(T, topo, r):
                hand_on(g, core, T, topo, r)
        return
    ops = build(g, T, topo, core, rank)
    if "order" not in PLAN:
        PLAN["deps"] = depend(ops)
        PLAN["order"], PLAN["fin"] = schedule(ops, PLAN["deps"])
    deps = PLAN["deps"]
    eng = {"V": g.vector, "S": g.scalar, "P": g.tensor, "G": g, "Y": g.sync}
    count = {e: 0 for e in "VSPG"}
    token, known, born = {}, {}, {}
    seen = {e: {} for e in eng}
    total = {}
    sent = 0
    for i, k in PLAN["order"]:
        o = ops[i]
        e, f, _ = o["alts"][k]
        if f is None:
            if o["arr"]:
                token[i] = (o["arr"], o["n"])
                total[o["arr"]] = o["n"]
                born[token[i]] = len(born)
            continue
        need = {}
        for j in deps[i]:
            if j in token and not (e == "P" and token[j][0] == "sP"):
                s, v = token[j]
                need[s] = max(need.get(s, 0), v)
        for s, v in sorted(need.items(), key=lambda x: -born[x]):
            if seen[e].get(s, 0) < v:
                eng[e].wait_ge(T.sem[s], v)
                seen[e][s] = v
                for s2, v2 in known.get((s, v), {}).items():
                    seen[e][s2] = max(seen[e].get(s2, 0), v2)
        ins = f(eng[e])
        if "send" in o:
            sent += o["send"]
        elif "dma" in o:
            for x in ins:
                x.then_inc(T.sem[o["dma"]], 16)
            token[i] = (o["dma"], o["n"])
            total[o["dma"]] = o["n"]
        else:
            for x in ins:
                x.then_inc(T.sem["s" + e], 1)
            count[e] += len(ins)
            token[i] = ("s" + e, count[e])
            total["s" + e] = count[e]
        if i in token:
            known[token[i]], born[token[i]] = dict(seen[e]), len(born)
    total["sent"] = sent
    for s, v in total.items():
        if seen["G"].get(s, 0) < v:
            g.wait_ge(T.sem[s], v)
